import numpy as np, ml_dtypes
CORES = [3,11,19,27,35,43]
N = 6
BF = ml_dtypes.bfloat16
def gentries(a):
    return np.ascontiguousarray(a.reshape(8, 16, -1).transpose(0, 2, 1)).reshape(8, -1)
def gtable(e):
    e = np.asarray(e); return np.ascontiguousarray(e.reshape(8, -1, 16).transpose(0, 2, 1)).reshape(128, -1).astype(np.int32)
W, P, V, EPS = 4096, 128, 6, 1
S = W // P
AG, LO, WIN, MAJ = 12, 4, 12, 9
def pick(rng, cl, want):
    out = np.zeros(want.shape, np.int64); z = rng.random(want.shape)
    for q in range(N):
        for g in range(8):
            o = np.argsort(cl[q, g], kind="stable"); lo = np.searchsorted(cl[q, g][o], np.arange(6)); n = np.maximum(lo[1:] - lo[:-1], 1); v = want[q, g]
            out[q, g] = o[np.minimum(lo[v] + (z[q, g] * n[v]).astype(np.int64), W - 1)]
    return out
def turned(a):
    return np.ascontiguousarray(np.swapaxes(a, 2, 3))
def pack(X, L, R, y, w):
    return {"xc": np.ascontiguousarray(X.reshape(N, 128, W)).astype(np.float32).astype(BF), "lsr": np.ascontiguousarray(L.reshape(N, 128, W)).astype(np.int32),
            "jur": np.stack([gtable(a.reshape(8, -1)) for a in R]), "own": np.ascontiguousarray(y.reshape(N, 128, P)).astype(np.float32).astype(BF), "wgt": w.reshape(N, 128, 1).astype(np.int32)}
def world(rng):
    pr = rng.integers(0, 16, (8, 4, 16)); gi = np.arange(8).reshape(1, 8, 1)
    z = np.where(rng.random((N, 8, W)) < 0.7, rng.random((1, 8, W)), rng.random((N, 8, W))); m = (0.45 + 0.04 * rng.permutation(8)).reshape(1, 8, 1)
    cl = (z >= m).astype(np.int64) + (z >= m + 0.15) + (z >= m + 0.2)
    p = pr[gi, cl]
    X = np.clip(p + rng.integers(-EPS, EPS + 1, p.shape), 0, 15)
    X = np.where(rng.random(p.shape) < rng.choice(np.array([0.04, 0.12, 0.3]), (N, 8, W, 1)), rng.integers(0, 16, p.shape), X)
    tr = (5 * np.arange(16) + rng.integers(0, 16, (N, 8, W, 1))) & 15
    X = np.where(cl[..., None] == 3, np.where(tr < 5 + rng.integers(0, 2, (N, 8, W, 1)), (p + 8) & 15, p), X)
    yc = rng.choice(4, (N, 8, P), p=[0.5, 0.25, 0.1, 0.15]); yp = pr[gi, yc]
    y = np.where(rng.random(yp.shape) < rng.choice(np.array([0.0, 0.1]), (N, 8, P, 1)), rng.integers(0, 16, yp.shape), yp)
    bias = rng.choice(np.array([0.0, 0.2, 0.5, 1.0]), (N, 8, P, 1)); want = np.repeat(yc[..., None], 16, axis=3)
    R = np.where(rng.random((N, 8, P, 16)) < bias, pick(rng, cl, want), rng.integers(0, W, (N, 8, P, 16)))
    return turned(X), rng.integers(0, W, (N, 8, 16, W)), R, turned(y), rng.integers(0, W, (N, 8, 16)), pr
def flood(rng, X, R, y):
    b = np.arange(16); h = np.where(b < 8, 15, 0); a = 15 * (b & 1)
    X[1, :, :, 0] = 0; X[1, :, :, W - 1] = 15; X[2, :, :, 0] = 15; X[2, :, :, W - 1] = h.reshape(1, 16)
    y[1] = h.reshape(1, 16, 1); y[2] = a.reshape(1, 16, 1); y[2, 7, :, P - 1] = h
    R[1] = (W - 1) * (np.argsort(rng.random((8, P, 16)), axis=2) < 5); R[2] = (W - 1) * rng.integers(0, 2, (8, P, 16)); R[2, 7, P - 1] = W - 1
def setup_inputs(rng):
    return pack(*world(rng)[:5])
def setup_inputs_spread(rng):
    X = (16 * rng.random((N, 8, 1, W)) ** 3 * rng.random((N, 8, 16, W))).astype(np.int64)
    y = (16 * rng.random((N, 8, 1, P)) ** 3 * rng.random((N, 8, 16, P))).astype(np.int64)
    e = 1 + 0.25 * rng.permutation(8); lw = W.bit_length() - 1
    L = (W * rng.random((N, 8, 16, W)) ** e.reshape(1, 8, 1, 1)).astype(np.int64)
    R = (W * rng.random((N, 8, P, 16)) ** e[::-1].reshape(1, 8, 1, 1)).astype(np.int64)
    w = np.minimum(np.exp2(lw * rng.random((N, 8, 16))).astype(np.int64), W - 1)
    return pack(X, L, R, y, w)
def setup_inputs_ends(rng):
    kind = rng.integers(0, 3, (N, 8, 1, W)); X = np.where(kind == 0, 0, np.where(kind == 1, 15, 15 * rng.integers(0, 2, (N, 8, 16, W))))
    L = (W - 1) * rng.integers(0, 2, (N, 8, 16, W)); flip = rng.integers(0, 2, (N, 8, 1)); X[..., 0] = 15 * flip; X[..., W - 1] = 15 - 15 * flip
    nf = rng.choice(np.array([0, 0, 1, 4, 5, 8]), (N, 8, 1, P)); base = rng.integers(0, 2, (N, 8, 1, P))
    y = 15 * np.where(np.argsort(rng.random((N, 8, 16, P)), axis=2) < nf, 1 - base, base)
    y[..., 0] = 15; y[..., 1] = 0; y[..., P - 1] = 15
    m = rng.choice(np.array([0, 4, 5, 11, 12, 16]), (N, 8, P, 1)); R = (W - 1) * (np.argsort(rng.random((N, 8, P, 16)), axis=3) < m)
    w = (W - 1) * rng.integers(0, 2, (N, 8, 16)); w[0, 0] = 0; w[N - 1, 7] = W - 1
    X[N - 1, 7, :, 0] = 0; X[N - 1, 7, :, W - 1] = 15; R[N - 1, 7, P - 1] = W - 1; R[N - 1, 7, 0] = W - 1
    h = P // 2
    for q, g in ((0, 2), (N - 1, 6)):
        w[q, g] = 0; w[q, g, 13:] = W - 1; X[q, g, :, W - 1] = 0; X[q, g, :, 0] = 15; L[q, g, :, W - 1] = 0
        y[q, g, :, h:] = 0; y[q, g, 15, h:] = 1; y[q, g, 13:15, h + h // 2:] = 15; R[q, g, h:] = W - 1; R[q, g, h::2, :4] = 0
    for q, g in ((0, 5), (N - 1, 7)):
        top = X[q, g, :, W - 1].copy(); X[q, g, :, W - 2] = top; X[q, g, 0, W - 2] = abs(int(top[0]) - 1); w[q, g, 0] = W - 1
        s = P - P // 4; i = np.arange(s, P - 1).reshape(-1, 1)
        y[q, g, :, s:P - 1] = (15 - top).reshape(16, 1); R[q, g, s:P - 1] = W - 1 - (np.arange(16) > i % 15).astype(np.int64)
    L[N - 1, 5, :, W - S:] = W - 1
    flood(rng, X, R, y)
    return pack(X, L, R, y, w)
def setup_inputs_corners(rng):
    b = np.arange(16); bb = np.where(b < 3, b, b - 1); pr = rng.integers(4, 12, (8, 16)); p = pr.reshape(1, 8, 1, 16)
    cl = rng.integers(0, 5, (N, 8, W)); c = cl[..., None]; tr = (4 * bb + rng.integers(0, 15, (N, 8, W, 1))) % 15
    off = ((b != 3) & (tr < np.where(c == 1, 5, np.where((c == 0) | (c == 2), 4, 0)))) | ((c == 2) & (b == 3))
    sg = np.where(b == 3, 1, 2 * rng.integers(0, 2, (N, 8, W, 16)) - 1); step = np.where(off, EPS + 1, np.where(c < 2, EPS, 0))
    X = np.where(c == 3, (p + 8) & 15, p + sg * step)
    na = rng.choice(np.array([0, 4, 5, 11, 12, 16]), (N, 8, P, 1)); kind = rng.integers(0, 5, (N, 8, P, 1)); o = np.argsort(rng.random((N, 8, P, 16)), axis=3)
    dis = np.where(kind < 3, kind + 1, np.where(o - na < np.where(kind == 3, 9, 8), 2, 1))
    R = pick(rng, cl, np.where(o < na, np.where((o & 1) == 1, 0, 4), dis)); h = P // 4
    R[:, 5, :h] = S * np.arange(h).reshape(1, h, 1) + (b & (S - 1)); R[:, 5, h:2 * h] = (W - 1) * rng.integers(0, 2, (N, h, 16))
    y = np.repeat(pr.reshape(1, 8, 16, 1), P, axis=3); y = np.repeat(y, N, axis=0); y[..., 7::8] = (y[..., 7::8] + 8) & 15
    way = rng.integers(0, 4, (N, 8, 16, W)); L = np.where(way == 0, np.arange(W), np.where(way == 1, 0, np.where(way == 2, W - 1, rng.integers(0, W, (N, 8, 16, W)))))
    L[:, 2] = np.arange(W); L[:, 3] = rng.integers(0, W, (N, 16, W)); L[:, 6] = rng.integers(0, W, (N, 16, W))
    w = rng.integers(0, W, (N, 8, 16)); w[:, 0] = 0; w[:, 1] = W - 1; w[:, 2] = 1; w[:, 3] = 0; w[:, 3, 15] = W - 1; w[:, 4] = 0; w[:, 4, 0] = 1
    return pack(turned(X), L, R, y, w)
def setup_inputs_crowd(rng):
    X, L, R, y, w, pr = world(rng); bc = rng.integers(1, W - 1, 8); b2 = rng.integers(1, W - 1, 8)
    for g in range(8):
        for q in range(N):
            X[q, g, :, b2[g]] = pr[g, (q >> 1) & 1]; X[q, g, :, bc[g]] = pr[g, q & 1]
        if (g & 3) < 2:
            one = np.argsort(rng.random((N, P, 16)), axis=2) == 0
            R[:, g] = np.where(one, R[:, g], bc[g]) if (g & 3) == 1 else bc[g]
        elif (g & 3) == 2: R[:, g] = rng.choice(np.array([0, bc[g], W - 1]), (N, P, 16))
        L[:, g] = rng.choice(np.array([bc[g], b2[g], 0, W - 1]), (N, 16, W)) if (g & 1) == 1 else b2[g]
    flood(rng, X, R, y)
    return pack(X, L, R, y, w)
def setup_inputs_calm(rng):
    pr = rng.integers(0, 16, (8, 16)); p = pr.reshape(1, 8, 16, 1)
    cl = (rng.random((8, W)) < (0.3 + 0.05 * rng.permutation(8)).reshape(8, 1)).astype(np.int64); cl[:, 1] = 0; cl[:, W - 1] = 1
    X = np.minimum(np.where(cl.reshape(1, 8, 1, W) == 1, (p + 8) & 15, p) + rng.integers(0, 2, (N, 8, 16, W)), 15)
    X[..., 0::2] = rng.integers(0, 16, (N, 8, 16, W // 2))
    y = np.minimum(p + rng.integers(0, 2, (N, 8, 16, P)), 15); w = 2 * rng.integers(0, W // 2, (N, 8, 16))
    o = np.argsort(rng.random((N, 8, P)), axis=2); c = np.where(o < P // 4, 5, rng.integers(6, 17, (N, 8, P)))
    few = np.array([0, 2, 1, 3])[(np.arange(N) + int(rng.integers(0, 4))) & 3]
    for q in range(N):
        for g in rng.permutation(8)[:int(few[q])]:
            c[q, g, np.argmax(o[q, g])] = rng.integers(0, 5)
    near = np.argsort(rng.random((N, 8, P, 16)), axis=3) < c[..., None]
    L = np.zeros((N, 8, 16, W), np.int64); R = np.zeros((N, 8, P, 16), np.int64); odd = np.arange(1, W, 2)
    for g in range(8):
        good, far = odd[cl[g, odd] == 0], odd[cl[g, odd] == 1]
        L[:, g] = np.where(cl[g] == 0, good[rng.integers(0, len(good), (N, 16, W))], far[rng.integers(0, len(far), (N, 16, W))])
        R[:, g] = np.where(near[:, g], good[rng.integers(0, len(good), (N, P, 16))], far[rng.integers(0, len(far), (N, P, 16))])
    return pack(X, L, R, y, w)
def check_inputs(d):
    bad = []
    for k, hi in (("xc", 15), ("lsr", W - 1), ("jur", W - 1), ("own", 15), ("wgt", W - 1)):
        v = np.asarray(d[k]).astype(np.float64)
        if not (np.min(v) >= 0 and np.max(v) <= hi): bad.append("range of " + k)
        elif np.any(v != np.floor(v)): bad.append("whole numbers of " + k)
    return bad
def reference(xc, lsr, jur, own, wgt):
    X = xc.astype(np.float32).astype(np.int32).reshape(N, 8, 16, W); L = lsr.astype(np.int64).reshape(N, 8, 16, W)
    R = np.stack([gentries(a) for a in jur]).astype(np.int64).reshape(N, 8, P, 16)
    y = own.astype(np.float32).astype(np.int32).reshape(N, 8, 16, P); w = wgt.astype(np.int64).reshape(N, 8, 16, 1)
    A = np.zeros(N, np.int64); k = np.arange(16); g3 = np.arange(8).reshape(8, 1, 1); g2 = np.arange(8).reshape(8, 1); i2 = np.arange(P).reshape(1, P); b3 = k.reshape(1, 16, 1)
    for t in range(V):
        for r in range(N):
            q = (r + t) % N; old = R[r].copy()
            x = np.take_along_axis(X[q], old.reshape(8, 1, 16 * P), 2).reshape(8, 16, P, 16)
            n = L[q][g3, (k + t) & 15, old]
            z = np.take_along_axis(X[q], n.reshape(8, 1, 16 * P), 2).reshape(8, 16, P, 16)
            v = y[r]; d = np.abs(x - v[..., None])
            a = np.sum(d <= EPS, axis=1) >= AG; c = np.sum(a, axis=2)
            lost = c <= LO + (A[q] & 1)
            rho = np.argmax(np.sum(d > EPS, axis=3) >= MAJ, axis=1)
            e = np.argmin(np.where(a, 1000, np.sum(d, axis=1)), axis=2)
            v = np.where(lost[:, None, :] & (b3 == rho[:, None, :]), x[g2, rho, i2, e][:, None, :], v)
            a = np.sum(np.abs(x - v[..., None]) <= EPS, axis=1) >= AG; c = np.sum(a, axis=2)[..., None]
            u = np.sum(w[q] * v, axis=1) & (W - 1)
            za = np.sum(np.abs(z - v[..., None]) <= EPS, axis=1) >= AG
            far = (((old * u[..., None]) >> 5) + old + 37 * k) & (W - 1)
            new = np.where((c >= WIN) & a, np.where(za, n, far), np.where((c > LO) & (c < WIN) & ~a, n, old))
            col = (S * i2 + (u & (S - 1)))[:, None, :]
            if t < V - 1: X[q][g3, b3, col] = v
            L[q][g3, b3, col] = new.transpose(0, 2, 1)
            R[r] = new; y[r] = v; A[q] = np.sum(lost)
    return {"yj": np.ascontiguousarray(R.transpose(0, 1, 3, 2)).reshape(N, 128, P).astype(np.float32), "yo": y.reshape(N, 128, P).astype(np.float32).astype(BF),
            "yz": np.sum(L * (k + 1).reshape(1, 1, 16, 1), axis=2).astype(np.float32)}

@@ -1,0 +1,575 @@
+from concourse.mybir import dt, AluOpType, ActivationFunctionType
+
+ALU = AluOpType
+ACT = ActivationFunctionType
+NR, V, W, P = 6, 6, 4096, 128
+NH = 2
+PW = P // NH
+NC = 16 * PW // 512
+KK = 16 // NC
+M4 = float((2 ** 23 + 1) * 4)
+M16 = float((2 ** 23 + 1) * 16)
+M32 = float(3 * 2 ** 27)
+PEN = float(2 ** 18)
+BIGV = float(2 ** 22)
+
+B, F, I32, U16, H16 = "bfloat16", "float32", "int32", "uint16", "float16"
+SCRATCH = {
+    "xw": ("sbuf", [128, W], B), "lw": ("sbuf", [128, W], I32), "l16": ("sbuf", [128, W], H16),
+    "rin": ("sbuf", [128, (V + 1) * P], I32), "yin": ("sbuf", [128, (V + 1) * P], B),
+    "rout": ("sbuf", [128, V * P], I32), "yout": ("sbuf", [128, V * P], B),
+    "wi": ("sbuf", [128, 8], I32), "yjf": ("sbuf", [128, P], F), "yzf": ("sbuf", [128, 256], F),
+    "ci": ("sbuf", [128, 8], I32), "cf": ("sbuf", [128, 32], F), "rm": ("sbuf", [128, 16], F),
+    "ioc": ("sbuf", [128, 144], F), "iob": ("sbuf", [128, 128], F), "iom": ("sbuf", [128, 128], F),
+    "c32": ("sbuf", [128, 8], F), "c32i": ("sbuf", [128, 8], F),
+    "hh": ("sbuf", [128, 144], B), "hw5": ("sbuf", [128, 144], B), "hj": ("sbuf", [128, 144], H16),
+    "ba": ("sbuf", [128, 16 * 144], H16), "kc": ("sbuf", [128, 512], B),
+    "sel": ("sbuf", [128, 128], F), "acc": ("sbuf", [128, 8], F), "hn": ("sbuf", [128, 144], B),
+    "o16": ("sbuf", [128, 16], B), "o512": ("sbuf", [128, 8], B),
+    "rst": ("sbuf", [128, 128], F), "keep": ("sbuf", [128, 128], F), "thr": ("sbuf", [128, 8 * V], F),
+    "ai": ("sbuf", [128, 16], I32), "wo": ("sbuf", [128, 32], I32), "wof": ("sbuf", [128, 16], F), "wou": ("sbuf", [128, 16], U16),
+}
+for _n in ("idn", "nid", "n2", "i64", "nbo", "c73", "bo", "tri", "tri0", "tri1", "pen", "m1", "n16", "n32", "whi", "wlo", "ones", "c2048", "cm7"):
+    SCRATCH[_n] = ("sbuf", [128, 128], B)
+for _n in ("xg", "zg", "ad", "nx", "dm", "az", "nz"):
+    SCRATCH[_n] = ("sbuf", [128, 2 * 2048], B)
+SCRATCH["lg"] = ("sbuf", [128, 2 * 2048], H16)
+for _n, _d in (("ru", U16), ("nu", U16), ("nm", F), ("nmk", F), ("good", B), ("cnt", B), ("sa", B), ("oh", B), ("yy", B),
+               ("nl", B), ("sa2", B), ("ch", B), ("si", I32), ("ui", I32), ("pi", I32), ("qi", I32), ("df", F),
+               ("nmc", F), ("base", F), ("ff", F), ("fdf", F), ("ni", I32)):
+    SCRATCH[_n] = ("sbuf", [128, 2 * P], _d)
+for _n, _d, _w in (("sc", F, 128), ("zz", F, 128), ("zb", B, 128), ("dr", B, 128), ("nn", B, 2 * PW), ("lost", B, 8), ("rd", F, 8), ("dl", F, 8)):
+    SCRATCH[_n] = ("sbuf", [128, 2 * NH * _w], _d)
+for _n in range(8):
+    SCRATCH["pb%d" % _n] = ("psum", [128, 512], F)
+SEMAPHORES = (["cV", "cS", "cP", "cG", "sent", "ljur", "lown", "lwgt", "lx", "ll", "oyz"]
+              + ["oj%d" % h for h in range(NH)] + ["oo%d" % h for h in range(NH)]
+              + ["a%s%d_%d" % (k, t, h) for k in "ry" for t in range(1, V + 1) for h in range(NH)])
+
+PAR = {"fix": 50.0, "gam": 1.5, "sca": 3.5, "pe": 0.5, "hop": 110.0, "self": 60.0, "net": 3600.0, "rounds": 1, "serial": 0}
+PAR.update({'xs': (1, 1, 1, 1), 'ds': (0, 1, 0, 1), 'zs': (0, 1, 0, 1), 'xgv': (1, 1), 'zgv': (0, 0), 'sg': (), 'look': 200.0, 'beta': 4.0, 'dmax': 5, 'bias': 4000.0, 'gs': {'xg': 4, 'lg': 2, 'zg': 2}})
+PAR["off"] = {'Vru0': 5, 'Vl0': 20, 'Pn1': -40, 'PDz1': 40, 'Ssa1': 30, 'PDz0': 40, 'Pcw1': 20, 'Vnmk0': 20, 'PDm1': 10, 'Vnmc0': 10, 'Vnu0': -10, 'Sad0': -40, 'Snl0': 40, 'Vxg0': -10, 'Sdm0': 40, 'Vyout0': 10, 'Vxw0': 5, 'Vhj0': 40, 'Vrout1': -10, 'Vnu1': -10, 'Vwlo0': 10, 'Vnmk1': -15, 'Vyjf0': -5, 'Vlg0': -40, 'Vqi1': 40, 'Sad1': 5, 'Vwob0': 10, 'Ssa0': 40, 'Vaj0': -25, 'Pc1': 10, 'Vni0': -10, 'Vfdf0': -10}
+
+
+def build_ops(par):
+    ops, lastw, readers = [], {}, {}
+    fix, gam = par["fix"], par["gam"]
+    cur = [0]
+
+    def op(eng, cost, fn, r=(), w=(), ps=(), sem=None, lat=0.0, after=None):
+        deps = set()
+        for n in r:
+            if n in lastw: deps.add(lastw[n])
+        for n in w:
+            if n in lastw: deps.add(lastw[n])
+            deps.update(readers.get(n, []))
+        k = len(ops)
+        for n in r: readers.setdefault(n, []).append(k)
+        for n in w:
+            lastw[n] = k; readers[n] = []
+        deps.discard(k)
+        ops.append({"eng": eng, "cost": cost, "fn": fn, "deps": deps, "ps": tuple(ps), "sem": sem, "lat": lat, "after": after, "h": cur[0], "nm": (list(w) + [sem])[0]})
+        return k
+
+    def vc(n, c=1.0): return max(64.0, fix + n * c)
+
+    def ts(out, in0, s1, s2, o0, o1, r, w, n, c=1.0, ps=()):
+        def fn(g, T, Q):
+            a = [x(T, Q) if not isinstance(x, (int, float)) and x is not None else x for x in (s1, s2)]
+            if o1 is None: return g.vector.tensor_scalar(out(T, Q), in0(T, Q), a[0], None, o0)
+            return g.vector.tensor_scalar(out(T, Q), in0(T, Q), a[0], a[1], o0, o1)
+        return op("V", vc(n, c), fn, r, w, ps)
+
+    def tt(out, in0, in1, o, r, w, n, c=2.0, ps=()):
+        return op("V", vc(n, c), lambda g, T, Q: g.vector.tensor_tensor(out(T, Q), in0(T, Q), in1(T, Q), o), r, w, ps)
+
+    def cp(out, in_, r, w, n, c=1.0, ps=()):
+        return op("V", vc(n, c), lambda g, T, Q: g.vector.tensor_copy(out(T, Q), in_(T, Q)), r, w, ps)
+
+    def scan(out, d0, d1, o0, o1, r, w, n, ps=()):
+        return op("V", vc(n), lambda g, T, Q: g.vector.tensor_tensor_scan(out(T, Q), d0(T, Q), d1(T, Q), 0.0, o0, o1), r, w, ps)
+
+    def ms(ap, val, w, n):
+        return op("V", vc(n), lambda g, T, Q: g.vector.memset(ap(T, Q), val), (), w)
+
+    def act(out, in_, func, bias, r, w, n, c=1.0, ps=(), scale=1.0, acc=None):
+        def fn(g, T, Q):
+            return g.scalar.activation(out(T, Q), in_(T, Q), func, bias=bias if isinstance(bias, float) else bias(T, Q), scale=scale,
+                                       accum_out=acc(T, Q) if acc else None)
+        return op("S", fix + 20 + n * c, fn, r, w, ps)
+
+    def step(name, out, in_, bound, big, up, r, w, n, tl):
+        if name in par["sg"]: return act(out, in_, ACT.Sigmoid, big, r, w, n, 1, [tl], 256.0 if up else -256.0)
+        return ts(out, in_, bound, None, ALU.is_ge if up else ALU.is_le, None, r, w, n, 1, [tl])
+
+    def mm(tile, items, r, first=True, last=True, each=False):
+        def fn(g, T, Q):
+            ins = None
+            for j, it in enumerate(items):
+                ins = g.tensor.matmul(it[0](T, Q), it[1](T, Q), it[2](T, Q), each or (first and j == 0), each or (last and j == len(items) - 1))
+            return ins
+        return op("P", 30 + sum(max(64, it[3]) for it in items) * par["pe"], fn, r, [tile], [tile])
+
+    def S(name, a=None, b=None, s=None, p=128):
+        return lambda T, Q: T[name][0:p, a:b:s] if s else T[name][0:p, a:b]
+
+    def PS(tile, a, b, s=None, p=128):
+        return lambda T, Q: Q(tile)[0:p, a:b:s] if s else Q(tile)[0:p, a:b]
+
+    def col(j, p=128): return S("cf", j, j + 1, None, p)
+
+    def dma(q, out, in_, sem, r, w, lat, slow=False):
+        def fn(g, T, Q):
+            e = g.sync if q == "Y" else g.scalar
+            return e.dma_start(out(T, Q), in_(T, Q))
+        return op(q, 60.0, fn, r, w, (), sem, lat)
+
+    dma("Y", S("rin", 0, P), lambda T, Q: T.jur[:, :], "ljur", [], ["rin0_%d" % h for h in range(NH)], 2500)
+    dma("Y", S("xw", 0, W), lambda T, Q: T.xc[:, :], "lx", [], ["xw"], 5000)
+    dma("S", S("yin", 0, P), lambda T, Q: T.own[:, :], "lown", [], ["yin0_%d" % h for h in range(NH)], 2500)
+    dma("S", S("wi", 0, 1), lambda T, Q: T.wgt[:, :], "lwgt", [], ["wi"], 2500)
+    dma("Y", S("lw", 0, W), lambda T, Q: T.lsr[:, :], "ll", [], ["lw"], 11000)
+
+    def iota(name, n, pat, cm, flag=True):
+        def fn(g, T, Q):
+            if flag: return g.iota(T[name][:, 0:n], pat, 0, cm, allow_small_or_imprecise_dtypes=True)
+            return g.iota(T[name][:, 0:n], pat, 0, cm)
+        op("G", 160 + 2 * n, fn, (), [name])
+    iota("ci", 1, [[0, 1]], 1, False)
+    iota("ioc", 144, [[1, 144]], 0)
+    iota("iob", 128, [[16, 8], [0, 16]], 0)
+    iota("iom", 128, [[0, 8], [1, 16]], 0)
+    iota("c32", 8, [[512, 8]], 0)
+    cp(col(0), S("ci", 0, 1), ["ci"], ["cf0"], 1)
+    ts(S("ci", 4, 5), S("ci", 0, 1), 15, None, ALU.bitwise_and, None, ["ci"], ["ci4"], 1)
+    cp(col(1), S("ci", 4, 5), ["ci4"], ["cf1"], 1)
+    tt(col(2), col(0), col(1), ALU.subtract, ["cf0", "cf1"], ["cf2"], 1)
+    ts(col(3), col(2), 15.0, None, ALU.add, None, ["cf2"], ["cf3"], 1)
+    ts(col(4), col(1), 32.0, None, ALU.mult, None, ["cf1"], ["cf4"], 1)
+    ts(col(5), col(1), 37.0, 8192.0, ALU.mult, ALU.add, ["cf1"], ["cf5"], 1)
+    ts(col(6), col(1), 1.0, None, ALU.add, None, ["cf1"], ["cf6"], 1)
+    ts(col(7), col(1), 0.0, None, ALU.is_equal, None, ["cf1"], ["cf7"], 1)
+    ts(col(8), col(7), 17.0, -1.0, ALU.mult, ALU.add, ["cf7"], ["cf8"], 1)
+    tt(col(9), col(7), col(1), ALU.subtract, ["cf7", "cf1"], ["cf9"], 1)
+    ts(S("ci", 5, 6), S("ci", 0, 1), 1, None, ALU.bitwise_and, None, ["ci"], ["ci5"], 1)
+    for h in range(NH):
+        v0, v1 = (0.0 if par["ds"][h * NC + c] else -240.0 for c in range(NC))
+        ts(col(14 + h), S("ci", 5, 6), v1 - v0, v0, ALU.mult, ALU.add, ["ci5"], ["cf%d" % (14 + h)], 1)
+        tt(col(16 + h), col(14 + h), col(4), ALU.add, ["cf%d" % (14 + h), "cf4"], ["cf%d" % (16 + h)], 1)
+    for nme, sc in (("idn", 1.0), ("n2", -16.0), ("i64", 64.0), ("nid", -1.0), ("pen", PEN), ("n16", 2.0 ** 20), ("n32", 2.0 ** 21), ("tri0", -7.0)):
+        ts(S(nme, 0, 128), S("ioc", 0, 128), col(0), sc, ALU.is_equal, ALU.mult, ["ioc", "cf0"], [nme], 128)
+    ts(S("hh", 0, 144), S("ioc", 0, 144), col(3), None, ALU.is_equal, None, ["ioc", "cf3"], ["hh"], 144)
+    ts(S("bo", 0, 128), S("iob", 0, 128), col(2), None, ALU.is_equal, None, ["iob", "cf2"], ["bo"], 128)
+    tt(S("m1", 0, 128), S("bo", 0, 128), S("tri0", 0, 128), ALU.add, ["bo", "tri0"], ["m1"], 128)
+    ts(S("tri0", 0, 128), S("iom", 0, 128), col(1), -1.0, ALU.is_gt, ALU.mult, ["iom", "cf1"], ["tri0"], 128)
+    tt(S("tri1", 0, 128), S("tri0", 0, 128), S("idn", 0, 128), ALU.add, ["tri0", "idn"], ["tri1"], 128)
+    ts(S("tri1", 0, 128, 16), S("c32", 0, 8), 0.0, col(8), ALU.mult, ALU.add, ["c32", "cf8"], ["tri1"], 8)
+    tt(S("tri", 0, 128), S("tri1", 0, 128), S("bo", 0, 128), ALU.mult, ["tri1", "bo"], ["tri"], 128)
+    for a in (0, 8):
+        cp(S("o16", a, a + 8), S("bo", 0, 128, 16), ["bo"], ["o16_%d" % a], 8)
+    ts(S("o512", 0, 8), S("bo", 0, 128, 16), 512.0, None, ALU.mult, None, ["bo"], ["o512"], 8)
+    for h in range(NH):
+        for j in (0, 1):
+            n = 16 - 2 * j + h
+            ts(S("kc", 256 * h + 128 * j, 256 * h + 128 * j + 128), S("idn", 0, 128), col(n), None, ALU.mult, None, ["idn", "cf%d" % n], ["kc%d%d" % (j, h)], 128, .5)
+    ts(S("nbo", 0, 128), S("bo", 0, 128), -1.0, None, ALU.mult, None, ["bo"], ["nbo"], 128, .5)
+    ts(S("hn", 0, 144), S("hh", 0, 144), -65536.0, None, ALU.mult, None, ["hh"], ["hn"], 144, .5)
+    ms(S("c73", 0, 128), -73.0 * 32768, ["c73"], 64)
+    ms(S("ones", 0, 128), 1.0, ["ones"], 64)
+    ms(S("c2048", 0, 128), 2048.0, ["c2048"], 64)
+    ms(S("cm7", 0, 128), -7.0, ["cm7"], 64)
+    ms(S("zz", 0, 2 * NH * 128), 0.0, ["zz%d_%d" % (a, h) for a in range(2) for h in range(NH)], 2 * NH * 128)
+    lo, st = 1792.0, -512.0
+    ts(S("sel", 0, 128), S("iom", 0, 128), 0.0, col(7), ALU.mult, ALU.add, ["iom", "cf7"], ["sel"], 128)
+    ms(S("thr", 0, 1), lo, ["thr0"], 1)
+    ts(S("rst", 0, 128), S("iom", 0, 128), 0.0, BIGV, ALU.is_equal, ALU.mult, ["iom"], ["rst"], 128)
+    ts(S("keep", 0, 128), S("iom", 0, 128), 0.0, None, ALU.not_equal, None, ["iom"], ["keep"], 128)
+    ts(S("c32i", 0, 8), S("c32", 0, 8), col(4), None, ALU.add, None, ["c32", "cf4"], ["c32i"], 8)
+    ts(S("rm", 0, 16), S("ioc", 0, 16), col(1), None, ALU.is_equal, None, ["ioc", "cf1"], ["rm"], 16)
+    for a in range(16):
+        ts(S("ba", 144 * a, 144 * a + 144), S("hh", 0, 144), S("rm", a, a + 1), None, ALU.mult, None, ["hh", "rm"], ["ba%d" % a], 144, .5)
+    ts(S("hj", 0, 144), S("hh", 0, 144), col(6), None, ALU.mult, None, ["hh", "cf6"], ["hj"], 144, .5)
+    for j, msk, nme, src, n in ((10, 31, "hw5", "hh", 144), (11, 63, "wlo", "bo", 128), (12, 4032, "whi", "bo", 128)):
+        ts(S("wi", j - 6, j - 5), S("wi", 0, 1), msk, None, ALU.bitwise_and, None, ["wi"], ["wi%d" % j], 1)
+        cp(col(j), S("wi", j - 6, j - 5), ["wi%d" % j], ["cf%d" % j], 1)
+        ts(S(nme, 0, n), S(src, 0, n), col(j), None, ALU.mult, None, [src, "cf%d" % j], [nme], n, .5)
+
+    IDN, NID = S("idn", 0, 128), S("nid", 0, 128)
+
+    def hk(name, k): return S(name, 15 - k, 143 - k)
+
+    sends = {}
+    for t in range(V):
+        a = t & 1
+        for h in range(NH):
+            cur[0] = h
+            u = "%d_%d" % (a, h); v = "%d_%d" % (t, h)
+            o = a * P + h * PW; ob = a * 2048 + h * 16 * PW; oi = t * P + h * PW; o3 = a * NH + h
+
+            def sm(name, o=o): return S(name, o, o + PW)
+
+            def t8(name, o3=o3): return S(name, 8 * o3, 8 * o3 + 8, None, PW)
+
+            def t128(name, o3=o3): return S(name, 128 * o3, 128 * o3 + 128, None, PW)
+
+            def cls(name, c, ob=ob): return S(name, ob + 512 * c, ob + 512 * c + 512)
+
+            def ks(name, k, ob=ob): return S(name, ob + 512 * (k % NC) + k // NC, ob + 512 * (k % NC) + 512, KK)
+
+            def jc(name, c, ob=ob): return S(name, ob + c, ob + 16 * PW, NC)
+
+            RIN, YIN, YN, RN = S("rin", oi, oi + PW), S("yin", oi, oi + PW), S("yout", oi, oi + PW), S("rout", oi, oi + PW)
+            rin, yin, yn, rn = "rin" + v, "yin" + v, "yout" + v, "rout" + v
+            if t:
+                op("N", 0, None, (), [rin], (), "ar" + v, par["net"], sends["r%d_%d" % (t - 1, h)])
+                op("N", 0, None, (), [yin], (), "ay" + v, par["net"], sends["y%d_%d" % (t - 1, h)])
+            n16 = 16 * PW
+            cp(sm("ru"), RIN, [rin], ["ru" + u], PW)
+
+            def gather(name, win, offs, o=o, ob=ob, u=u):
+                gs = par["gs"][name]; pw = PW // gs
+                for j in range(gs):
+                    out = S(name, ob + 16 * pw * j, ob + 16 * pw * (j + 1))
+
+                    def src(T, Q, j=j): return T[win][:, 0:W].indirect(T[offs][:, o + pw * j:o + pw * (j + 1)])
+                    if name == "lg": ts(out, src, -2048.0, None, ALU.add, None, [win, offs + u], ["%s%d_%s" % (name, j, u)], 16 * pw, gam)
+                    elif j == gs - 1 and par[name + "v"][h]: cp(out, src, [win, offs + u], ["%s%d_%s" % (name, j, u)], 16 * pw, gam)
+                    else: act(out, src, ACT.Identity, 0.0, [win, offs + u], ["%s%d_%s" % (name, j, u)], 16 * pw, gam)
+                return ["%s%d_%s" % (name, j, u) for j in range(gs)]
+            XG = gather("xg", "xw", "ru")
+            LG = gather("lg", "lw", "ru")
+            tl = "n" + v
+            mm(tl, [(PS(tl, 0, PW), IDN, S("c2048", 0, PW), PW)]
+               + [(PS(tl, 0, PW), S("ba", 144 * ((k + t) % 16) + 15 - k, 144 * ((k + t) % 16) + 143 - k), S("lg", ob + k, ob + n16, 16), PW) for k in range(16)],
+               ["idn", "c2048"] + LG + ["ba%d" % j for j in range(16)])
+            cp(sm("nu"), PS(tl, 0, PW), [tl], ["nu" + u], PW, 1, [tl])
+            act(sm("nm"), PS(tl, 0, PW), ACT.Identity, 4096.0, [tl], ["nm" + u], PW, 1, [tl])
+            ts(sm("nmk"), RIN, col(5), None, ALU.add, None, [rin, "cf5"], ["nmk" + u], PW)
+            ZG = gather("zg", "xw", "nu")
+
+            def sub(tl, src, c, Y, r, ry, last):
+                mm(tl, [(PS(tl, 0, 512), IDN, jc(src, c), 512)], ["idn"] + r, True, False)
+                mm(tl, [(PS(tl, j, 512, KK), NID, Y, PW) for j in range(KK)], ["nid", ry], False, last)
+            for c in range(NC):
+                tl = "Dx%s_%d" % (v, c)
+                sub(tl, "xg", c, YIN, XG + [yin], yin, True)
+                act(cls("ad", c), PS(tl, 0, 512), ACT.Abs, 0.0, [tl], ["ad%s_%d" % (u, c)], 512, 1, [tl])
+                if par["xs"][h * NC + c]:
+                    ts(cls("nx", c), cls("ad", c), 1.0, None, ALU.is_le, None, ["ad%s_%d" % (u, c)], ["nx%s_%d" % (u, c)], 512, .5)
+                else:
+                    ts(cls("nx", c), PS(tl, 0, 512), M4, M4, ALU.add, ALU.is_equal, [tl], ["nx%s_%d" % (u, c)], 512, 1, [tl])
+            korder = [k for c in range(NC) for k in range(c, 16, NC)]
+
+            def byclass(tl, item, r, name, head=(), tail=(), rt=(), first=True, last=True):
+                for c in range(NC):
+                    its = (list(head) if c == 0 else []) + [item(k) for k in range(c, 16, NC)] + (list(tail) if c == NC - 1 else [])
+                    mm(tl, its, r + ["%s%s_%d" % (name, u, c)] + (list(rt) if c == NC - 1 else []), first and c == 0, last and c == NC - 1)
+            tl = "nb" + v
+            byclass(tl, lambda k: (PS(tl, 0, PW), IDN, ks("nx", k), PW), ["idn"], "nx")
+            step("good", sm("good"), PS(tl, 0, PW), 8.0, -1920.0, True, [tl], ["good" + u], PW, tl)
+            tl = "pre" + v
+            mm(tl, [(PS(tl, 0, PW), S("tri", 0, 128), sm("good"), PW)], ["tri", "good" + u])
+            ts(sm("oh"), PS(tl, 0, PW), col(9), 16.0, ALU.is_gt, ALU.mult, [tl, "cf9"], ["oh" + u], PW, 1, [tl])
+            tl = "cnt" + v
+            mm(tl, [(PS(tl, 0, PW), hk("hh", k), ks("nx", k), PW) for k in korder], ["hh"] + ["nx%s_%d" % (u, c) for c in range(NC)])
+            act(sm("sa"), PS(tl, 0, PW), ACT.Sign, -11.5, [tl], ["sa" + u], PW, 1, [tl])
+            act(sm("cnt"), PS(tl, 0, PW), ACT.Identity, 0.0, [tl], ["cnt" + u], PW, 1, [tl])
+            tl = "cT" + v
+            mm(tl, [(PS(tl, 0, PW), S("bo", 0, 128), sm("sa"), PW)], ["sa" + u, "bo"])
+            act(sm("nl"), PS(tl, 0, PW), ACT.Sigmoid, S("thr", 8 * t, 8 * t + 1), [tl, "thr%d" % t], ["nl" + u], PW, 1, [tl], 256.0, S("acc", o3, o3 + 1))
+            tl = "ya" + v
+            mm(tl, [(PS(tl, 0, PW), IDN, sm("oh"), PW), (PS(tl, 0, PW), S("i64", 0, 128), sm("nl"), PW)], ["idn", "i64", "oh" + u, "nl" + u])
+            tt(sm("yy"), YIN, PS(tl, 0, PW), ALU.min, [yin, tl], ["yy" + u], PW, 1, [tl])
+            for c in range(NC):
+                tl = "Dm%s_%d" % (v, c)
+                if par["ds"][h * NC + c]:
+                    sub(tl, "xg", c, sm("oh"), XG + ["good" + u], "oh" + u, True)
+                    act(cls("dm", c), PS(tl, 0, 512), ACT.Relu, 0.0, [tl], ["dm%s_%d" % (u, c)], 512, 1, [tl])
+                else:
+                    mm(tl, [(PS(tl, j, 512, KK), IDN, sm("oh"), PW) for j in range(KK)], ["idn", "oh" + u], each=True)
+                    tt(cls("dm", c), jc("xg", c), PS(tl, 0, 512), ALU.max, [tl] + XG, ["dm%s_%d" % (u, c)], 512, 1, [tl])
+            tl = "K" + v
+            mm(tl, [(PS(tl, 0, 256, None, PW), S("ones", 0, PW), S("kc", 256 * h, 256 * h + 256), 256)]
+               + [(PS(tl, k, 128, 16, PW), ks("ad", k), S("o512", 0, 8), 8) for k in korder],
+               ["ones", "kc0%d" % h, "kc1%d" % h, "good" + u, "o512"] + ["ad%s_%d" % (u, c) for c in range(NC)], True, False)
+            mm(tl, [(PS(tl, 0, 128, None, PW), sm("sa"), S("pen", 0, 128), 128)], ["sa" + u, "pen"], False, False)
+            byclass(tl, lambda k: (PS(tl, k, 256, 16, PW), ks("dm", k), S("o16", 0, 16), 16), ["o16_0", "o16_8"], "dm", first=False)
+            scan(t128("sc"), S("rst", 0, 128, None, PW), PS(tl, 0, 128, None, PW), ALU.add, ALU.min, [tl, "rst"], ["sc" + u], 128, [tl])
+            act(t128("dr"), PS(tl, 128, 256, None, PW), ACT.Identity, 0.0, [tl], ["dr" + u], 128, 1, [tl])
+            ends = S("sc", 128 * o3 + 15, 128 * o3 + 128, 16, PW)
+            ts(t8("rd"), ends, M32, M32, ALU.add, ALU.subtract, ["sc" + u], ["rd" + u], 8)
+            tt(S("zz", 128 * o3, 128 * o3 + 128, 16, PW), ends, t8("rd"), ALU.subtract, ["sc" + u, "rd" + u], ["zz" + u], 8)
+            scan(t128("zb"), S("keep", 0, 128, None, PW), t128("zz"), ALU.mult, ALU.add, ["keep", "zz" + u], ["zb" + u], 128)
+            IW, NW = S("idn", 0, PW, None, PW), S("nid", 0, PW, None, PW)
+            tl = "del" + v
+            mm(tl, [(PS(tl, 0, PW), NID, sm("oh"), PW), (PS(tl, 0, PW), S("n2", 0, 128), sm("nl"), PW)], ["nid", "n2", "nl" + u, "oh" + u, "sc" + u], True, False)
+            mm(tl, [(PS(tl, 0, PW), t128("zb"), IW, PW)], ["zb" + u, "idn"], False, True)
+            tt(YN, sm("yy"), PS(tl, 0, PW), ALU.max, [tl, "yy" + u], [yn], PW, 1, [tl])
+
+            def send(kind, src, dst, r, oi=oi, t=t, h=h):
+                def fn(g, T, Q):
+                    return g.remote_dma(T[dst][:, oi + P:oi + P + PW], T[src][:, oi:oi + PW], T.sem["a%s%d_%d" % (kind, t + 1, h)], T.sem.sent, Q("pid"), Q("rid"), Q("mask"))
+                sends["%s%d_%d" % (kind, t, h)] = op("G", 900.0, fn, [r], (), (), "remote")
+            send("y", "yout", "yin", yn)
+            tl = "dd" + v
+            far = S("i64", 0, 128)
+            mm(tl, [(PS(tl, 0, PW), t128("dr"), IW, PW), (PS(tl, 0, PW), S("nbo", 0, 128), YIN, PW), (PS(tl, 0, PW), S("bo", 0, 128), sm("yy"), PW), (PS(tl, 0, PW), far, sm("nl"), PW)],
+               ["dr" + u, "idn", "nbo", "bo", "i64", yin, "yy" + u, "nl" + u])
+            mm(tl, [(PS(tl, PW, 2 * PW), t128("dr"), IW, PW), (PS(tl, PW, 2 * PW), far, sm("nl"), PW), (PS(tl, PW, 2 * PW), t128("zb"), NW, PW)],
+               ["dr" + u, "zb" + u, "idn", "nid", "i64", "nl" + u])
+            on = 2 * PW * o3
+            ts(S("nn", on, on + 2 * PW), PS(tl, 0, 2 * PW), M4, M4, ALU.add, ALU.is_equal, [tl], ["nn" + u], 2 * PW, 1, [tl])
+            tl = "c2" + v
+            mm(tl, [(PS(tl, 0, PW), IDN, sm("cnt"), PW), (PS(tl, 0, PW), NID, S("nn", on, on + PW), PW), (PS(tl, 0, PW), IDN, S("nn", on + PW, on + 2 * PW), PW)],
+               ["idn", "nid", "cnt" + u, "nn" + u])
+            act(sm("sa2"), PS(tl, 0, PW), ACT.Sign, -11.5, [tl], ["sa2" + u], PW, 1, [tl])
+            tl = "cw" + v
+            mm(tl, [(PS(tl, 0, PW), IDN, S("cm7", 0, PW), PW), (PS(tl, 0, PW), S("m1", 0, 128), sm("sa2"), PW)], ["idn", "cm7", "m1", "sa2" + u])
+            ts(sm("ch"), PS(tl, 0, PW), M16, M16, ALU.add, ALU.is_equal, [tl], ["ch" + u], PW, 1, [tl])
+            tt(sm("nmc"), sm("ch"), sm("nm"), ALU.mult, ["ch" + u, "nm" + u], ["nmc" + u], PW)
+            tt(sm("base"), sm("nmc"), RIN, ALU.max, ["nmc" + u, rin], ["base" + u], PW)
+            tl = "u" + v
+            mm(tl, [(PS(tl, 0, PW), S("whi", 0, 128), YN, PW), (PS(tl, 0, PW), S("wlo", 0, 128), YN, PW)], ["whi", "wlo", yn])
+            cp(sm("si"), PS(tl, 0, PW), [tl], ["si" + u], PW, 1, [tl])
+            ts(sm("ui"), sm("si"), W - 1, None, ALU.bitwise_and, None, ["si" + u], ["ui" + u], PW)
+            tt(sm("pi"), sm("ui"), RIN, ALU.mult, ["ui" + u, rin], ["pi" + u], PW)
+            ts(sm("qi"), sm("pi"), 5, W - 1, ALU.logical_shift_right, ALU.bitwise_and, ["pi" + u], ["qi" + u], PW)
+            tt(sm("df"), sm("qi"), sm("nmk"), ALU.add, ["qi" + u, "nmk" + u], ["df" + u], PW)
+            for c in range(NC):
+                tl = "Dz%s_%d" % (v, c)
+                sub(tl, "zg", c, YN, ZG + ["zb" + u], yn, True)
+                if par["zs"][h * NC + c]:
+                    act(cls("az", c), PS(tl, 0, 512), ACT.Abs, 0.0, [tl], ["az%s_%d" % (u, c)], 512, 1, [tl])
+                    ts(cls("nz", c), cls("az", c), 1.0, None, ALU.is_le, None, ["az%s_%d" % (u, c)], ["nz%s_%d" % (u, c)], 512, .5)
+                else:
+                    ts(cls("nz", c), PS(tl, 0, 512), M4, M4, ALU.add, ALU.is_equal, [tl], ["nz%s_%d" % (u, c)], 512, 1, [tl])
+            tl = "cz" + v
+            byclass(tl, lambda k: (PS(tl, 0, PW), hk("hn", k), ks("nz", k), PW), ["hn", "idn", "c73"], "nz", head=[(PS(tl, 0, PW), IDN, S("c73", 0, PW), PW)],
+                    tail=[(PS(tl, 0, PW), S("n16", 0, 128), sm("sa2"), PW), (PS(tl, 0, PW), S("n32", 0, 128), sm("ch"), PW)], rt=["n16", "n32", "sa2" + u, "ch" + u])
+            tt(sm("fdf"), sm("df"), PS(tl, 0, PW), ALU.min, [tl, "df" + u], ["fdf" + u], PW, 1, [tl])
+            tt(sm("ni"), sm("fdf"), sm("base"), ALU.max, ["fdf" + u, "base" + u], ["ni" + u], PW)
+            ts(RN, sm("ni"), W - 1, None, ALU.bitwise_and, None, ["ni" + u], [rn], PW)
+            send("r", "rout", "rin", rn)
+        hs = range(NH); s = str(a); cur[0] = 0
+        if t < V - 1:
+            tl = "A%d" % t
+            mm(tl, [(PS(tl, 0, 1), S("sel", 0, 128), S("acc", a * NH + h, a * NH + h + 1), 256) for h in hs], ["sel"] + ["nl%d_%d" % (a, h) for h in hs])
+            cp(S("ai", 8 * a, 8 * a + 1), PS(tl, 0, 1), [tl], ["ai" + s], 1, 1, [tl])
+            ts(S("ai", 8 * a + 4, 8 * a + 5), S("ai", 8 * a, 8 * a + 1), 1, None, ALU.bitwise_and, None, ["ai" + s], ["aj" + s], 1)
+            ts(S("thr", 8 * t + 8, 8 * t + 9), S("ai", 8 * a + 4, 8 * a + 5), st, lo, ALU.mult, ALU.add, ["aj" + s], ["thr%d" % (t + 1)], 1)
+        tl = "wo%d" % t
+        yns = ["yout%d_%d" % (t, h) for h in hs]
+        mm(tl, [(PS(tl, 0, 8), hk("hw5", m), S("yout", t * P + m, t * P + P, 16), 8) for m in range(16)], ["hw5"] + yns)
+        cp(S("wo", 16 * a, 16 * a + 8), PS(tl, 0, 8), [tl], ["woa" + s], 8, 1, [tl])
+        ts(S("wo", 16 * a + 8, 16 * a + 16), S("wo", 16 * a, 16 * a + 8), 31, None, ALU.bitwise_and, None, ["woa" + s], ["wob" + s], 8)
+        tt(S("wof", 8 * a, 8 * a + 8), S("wo", 16 * a + 8, 16 * a + 16), S("c32i", 0, 8), ALU.add, ["wob" + s, "c32i"], ["wof" + s], 8)
+        cp(S("wou", 8 * a, 8 * a + 8), S("wof", 8 * a, 8 * a + 8), ["wof" + s], ["wou" + s], 8)
+        if t < V - 1:
+            cp(lambda T, Q, a=a: T.xw[:, 0:W].indirect(T.wou[:, 8 * a:8 * a + 8]), S("yout", t * P, t * P + P), ["wou" + s] + yns, ["xw"], P, par["sca"])
+        cp(lambda T, Q, a=a: T.lw[:, 0:W].indirect(T.wou[:, 8 * a:8 * a + 8]), S("rout", t * P, t * P + P),
+           ["wou" + s] + ["rout%d_%d" % (t, h) for h in hs], ["lw"], P, par["sca"])
+    for h in range(NH):
+        v = "%d_%d" % (V, h); oi = V * P + h * PW
+        op("N", 0, None, (), ["rin" + v], (), "ar" + v, par["net"], sends["r%d_%d" % (V - 1, h)])
+        op("N", 0, None, (), ["yin" + v], (), "ay" + v, par["net"], sends["y%d_%d" % (V - 1, h)])
+        dma("Y", lambda T, Q, h=h: T.yo[:, h * PW:h * PW + PW], S("yin", oi, oi + PW), "oo%d" % h, ["yin" + v], [], 2500)
+        cp(S("yjf", h * PW, h * PW + PW), S("rin", oi, oi + PW), ["rin" + v], ["yjf%d" % h], PW)
+        dma("Y", lambda T, Q, h=h: T.yj[:, h * PW:h * PW + PW], S("yjf", h * PW, h * PW + PW), "oj%d" % h, ["yjf%d" % h], [], 2500)
+    cuts = (0, 5, 10, 14, 16)
+    for j in range(4):
+        c0, c1 = cuts[j], cuts[j + 1]
+        ts(S("l16", 256 * c0, 256 * c1), S("lw", 256 * c0, 256 * c1), -2048.0, None, ALU.add, None, ["lw"], ["l16_%d" % j], 256 * (c1 - c0))
+        mm("yz", [(PS("yz", 0, 256), hk("hj", c), S("l16", 256 * c, 256 * c + 256), 256) for c in range(c0, c1)], ["hj", "l16_%d" % j], j == 0, j == 3)
+    act(S("yzf", 0, 256), PS("yz", 0, 256), ACT.Identity, 2048.0 * 136, ["yz"], ["yzf"], 256, 1, ["yz"])
+    dma("Y", lambda T, Q: T.yz[:, :], S("yzf", 0, 256), "oyz", ["yzf"], [], 2500)
+    return ops
+
+
+def kind(o):
+    return o["eng"] + "".join(x for x in o["nm"] if x.isalpha()) + str(o["h"])
+
+
+def late_starts(ops, par, fin):
+    n = len(ops); need = [0.0] * n; back = [0.0] * n; busy = {e: [] for e in "VSPGYN"}
+    for k in sorted(range(n), key=lambda k: (-fin[k], -k)):
+        o = ops[k]; s = need[k] + o["lat"]; c = o["cost"]; bz = busy[o["eng"]]
+        for j, (x0, x1) in enumerate(bz):
+            if x1 <= s: continue
+            if x0 >= s + c: break
+            s = x1
+        bz.append((s, s + c)); bz.sort(); back[k] = s + c
+        for d in o["deps"]:
+            gap = par["hop"] if ops[d]["eng"] != o["eng"] else 0.0 if o["eng"] == "P" else par["self"]
+            need[d] = max(need[d], back[k] + gap)
+        if o["after"] is not None: need[o["after"]] = max(need[o["after"]], back[k])
+    return back
+
+
+def best_order(ops, par):
+    best = None; given = None
+    for _ in range(par["rounds"]):
+        try:
+            r = lay_out(ops, par, given)
+        except ValueError:
+            break
+        if best is None or max(r[3]) < max(best[0][3]): best = (r, given)
+        given = late_starts(ops, par, r[3])
+    return lay_out(ops, par, best[1])
+
+
+def place(ops, par, pr, succ, left):
+    n = len(ops); busy = {e: [] for e in "VSPGYN"}; held = {}; start = [0.0] * n; fin = [0.0] * n; hop = par["hop"]
+    ready = [k for k in range(n) if left[k] == 0]
+    while ready:
+        k = max(ready, key=lambda k: (pr[k], -k)); ready.remove(k)
+        o = ops[k]; e = o["eng"]; c = o["cost"]; s = 0.0
+        for d in o["deps"]:
+            s = max(s, fin[d] + (hop if ops[d]["eng"] != e else 0.0 if e == "P" else par["self"]))
+        if o["after"] is not None: s = max(s, fin[o["after"]])
+        block = [(x0 - hop, x1 + hop) for tl in o["ps"] for x0, x1, e2 in held.get(tl, []) if e2 != e]
+        bz = busy[e]; moved = True
+        while moved:
+            moved = False
+            for x0, x1 in bz[max(0, lower(bz, s) - 1):]:
+                if x0 >= s + c: break
+                if x1 > s: s = x1
+            for x0, x1 in block:
+                if x1 > s and x0 < s + c: s = x1; moved = True
+        bz.insert(lower(bz, s), (s, s + c)); start[k] = s; fin[k] = s + c + o["lat"]
+        for tl in o["ps"]: held.setdefault(tl, []).append((s, s + c, e))
+        for x in succ[k]:
+            left[x] -= 1
+            if left[x] == 0: ready.append(x)
+    order = sorted(range(n), key=lambda k: (start[k], k))
+    end = {tl: max(x[1] for x in v) for tl, v in held.items()}
+    bank, last = {}, {}; past = [[] for _ in range(8)]; till = [-1e9] * 8
+    for k in order:
+        o = ops[k]; extra = set()
+        for tl in o["ps"]:
+            if tl not in bank:
+                b = min(range(8), key=lambda j: till[j])
+                if till[b] > start[k]: raise ValueError("no bank")
+                bank[tl] = b; till[b] = end[tl]; extra.update(past[b]); past[b] = []
+            elif ops[last[tl]]["eng"] != o["eng"]: extra.add(last[tl])
+            last[tl] = k; past[bank[tl]].append(k)
+        o["all"] = set(o["deps"]) | extra
+    return order, bank, start, fin
+
+
+def lower(bz, s):
+    a, b = 0, len(bz)
+    while a < b:
+        m = (a + b) // 2
+        if bz[m][0] < s: a = m + 1
+        else: b = m
+    return a
+
+
+def lay_out(ops, par, given=None):
+    n = len(ops); succ = [[] for _ in ops]; left = [0] * n
+    for k, o in enumerate(ops):
+        pre = set(o["deps"])
+        if o["after"] is not None: pre.add(o["after"])
+        left[k] = len(pre)
+        for d in pre: succ[d].append(k)
+    pr = [0.0] * n
+    for k in range(n - 1, -1, -1):
+        pr[k] = ops[k]["cost"] + ops[k]["lat"] + par["hop"] + max([pr[s] for s in succ[k]] + [0.0])
+    for k in range(n): pr[k] += par["off"].get(kind(ops[k]), 0) * 100.0 - par["bias"] * ops[k]["h"]
+    if given: pr = given
+    if par["serial"]: return place(ops, par, pr, succ, left)
+    users = {}
+    for k, o in enumerate(ops):
+        for tl in o["ps"]: users.setdefault(tl, []).append(k)
+    rem = {tl: len(u) for tl, u in users.items()}
+    bank, lastacc = {}, {}
+    holder = [None] * 8; past = [[] for _ in range(8)]; bfree = [0.0] * 8
+    free = {e: 0.0 for e in "VSPGYN"}; fin = [0.0] * n; start = [0.0] * n
+    ready = [k for k in range(n) if left[k] == 0]; order = []
+
+    def edge(d, k):
+        if ops[d]["eng"] == ops[k]["eng"]:
+            return fin[d] + (0.0 if ops[k]["eng"] == "P" else par["self"])
+        return fin[d] + par["hop"]
+    while ready:
+        cands = []
+        for k in ready:
+            o = ops[k]; s = free[o["eng"]]; b = None
+            for d in o["deps"]: s = max(s, edge(d, k))
+            if o["after"] is not None: s = max(s, fin[o["after"]])
+            ok = True
+            for tl in o["ps"]:
+                if tl in bank:
+                    d = lastacc[bank[tl]]
+                    if ops[d]["eng"] != o["eng"]: s = max(s, edge(d, k))
+                else:
+                    fb = [j for j in range(8) if holder[j] is None]
+                    nd = sum(1 for x in holder if x is not None and x[0] == "D")
+                    if not fb or (tl[0] == "D" and nd >= par["dmax"]) or (tl[0] in "DKnA" and len(fb) < 2): ok = False; break
+                    b = min(fb, key=lambda j: bfree[j]); s = max(s, bfree[b] + par["hop"])
+            if ok: cands.append((s, k, b))
+        if not cands: raise ValueError("no bank")
+        s0, k0, _ = min(cands, key=lambda c: (c[0], -pr[c[1]]))
+        e = ops[k0]["eng"]
+        s, k, b = max([c for c in cands if ops[c[1]]["eng"] == e and c[0] <= s0 + min(par["look"], ops[k0]["cost"])], key=lambda c: (pr[c[1]] - par["beta"] * (c[0] - s0), -c[1]))
+        o = ops[k]; extra = set()
+        for tl in o["ps"]:
+            if tl not in bank:
+                bank[tl] = b; holder[b] = tl; extra.update(past[b]); past[b] = []
+            elif ops[lastacc[bank[tl]]]["eng"] != e: extra.add(lastacc[bank[tl]])
+            j = bank[tl]; lastacc[j] = k; past[j].append(k); rem[tl] -= 1
+            if rem[tl] == 0: holder[j] = None; bfree[j] = s + o["cost"]
+        o["all"] = set(o["deps"]) | extra
+        start[k] = s; free[e] = s + o["cost"]; fin[k] = s + o["cost"] + o["lat"]
+        order.append(k); ready.remove(k)
+        for x in succ[k]:
+            left[x] -= 1
+            if left[x] == 0: ready.append(x)
+    return order, bank, start, fin
+
+
+PLAN = []
+
+
+def rank_program(g, core, T, topo):
+    rank = T.rank_of(core)
+    if rank is None:
+        return
+    if not PLAN:
+        ops = build_ops(PAR)
+        PLAN.append((ops,) + best_order(ops, PAR))
+    ops, order, bank = PLAN[0][:3]
+    nxt = T.cores[(rank + 1) % len(T.cores)]; prv = T.cores[(rank - 1) % len(T.cores)]
+    rid, pid, _ = topo.addr(nxt)
+    env = {"rid": rid, "pid": pid, "mask": topo.mask(core, nxt)}
+    n_out, n_in = len(topo.engines(core, nxt)), len(topo.engines(prv, core))
+
+    def Q(name):
+        return env[name] if name in env else T["pb%d" % bank[name]]
+    queue = {"V": g.vector, "S": g.scalar, "P": g.tensor, "G": g, "Y": g.sync}
+    count = {e: 0 for e in "VSPG"}; known = {e: {} for e in queue}; mark = {}; top = {}; sent = 0
+    for k in order:
+        o = ops[k]; e = o["eng"]
+        if e == "N":
+            mark[k] = (o["sem"], n_in, {}); top[o["sem"]] = n_in
+            continue
+        kn = known[e]
+        need = sorted((mark[d] for d in o["all"] if d in mark and not (e == "P" and ops[d]["eng"] == "P")), key=lambda m: -m[1])
+        for sem, val, clock in need:
+            if kn.get(sem, 0) >= val: continue
+            if any(c2.get(sem, 0) >= val for s2, v2, c2 in need): continue
+            queue[e].wait_ge(T.sem[sem], val)
+            kn[sem] = val
+        for sem, val, clock in need:
+            for s2, v2 in list(clock.items()) + [(sem, val)]:
+                if kn.get(s2, 0) < v2: kn[s2] = v2
+        ins = o["fn"](g, T, Q)
+        if o["sem"] == "remote":
+            sent += n_out
+        elif o["sem"]:
+            ins.then_inc(T.sem[o["sem"]], 16); mark[k] = (o["sem"], 16, dict(kn)); top[o["sem"]] = 16
+        else:
+            count[e] += 1; ins.then_inc(T.sem["c" + e], 1); mark[k] = ("c" + e, count[e], dict(kn)); top["c" + e] = count[e]
+    g.wait_ge(T.sem.sent, sent)
+    for sem, val in top.items():
+        if sem[0] in "co": g.wait_ge(T.sem[sem], val)

@@ -24,21 +24,21 @@ SCRATCH = {
     "c32": ("sbuf", [128, 8], F), "c32i": ("sbuf", [128, 8], F),
     "hh": ("sbuf", [128, 144], B), "hw5": ("sbuf", [128, 144], B), "hj": ("sbuf", [128, 144], H16),
     "ba": ("sbuf", [128, 16 * 144], H16), "kc": ("sbuf", [128, 512], B),
-    "sel": ("sbuf", [128, 128], F), "acc": ("sbuf", [128, 8], F), "hn": ("sbuf", [128, 144], B),
+    "pen2": ("sbuf", [128, 256], B), "sel": ("sbuf", [128, 128], F), "acc": ("sbuf", [128, 8], F), "hn": ("sbuf", [128, 144], B),
     "o16": ("sbuf", [128, 16], B), "o512": ("sbuf", [128, 8], B),
     "rst": ("sbuf", [128, 128], F), "keep": ("sbuf", [128, 128], F), "thr": ("sbuf", [128, 8 * V], F),
-    "ai": ("sbuf", [128, 16], I32), "wo": ("sbuf", [128, 32], I32), "wof": ("sbuf", [128, 16], F), "wou": ("sbuf", [128, 16], U16),
+    "ai": ("sbuf", [128, 16], I32), "wo": ("sbuf", [128, 32], I32), "wof": ("sbuf", [128, 16], F), "wou": ("sbuf", [128, 16], U16), "wov": ("sbuf", [128, 8], U16),
 }
-for _n in ("idn", "nid", "n2", "i64", "nbo", "c73", "bo", "tri", "tri0", "tri1", "pen", "m1", "n16", "n32", "whi", "wlo", "ones", "c2048", "cm7"):
+for _n in ("idn", "nid", "n2", "i64", "nbo", "c73", "bo", "tri", "tri0", "tri1", "lp", "m1", "n16", "n32", "whi", "wlo", "cm7"):
     SCRATCH[_n] = ("sbuf", [128, 128], B)
 for _n in ("xg", "zg", "ad", "nx", "dm", "az", "nz"):
     SCRATCH[_n] = ("sbuf", [128, 2 * 2048], B)
 SCRATCH["lg"] = ("sbuf", [128, 2 * 2048], H16)
 for _n, _d in (("ru", U16), ("nu", U16), ("nm", F), ("nmk", F), ("good", B), ("cnt", B), ("sa", B), ("oh", B), ("yy", B),
                ("nl", B), ("sa2", B), ("ch", B), ("si", I32), ("ui", I32), ("pi", I32), ("qi", I32), ("df", F),
-               ("nmc", F), ("base", F), ("ff", F), ("fdf", F), ("ni", I32)):
+               ("nmc", F), ("base", F), ("ct", B), ("fdf", F), ("ni", I32)):
     SCRATCH[_n] = ("sbuf", [128, 2 * P], _d)
-for _n, _d, _w in (("sc", F, 128), ("zz", F, 128), ("zb", B, 128), ("dr", B, 128), ("nn", B, 2 * PW), ("lost", B, 8), ("rd", F, 8), ("dl", F, 8)):
+for _n, _d, _w in (("sc", F, 128), ("zz", F, 128), ("zb", B, 128), ("dr", B, 144), ("nn", B, 2 * PW), ("nt", B, 2 * PW), ("rd", F, 8), ("dl", F, 8)):
     SCRATCH[_n] = ("sbuf", [128, 2 * NH * _w], _d)
 for _n in range(8):
     SCRATCH["pb%d" % _n] = ("psum", [128, 512], F)
@@ -49,6 +49,10 @@ SEMAPHORES = (["cV", "cS", "cP", "cG", "sent", "ljur", "lown", "lwgt", "lx", "ll
 PAR = {"fix": 50.0, "gam": 1.5, "sca": 3.5, "pe": 0.5, "hop": 110.0, "self": 60.0, "net": 3600.0, "rounds": 1, "serial": 0}
 PAR.update({'xs': (1, 1, 1, 1), 'ds': (0, 1, 0, 1), 'zs': (0, 1, 0, 1), 'xgv': (1, 1), 'zgv': (0, 0), 'sg': (), 'look': 200.0, 'beta': 4.0, 'dmax': 5, 'bias': 4000.0, 'gs': {'xg': 4, 'lg': 2, 'zg': 2}})
 PAR["off"] = {'Vru0': 5, 'Vl0': 20, 'Pn1': -40, 'PDz1': 40, 'Ssa1': 30, 'PDz0': 40, 'Pcw1': 20, 'Vnmk0': 20, 'PDm1': 10, 'Vnmc0': 10, 'Vnu0': -10, 'Sad0': -40, 'Snl0': 40, 'Vxg0': -10, 'Sdm0': 40, 'Vyout0': 10, 'Vxw0': 5, 'Vhj0': 40, 'Vrout1': -10, 'Vnu1': -10, 'Vwlo0': 10, 'Vnmk1': -15, 'Vyjf0': -5, 'Vlg0': -40, 'Vqi1': 40, 'Sad1': 5, 'Vwob0': 10, 'Ssa0': 40, 'Vaj0': -25, 'Pc1': 10, 'Vni0': -10, 'Vfdf0': -10}
+PAR.update({"pe": .6, "hop": 180., "self": 110., "fix": 70., "net": 4500., "bias": 0.})
+PAR.update({'xs': (1, 2, 0, 0), 'ds': (0, 0, 1, 0), 'zs': (0, 1, 0, 1), 'xgv': (1, 0), 'zgv': (0, 0), 'sg': ('good1', 'nn0', 'nn1', 'ch0', 'ch1'), 'look': 200.0, 'beta': 4.0, 'dmax': 5, 'gs': {'xg': 2, 'lg': 2, 'zg': 2}, 'T': 24000.0, 'delta': 5000.0, 'lam': 1.4})
+PAR["off"] = {'Vl0': -20, 'Vsd0': 40, 'Vwof0': 30, 'Syzf0': -15, 'Vpi1': 60, 'Vgood0': 5, 'Pyz0': 30, 'Vyjf0': -75, 'Vrd1': 150, 'PDm1': 5, 'Vfdf1': 25, 'Vai0': -40, 'Pn0': -30, 'Vrout0': 5, 'PDx0': 20, 'Vdm0': 35, 'Vyout0': 30, 'Pya1': 50, 'Pya0': 15, 'Pc1': 50, 'Vyy1': -5, 'Sdr1': -20, 'Vxg0': -10, 'Pcz1': 20, 'Snl0': 50, 'PA0': -35, 'Pcw1': -20, 'PDz1': -10, 'Vnmc1': -5, 'Vwoa0': 5, 'Vsi0': 60, 'Sxg0': -5, 'Vsi1': -100, 'Sdm0': 60, 'Snl1': -30, 'Vnmk1': 5, 'Szg0': 20, 'Saz1': 40, 'Pcnt0': -20, 'Vnx0': -30, 'Vyout1': 15, 'Pwo0': -80, 'Sch1': 45, 'Sct1': 40, 'Sct0': 5, 'Sch0': 100, 'Scnt1': -70, 'Saz0': -45, 'Ssa1': -35, 'Sad0': -10, 'Snm1': 30, 'Vnz1': 15, 'Snm0': -5, 'Sxg1': 5, 'Vthr0': -10, 'Vxw0': -50, 'Sdm1': -20, 'Scnt0': 50, 'Szg1': -30, 'Snn1': 5, 'Vzz0': 70, 'Ssa0': 15, 'Vui1': -30, 'PDx1': 20, 'Gremote0': 95, 'Vqi1': 60, 'Pcw0': 40, 'Vnu0': -20, 'Yoyz0': 5, 'Vsc1': -20, 'Voh0': 25, 'Ppre0': 55, 'Sdr0': 70, 'Vwob0': -60, 'PcT0': 5, 'Ppre1': 15, 'Snn0': 10, 'Vwov0': 5, 'Vyy0': 45, 'Yoj0': 5, 'Snx0': 15, 'Vni0': -5, 'Sgood1': -5, 'Snt1': 110, 'Vbase1': 15, 'Vhj0': -15, 'Vzb0': -5, 'Sad1': -55, 'Yoo0': 35, 'Gremote1': 15, 'Snt0': 5, 'Vsc0': 5, 'Vaj0': -20, 'Vwlo0': -5, 'Pdel1': -5, 'Vhw0': 15, 'Vdm1': 35, 'Vni1': -5, 'Pcz0': -10, 'PDm0': -5, 'Pdd1': 5, 'Pcnt1': 5, 'Vru1': 10, 'Vwou0': -40}
+PAR["off"].update({'Vl0': -15, 'Vsd0': 25, 'Vwof0': 15, 'Syzf0': 25, 'Vpi1': 40, 'Vgood0': -5, 'Pyz0': -5, 'Vyjf0': -135, 'Vrd1': 70, 'PDm1': 25, 'Vfdf1': 5, 'Vai0': -20, 'Pn0': -5, 'Vrout0': 15, 'PDx0': -10, 'Vdm0': 60, 'Vyout0': 85, 'Pya1': 65, 'Pya0': 10, 'Pc1': 80, 'Sdr1': -40, 'Vxg0': 15, 'Pcz1': -5, 'Snl0': 135, 'PA0': -65, 'Pcw1': -35, 'PDz1': -40, 'Vnmc1': 25, 'Vwoa0': 35, 'Vsi0': 20, 'Vsi1': -85, 'Vnmk1': 0, 'Szg0': 60, 'Saz1': 35, 'Pcnt0': 15, 'Vyout1': 100, 'Pwo0': -65, 'Sch1': 30, 'Sct1': 45, 'Sct0': -5, 'Sch0': 160, 'Scnt1': -20, 'Saz0': -25, 'Ssa1': 5, 'Sad0': -5, 'Snm1': 55, 'Vnz1': 20, 'Snm0': 35, 'Sxg1': 25, 'Vxw0': -60, 'Scnt0': 60, 'Szg1': 55, 'Snn1': -10, 'Ssa0': 10, 'Vui1': -45, 'PDx1': 0, 'Vqi1': 105, 'Pcw0': 55, 'Vnu0': 40, 'Voh0': 45, 'Ppre0': 30, 'Sdr0': 65, 'Vwob0': -45, 'PcT0': 0, 'Snn0': 50, 'Vwov0': -30, 'Vyy0': 105, 'Yoj0': 50, 'Snx0': -20, 'Vni0': -10, 'Snt1': 115, 'Vbase1': 45, 'Vhj0': -5, 'Vzb0': -10, 'Sad1': -65, 'Yoo0': 20, 'Gremote1': -5, 'Snt0': 0, 'Vsc0': -5, 'Vaj0': -25, 'Vwlo0': -10, 'Pdel1': -40, 'Vhw0': -35, 'Vdm1': -5, 'Vni1': 5, 'PDm0': 15, 'Pdd1': 0, 'Vru1': 30, 'Vwou0': -20, 'Voh1': 15, 'Vui0': -35, 'Vzb1': -15, 'Pdd0': 5, 'Vlg0': -20, 'Pu0': 30, 'Vfdf0': -5, 'Pnb0': 40, 'Pdel0': 5, 'Vlg1': -5, 'PcT1': 20, 'Vwhi0': -40, 'Vbase0': -15, 'Pu1': 60, 'Vzz1': -5, 'Vnmc0': -10, 'Vsd1': -15, 'Vru0': 20, 'Vrout1': 20, 'Vqi0': 10, 'Vpi0': -10, 'Vwi0': -5, 'Vnmk0': -40})
 
 
 def build_ops(par):
@@ -99,7 +103,7 @@ def build_ops(par):
         return op("S", fix + 20 + n * c, fn, r, w, ps)
 
     def step(name, out, in_, bound, big, up, r, w, n, tl):
-        if name in par["sg"]: return act(out, in_, ACT.Sigmoid, big, r, w, n, 1, [tl], 256.0 if up else -256.0)
+        if name + str(cur[0]) in par["sg"]: return act(out, in_, ACT.Sigmoid, big, r, w, n, 1, [tl], 256.0 if up else -256.0)
         return ts(out, in_, bound, None, ALU.is_ge if up else ALU.is_le, None, r, w, n, 1, [tl])
 
     def mm(tile, items, r, first=True, last=True, each=False):
@@ -156,7 +160,7 @@ def build_ops(par):
         v0, v1 = (0.0 if par["ds"][h * NC + c] else -240.0 for c in range(NC))
         ts(col(14 + h), S("ci", 5, 6), v1 - v0, v0, ALU.mult, ALU.add, ["ci5"], ["cf%d" % (14 + h)], 1)
         tt(col(16 + h), col(14 + h), col(4), ALU.add, ["cf%d" % (14 + h), "cf4"], ["cf%d" % (16 + h)], 1)
-    for nme, sc in (("idn", 1.0), ("n2", -16.0), ("i64", 64.0), ("nid", -1.0), ("pen", PEN), ("n16", 2.0 ** 20), ("n32", 2.0 ** 21), ("tri0", -7.0)):
+    for nme, sc in (("idn", 1.0), ("n2", -16.0), ("i64", 64.0), ("nid", -1.0), ("n16", 2.0 ** 20), ("n32", 2.0 ** 21), ("tri0", -7.0)):
         ts(S(nme, 0, 128), S("ioc", 0, 128), col(0), sc, ALU.is_equal, ALU.mult, ["ioc", "cf0"], [nme], 128)
     ts(S("hh", 0, 144), S("ioc", 0, 144), col(3), None, ALU.is_equal, None, ["ioc", "cf3"], ["hh"], 144)
     ts(S("bo", 0, 128), S("iob", 0, 128), col(2), None, ALU.is_equal, None, ["iob", "cf2"], ["bo"], 128)
@@ -168,15 +172,22 @@ def build_ops(par):
     for a in (0, 8):
         cp(S("o16", a, a + 8), S("bo", 0, 128, 16), ["bo"], ["o16_%d" % a], 8)
     ts(S("o512", 0, 8), S("bo", 0, 128, 16), 512.0, None, ALU.mult, None, ["bo"], ["o512"], 8)
+    cp(col(18), S("ci", 5, 6), ["ci5"], ["cf18"], 1)
+    tt(col(19), col(0), col(18), ALU.subtract, ["cf0", "cf18"], ["cf19"], 1)
+    ts(col(20), col(18), -PEN, PEN, ALU.mult, ALU.add, ["cf18"], ["cf20"], 1)
+    ts(col(21), col(18), PEN, None, ALU.mult, None, ["cf18"], ["cf21"], 1)
+    for c in range(NC):
+        ts(S("pen2", 128 * c, 128 * c + 128), S("ioc", 0, 128), col(19), col(20 + c), ALU.is_equal, ALU.mult, ["ioc", "cf19", "cf%d" % (20 + c)], ["pen%d" % c], 128)
+    ts(S("lp", 0, 128), S("ioc", 0, 128), float(PW), col(18), ALU.is_ge, ALU.is_equal, ["ioc", "cf18"], ["lp"], 128)
     for h in range(NH):
         for j in (0, 1):
             n = 16 - 2 * j + h
-            ts(S("kc", 256 * h + 128 * j, 256 * h + 128 * j + 128), S("idn", 0, 128), col(n), None, ALU.mult, None, ["idn", "cf%d" % n], ["kc%d%d" % (j, h)], 128, .5)
+            ts(S("kc", 256 * h + 128 * j, 256 * h + 128 * j + 128), S("ioc", 0, 128), col(19), col(n), ALU.is_equal, ALU.mult, ["ioc", "cf19", "cf%d" % n], ["kc%d%d" % (j, h)], 128)
+        ts(S("kc", 256 * h + 1, 256 * h + 128, 2), S("ioc", 0, 128, 2), col(19), 8 * PEN, ALU.is_equal, ALU.mult, ["ioc", "cf19"], ["kc0%d" % h], 64)
+    ms(S("dr", 0, 2 * NH * 144), 0.0, ["dr%d_%d" % (a, h) for a in range(2) for h in range(NH)], NH * 144)
     ts(S("nbo", 0, 128), S("bo", 0, 128), -1.0, None, ALU.mult, None, ["bo"], ["nbo"], 128, .5)
     ts(S("hn", 0, 144), S("hh", 0, 144), -65536.0, None, ALU.mult, None, ["hh"], ["hn"], 144, .5)
     ms(S("c73", 0, 128), -73.0 * 32768, ["c73"], 64)
-    ms(S("ones", 0, 128), 1.0, ["ones"], 64)
-    ms(S("c2048", 0, 128), 2048.0, ["c2048"], 64)
     ms(S("cm7", 0, 128), -7.0, ["cm7"], 64)
     ms(S("zz", 0, 2 * NH * 128), 0.0, ["zz%d_%d" % (a, h) for a in range(2) for h in range(NH)], 2 * NH * 128)
     lo, st = 1792.0, -512.0
@@ -238,12 +249,12 @@ def build_ops(par):
                 return ["%s%d_%s" % (name, j, u) for j in range(gs)]
             XG = gather("xg", "xw", "ru")
             LG = gather("lg", "lw", "ru")
+            LGS = LG + (LGS if h else [])
             tl = "n" + v
-            mm(tl, [(PS(tl, 0, PW), IDN, S("c2048", 0, PW), PW)]
-               + [(PS(tl, 0, PW), S("ba", 144 * ((k + t) % 16) + 15 - k, 144 * ((k + t) % 16) + 143 - k), S("lg", ob + k, ob + n16, 16), PW) for k in range(16)],
-               ["idn", "c2048"] + LG + ["ba%d" % j for j in range(16)])
-            cp(sm("nu"), PS(tl, 0, PW), [tl], ["nu" + u], PW, 1, [tl])
-            act(sm("nm"), PS(tl, 0, PW), ACT.Identity, 4096.0, [tl], ["nm" + u], PW, 1, [tl])
+            mm(tl, [(PS(tl, 0, PW), S("ba", 144 * ((k + t) % 16) + 15 - k, 144 * ((k + t) % 16) + 143 - k), S("lg", ob + k, ob + n16, 16), PW) for k in range(16)],
+               LG + ["ba%d" % j for j in range(16)])
+            ts(sm("nu"), PS(tl, 0, PW), 2048.0, None, ALU.add, None, [tl], ["nu" + u], PW, 1, [tl])
+            act(sm("nm"), PS(tl, 0, PW), ACT.Identity, 6144.0, [tl], ["nm" + u], PW, 1, [tl])
             ts(sm("nmk"), RIN, col(5), None, ALU.add, None, [rin, "cf5"], ["nmk" + u], PW)
             ZG = gather("zg", "xw", "nu")
 
@@ -254,7 +265,9 @@ def build_ops(par):
                 tl = "Dx%s_%d" % (v, c)
                 sub(tl, "xg", c, YIN, XG + [yin], yin, True)
                 act(cls("ad", c), PS(tl, 0, 512), ACT.Abs, 0.0, [tl], ["ad%s_%d" % (u, c)], 512, 1, [tl])
-                if par["xs"][h * NC + c]:
+                if par["xs"][h * NC + c] == 2:
+                    act(cls("nx", c), cls("ad", c), ACT.Sigmoid, 384.0, ["ad%s_%d" % (u, c)], ["nx%s_%d" % (u, c)], 512, 1, (), -256.0)
+                elif par["xs"][h * NC + c]:
                     ts(cls("nx", c), cls("ad", c), 1.0, None, ALU.is_le, None, ["ad%s_%d" % (u, c)], ["nx%s_%d" % (u, c)], 512, .5)
                 else:
                     ts(cls("nx", c), PS(tl, 0, 512), M4, M4, ALU.add, ALU.is_equal, [tl], ["nx%s_%d" % (u, c)], 512, 1, [tl])
@@ -289,14 +302,23 @@ def build_ops(par):
                     mm(tl, [(PS(tl, j, 512, KK), IDN, sm("oh"), PW) for j in range(KK)], ["idn", "oh" + u], each=True)
                     tt(cls("dm", c), jc("xg", c), PS(tl, 0, 512), ALU.max, [tl] + XG, ["dm%s_%d" % (u, c)], 512, 1, [tl])
             tl = "K" + v
-            mm(tl, [(PS(tl, 0, 256, None, PW), S("ones", 0, PW), S("kc", 256 * h, 256 * h + 256), 256)]
-               + [(PS(tl, k, 128, 16, PW), ks("ad", k), S("o512", 0, 8), 8) for k in korder],
-               ["ones", "kc0%d" % h, "kc1%d" % h, "good" + u, "o512"] + ["ad%s_%d" % (u, c) for c in range(NC)], True, False)
-            mm(tl, [(PS(tl, 0, 128, None, PW), sm("sa"), S("pen", 0, 128), 128)], ["sa" + u, "pen"], False, False)
-            byclass(tl, lambda k: (PS(tl, k, 256, 16, PW), ks("dm", k), S("o16", 0, 16), 16), ["o16_0", "o16_8"], "dm", first=False)
-            scan(t128("sc"), S("rst", 0, 128, None, PW), PS(tl, 0, 128, None, PW), ALU.add, ALU.min, [tl, "rst"], ["sc" + u], 128, [tl])
-            act(t128("dr"), PS(tl, 128, 256, None, PW), ACT.Identity, 0.0, [tl], ["dr" + u], 128, 1, [tl])
-            ends = S("sc", 128 * o3 + 15, 128 * o3 + 128, 16, PW)
+            def both(name, j, ob=ob): return S(name, ob + j, ob + n16, KK)
+            mm(tl, [(PS(tl, 0, 256), S("lp", 0, 128), S("kc", 256 * h, 256 * h + 256), 256)]
+               + [(PS(tl, 2 * j, 128, 16), both("ad", j), S("o512", 0, 8), 8) for j in range(KK)],
+               ["lp", "kc0%d" % h, "kc1%d" % h, "good" + u, "o512"] + ["ad%s_%d" % (u, c) for c in range(NC)], True, False)
+            mm(tl, [(lambda T, Q, c=c, tl=tl: Q(tl)[PW * c:PW * c + PW, 0:128], sm("sa"), S("pen2", 128 * c, 128 * c + 128), 128) for c in range(NC)],
+               ["sa" + u, "pen0", "pen1"], False, False)
+            mm(tl, [(PS(tl, 2 * j, 256, 16), both("dm", j), S("o16", 0, 16), 16) for j in range(KK)], ["o16_0", "o16_8"] + ["dm%s_%d" % (u, c) for c in range(NC)], False, True)
+            scan(S("sc", 128 * o3, 128 * o3 + 128), S("rst", 0, 128), PS(tl, 0, 128), ALU.add, ALU.min, [tl, "rst"], ["sd" + u], 128, [tl])
+            od = 144 * o3 + 8
+            act(S("dr", od, od + 128), PS(tl, 128, 256), ACT.Identity, 0.0, [tl], ["dr" + u], 128, 1, [tl])
+            ends = t8("dl")
+            k = tt(ends, S("sc", 128 * o3 + 15, 128 * o3 + 128, 16, PW), lambda T, Q, o3=o3: T.sc[PW:128, 128 * o3 + 15:128 * o3 + 128:16], ALU.min, ["sd" + u], ["sc" + u], 8)
+            ops[k]["drain"] = True
+            ops[k]["cost"] += par["self"]
+
+            def xr(tl, a0, od=od):
+                return [(PS(tl, a0, a0 + PW), S("dr", od - c, od - c + 128), S("idn", PW * c, PW * c + PW), PW) for c in range(NC)]
             ts(t8("rd"), ends, M32, M32, ALU.add, ALU.subtract, ["sc" + u], ["rd" + u], 8)
             tt(S("zz", 128 * o3, 128 * o3 + 128, 16, PW), ends, t8("rd"), ALU.subtract, ["sc" + u, "rd" + u], ["zz" + u], 8)
             scan(t128("zb"), S("keep", 0, 128, None, PW), t128("zz"), ALU.mult, ALU.add, ["keep", "zz" + u], ["zb" + u], 128)
@@ -313,19 +335,28 @@ def build_ops(par):
             send("y", "yout", "yin", yn)
             tl = "dd" + v
             far = S("i64", 0, 128)
-            mm(tl, [(PS(tl, 0, PW), t128("dr"), IW, PW), (PS(tl, 0, PW), S("nbo", 0, 128), YIN, PW), (PS(tl, 0, PW), S("bo", 0, 128), sm("yy"), PW), (PS(tl, 0, PW), far, sm("nl"), PW)],
+            mm(tl, xr(tl, 0) + [(PS(tl, 0, PW), S("nbo", 0, 128), YIN, PW), (PS(tl, 0, PW), S("bo", 0, 128), sm("yy"), PW), (PS(tl, 0, PW), far, sm("nl"), PW)],
                ["dr" + u, "idn", "nbo", "bo", "i64", yin, "yy" + u, "nl" + u])
-            mm(tl, [(PS(tl, PW, 2 * PW), t128("dr"), IW, PW), (PS(tl, PW, 2 * PW), far, sm("nl"), PW), (PS(tl, PW, 2 * PW), t128("zb"), NW, PW)],
+            mm(tl, xr(tl, PW) + [(PS(tl, PW, 2 * PW), far, sm("nl"), PW), (PS(tl, PW, 2 * PW), t128("zb"), NW, PW)],
                ["dr" + u, "zb" + u, "idn", "nid", "i64", "nl" + u])
             on = 2 * PW * o3
-            ts(S("nn", on, on + 2 * PW), PS(tl, 0, 2 * PW), M4, M4, ALU.add, ALU.is_equal, [tl], ["nn" + u], 2 * PW, 1, [tl])
+            if "nn%d" % h in par["sg"]:
+                act(S("nt", on, on + 2 * PW), PS(tl, 0, 2 * PW), ACT.Abs, 0.0, [tl], ["nt" + u], 2 * PW, 1, [tl])
+                act(S("nn", on, on + 2 * PW), S("nt", on, on + 2 * PW), ACT.Sigmoid, 384.0, ["nt" + u], ["nn" + u], 2 * PW, 1, (), -256.0)
+            else:
+                ts(S("nn", on, on + 2 * PW), PS(tl, 0, 2 * PW), M4, M4, ALU.add, ALU.is_equal, [tl], ["nn" + u], 2 * PW, 1, [tl])
             tl = "c2" + v
             mm(tl, [(PS(tl, 0, PW), IDN, sm("cnt"), PW), (PS(tl, 0, PW), NID, S("nn", on, on + PW), PW), (PS(tl, 0, PW), IDN, S("nn", on + PW, on + 2 * PW), PW)],
                ["idn", "nid", "cnt" + u, "nn" + u])
             act(sm("sa2"), PS(tl, 0, PW), ACT.Sign, -11.5, [tl], ["sa2" + u], PW, 1, [tl])
             tl = "cw" + v
-            mm(tl, [(PS(tl, 0, PW), IDN, S("cm7", 0, PW), PW), (PS(tl, 0, PW), S("m1", 0, 128), sm("sa2"), PW)], ["idn", "cm7", "m1", "sa2" + u])
-            ts(sm("ch"), PS(tl, 0, PW), M16, M16, ALU.add, ALU.is_equal, [tl], ["ch" + u], PW, 1, [tl])
+            if "ch%d" % h in par["sg"]:
+                mm(tl, [(PS(tl, 0, PW), S("m1", 0, 128), sm("sa2"), PW)], ["m1", "sa2" + u])
+                act(sm("ct"), PS(tl, 0, PW), ACT.Abs, -7.0, [tl], ["ct" + u], PW, 1, [tl])
+                act(sm("ch"), sm("ct"), ACT.Sigmoid, 1792.0, ["ct" + u], ["ch" + u], PW, 1, (), -256.0)
+            else:
+                mm(tl, [(PS(tl, 0, PW), IDN, S("cm7", 0, PW), PW), (PS(tl, 0, PW), S("m1", 0, 128), sm("sa2"), PW)], ["idn", "cm7", "m1", "sa2" + u])
+                ts(sm("ch"), PS(tl, 0, PW), M16, M16, ALU.add, ALU.is_equal, [tl], ["ch" + u], PW, 1, [tl])
             tt(sm("nmc"), sm("ch"), sm("nm"), ALU.mult, ["ch" + u, "nm" + u], ["nmc" + u], PW)
             tt(sm("base"), sm("nmc"), RIN, ALU.max, ["nmc" + u, rin], ["base" + u], PW)
             tl = "u" + v
@@ -340,7 +371,10 @@ def build_ops(par):
                 sub(tl, "zg", c, YN, ZG + ["zb" + u], yn, True)
                 if par["zs"][h * NC + c]:
                     act(cls("az", c), PS(tl, 0, 512), ACT.Abs, 0.0, [tl], ["az%s_%d" % (u, c)], 512, 1, [tl])
-                    ts(cls("nz", c), cls("az", c), 1.0, None, ALU.is_le, None, ["az%s_%d" % (u, c)], ["nz%s_%d" % (u, c)], 512, .5)
+                    if par["zs"][h * NC + c] == 2:
+                        act(cls("nz", c), cls("az", c), ACT.Sigmoid, 384.0, ["az%s_%d" % (u, c)], ["nz%s_%d" % (u, c)], 512, 1, (), -256.0)
+                    else:
+                        ts(cls("nz", c), cls("az", c), 1.0, None, ALU.is_le, None, ["az%s_%d" % (u, c)], ["nz%s_%d" % (u, c)], 512, .5)
                 else:
                     ts(cls("nz", c), PS(tl, 0, 512), M4, M4, ALU.add, ALU.is_equal, [tl], ["nz%s_%d" % (u, c)], 512, 1, [tl])
             tl = "cz" + v
@@ -366,8 +400,14 @@ def build_ops(par):
         cp(S("wou", 8 * a, 8 * a + 8), S("wof", 8 * a, 8 * a + 8), ["wof" + s], ["wou" + s], 8)
         if t < V - 1:
             cp(lambda T, Q, a=a: T.xw[:, 0:W].indirect(T.wou[:, 8 * a:8 * a + 8]), S("yout", t * P, t * P + P), ["wou" + s] + yns, ["xw"], P, par["sca"])
-        cp(lambda T, Q, a=a: T.lw[:, 0:W].indirect(T.wou[:, 8 * a:8 * a + 8]), S("rout", t * P, t * P + P),
-           ["wou" + s] + ["rout%d_%d" % (t, h) for h in hs], ["lw"], P, par["sca"])
+        if t < V - 1:
+            cp(lambda T, Q, a=a: T.lw[:, 0:W].indirect(T.wou[:, 8 * a:8 * a + 8]), S("rout", t * P, t * P + P),
+               ["wou" + s] + ["rout%d_%d" % (t, h) for h in hs], ["lw", "lw0", "lw1"], P, par["sca"])
+        else:
+            ts(S("wov", 4, 8), S("wof", 8 * a + 4, 8 * a + 8), -W / 2, None, ALU.add, None, ["wof" + s], ["wov"], 4)
+            for h in hs:
+                cp(lambda T, Q, a=a, h=h: T.lw[:, h * W // 2:(h + 1) * W // 2].indirect(T.wov[:, 4:8] if h else T.wou[:, 8 * a:8 * a + 4]),
+                   S("rout", t * P + h * PW, t * P + h * PW + PW), ["wou" + s, "wov", "rout%d_%d" % (t, h)] + LGS, ["lw%d" % h], PW, par["sca"])
     for h in range(NH):
         v = "%d_%d" % (V, h); oi = V * P + h * PW
         op("N", 0, None, (), ["rin" + v], (), "ar" + v, par["net"], sends["r%d_%d" % (V - 1, h)])
@@ -375,11 +415,11 @@ def build_ops(par):
         dma("Y", lambda T, Q, h=h: T.yo[:, h * PW:h * PW + PW], S("yin", oi, oi + PW), "oo%d" % h, ["yin" + v], [], 2500)
         cp(S("yjf", h * PW, h * PW + PW), S("rin", oi, oi + PW), ["rin" + v], ["yjf%d" % h], PW)
         dma("Y", lambda T, Q, h=h: T.yj[:, h * PW:h * PW + PW], S("yjf", h * PW, h * PW + PW), "oj%d" % h, ["yjf%d" % h], [], 2500)
-    cuts = (0, 5, 10, 14, 16)
-    for j in range(4):
+    cuts = (0, 2, 4, 6, 8, 11, 14, 16)
+    for j in range(7):
         c0, c1 = cuts[j], cuts[j + 1]
-        ts(S("l16", 256 * c0, 256 * c1), S("lw", 256 * c0, 256 * c1), -2048.0, None, ALU.add, None, ["lw"], ["l16_%d" % j], 256 * (c1 - c0))
-        mm("yz", [(PS("yz", 0, 256), hk("hj", c), S("l16", 256 * c, 256 * c + 256), 256) for c in range(c0, c1)], ["hj", "l16_%d" % j], j == 0, j == 3)
+        ts(S("l16", 256 * c0, 256 * c1), S("lw", 256 * c0, 256 * c1), -2048.0, None, ALU.add, None, ["lw%d" % (c0 // 8)], ["l16_%d" % j], 256 * (c1 - c0))
+        mm("yz", [(PS("yz", 0, 256), hk("hj", c), S("l16", 256 * c, 256 * c + 256), 256) for c in range(c0, c1)], ["hj", "l16_%d" % j], j == 0, j == 6)
     act(S("yzf", 0, 256), PS("yz", 0, 256), ACT.Identity, 2048.0 * 136, ["yz"], ["yzf"], 256, 1, ["yz"])
     dma("Y", lambda T, Q: T.yz[:, :], S("yzf", 0, 256), "oyz", ["yzf"], [], 2500)
     return ops
@@ -475,6 +515,12 @@ def lay_out(ops, par, given=None):
     pr = [0.0] * n
     for k in range(n - 1, -1, -1):
         pr[k] = ops[k]["cost"] + ops[k]["lat"] + par["hop"] + max([pr[s] for s in succ[k]] + [0.0])
+    if par.get("T"):
+        rs = [k for k in range(n) if ops[k]["sem"] == "remote"][1::2]
+        dead = {k: (j // NH) * par["T"] + (j % NH) * par["delta"] for j, k in enumerate(rs)}
+        last = max(dead.values()) + par["net"] + 3000.0
+        for k in range(n - 1, -1, -1):
+            pr[k] = ops[k]["cost"] * par["lam"] + ops[k]["lat"] + par["hop"] + (-dead[k] if k in dead else max([pr[s] for s in succ[k]] + [-last]))
     for k in range(n): pr[k] += par["off"].get(kind(ops[k]), 0) * 100.0 - par["bias"] * ops[k]["h"]
     if given: pr = given
     if par["serial"]: return place(ops, par, pr, succ, left)
@@ -547,14 +593,17 @@ def rank_program(g, core, T, topo):
     def Q(name):
         return env[name] if name in env else T["pb%d" % bank[name]]
     queue = {"V": g.vector, "S": g.scalar, "P": g.tensor, "G": g, "Y": g.sync}
-    count = {e: 0 for e in "VSPG"}; known = {e: {} for e in queue}; mark = {}; top = {}; sent = 0
+    count = {e: 0 for e in "VSPG"}; known = {e: {} for e in queue}; mark = {}; top = {}; sent = 0; drain = []
     for k in order:
         o = ops[k]; e = o["eng"]
         if e == "N":
             mark[k] = (o["sem"], n_in, {}); top[o["sem"]] = n_in
             continue
         kn = known[e]
-        need = sorted((mark[d] for d in o["all"] if d in mark and not (e == "P" and ops[d]["eng"] == "P")), key=lambda m: -m[1])
+        pre = set(o["all"])
+        if e == "V":
+            pre.update(drain); drain[:] = [k] if o.get("drain") else []
+        need = sorted((mark[d] for d in pre if d in mark and not (e == "P" and ops[d]["eng"] == "P")), key=lambda m: -m[1])
         for sem, val, clock in need:
             if kn.get(sem, 0) >= val: continue
             if any(c2.get(sem, 0) >= val for s2, v2, c2 in need): continue

@@ -2,576 +2,578 @@ from concourse.mybir import dt, AluOpType, ActivationFunctionType
 
 ALU = AluOpType
 ACT = ActivationFunctionType
-NR, V, W, P = 6, 6, 4096, 128
+V, W, P = 6, 4096, 128
 NH = 2
 PW = P // NH
-NC = 16 * PW // 512
+NC = 2
 KK = 16 // NC
 M4 = float((2 ** 23 + 1) * 4)
-M16 = float((2 ** 23 + 1) * 16)
-M32 = float(3 * 2 ** 27)
-PEN = float(2 ** 18)
-BIGV = float(2 ** 22)
+M1, M32, M4096 = float(3 * 2 ** 22), float(3 * 2 ** 27), float(3 * 2 ** 34)
+PEN = float(2 ** 17)
+BIG = float(2 ** 22)
+SEG = 18
 
 B, F, I32, U16, H16 = "bfloat16", "float32", "int32", "uint16", "float16"
 SCRATCH = {
-    "xw": ("sbuf", [128, W], B), "lw": ("sbuf", [128, W], I32), "l16": ("sbuf", [128, W], H16),
-    "rin": ("sbuf", [128, (V + 1) * P], I32), "yin": ("sbuf", [128, (V + 1) * P], B),
-    "rout": ("sbuf", [128, V * P], I32), "yout": ("sbuf", [128, V * P], B),
-    "wi": ("sbuf", [128, 8], I32), "yjf": ("sbuf", [128, P], F), "yzf": ("sbuf", [128, 256], F),
-    "ci": ("sbuf", [128, 8], I32), "cf": ("sbuf", [128, 32], F), "rm": ("sbuf", [128, 16], F),
-    "ioc": ("sbuf", [128, 144], F), "iob": ("sbuf", [128, 128], F), "iom": ("sbuf", [128, 128], F),
-    "c32": ("sbuf", [128, 8], F), "c32i": ("sbuf", [128, 8], F),
-    "hh": ("sbuf", [128, 144], B), "hw5": ("sbuf", [128, 144], B), "hj": ("sbuf", [128, 144], H16),
-    "ba": ("sbuf", [128, 16 * 144], H16), "kc": ("sbuf", [128, 512], B),
-    "pen2": ("sbuf", [128, 256], B), "sel": ("sbuf", [128, 128], F), "acc": ("sbuf", [128, 8], F), "hn": ("sbuf", [128, 144], B),
-    "o16": ("sbuf", [128, 16], B), "o512": ("sbuf", [128, 8], B),
-    "rst": ("sbuf", [128, 128], F), "keep": ("sbuf", [128, 128], F), "thr": ("sbuf", [128, 8 * V], F),
-    "ai": ("sbuf", [128, 16], I32), "wo": ("sbuf", [128, 32], I32), "wof": ("sbuf", [128, 16], F), "wou": ("sbuf", [128, 16], U16), "wov": ("sbuf", [128, 8], U16),
+    "xw": [W, B], "li": [W, I32], "lw": [W, F], "l16": [W, H16],
+    "rin": [V * P, U16], "yin": [(V + 1) * P, B], "rout": [V * P, U16], "yout": [V * P, B], "rfin": [P, F], "rlast": [P, F],
+    "wi": [8, I32], "yzf": [256, F], "ci": [8, I32], "cf": [32, F], "rm": [16, F],
+    "ioc": [144, F], "iob": [128, F], "iom": [128, F], "ioj": [64, F], "iog": [64, F], "tmp": [256, F],
+    "hh": [144, B], "hz": [144, B], "hj": [144, H16], "ba": [16 * 144, H16], "kc": [128 * NH, B], "pen": [128, B],
+    "sel": [128, F], "acc": [8, F], "o16": [16, B], "o512": [8, B], "f0": [192, B], "rs8": [64, F], "rs16": [128, F],
+    "thr": [8 * V, F], "ai": [16, I32], "wou": [32, U16], "ws": [2 * P, F], "wp": [128, H16], "wn": [128, H16],
+    "lg": [2 * 2048, H16], "dr": [2 * NH * 144, B], "nn": [2 * 2 * P, B], "nt": [2 * 2 * P, B], "qq": [2 * NH * 8, I32],
+    "zz": [2 * NH * 128, I32], "zb": [2 * NH * 128, B], "keep": [128, F],
+    "s3": [2 * 3 * P, F], "s3o": [2 * 3 * P, F],
 }
-for _n in ("idn", "nid", "n2", "i64", "nbo", "c73", "bo", "tri", "tri0", "tri1", "lp", "m1", "n16", "n32", "whi", "wlo", "cm7"):
-    SCRATCH[_n] = ("sbuf", [128, 128], B)
-for _n in ("xg", "zg", "ad", "nx", "dm", "az", "nz"):
-    SCRATCH[_n] = ("sbuf", [128, 2 * 2048], B)
-SCRATCH["lg"] = ("sbuf", [128, 2 * 2048], H16)
-for _n, _d in (("ru", U16), ("nu", U16), ("nm", F), ("nmk", F), ("good", B), ("cnt", B), ("sa", B), ("oh", B), ("yy", B),
-               ("nl", B), ("sa2", B), ("ch", B), ("si", I32), ("ui", I32), ("pi", I32), ("qi", I32), ("df", F),
-               ("nmc", F), ("base", F), ("ct", B), ("fdf", F), ("ni", I32)):
-    SCRATCH[_n] = ("sbuf", [128, 2 * P], _d)
-for _n, _d, _w in (("sc", F, 128), ("zz", F, 128), ("zb", B, 128), ("dr", B, 144), ("nn", B, 2 * PW), ("nt", B, 2 * PW), ("rd", F, 8), ("dl", F, 8)):
-    SCRATCH[_n] = ("sbuf", [128, 2 * NH * _w], _d)
+for _n in ("idn", "nid", "i16", "n16", "i64", "q25", "nbo", "bo", "tri", "mA", "mB", "w5p", "w5n", "wb", "c1", "c32", "c4096", "cc", "c155", "c2048"):
+    SCRATCH[_n] = [128, B]
+for _n in ("xg", "zg", "ad", "nx", "dm", "az", "nz", "dx", "dz"):
+    SCRATCH[_n] = [2 * 2048, B]
+for _n, _d in (("nu", U16), ("nm", F), ("kp", F), ("good", B), ("cnt", B), ("sa", B), ("oh", B), ("yy", B), ("nl", B), ("sa2", B),
+               ("pi", I32), ("pj", I32), ("far", I32), ("sc", F)):
+    SCRATCH[_n] = [2 * P, _d]
+SCRATCH = {_n: ("sbuf", [128, _v[0]], _v[1]) for _n, _v in SCRATCH.items()}
 for _n in range(8):
     SCRATCH["pb%d" % _n] = ("psum", [128, 512], F)
-SEMAPHORES = (["cV", "cS", "cP", "cG", "sent", "ljur", "lown", "lwgt", "lx", "ll", "oyz"]
+LCH = 4
+SEMAPHORES = (["cV", "cS", "cP", "cG", "sent", "ljur", "lown", "lwgt", "lx", "oyz"] + ["ll%d" % j for j in range(LCH)]
               + ["oj%d" % h for h in range(NH)] + ["oo%d" % h for h in range(NH)]
               + ["a%s%d_%d" % (k, t, h) for k in "ry" for t in range(1, V + 1) for h in range(NH)])
 
-PAR = {"fix": 50.0, "gam": 1.5, "sca": 3.5, "pe": 0.5, "hop": 110.0, "self": 60.0, "net": 3600.0, "rounds": 1, "serial": 0}
-PAR.update({'xs': (1, 1, 1, 1), 'ds': (0, 1, 0, 1), 'zs': (0, 1, 0, 1), 'xgv': (1, 1), 'zgv': (0, 0), 'sg': (), 'look': 200.0, 'beta': 4.0, 'dmax': 5, 'bias': 4000.0, 'gs': {'xg': 4, 'lg': 2, 'zg': 2}})
-PAR["off"] = {'Vru0': 5, 'Vl0': 20, 'Pn1': -40, 'PDz1': 40, 'Ssa1': 30, 'PDz0': 40, 'Pcw1': 20, 'Vnmk0': 20, 'PDm1': 10, 'Vnmc0': 10, 'Vnu0': -10, 'Sad0': -40, 'Snl0': 40, 'Vxg0': -10, 'Sdm0': 40, 'Vyout0': 10, 'Vxw0': 5, 'Vhj0': 40, 'Vrout1': -10, 'Vnu1': -10, 'Vwlo0': 10, 'Vnmk1': -15, 'Vyjf0': -5, 'Vlg0': -40, 'Vqi1': 40, 'Sad1': 5, 'Vwob0': 10, 'Ssa0': 40, 'Vaj0': -25, 'Pc1': 10, 'Vni0': -10, 'Vfdf0': -10}
-PAR.update({"pe": .6, "hop": 180., "self": 110., "fix": 70., "net": 4500., "bias": 0.})
-PAR.update({'xs': (1, 2, 0, 0), 'ds': (0, 0, 1, 0), 'zs': (0, 1, 0, 1), 'xgv': (1, 0), 'zgv': (0, 0), 'sg': ('good1', 'nn0', 'nn1', 'ch0', 'ch1'), 'look': 200.0, 'beta': 4.0, 'dmax': 5, 'gs': {'xg': 2, 'lg': 2, 'zg': 2}, 'T': 24000.0, 'delta': 5000.0, 'lam': 1.4})
-PAR["off"] = {'Vl0': -20, 'Vsd0': 40, 'Vwof0': 30, 'Syzf0': -15, 'Vpi1': 60, 'Vgood0': 5, 'Pyz0': 30, 'Vyjf0': -75, 'Vrd1': 150, 'PDm1': 5, 'Vfdf1': 25, 'Vai0': -40, 'Pn0': -30, 'Vrout0': 5, 'PDx0': 20, 'Vdm0': 35, 'Vyout0': 30, 'Pya1': 50, 'Pya0': 15, 'Pc1': 50, 'Vyy1': -5, 'Sdr1': -20, 'Vxg0': -10, 'Pcz1': 20, 'Snl0': 50, 'PA0': -35, 'Pcw1': -20, 'PDz1': -10, 'Vnmc1': -5, 'Vwoa0': 5, 'Vsi0': 60, 'Sxg0': -5, 'Vsi1': -100, 'Sdm0': 60, 'Snl1': -30, 'Vnmk1': 5, 'Szg0': 20, 'Saz1': 40, 'Pcnt0': -20, 'Vnx0': -30, 'Vyout1': 15, 'Pwo0': -80, 'Sch1': 45, 'Sct1': 40, 'Sct0': 5, 'Sch0': 100, 'Scnt1': -70, 'Saz0': -45, 'Ssa1': -35, 'Sad0': -10, 'Snm1': 30, 'Vnz1': 15, 'Snm0': -5, 'Sxg1': 5, 'Vthr0': -10, 'Vxw0': -50, 'Sdm1': -20, 'Scnt0': 50, 'Szg1': -30, 'Snn1': 5, 'Vzz0': 70, 'Ssa0': 15, 'Vui1': -30, 'PDx1': 20, 'Gremote0': 95, 'Vqi1': 60, 'Pcw0': 40, 'Vnu0': -20, 'Yoyz0': 5, 'Vsc1': -20, 'Voh0': 25, 'Ppre0': 55, 'Sdr0': 70, 'Vwob0': -60, 'PcT0': 5, 'Ppre1': 15, 'Snn0': 10, 'Vwov0': 5, 'Vyy0': 45, 'Yoj0': 5, 'Snx0': 15, 'Vni0': -5, 'Sgood1': -5, 'Snt1': 110, 'Vbase1': 15, 'Vhj0': -15, 'Vzb0': -5, 'Sad1': -55, 'Yoo0': 35, 'Gremote1': 15, 'Snt0': 5, 'Vsc0': 5, 'Vaj0': -20, 'Vwlo0': -5, 'Pdel1': -5, 'Vhw0': 15, 'Vdm1': 35, 'Vni1': -5, 'Pcz0': -10, 'PDm0': -5, 'Pdd1': 5, 'Pcnt1': 5, 'Vru1': 10, 'Vwou0': -40}
-PAR["off"].update({'Vl0': -15, 'Vsd0': 25, 'Vwof0': 15, 'Syzf0': 25, 'Vpi1': 40, 'Vgood0': -5, 'Pyz0': -5, 'Vyjf0': -135, 'Vrd1': 70, 'PDm1': 25, 'Vfdf1': 5, 'Vai0': -20, 'Pn0': -5, 'Vrout0': 15, 'PDx0': -10, 'Vdm0': 60, 'Vyout0': 85, 'Pya1': 65, 'Pya0': 10, 'Pc1': 80, 'Sdr1': -40, 'Vxg0': 15, 'Pcz1': -5, 'Snl0': 135, 'PA0': -65, 'Pcw1': -35, 'PDz1': -40, 'Vnmc1': 25, 'Vwoa0': 35, 'Vsi0': 20, 'Vsi1': -85, 'Vnmk1': 0, 'Szg0': 60, 'Saz1': 35, 'Pcnt0': 15, 'Vyout1': 100, 'Pwo0': -65, 'Sch1': 30, 'Sct1': 45, 'Sct0': -5, 'Sch0': 160, 'Scnt1': -20, 'Saz0': -25, 'Ssa1': 5, 'Sad0': -5, 'Snm1': 55, 'Vnz1': 20, 'Snm0': 35, 'Sxg1': 25, 'Vxw0': -60, 'Scnt0': 60, 'Szg1': 55, 'Snn1': -10, 'Ssa0': 10, 'Vui1': -45, 'PDx1': 0, 'Vqi1': 105, 'Pcw0': 55, 'Vnu0': 40, 'Voh0': 45, 'Ppre0': 30, 'Sdr0': 65, 'Vwob0': -45, 'PcT0': 0, 'Snn0': 50, 'Vwov0': -30, 'Vyy0': 105, 'Yoj0': 50, 'Snx0': -20, 'Vni0': -10, 'Snt1': 115, 'Vbase1': 45, 'Vhj0': -5, 'Vzb0': -10, 'Sad1': -65, 'Yoo0': 20, 'Gremote1': -5, 'Snt0': 0, 'Vsc0': -5, 'Vaj0': -25, 'Vwlo0': -10, 'Pdel1': -40, 'Vhw0': -35, 'Vdm1': -5, 'Vni1': 5, 'PDm0': 15, 'Pdd1': 0, 'Vru1': 30, 'Vwou0': -20, 'Voh1': 15, 'Vui0': -35, 'Vzb1': -15, 'Pdd0': 5, 'Vlg0': -20, 'Pu0': 30, 'Vfdf0': -5, 'Pnb0': 40, 'Pdel0': 5, 'Vlg1': -5, 'PcT1': 20, 'Vwhi0': -40, 'Vbase0': -15, 'Pu1': 60, 'Vzz1': -5, 'Vnmc0': -10, 'Vsd1': -15, 'Vru0': 20, 'Vrout1': 20, 'Vqi0': 10, 'Vpi0': -10, 'Vwi0': -5, 'Vnmk0': -40})
+PAR = {"xg": ("SS", "SS"), "lg": ("SS", "SS"), "zg": ("SS", "SS"),
+       "xm": (1, 1), "zm": (1, 1),
+       "xs": ((1, 1), (1, 1)), "zs": ((0, 0), (0, 0)), "ds": ((0, 0), (0, 0)),
+       "sg": ("good", "oh"), "split": 1, "fin": "VSVSVSVS",
+       "look": 200.0, "beta": 4.0, "dmax": 5, "T": 17000.0, "delta": 7000.0, "lam": 1.3, "rounds": 3500, "seed": 1}
+PAR.update({'zm': (2, 1), 'T': 19000., 'zs': ((0, 0), (0, 1)), 'xs': ((0, 1), (0, 1))})
+COST = {"fix": 70.0, "gam": 1.5, "sca": 3.5, "pe": 0.6, "pfix": 30.0, "hop": 180.0, "self": 110.0, "net": 4500.0, "rem": 900.0}
+
+
+def S(name, a, b, s=1, p0=0, p1=128): return ("s", name, p0, p1, a, b, s)
+
+
+def PS(tile, a, b, s=1, p0=0, p1=128): return ("p", tile, p0, p1, a, b, s)
+
+
+def IND(win, a, b, offs): return ("i", win, 0, 128, a, b, offs)
+
+
+def Z3(a, b, c0, c1): return ("3", "zb", 0, PW, a, b, (c0, c1))
+
+
+def HBM(name, a=None, b=None): return ("d", name, 0, 128, a, b, 1)
+
+
+def width(x):
+    if x[0] == "i": return 16 * width(x[6])
+    if x[0] == "3": return (x[5] - x[4]) * (x[6][1] - x[6][0])
+    return len(range(x[4], x[5], x[6]))
+
+
+def ap(T, Q, x):
+    if not isinstance(x, tuple): return x
+    k, name, p0, p1, a, b, s = x
+    if k == "i": return T[name][:, a:b].indirect(ap(T, Q, s))
+    if k == "3": return T[name][p0:p1, a:b, s[0]:s[1]]
+    if k == "d": return T[name][:, a:b]
+    t = Q(name) if k == "p" else T[name]
+    return t[p0:p1, a:b:s] if s > 1 else t[p0:p1, a:b]
+
+
+MASKS = {}
+
+
+def places(x):
+    if not isinstance(x, tuple) or x[0] == "d": return []
+    k, name, p0, p1, a, b, s = x
+    if k == "p": return [("ps " + name, 1)]
+    if k == "i": return [(name, ((1 << (b - a)) - 1) << a)] + places(s)
+    if k == "3": return [(name, ((1 << (b - a)) - 1) << a)]
+    if (a, b, s) not in MASKS: MASKS[(a, b, s)] = sum(1 << j for j in range(a, b, s))
+    return [(name, MASKS[(a, b, s)])]
 
 
 def build_ops(par):
-    ops, lastw, readers = [], {}, {}
-    fix, gam = par["fix"], par["gam"]
-    cur = [0]
+    ops, live = [], {}
+    cur = [0, 0]
 
-    def op(eng, cost, fn, r=(), w=(), ps=(), sem=None, lat=0.0, after=None):
-        deps = set()
-        for n in r:
-            if n in lastw: deps.add(lastw[n])
-        for n in w:
-            if n in lastw: deps.add(lastw[n])
-            deps.update(readers.get(n, []))
-        k = len(ops)
-        for n in r: readers.setdefault(n, []).append(k)
-        for n in w:
-            lastw[n] = k; readers[n] = []
+    def op(eng, size, fn, r, w, nm, sem=None, lat=0.0, after=None, more=()):
+        k = len(ops); deps = set(more)
+        rd = [y for x in r for y in places(x)]
+        wr = [places(x)[0] for x in w if places(x)]
+        rd += [y for x in w for y in places(x)[1:]]
+        for name, m in rd:
+            deps.update(j for j, m2, isw in live.get(name, []) if isw and m & m2)
+        for name, m in wr:
+            deps.update(j for j, m2, isw in live.get(name, []) if m & m2)
+        for name, m in wr:
+            live[name] = [(j, m2 & ~m, isw) for j, m2, isw in live.get(name, []) if m2 & ~m] + [(k, m, True)]
+        for name, m in rd:
+            live.setdefault(name, []).append((k, m, False))
         deps.discard(k)
-        ops.append({"eng": eng, "cost": cost, "fn": fn, "deps": deps, "ps": tuple(ps), "sem": sem, "lat": lat, "after": after, "h": cur[0], "nm": (list(w) + [sem])[0]})
+        ps = tuple(sorted({x[1] for x in list(r) + list(w) if isinstance(x, tuple) and x[0] == "p"}))
+        ops.append({"eng": eng, "size": size, "fn": fn, "deps": deps, "ps": ps, "sem": sem, "lat": lat, "after": after, "h": cur[0], "t": cur[1], "nm": nm})
         return k
 
-    def vc(n, c=1.0): return max(64.0, fix + n * c)
+    def two(*xs): return all(x[0] in "s3" and SCRATCH[x[1]][2] in (B, H16, U16) for x in xs)
 
-    def ts(out, in0, s1, s2, o0, o1, r, w, n, c=1.0, ps=()):
+    def rate(out, in0, other):
+        if in0[0] == "i": return ("gam", width(in0))
+        if out[0] == "i": return ("sca", width(in0))
+        return (other, width(in0))
+
+    def ts(out, in0, s1, s2, o0, o1=None, nm=None):
         def fn(g, T, Q):
-            a = [x(T, Q) if not isinstance(x, (int, float)) and x is not None else x for x in (s1, s2)]
-            if o1 is None: return g.vector.tensor_scalar(out(T, Q), in0(T, Q), a[0], None, o0)
-            return g.vector.tensor_scalar(out(T, Q), in0(T, Q), a[0], a[1], o0, o1)
-        return op("V", vc(n, c), fn, r, w, ps)
+            if o1 is None: return g.vector.tensor_scalar(ap(T, Q, out), ap(T, Q, in0), ap(T, Q, s1), None, o0)
+            return g.vector.tensor_scalar(ap(T, Q, out), ap(T, Q, in0), ap(T, Q, s1), ap(T, Q, s2), o0, o1)
+        return op("V", rate(out, in0, .5 if two(out, in0) else 1.0), fn, [in0, s1, s2], [out], nm or out[1])
 
-    def tt(out, in0, in1, o, r, w, n, c=2.0, ps=()):
-        return op("V", vc(n, c), lambda g, T, Q: g.vector.tensor_tensor(out(T, Q), in0(T, Q), in1(T, Q), o), r, w, ps)
+    def tt(out, in0, in1, o, nm=None):
+        c = 1.0 if "p" in (in0[0], in1[0]) else 2.0
+        return op("V", rate(out, in0, c), lambda g, T, Q: g.vector.tensor_tensor(ap(T, Q, out), ap(T, Q, in0), ap(T, Q, in1), o), [in0, in1], [out], nm or out[1])
 
-    def cp(out, in_, r, w, n, c=1.0, ps=()):
-        return op("V", vc(n, c), lambda g, T, Q: g.vector.tensor_copy(out(T, Q), in_(T, Q)), r, w, ps)
+    def cp(out, in_, nm=None, more=()):
+        return op("V", rate(out, in_, .5 if two(out, in_) else 1.0), lambda g, T, Q: g.vector.tensor_copy(ap(T, Q, out), ap(T, Q, in_)), [in_], [out], nm or out[1], more=more)
 
-    def scan(out, d0, d1, o0, o1, r, w, n, ps=()):
-        return op("V", vc(n), lambda g, T, Q: g.vector.tensor_tensor_scan(out(T, Q), d0(T, Q), d1(T, Q), 0.0, o0, o1), r, w, ps)
+    def scan(out, d0, d1, o0, o1):
+        return op("V", (1.0, width(d0)), lambda g, T, Q: g.vector.tensor_tensor_scan(ap(T, Q, out), ap(T, Q, d0), ap(T, Q, d1), 0.0, o0, o1), [d0, d1], [out], out[1])
 
-    def ms(ap, val, w, n):
-        return op("V", vc(n), lambda g, T, Q: g.vector.memset(ap(T, Q), val), (), w)
+    def ms(out, val):
+        return op("V", (.5 if two(out) else 1.0, width(out)), lambda g, T, Q: g.vector.memset(ap(T, Q, out), val), [], [out], out[1])
 
-    def act(out, in_, func, bias, r, w, n, c=1.0, ps=(), scale=1.0, acc=None):
+    def act(out, in_, func, bias=0.0, scale=1.0, acc=None, nm=None):
         def fn(g, T, Q):
-            return g.scalar.activation(out(T, Q), in_(T, Q), func, bias=bias if isinstance(bias, float) else bias(T, Q), scale=scale,
-                                       accum_out=acc(T, Q) if acc else None)
-        return op("S", fix + 20 + n * c, fn, r, w, ps)
+            return g.scalar.activation(ap(T, Q, out), ap(T, Q, in_), func, bias=ap(T, Q, bias), scale=scale, accum_out=ap(T, Q, acc) if acc else None)
+        return op("S", rate(out, in_, 1.0), fn, [in_, bias], [out] + ([acc] if acc else []), nm or out[1])
 
-    def step(name, out, in_, bound, big, up, r, w, n, tl):
-        if name + str(cur[0]) in par["sg"]: return act(out, in_, ACT.Sigmoid, big, r, w, n, 1, [tl], 256.0 if up else -256.0)
-        return ts(out, in_, bound, None, ALU.is_ge if up else ALU.is_le, None, r, w, n, 1, [tl])
-
-    def mm(tile, items, r, first=True, last=True, each=False):
+    def mm(items, first=True, last=True, nm=None):
         def fn(g, T, Q):
             ins = None
             for j, it in enumerate(items):
-                ins = g.tensor.matmul(it[0](T, Q), it[1](T, Q), it[2](T, Q), each or (first and j == 0), each or (last and j == len(items) - 1))
+                ins = g.tensor.matmul(ap(T, Q, it[0]), ap(T, Q, it[1]), ap(T, Q, it[2]), first and j == 0, last and j == len(items) - 1)
             return ins
-        return op("P", 30 + sum(max(64, it[3]) for it in items) * par["pe"], fn, r, [tile], [tile])
+        cols = sum(max(min(64, width(l)), width(r)) * (4 if SCRATCH[r[1]][2] == F else 1) for o, l, r in items)
+        return op("P", ("pe", cols), fn, [x for it in items for x in it[1:]], [items[0][0]], nm or "".join(x for x in items[0][0][1] if x.isalpha()))
 
-    def S(name, a=None, b=None, s=None, p=128):
-        return lambda T, Q: T[name][0:p, a:b:s] if s else T[name][0:p, a:b]
+    def col(j): return S("cf", j, j + 1)
 
-    def PS(tile, a, b, s=None, p=128):
-        return lambda T, Q: Q(tile)[0:p, a:b:s] if s else Q(tile)[0:p, a:b]
+    def dma(q, out, in_, sem, lat):
+        def fn(g, T, Q): return (g.sync if q == "Y" else g.scalar).dma_start(ap(T, Q, out), ap(T, Q, in_))
+        return op(q, (0.0, 0), fn, [in_], [out], sem, sem, lat)
 
-    def col(j, p=128): return S("cf", j, j + 1, None, p)
-
-    def dma(q, out, in_, sem, r, w, lat, slow=False):
+    def iota(name, n, pat, cm):
         def fn(g, T, Q):
-            e = g.sync if q == "Y" else g.scalar
-            return e.dma_start(out(T, Q), in_(T, Q))
-        return op(q, 60.0, fn, r, w, (), sem, lat)
+            if SCRATCH[name][2] == I32: return g.iota(T[name][:, 0:n], pat, 0, cm)
+            return g.iota(T[name][:, 0:n], pat, 0, cm, allow_small_or_imprecise_dtypes=True)
+        op("G", ("g", 160 + 2 * n), fn, [], [S(name, 0, n)], name)
 
-    dma("Y", S("rin", 0, P), lambda T, Q: T.jur[:, :], "ljur", [], ["rin0_%d" % h for h in range(NH)], 2500)
-    dma("Y", S("xw", 0, W), lambda T, Q: T.xc[:, :], "lx", [], ["xw"], 5000)
-    dma("S", S("yin", 0, P), lambda T, Q: T.own[:, :], "lown", [], ["yin0_%d" % h for h in range(NH)], 2500)
-    dma("S", S("wi", 0, 1), lambda T, Q: T.wgt[:, :], "lwgt", [], ["wi"], 2500)
-    dma("Y", S("lw", 0, W), lambda T, Q: T.lsr[:, :], "ll", [], ["lw"], 11000)
+    def full(name): return S(name, 0, 128)
 
-    def iota(name, n, pat, cm, flag=True):
-        def fn(g, T, Q):
-            if flag: return g.iota(T[name][:, 0:n], pat, 0, cm, allow_small_or_imprecise_dtypes=True)
-            return g.iota(T[name][:, 0:n], pat, 0, cm)
-        op("G", 160 + 2 * n, fn, (), [name])
-    iota("ci", 1, [[0, 1]], 1, False)
+    dma("Y", S("li", 0, P), HBM("jur"), "ljur", 2500)
+    dma("Y", S("xw", 0, W), HBM("xc"), "lx", 5000)
+    dma("S", S("yin", 0, P), HBM("own"), "lown", 2500)
+    dma("S", S("wi", 0, 1), HBM("wgt"), "lwgt", 2500)
+    for h in range(NH):
+        cp(S("rin", h * PW, h * PW + PW), S("li", h * PW, h * PW + PW), "ru")
+    for j in list(range(1, LCH)) + [0]:
+        a, b = j * W // LCH, (j + 1) * W // LCH
+        dma("Y", S("li", a, b), HBM("lsr", a, b), "ll%d" % j, 5000 + 6000 * ((j - 1) % LCH + 1) / LCH)
+        cp(S("lw", a, b), S("li", a, b), "lw0")
+
+    iota("ci", 1, [[0, 1]], 1)
     iota("ioc", 144, [[1, 144]], 0)
     iota("iob", 128, [[16, 8], [0, 16]], 0)
     iota("iom", 128, [[0, 8], [1, 16]], 0)
-    iota("c32", 8, [[512, 8]], 0)
-    cp(col(0), S("ci", 0, 1), ["ci"], ["cf0"], 1)
-    ts(S("ci", 4, 5), S("ci", 0, 1), 15, None, ALU.bitwise_and, None, ["ci"], ["ci4"], 1)
-    cp(col(1), S("ci", 4, 5), ["ci4"], ["cf1"], 1)
-    tt(col(2), col(0), col(1), ALU.subtract, ["cf0", "cf1"], ["cf2"], 1)
-    ts(col(3), col(2), 15.0, None, ALU.add, None, ["cf2"], ["cf3"], 1)
-    ts(col(4), col(1), 32.0, None, ALU.mult, None, ["cf1"], ["cf4"], 1)
-    ts(col(5), col(1), 37.0, 8192.0, ALU.mult, ALU.add, ["cf1"], ["cf5"], 1)
-    ts(col(6), col(1), 1.0, None, ALU.add, None, ["cf1"], ["cf6"], 1)
-    ts(col(7), col(1), 0.0, None, ALU.is_equal, None, ["cf1"], ["cf7"], 1)
-    ts(col(8), col(7), 17.0, -1.0, ALU.mult, ALU.add, ["cf7"], ["cf8"], 1)
-    tt(col(9), col(7), col(1), ALU.subtract, ["cf7", "cf1"], ["cf9"], 1)
-    ts(S("ci", 5, 6), S("ci", 0, 1), 1, None, ALU.bitwise_and, None, ["ci"], ["ci5"], 1)
-    for h in range(NH):
-        v0, v1 = (0.0 if par["ds"][h * NC + c] else -240.0 for c in range(NC))
-        ts(col(14 + h), S("ci", 5, 6), v1 - v0, v0, ALU.mult, ALU.add, ["ci5"], ["cf%d" % (14 + h)], 1)
-        tt(col(16 + h), col(14 + h), col(4), ALU.add, ["cf%d" % (14 + h), "cf4"], ["cf%d" % (16 + h)], 1)
-    for nme, sc in (("idn", 1.0), ("n2", -16.0), ("i64", 64.0), ("nid", -1.0), ("n16", 2.0 ** 20), ("n32", 2.0 ** 21), ("tri0", -7.0)):
-        ts(S(nme, 0, 128), S("ioc", 0, 128), col(0), sc, ALU.is_equal, ALU.mult, ["ioc", "cf0"], [nme], 128)
-    ts(S("hh", 0, 144), S("ioc", 0, 144), col(3), None, ALU.is_equal, None, ["ioc", "cf3"], ["hh"], 144)
-    ts(S("bo", 0, 128), S("iob", 0, 128), col(2), None, ALU.is_equal, None, ["iob", "cf2"], ["bo"], 128)
-    tt(S("m1", 0, 128), S("bo", 0, 128), S("tri0", 0, 128), ALU.add, ["bo", "tri0"], ["m1"], 128)
-    ts(S("tri0", 0, 128), S("iom", 0, 128), col(1), -1.0, ALU.is_gt, ALU.mult, ["iom", "cf1"], ["tri0"], 128)
-    tt(S("tri1", 0, 128), S("tri0", 0, 128), S("idn", 0, 128), ALU.add, ["tri0", "idn"], ["tri1"], 128)
-    ts(S("tri1", 0, 128, 16), S("c32", 0, 8), 0.0, col(8), ALU.mult, ALU.add, ["c32", "cf8"], ["tri1"], 8)
-    tt(S("tri", 0, 128), S("tri1", 0, 128), S("bo", 0, 128), ALU.mult, ["tri1", "bo"], ["tri"], 128)
+    iota("ioj", 64, [[0, 8], [64, 8]], 0)
+    iota("iog", 64, [[2, 64]], 0)
+    cp(col(0), S("ci", 0, 1))
+    ts(S("ci", 4, 5), S("ci", 0, 1), 15, None, ALU.bitwise_and)
+    cp(col(1), S("ci", 4, 5))
+    tt(col(2), col(0), col(1), ALU.subtract)
+    ts(col(3), col(2), 15.0, None, ALU.add)
+    ts(col(4), col(0), float(PW), 32.0, ALU.is_ge, ALU.mult)
+    ts(col(5), col(1), 37.0 * 32, -2.0 ** 23, ALU.mult, ALU.add)
+    ts(col(6), col(1), 1.0, None, ALU.add)
+    ts(col(7), col(1), 0.0, None, ALU.is_equal)
+    ts(col(8), col(7), 17.0, -1.0, ALU.mult, ALU.add)
+    tt(col(9), col(7), col(1), ALU.subtract)
+    ts(col(14), col(9), -256.0, -128.0, ALU.mult, ALU.add)
+    for nme, sc in (("idn", 1.0), ("nid", -1.0), ("i16", 16.0), ("n16", -16.0), ("i64", 64.0), ("q25", .25)):
+        ts(full(nme), full("ioc"), col(0), sc, ALU.is_equal, ALU.mult)
+    ts(S("hh", 0, 144), S("ioc", 0, 144), col(3), None, ALU.is_equal)
+    ts(S("hz", 0, 144), S("hh", 0, 144), -1.0 / 32, None, ALU.mult)
+    ts(full("bo"), full("iob"), col(2), None, ALU.is_equal)
+    ts(full("nbo"), full("bo"), -1.0, None, ALU.mult)
+    for nme, off, dg in (("mA", 1.0 / 64, -39.0 / 64), ("mB", -1.0 / 64, 89.0 / 128)):
+        ts(S("tmp", 0, 128), full("bo"), off, None, ALU.mult)
+        ts(S("tmp", 128, 256), full("idn"), dg, None, ALU.mult)
+        tt(full(nme), S("tmp", 0, 128), S("tmp", 128, 256), ALU.add)
+    ts(S("tmp", 0, 128), full("iom"), col(1), -1.0, ALU.is_gt, ALU.mult)
+    tt(S("tmp", 128, 256), S("tmp", 0, 128), full("idn"), ALU.add)
+    ts(S("tmp", 128, 256, 16), S("ioc", 0, 8), 0.0, col(8), ALU.mult, ALU.add)
+    tt(full("tri"), S("tmp", 128, 256), full("bo"), ALU.mult)
     for a in (0, 8):
-        cp(S("o16", a, a + 8), S("bo", 0, 128, 16), ["bo"], ["o16_%d" % a], 8)
-    ts(S("o512", 0, 8), S("bo", 0, 128, 16), 512.0, None, ALU.mult, None, ["bo"], ["o512"], 8)
-    cp(col(18), S("ci", 5, 6), ["ci5"], ["cf18"], 1)
-    tt(col(19), col(0), col(18), ALU.subtract, ["cf0", "cf18"], ["cf19"], 1)
-    ts(col(20), col(18), -PEN, PEN, ALU.mult, ALU.add, ["cf18"], ["cf20"], 1)
-    ts(col(21), col(18), PEN, None, ALU.mult, None, ["cf18"], ["cf21"], 1)
+        cp(S("o16", a, a + 8), S("bo", 0, 128, 16))
+    ts(S("o512", 0, 8), S("bo", 0, 128, 16), 512.0, None, ALU.mult)
     for c in range(NC):
-        ts(S("pen2", 128 * c, 128 * c + 128), S("ioc", 0, 128), col(19), col(20 + c), ALU.is_equal, ALU.mult, ["ioc", "cf19", "cf%d" % (20 + c)], ["pen%d" % c], 128)
-    ts(S("lp", 0, 128), S("ioc", 0, 128), float(PW), col(18), ALU.is_ge, ALU.is_equal, ["ioc", "cf18"], ["lp"], 128)
+        ts(col(15 + c), col(0), -float(c), None, ALU.add)
+        ts(S("pen", 64 * c, 64 * c + 64), S("iog", 0, 64), col(15 + c), PEN, ALU.is_equal, ALU.mult)
     for h in range(NH):
-        for j in (0, 1):
-            n = 16 - 2 * j + h
-            ts(S("kc", 256 * h + 128 * j, 256 * h + 128 * j + 128), S("ioc", 0, 128), col(19), col(n), ALU.is_equal, ALU.mult, ["ioc", "cf19", "cf%d" % n], ["kc%d%d" % (j, h)], 128)
-        ts(S("kc", 256 * h + 1, 256 * h + 128, 2), S("ioc", 0, 128, 2), col(19), 8 * PEN, ALU.is_equal, ALU.mult, ["ioc", "cf19"], ["kc0%d" % h], 64)
-    ms(S("dr", 0, 2 * NH * 144), 0.0, ["dr%d_%d" % (a, h) for a in range(2) for h in range(NH)], NH * 144)
-    ts(S("nbo", 0, 128), S("bo", 0, 128), -1.0, None, ALU.mult, None, ["bo"], ["nbo"], 128, .5)
-    ts(S("hn", 0, 144), S("hh", 0, 144), -65536.0, None, ALU.mult, None, ["hh"], ["hn"], 144, .5)
-    ms(S("c73", 0, 128), -73.0 * 32768, ["c73"], 64)
-    ms(S("cm7", 0, 128), -7.0, ["cm7"], 64)
-    ms(S("zz", 0, 2 * NH * 128), 0.0, ["zz%d_%d" % (a, h) for a in range(2) for h in range(NH)], 2 * NH * 128)
+        v0, v1 = (0.0 if par["ds"][h][c] else -240.0 for c in range(NC))
+        ts(col(18 + h), col(4), (v1 - v0) / 32, v0, ALU.mult, ALU.add)
+        tt(col(20 + h), col(18 + h), col(4), ALU.add)
+        ts(S("kc", 128 * h, 128 * h + 64), S("ioj", 0, 64), col(20 + h), None, ALU.add)
+        ts(S("kc", 128 * h + 64, 128 * h + 128), S("ioj", 0, 64), 0.0, col(18 + h), ALU.mult, ALU.add)
+    ms(S("dr", 0, 2 * NH * 144), 0.0)
+    ms(S("zz", 0, 2 * NH * 128), 0)
+    ts(full("keep"), full("iom"), 0.0, None, ALU.not_equal)
+    for nme, v in (("c1", M1), ("c32", M32), ("c4096", M4096), ("c155", 15.5), ("c2048", 2048.0)):
+        ms(full(nme), v)
+    for j, v in enumerate((0.0, 39.0 / 64, 39.0 / 128)):
+        ms(S("f0", j, 192, 3), v)
+    ts(col(17), col(1), 1.0, -0.5, ALU.is_equal, ALU.mult)
+    ts(col(22), col(7), 2048.0, col(17), ALU.mult, ALU.add)
+    ts(full("cc"), full("iom"), 0.0, col(22), ALU.mult, ALU.add)
     lo, st = 1792.0, -512.0
-    ts(S("sel", 0, 128), S("iom", 0, 128), 0.0, col(7), ALU.mult, ALU.add, ["iom", "cf7"], ["sel"], 128)
-    ms(S("thr", 0, 1), lo, ["thr0"], 1)
-    ts(S("rst", 0, 128), S("iom", 0, 128), 0.0, BIGV, ALU.is_equal, ALU.mult, ["iom"], ["rst"], 128)
-    ts(S("keep", 0, 128), S("iom", 0, 128), 0.0, None, ALU.not_equal, None, ["iom"], ["keep"], 128)
-    ts(S("c32i", 0, 8), S("c32", 0, 8), col(4), None, ALU.add, None, ["c32", "cf4"], ["c32i"], 8)
-    ts(S("rm", 0, 16), S("ioc", 0, 16), col(1), None, ALU.is_equal, None, ["ioc", "cf1"], ["rm"], 16)
+    ts(full("sel"), full("iom"), 0.0, col(7), ALU.mult, ALU.add)
+    ms(S("thr", 0, 1), lo)
+    ts(S("rs8", 0, 64), S("ioj", 0, 64), 0.0, BIG, ALU.is_equal, ALU.mult)
+    ts(full("rs16"), full("iom"), 0.0, -BIG, ALU.is_equal, ALU.mult)
+    ts(S("tmp", 0, 128), full("iom"), col(1), None, ALU.is_equal)
+    ts(S("tmp", 128, 256), full("ioc"), 32.0, 32768.0, ALU.mult, ALU.add)
+    tt(S("tmp", 128, 256), S("tmp", 128, 256), S("tmp", 0, 128), ALU.mult)
+    ts(full("wb"), S("tmp", 128, 256), -32768.0, None, ALU.add)
+    ts(S("rm", 0, 16), S("ioc", 0, 16), col(1), None, ALU.is_equal)
     for a in range(16):
-        ts(S("ba", 144 * a, 144 * a + 144), S("hh", 0, 144), S("rm", a, a + 1), None, ALU.mult, None, ["hh", "rm"], ["ba%d" % a], 144, .5)
-    ts(S("hj", 0, 144), S("hh", 0, 144), col(6), None, ALU.mult, None, ["hh", "cf6"], ["hj"], 144, .5)
-    for j, msk, nme, src, n in ((10, 31, "hw5", "hh", 144), (11, 63, "wlo", "bo", 128), (12, 4032, "whi", "bo", 128)):
-        ts(S("wi", j - 6, j - 5), S("wi", 0, 1), msk, None, ALU.bitwise_and, None, ["wi"], ["wi%d" % j], 1)
-        cp(col(j), S("wi", j - 6, j - 5), ["wi%d" % j], ["cf%d" % j], 1)
-        ts(S(nme, 0, n), S(src, 0, n), col(j), None, ALU.mult, None, [src, "cf%d" % j], [nme], n, .5)
+        ts(S("ba", 144 * a, 144 * a + 144), S("hh", 0, 144), S("rm", a, a + 1), None, ALU.mult)
+    ts(S("hj", 0, 144), S("hh", 0, 144), col(6), None, ALU.mult)
+    ts(S("wi", 4, 5), S("wi", 0, 1), 31, None, ALU.bitwise_and)
+    cp(col(10), S("wi", 4, 5))
+    ts(col(11), S("wi", 0, 1), 2048.0, -4096.0, ALU.is_ge, ALU.mult)
+    tt(col(12), col(11), S("wi", 0, 1), ALU.add)
+    for nme, j, sg in (("w5p", 10, 1.0), ("w5n", 10, -1.0), ("wp", 12, 1.0), ("wn", 12, -1.0)):
+        ts(full(nme), full("bo"), col(j), sg, ALU.mult, ALU.mult)
 
-    IDN, NID = S("idn", 0, 128), S("nid", 0, 128)
+    IDN, NID = full("idn"), full("nid")
 
     def hk(name, k): return S(name, 15 - k, 143 - k)
 
+    def cst(name, n=PW): return S(name, 0, n)
+
     sends = {}
     for t in range(V):
-        a = t & 1
+        a = t & 1; cur[1] = t
         for h in range(NH):
             cur[0] = h
-            u = "%d_%d" % (a, h); v = "%d_%d" % (t, h)
-            o = a * P + h * PW; ob = a * 2048 + h * 16 * PW; oi = t * P + h * PW; o3 = a * NH + h
+            v = "%d_%d" % (t, h)
+            o = a * P + h * PW; ob = a * 2048 + h * 16 * PW; oi = t * P + h * PW; o3 = a * NH + h; n16 = 16 * PW
 
-            def sm(name, o=o): return S(name, o, o + PW)
+            def sm(name): return S(name, o, o + PW)
 
-            def t8(name, o3=o3): return S(name, 8 * o3, 8 * o3 + 8, None, PW)
+            def cls(name, c): return S(name, ob + 512 * c, ob + 512 * c + 512)
 
-            def t128(name, o3=o3): return S(name, 128 * o3, 128 * o3 + 128, None, PW)
+            def ks(name, k): return S(name, ob + 512 * (k % NC) + k // NC, ob + 512 * (k % NC) + 512, KK)
 
-            def cls(name, c, ob=ob): return S(name, ob + 512 * c, ob + 512 * c + 512)
+            def jc(name, c, i0=0, i1=PW): return S(name, ob + 16 * i0 + c, ob + 16 * i1, NC)
 
-            def ks(name, k, ob=ob): return S(name, ob + 512 * (k % NC) + k // NC, ob + 512 * (k % NC) + 512, KK)
+            def s3(j, name="s3"): return S(name, 3 * o + j, 3 * o + 3 * PW, 3)
 
-            def jc(name, c, ob=ob): return S(name, ob + c, ob + 16 * PW, NC)
-
-            RIN, YIN, YN, RN = S("rin", oi, oi + PW), S("yin", oi, oi + PW), S("yout", oi, oi + PW), S("rout", oi, oi + PW)
-            rin, yin, yn, rn = "rin" + v, "yin" + v, "yout" + v, "rout" + v
+            RU, YIN, YN = S("rin", oi, oi + PW), S("yin", oi, oi + PW), S("yout", oi, oi + PW)
             if t:
-                op("N", 0, None, (), [rin], (), "ar" + v, par["net"], sends["r%d_%d" % (t - 1, h)])
-                op("N", 0, None, (), [yin], (), "ay" + v, par["net"], sends["y%d_%d" % (t - 1, h)])
-            n16 = 16 * PW
-            cp(sm("ru"), RIN, [rin], ["ru" + u], PW)
+                op("N", (0.0, 0), None, [], [RU], "ar", "ar" + v, -1.0, sends["r%d_%d" % (t - 1, h)])
+                op("N", (0.0, 0), None, [], [YIN], "ay", "ay" + v, -1.0, sends["y%d_%d" % (t - 1, h)])
 
-            def gather(name, win, offs, o=o, ob=ob, u=u):
-                gs = par["gs"][name]; pw = PW // gs
-                for j in range(gs):
+            def gather(name, win, offs, at):
+                who = par[name][h]; pw = PW // len(who); add = -2048.0 if name == "lg" else 0.0
+                for j, e in enumerate(who):
                     out = S(name, ob + 16 * pw * j, ob + 16 * pw * (j + 1))
+                    src = IND(win, 0, W, S(offs, at + pw * j, at + pw * (j + 1)))
+                    if e == "S": act(out, src, ACT.Identity, add)
+                    elif add: ts(out, src, add, None, ALU.add)
+                    else: cp(out, src)
+                return [(pw * j, pw * (j + 1)) for j in range(len(who))]
 
-                    def src(T, Q, j=j): return T[win][:, 0:W].indirect(T[offs][:, o + pw * j:o + pw * (j + 1)])
-                    if name == "lg": ts(out, src, -2048.0, None, ALU.add, None, [win, offs + u], ["%s%d_%s" % (name, j, u)], 16 * pw, gam)
-                    elif j == gs - 1 and par[name + "v"][h]: cp(out, src, [win, offs + u], ["%s%d_%s" % (name, j, u)], 16 * pw, gam)
-                    else: act(out, src, ACT.Identity, 0.0, [win, offs + u], ["%s%d_%s" % (name, j, u)], 16 * pw, gam)
-                return ["%s%d_%s" % (name, j, u) for j in range(gs)]
-            XG = gather("xg", "xw", "ru")
-            LG = gather("lg", "lw", "ru")
-            LGS = LG + (LGS if h else [])
+            def fill(tl, lhs, Y, first, last):
+                mm([(PS(tl, j, 512, KK), lhs, Y) for j in range(KK)], first, last, nm="fill" + tl[:2])
+
+            def near(out, d): ts(out, d, M4, M4, ALU.add, ALU.is_equal)
+
+            def test(out, ab, d, way):
+                if way == 0: return near(out, d)
+                act(ab, d, ACT.Abs)
+                if way == 1: ts(out, ab, 1.0, None, ALU.is_le)
+                else: act(out, ab, ACT.Sigmoid, 384.0, -256.0)
+
+            xp = gather("xg", "xw", "rin", oi)
+            cp(s3(2), RU, "rf")
+            ts(sm("kp"), RU, 32.0, col(5), ALU.mult, ALU.add)
+            if par["xm"][h] == 2: fill("Dx" + v, IDN, YIN, True, True)
+            for c in range(NC):
+                if par["xm"][h] == 1:
+                    tl = "Dx%s_%d" % (v, c); d = PS(tl, 0, 512)
+                    fill(tl, NID, YIN, True, False)
+                    for j, (i0, i1) in enumerate(xp):
+                        mm([(PS(tl, KK * i0, KK * i1), IDN, jc("xg", c, i0, i1))], False, j == len(xp) - 1)
+                else:
+                    d = cls("dx", c)
+                    tt(d, jc("xg", c), PS("Dx" + v, 0, 512), ALU.subtract)
+                test(cls("nx", c), cls("ad", c), d, par["xs"][h][c])
+                if par["xs"][h][c] == 0: act(cls("ad", c), d, ACT.Abs)
+            gather("lg", "lw", "rin", oi)
             tl = "n" + v
-            mm(tl, [(PS(tl, 0, PW), S("ba", 144 * ((k + t) % 16) + 15 - k, 144 * ((k + t) % 16) + 143 - k), S("lg", ob + k, ob + n16, 16), PW) for k in range(16)],
-               LG + ["ba%d" % j for j in range(16)])
-            ts(sm("nu"), PS(tl, 0, PW), 2048.0, None, ALU.add, None, [tl], ["nu" + u], PW, 1, [tl])
-            act(sm("nm"), PS(tl, 0, PW), ACT.Identity, 6144.0, [tl], ["nm" + u], PW, 1, [tl])
-            ts(sm("nmk"), RIN, col(5), None, ALU.add, None, [rin, "cf5"], ["nmk" + u], PW)
-            ZG = gather("zg", "xw", "nu")
+            mm([(PS(tl, 0, PW), IDN, cst("c2048"))]
+               + [(PS(tl, 0, PW), S("ba", 144 * ((k + t) % 16) + 15 - k, 144 * ((k + t) % 16) + 143 - k), S("lg", ob + k, ob + n16, 16)) for k in range(16)])
+            cp(sm("nu"), PS(tl, 0, PW))
+            tt(s3(1), PS(tl, 0, PW), s3(2), ALU.subtract, "nr")
+            act(sm("nm"), PS(tl, 0, PW), ACT.Identity)
+            zp = gather("zg", "xw", "nu", o)
 
-            def sub(tl, src, c, Y, r, ry, last):
-                mm(tl, [(PS(tl, 0, 512), IDN, jc(src, c), 512)], ["idn"] + r, True, False)
-                mm(tl, [(PS(tl, j, 512, KK), NID, Y, PW) for j in range(KK)], ["nid", ry], False, last)
-            for c in range(NC):
-                tl = "Dx%s_%d" % (v, c)
-                sub(tl, "xg", c, YIN, XG + [yin], yin, True)
-                act(cls("ad", c), PS(tl, 0, 512), ACT.Abs, 0.0, [tl], ["ad%s_%d" % (u, c)], 512, 1, [tl])
-                if par["xs"][h * NC + c] == 2:
-                    act(cls("nx", c), cls("ad", c), ACT.Sigmoid, 384.0, ["ad%s_%d" % (u, c)], ["nx%s_%d" % (u, c)], 512, 1, (), -256.0)
-                elif par["xs"][h * NC + c]:
-                    ts(cls("nx", c), cls("ad", c), 1.0, None, ALU.is_le, None, ["ad%s_%d" % (u, c)], ["nx%s_%d" % (u, c)], 512, .5)
-                else:
-                    ts(cls("nx", c), PS(tl, 0, 512), M4, M4, ALU.add, ALU.is_equal, [tl], ["nx%s_%d" % (u, c)], 512, 1, [tl])
-            korder = [k for c in range(NC) for k in range(c, 16, NC)]
-
-            def byclass(tl, item, r, name, head=(), tail=(), rt=(), first=True, last=True):
+            def byclass(out, lhs, name, first=True, last=True):
                 for c in range(NC):
-                    its = (list(head) if c == 0 else []) + [item(k) for k in range(c, 16, NC)] + (list(tail) if c == NC - 1 else [])
-                    mm(tl, its, r + ["%s%s_%d" % (name, u, c)] + (list(rt) if c == NC - 1 else []), first and c == 0, last and c == NC - 1)
+                    mm([(out, lhs(k), ks(name, k)) for k in range(c, 16, NC)], first and c == 0, last and c == NC - 1)
             tl = "nb" + v
-            byclass(tl, lambda k: (PS(tl, 0, PW), IDN, ks("nx", k), PW), ["idn"], "nx")
-            step("good", sm("good"), PS(tl, 0, PW), 8.0, -1920.0, True, [tl], ["good" + u], PW, tl)
+            byclass(PS(tl, 0, PW), lambda k: IDN, "nx")
+            if "good" in par["sg"]: act(sm("good"), PS(tl, 0, PW), ACT.Sigmoid, -1920.0, 256.0)
+            else: ts(sm("good"), PS(tl, 0, PW), 8.0, None, ALU.is_ge)
             tl = "pre" + v
-            mm(tl, [(PS(tl, 0, PW), S("tri", 0, 128), sm("good"), PW)], ["tri", "good" + u])
-            ts(sm("oh"), PS(tl, 0, PW), col(9), 16.0, ALU.is_gt, ALU.mult, [tl, "cf9"], ["oh" + u], PW, 1, [tl])
+            mm([(PS(tl, 0, PW), full("tri"), sm("good"))])
+            if "oh" in par["sg"]: act(sm("oh"), PS(tl, 0, PW), ACT.Sigmoid, col(14), 256.0)
+            else: ts(sm("oh"), PS(tl, 0, PW), col(9), None, ALU.is_gt)
             tl = "cnt" + v
-            mm(tl, [(PS(tl, 0, PW), hk("hh", k), ks("nx", k), PW) for k in korder], ["hh"] + ["nx%s_%d" % (u, c) for c in range(NC)])
-            act(sm("sa"), PS(tl, 0, PW), ACT.Sign, -11.5, [tl], ["sa" + u], PW, 1, [tl])
-            act(sm("cnt"), PS(tl, 0, PW), ACT.Identity, 0.0, [tl], ["cnt" + u], PW, 1, [tl])
+            byclass(PS(tl, 0, PW), lambda k: hk("hh", k), "nx")
+            act(sm("sa"), PS(tl, 0, PW), ACT.Sign, -11.5)
+            act(sm("cnt"), PS(tl, 0, PW), ACT.Identity)
             tl = "cT" + v
-            mm(tl, [(PS(tl, 0, PW), S("bo", 0, 128), sm("sa"), PW)], ["sa" + u, "bo"])
-            act(sm("nl"), PS(tl, 0, PW), ACT.Sigmoid, S("thr", 8 * t, 8 * t + 1), [tl, "thr%d" % t], ["nl" + u], PW, 1, [tl], 256.0, S("acc", o3, o3 + 1))
+            mm([(PS(tl, 0, PW), full("bo"), sm("sa"))])
+            act(sm("nl"), PS(tl, 0, PW), ACT.Sigmoid, S("thr", 8 * t, 8 * t + 1), 256.0, S("acc", o3, o3 + 1))
             tl = "ya" + v
-            mm(tl, [(PS(tl, 0, PW), IDN, sm("oh"), PW), (PS(tl, 0, PW), S("i64", 0, 128), sm("nl"), PW)], ["idn", "i64", "oh" + u, "nl" + u])
-            tt(sm("yy"), YIN, PS(tl, 0, PW), ALU.min, [yin, tl], ["yy" + u], PW, 1, [tl])
+            mm([(PS(tl, 0, PW), full("i16"), sm("oh")), (PS(tl, 0, PW), full("i64"), sm("nl"))])
+            tt(sm("yy"), YIN, PS(tl, 0, PW), ALU.min)
+            if 0 in par["ds"][h]: fill("Dm" + v, full("i16"), sm("oh"), True, True)
             for c in range(NC):
-                tl = "Dm%s_%d" % (v, c)
-                if par["ds"][h * NC + c]:
-                    sub(tl, "xg", c, sm("oh"), XG + ["good" + u], "oh" + u, True)
-                    act(cls("dm", c), PS(tl, 0, 512), ACT.Relu, 0.0, [tl], ["dm%s_%d" % (u, c)], 512, 1, [tl])
+                if par["ds"][h][c]:
+                    tl = "Dm%s_%d" % (v, c)
+                    mm([(PS(tl, 0, 512), IDN, jc("xg", c))], True, False)
+                    fill(tl, full("n16"), sm("oh"), False, True)
+                    act(cls("dm", c), PS(tl, 0, 512), ACT.Relu)
                 else:
-                    mm(tl, [(PS(tl, j, 512, KK), IDN, sm("oh"), PW) for j in range(KK)], ["idn", "oh" + u], each=True)
-                    tt(cls("dm", c), jc("xg", c), PS(tl, 0, 512), ALU.max, [tl] + XG, ["dm%s_%d" % (u, c)], 512, 1, [tl])
+                    tt(cls("dm", c), jc("xg", c), PS("Dm" + v, 0, 512), ALU.max)
             tl = "K" + v
-            def both(name, j, ob=ob): return S(name, ob + j, ob + n16, KK)
-            mm(tl, [(PS(tl, 0, 256), S("lp", 0, 128), S("kc", 256 * h, 256 * h + 256), 256)]
-               + [(PS(tl, 2 * j, 128, 16), both("ad", j), S("o512", 0, 8), 8) for j in range(KK)],
-               ["lp", "kc0%d" % h, "kc1%d" % h, "good" + u, "o512"] + ["ad%s_%d" % (u, c) for c in range(NC)], True, False)
-            mm(tl, [(lambda T, Q, c=c, tl=tl: Q(tl)[PW * c:PW * c + PW, 0:128], sm("sa"), S("pen2", 128 * c, 128 * c + 128), 128) for c in range(NC)],
-               ["sa" + u, "pen0", "pen1"], False, False)
-            mm(tl, [(PS(tl, 2 * j, 256, 16), both("dm", j), S("o16", 0, 16), 16) for j in range(KK)], ["o16_0", "o16_8"] + ["dm%s_%d" % (u, c) for c in range(NC)], False, True)
-            scan(S("sc", 128 * o3, 128 * o3 + 128), S("rst", 0, 128), PS(tl, 0, 128), ALU.add, ALU.min, [tl, "rst"], ["sd" + u], 128, [tl])
-            od = 144 * o3 + 8
-            act(S("dr", od, od + 128), PS(tl, 128, 256), ACT.Identity, 0.0, [tl], ["dr" + u], 128, 1, [tl])
-            ends = t8("dl")
-            k = tt(ends, S("sc", 128 * o3 + 15, 128 * o3 + 128, 16, PW), lambda T, Q, o3=o3: T.sc[PW:128, 128 * o3 + 15:128 * o3 + 128:16], ALU.min, ["sd" + u], ["sc" + u], 8)
+
+            def both(name, j): return S(name, ob + j, ob + n16, KK)
+            mm([(PS(tl, 0, 128), IDN, S("kc", 128 * h, 128 * h + 128))] + [(PS(tl, j, 64, 8), both("ad", j), S("o512", 0, 8)) for j in range(KK)], True, False, "Ka")
+            mm([(PS(tl, 0, 64, 1, PW * c, PW * c + PW), sm("sa"), S("pen", 64 * c, 64 * c + 64)) for c in range(NC)], False, False, "Kp")
+            mm([(PS(tl, j, 128, 8), both("dm", j), S("o16", 0, 16)) for j in range(KK)], False, True, "Kd")
+            scan(sm("sc"), S("rs8", 0, 64), PS(tl, 0, 64), ALU.add, ALU.min)
+            od = 144 * o3 + 8; oq = 128 * o3
+            act(S("dr", od, od + 128, 2), PS(tl, 64, 128), ACT.Identity)
+            least = S("qq", 8 * o3, 8 * o3 + 8, 1, 0, PW)
+            k = tt(least, S("sc", o + 7, o + PW, 8, 0, PW), S("sc", o + 7, o + PW, 8, PW, 128), ALU.min)
             ops[k]["drain"] = True
-            ops[k]["cost"] += par["self"]
-
-            def xr(tl, a0, od=od):
-                return [(PS(tl, a0, a0 + PW), S("dr", od - c, od - c + 128), S("idn", PW * c, PW * c + PW), PW) for c in range(NC)]
-            ts(t8("rd"), ends, M32, M32, ALU.add, ALU.subtract, ["sc" + u], ["rd" + u], 8)
-            tt(S("zz", 128 * o3, 128 * o3 + 128, 16, PW), ends, t8("rd"), ALU.subtract, ["sc" + u, "rd" + u], ["zz" + u], 8)
-            scan(t128("zb"), S("keep", 0, 128, None, PW), t128("zz"), ALU.mult, ALU.add, ["keep", "zz" + u], ["zb" + u], 128)
-            IW, NW = S("idn", 0, PW, None, PW), S("nid", 0, PW, None, PW)
+            ts(S("zz", oq, oq + 128, 16, 0, PW), least, 31, None, ALU.bitwise_and)
+            ZB = S("zb", oq, oq + 128, 1, 0, PW)
+            scan(ZB, S("keep", 0, 128, 1, 0, PW), S("zz", oq, oq + 128, 1, 0, PW), ALU.mult, ALU.add)
+            IW, NW = S("idn", 0, PW, 1, 0, PW), S("nid", 0, PW, 1, 0, PW)
             tl = "del" + v
-            mm(tl, [(PS(tl, 0, PW), NID, sm("oh"), PW), (PS(tl, 0, PW), S("n2", 0, 128), sm("nl"), PW)], ["nid", "n2", "nl" + u, "oh" + u, "sc" + u], True, False)
-            mm(tl, [(PS(tl, 0, PW), t128("zb"), IW, PW)], ["zb" + u, "idn"], False, True)
-            tt(YN, sm("yy"), PS(tl, 0, PW), ALU.max, [tl, "yy" + u], [yn], PW, 1, [tl])
+            mm([(PS(tl, 0, PW), full("n16"), sm("oh")), (PS(tl, 0, PW), full("n16"), sm("nl"))], True, False)
+            mm([(PS(tl, 0, PW), ZB, IW)], False, True, "delz")
+            tt(YN, sm("yy"), PS(tl, 0, PW), ALU.max)
 
-            def send(kind, src, dst, r, oi=oi, t=t, h=h):
-                def fn(g, T, Q):
-                    return g.remote_dma(T[dst][:, oi + P:oi + P + PW], T[src][:, oi:oi + PW], T.sem["a%s%d_%d" % (kind, t + 1, h)], T.sem.sent, Q("pid"), Q("rid"), Q("mask"))
-                sends["%s%d_%d" % (kind, t, h)] = op("G", 900.0, fn, [r], (), (), "remote")
-            send("y", "yout", "yin", yn)
+            def send(kind, src, dst):
+                def fn(g, T, Q, t=t, h=h):
+                    return g.remote_dma(ap(T, Q, dst), ap(T, Q, src), T.sem["a%s%d_%d" % (kind, t + 1, h)], T.sem.sent, Q("pid"), Q("rid"), Q("mask"))
+                sends["%s%d_%d" % (kind, t, h)] = op("G", ("rem", 1), fn, [src], [], "send" + kind, "remote")
+            send("y", YN, S("yin", oi + P, oi + P + PW))
             tl = "dd" + v
-            far = S("i64", 0, 128)
-            mm(tl, xr(tl, 0) + [(PS(tl, 0, PW), S("nbo", 0, 128), YIN, PW), (PS(tl, 0, PW), S("bo", 0, 128), sm("yy"), PW), (PS(tl, 0, PW), far, sm("nl"), PW)],
-               ["dr" + u, "idn", "nbo", "bo", "i64", yin, "yy" + u, "nl" + u])
-            mm(tl, xr(tl, PW) + [(PS(tl, PW, 2 * PW), far, sm("nl"), PW), (PS(tl, PW, 2 * PW), t128("zb"), NW, PW)],
-               ["dr" + u, "zb" + u, "idn", "nid", "i64", "nl" + u])
-            on = 2 * PW * o3
-            if "nn%d" % h in par["sg"]:
-                act(S("nt", on, on + 2 * PW), PS(tl, 0, 2 * PW), ACT.Abs, 0.0, [tl], ["nt" + u], 2 * PW, 1, [tl])
-                act(S("nn", on, on + 2 * PW), S("nt", on, on + 2 * PW), ACT.Sigmoid, 384.0, ["nt" + u], ["nn" + u], 2 * PW, 1, (), -256.0)
-            else:
-                ts(S("nn", on, on + 2 * PW), PS(tl, 0, 2 * PW), M4, M4, ALU.add, ALU.is_equal, [tl], ["nn" + u], 2 * PW, 1, [tl])
+
+            def xr(a0):
+                return [(PS(tl, a0, a0 + PW), S("dr", od - c, od - c + 128), S("idn", PW * c, PW * c + PW)) for c in range(NC)] + [(PS(tl, a0, a0 + PW), full("i64"), sm("nl"))]
+            mm(xr(0) + [(PS(tl, 0, PW), full("nbo"), YIN), (PS(tl, 0, PW), full("bo"), sm("yy"))] + xr(PW), True, False)
+            mm([(PS(tl, PW, 2 * PW), ZB, NW)], False, True, "ddz")
+            on = 2 * o
+            test(S("nn", on, on + 2 * PW), S("nt", on, on + 2 * PW), PS(tl, 0, 2 * PW), 2 if "nn" in par["sg"] else 0)
             tl = "c2" + v
-            mm(tl, [(PS(tl, 0, PW), IDN, sm("cnt"), PW), (PS(tl, 0, PW), NID, S("nn", on, on + PW), PW), (PS(tl, 0, PW), IDN, S("nn", on + PW, on + 2 * PW), PW)],
-               ["idn", "nid", "cnt" + u, "nn" + u])
-            act(sm("sa2"), PS(tl, 0, PW), ACT.Sign, -11.5, [tl], ["sa2" + u], PW, 1, [tl])
-            tl = "cw" + v
-            if "ch%d" % h in par["sg"]:
-                mm(tl, [(PS(tl, 0, PW), S("m1", 0, 128), sm("sa2"), PW)], ["m1", "sa2" + u])
-                act(sm("ct"), PS(tl, 0, PW), ACT.Abs, -7.0, [tl], ["ct" + u], PW, 1, [tl])
-                act(sm("ch"), sm("ct"), ACT.Sigmoid, 1792.0, ["ct" + u], ["ch" + u], PW, 1, (), -256.0)
-            else:
-                mm(tl, [(PS(tl, 0, PW), IDN, S("cm7", 0, PW), PW), (PS(tl, 0, PW), S("m1", 0, 128), sm("sa2"), PW)], ["idn", "cm7", "m1", "sa2" + u])
-                ts(sm("ch"), PS(tl, 0, PW), M16, M16, ALU.add, ALU.is_equal, [tl], ["ch" + u], PW, 1, [tl])
-            tt(sm("nmc"), sm("ch"), sm("nm"), ALU.mult, ["ch" + u, "nm" + u], ["nmc" + u], PW)
-            tt(sm("base"), sm("nmc"), RIN, ALU.max, ["nmc" + u, rin], ["base" + u], PW)
+            mm([(PS(tl, 0, PW), IDN, sm("cnt")), (PS(tl, 0, PW), NID, S("nn", on, on + PW)), (PS(tl, 0, PW), IDN, S("nn", on + PW, on + 2 * PW))])
+            act(sm("sa2"), PS(tl, 0, PW), ACT.Sign, -11.5)
+
+            def modulo(out, neg, pos, Y, half, big):
+                return [(out,) + half, (out, neg, Y), (out, NID, big), (out, IDN, big), (out, pos, Y)]
             tl = "u" + v
-            mm(tl, [(PS(tl, 0, PW), S("whi", 0, 128), YN, PW), (PS(tl, 0, PW), S("wlo", 0, 128), YN, PW)], ["whi", "wlo", yn])
-            cp(sm("si"), PS(tl, 0, PW), [tl], ["si" + u], PW, 1, [tl])
-            ts(sm("ui"), sm("si"), W - 1, None, ALU.bitwise_and, None, ["si" + u], ["ui" + u], PW)
-            tt(sm("pi"), sm("ui"), RIN, ALU.mult, ["ui" + u, rin], ["pi" + u], PW)
-            ts(sm("qi"), sm("pi"), 5, W - 1, ALU.logical_shift_right, ALU.bitwise_and, ["pi" + u], ["qi" + u], PW)
-            tt(sm("df"), sm("qi"), sm("nmk"), ALU.add, ["qi" + u, "nmk" + u], ["df" + u], PW)
+            its = modulo(PS(tl, 0, PW), full("wn"), full("wp"), YN, (full("bo"), cst("cc")), cst("c4096"))
+            mm(its)
+            tt(sm("pi"), s3(2), PS(tl, 0, PW), ALU.mult)
+            tt(sm("pj"), sm("pi"), sm("kp"), ALU.add)
+            ts(sm("far"), sm("pj"), 5, W - 1, ALU.arith_shift_right, ALU.bitwise_and)
+            tt(s3(0), sm("far"), sm("nm"), ALU.subtract, "fn")
+            if par["zm"][h] == 2: fill("Dz" + v, IDN, YN, True, True)
             for c in range(NC):
-                tl = "Dz%s_%d" % (v, c)
-                sub(tl, "zg", c, YN, ZG + ["zb" + u], yn, True)
-                if par["zs"][h * NC + c]:
-                    act(cls("az", c), PS(tl, 0, 512), ACT.Abs, 0.0, [tl], ["az%s_%d" % (u, c)], 512, 1, [tl])
-                    if par["zs"][h * NC + c] == 2:
-                        act(cls("nz", c), cls("az", c), ACT.Sigmoid, 384.0, ["az%s_%d" % (u, c)], ["nz%s_%d" % (u, c)], 512, 1, (), -256.0)
-                    else:
-                        ts(cls("nz", c), cls("az", c), 1.0, None, ALU.is_le, None, ["az%s_%d" % (u, c)], ["nz%s_%d" % (u, c)], 512, .5)
+                if par["zm"][h] == 1:
+                    tl = "Dz%s_%d" % (v, c); d = PS(tl, 0, 512)
+                    mm([(d, IDN, jc("zg", c))], True, False)
+                    fill(tl, NID, YN, False, True)
                 else:
-                    ts(cls("nz", c), PS(tl, 0, 512), M4, M4, ALU.add, ALU.is_equal, [tl], ["nz%s_%d" % (u, c)], 512, 1, [tl])
-            tl = "cz" + v
-            byclass(tl, lambda k: (PS(tl, 0, PW), hk("hn", k), ks("nz", k), PW), ["hn", "idn", "c73"], "nz", head=[(PS(tl, 0, PW), IDN, S("c73", 0, PW), PW)],
-                    tail=[(PS(tl, 0, PW), S("n16", 0, 128), sm("sa2"), PW), (PS(tl, 0, PW), S("n32", 0, 128), sm("ch"), PW)], rt=["n16", "n32", "sa2" + u, "ch" + u])
-            tt(sm("fdf"), sm("df"), PS(tl, 0, PW), ALU.min, [tl, "df" + u], ["fdf" + u], PW, 1, [tl])
-            tt(sm("ni"), sm("fdf"), sm("base"), ALU.max, ["fdf" + u, "base" + u], ["ni" + u], PW)
-            ts(RN, sm("ni"), W - 1, None, ALU.bitwise_and, None, ["ni" + u], [rn], PW)
-            send("r", "rout", "rin", rn)
-        hs = range(NH); s = str(a); cur[0] = 0
+                    d = cls("dz", c)
+                    tt(d, jc("zg", c), PS("Dz" + v, 0, 512), ALU.subtract)
+                test(cls("nz", c), cls("az", c), d, par["zs"][h][c])
+            tl = "fin" + v
+            TF, CH = PS(tl, 1, 3 * PW, 3), PS(tl, 2, 3 * PW, 3)
+            mm([(PS(tl, 0, 3 * PW), IDN, S("f0", 0, 3 * PW)), (CH, full("mB"), sm("sa2")), (CH, IDN, cst("c1")), (CH, full("mA"), sm("sa2")), (CH, NID, cst("c1")),
+                (TF, full("q25"), sm("sa2"))], True, False, "finc")
+            byclass(TF, lambda k: hk("hz", k), "nz", False, False)
+            mm([(TF, IDN, cst("c1")), (TF, NID, cst("c1"))], False, True, "finr")
+            scan(S("s3o", 3 * o, 3 * o + 3 * PW), PS(tl, 0, 3 * PW), S("s3", 3 * o, 3 * o + 3 * PW), ALU.mult, ALU.add)
+            if t < V - 1:
+                RN = S("rout", oi, oi + PW); cp(RN, s3(2, "s3o"))
+                send("r", RN, S("rin", oi + P, oi + P + PW))
+            else:
+                RN = S("rlast", h * PW, h * PW + PW); cp(RN, s3(2, "s3o"), "rout")
+                send("r", RN, S("rfin", h * PW, h * PW + PW))
+        hs = range(NH); cur[0] = 0
         if t < V - 1:
             tl = "A%d" % t
-            mm(tl, [(PS(tl, 0, 1), S("sel", 0, 128), S("acc", a * NH + h, a * NH + h + 1), 256) for h in hs], ["sel"] + ["nl%d_%d" % (a, h) for h in hs])
-            cp(S("ai", 8 * a, 8 * a + 1), PS(tl, 0, 1), [tl], ["ai" + s], 1, 1, [tl])
-            ts(S("ai", 8 * a + 4, 8 * a + 5), S("ai", 8 * a, 8 * a + 1), 1, None, ALU.bitwise_and, None, ["ai" + s], ["aj" + s], 1)
-            ts(S("thr", 8 * t + 8, 8 * t + 9), S("ai", 8 * a + 4, 8 * a + 5), st, lo, ALU.mult, ALU.add, ["aj" + s], ["thr%d" % (t + 1)], 1)
-        tl = "wo%d" % t
-        yns = ["yout%d_%d" % (t, h) for h in hs]
-        mm(tl, [(PS(tl, 0, 8), hk("hw5", m), S("yout", t * P + m, t * P + P, 16), 8) for m in range(16)], ["hw5"] + yns)
-        cp(S("wo", 16 * a, 16 * a + 8), PS(tl, 0, 8), [tl], ["woa" + s], 8, 1, [tl])
-        ts(S("wo", 16 * a + 8, 16 * a + 16), S("wo", 16 * a, 16 * a + 8), 31, None, ALU.bitwise_and, None, ["woa" + s], ["wob" + s], 8)
-        tt(S("wof", 8 * a, 8 * a + 8), S("wo", 16 * a + 8, 16 * a + 16), S("c32i", 0, 8), ALU.add, ["wob" + s, "c32i"], ["wof" + s], 8)
-        cp(S("wou", 8 * a, 8 * a + 8), S("wof", 8 * a, 8 * a + 8), ["wof" + s], ["wou" + s], 8)
-        if t < V - 1:
-            cp(lambda T, Q, a=a: T.xw[:, 0:W].indirect(T.wou[:, 8 * a:8 * a + 8]), S("yout", t * P, t * P + P), ["wou" + s] + yns, ["xw"], P, par["sca"])
-        if t < V - 1:
-            cp(lambda T, Q, a=a: T.lw[:, 0:W].indirect(T.wou[:, 8 * a:8 * a + 8]), S("rout", t * P, t * P + P),
-               ["wou" + s] + ["rout%d_%d" % (t, h) for h in hs], ["lw", "lw0", "lw1"], P, par["sca"])
-        else:
-            ts(S("wov", 4, 8), S("wof", 8 * a + 4, 8 * a + 8), -W / 2, None, ALU.add, None, ["wof" + s], ["wov"], 4)
-            for h in hs:
-                cp(lambda T, Q, a=a, h=h: T.lw[:, h * W // 2:(h + 1) * W // 2].indirect(T.wov[:, 4:8] if h else T.wou[:, 8 * a:8 * a + 4]),
-                   S("rout", t * P + h * PW, t * P + h * PW + PW), ["wou" + s, "wov", "rout%d_%d" % (t, h)] + LGS, ["lw%d" % h], PW, par["sca"])
+            mm([(PS(tl, 0, 1), full("sel"), S("acc", a * NH + h, a * NH + h + 1)) for h in hs])
+            cp(S("ai", 8 * a, 8 * a + 1), PS(tl, 0, 1))
+            ts(S("ai", 8 * a + 4, 8 * a + 5), S("ai", 8 * a, 8 * a + 1), 1, None, ALU.bitwise_and, nm="aj")
+            ts(S("thr", 8 * t + 8, 8 * t + 9), S("ai", 8 * a + 4, 8 * a + 5), st, lo, ALU.mult, ALU.add)
+        parts = [(h * PW, PW) for h in hs] if par["split"] or t == V - 1 else [(0, P)]
+        for i0, n in parts:
+            cur[0] = i0 // PW
+            tl = "wo%d_%d" % (t, i0); Y = S("yout", t * P + i0, t * P + i0 + n); out = PS(tl, 0, n)
+            mm(modulo(out, full("w5n"), full("w5p"), Y, (IDN, cst("c155", n)), cst("c32", n)) + [(out, IDN, cst("wb", n))])
+            scan(S("ws", a * P + i0, a * P + i0 + n), cst("rs16", n), out, ALU.add, ALU.max)
+            offs = S("wou", 16 * a + i0 // 16, 16 * a + (i0 + n) // 16)
+            cp(offs, S("ws", a * P + i0 + 15, a * P + i0 + n, 16))
+            if t < V - 1: cp(IND("xw", 32 * i0, 32 * (i0 + n), offs), Y, "xw")
+            cp(IND("lw", 32 * i0, 32 * (i0 + n), offs), S("rout", t * P + i0, t * P + i0 + n) if t < V - 1 else S("rlast", i0, i0 + n), "lw")
+    cur[1] = V
     for h in range(NH):
+        cur[0] = h
         v = "%d_%d" % (V, h); oi = V * P + h * PW
-        op("N", 0, None, (), ["rin" + v], (), "ar" + v, par["net"], sends["r%d_%d" % (V - 1, h)])
-        op("N", 0, None, (), ["yin" + v], (), "ay" + v, par["net"], sends["y%d_%d" % (V - 1, h)])
-        dma("Y", lambda T, Q, h=h: T.yo[:, h * PW:h * PW + PW], S("yin", oi, oi + PW), "oo%d" % h, ["yin" + v], [], 2500)
-        cp(S("yjf", h * PW, h * PW + PW), S("rin", oi, oi + PW), ["rin" + v], ["yjf%d" % h], PW)
-        dma("Y", lambda T, Q, h=h: T.yj[:, h * PW:h * PW + PW], S("yjf", h * PW, h * PW + PW), "oj%d" % h, ["yjf%d" % h], [], 2500)
-    cuts = (0, 2, 4, 6, 8, 11, 14, 16)
-    for j in range(7):
-        c0, c1 = cuts[j], cuts[j + 1]
-        ts(S("l16", 256 * c0, 256 * c1), S("lw", 256 * c0, 256 * c1), -2048.0, None, ALU.add, None, ["lw%d" % (c0 // 8)], ["l16_%d" % j], 256 * (c1 - c0))
-        mm("yz", [(PS("yz", 0, 256), hk("hj", c), S("l16", 256 * c, 256 * c + 256), 256) for c in range(c0, c1)], ["hj", "l16_%d" % j], j == 0, j == 6)
-    act(S("yzf", 0, 256), PS("yz", 0, 256), ACT.Identity, 2048.0 * 136, ["yz"], ["yzf"], 256, 1, ["yz"])
-    dma("Y", lambda T, Q: T.yz[:, :], S("yzf", 0, 256), "oyz", ["yzf"], [], 2500)
+        op("N", (0.0, 0), None, [], [S("rfin", h * PW, h * PW + PW)], "ar", "ar" + v, -1.0, sends["r%d_%d" % (V - 1, h)])
+        op("N", (0.0, 0), None, [], [S("yin", oi, oi + PW)], "ay", "ay" + v, -1.0, sends["y%d_%d" % (V - 1, h)])
+        dma("Y", HBM("yo", h * PW, h * PW + PW), S("yin", oi, oi + PW), "oo%d" % h, 2500)
+        dma("Y", HBM("yj", h * PW, h * PW + PW), S("rfin", h * PW, h * PW + PW), "oj%d" % h, 2500)
+    n = len(par["fin"]); w = W // n
+    for j, e in enumerate(par["fin"]):
+        cur[0] = j * NH // n
+        if e == "V": ts(S("l16", w * j, w * j + w), S("lw", w * j, w * j + w), -2048.0, None, ALU.add)
+        else: act(S("l16", w * j, w * j + w), S("lw", w * j, w * j + w), ACT.Identity, -2048.0)
+        mm([(PS("yz", 0, 256), hk("hj", c), S("l16", 256 * c, 256 * c + 256)) for c in range(j * w // 256, (j + 1) * w // 256)], j == 0, j == n - 1)
+    act(S("yzf", 0, 256), PS("yz", 0, 256), ACT.Identity, 2048.0 * 136)
+    dma("Y", HBM("yz"), S("yzf", 0, 256), "oyz", 2500)
     return ops
 
 
+def price(ops, cost):
+    out = []
+    for o in ops:
+        c, n = o["size"]; e = o["eng"]
+        if e == "P": x = cost["pfix"] + n * cost["pe"]
+        elif e == "G": x = cost["rem"] if c == "rem" else float(n)
+        elif e == "N": x = 0.0
+        elif o["sem"]: x = 60.0
+        else: x = max(64.0, cost["fix"] + (20.0 if e == "S" else 0.0) + n * (cost[c] if isinstance(c, str) else c)) + (cost["self"] if o.get("drain") else 0.0)
+        out.append((x, cost["net"] if e == "N" else o["lat"]))
+    return out
+
+
 def kind(o):
-    return o["eng"] + "".join(x for x in o["nm"] if x.isalpha()) + str(o["h"])
+    return o["eng"] + o["nm"] + str(o["h"])
 
 
-def late_starts(ops, par, fin):
-    n = len(ops); need = [0.0] * n; back = [0.0] * n; busy = {e: [] for e in "VSPGYN"}
-    for k in sorted(range(n), key=lambda k: (-fin[k], -k)):
-        o = ops[k]; s = need[k] + o["lat"]; c = o["cost"]; bz = busy[o["eng"]]
-        for j, (x0, x1) in enumerate(bz):
-            if x1 <= s: continue
-            if x0 >= s + c: break
-            s = x1
-        bz.append((s, s + c)); bz.sort(); back[k] = s + c
-        for d in o["deps"]:
-            gap = par["hop"] if ops[d]["eng"] != o["eng"] else 0.0 if o["eng"] == "P" else par["self"]
-            need[d] = max(need[d], back[k] + gap)
-        if o["after"] is not None: need[o["after"]] = max(need[o["after"]], back[k])
-    return back
+def urgency(ops, par, cost, off):
+    n = len(ops); pc = price(ops, cost); succ = [[] for _ in ops]
+    for k, o in enumerate(ops):
+        for d in o["deps"]: succ[d].append(k)
+        if o["after"] is not None: succ[o["after"]].append(k)
+    last = (V - 1) * par["T"] + par["delta"] + cost["net"] + 3000.0
+    pr = [0.0] * n
+    for k in range(n - 1, -1, -1):
+        o = ops[k]
+        base = -(o["t"] * par["T"] + o["h"] * par["delta"]) if o["nm"] == "sendr" else max([pr[s] for s in succ[k]] + [-last])
+        pr[k] = pc[k][0] * par["lam"] + pc[k][1] + cost["hop"] + base
+    return [pr[k] + off.get(kind(ops[k]), 0.0) for k in range(n)]
 
 
-def best_order(ops, par):
-    best = None; given = None
-    for _ in range(par["rounds"]):
-        try:
-            r = lay_out(ops, par, given)
-        except ValueError:
-            break
-        if best is None or max(r[3]) < max(best[0][3]): best = (r, given)
-        given = late_starts(ops, par, r[3])
-    return lay_out(ops, par, best[1])
-
-
-def place(ops, par, pr, succ, left):
-    n = len(ops); busy = {e: [] for e in "VSPGYN"}; held = {}; start = [0.0] * n; fin = [0.0] * n; hop = par["hop"]
-    ready = [k for k in range(n) if left[k] == 0]
-    while ready:
-        k = max(ready, key=lambda k: (pr[k], -k)); ready.remove(k)
-        o = ops[k]; e = o["eng"]; c = o["cost"]; s = 0.0
-        for d in o["deps"]:
-            s = max(s, fin[d] + (hop if ops[d]["eng"] != e else 0.0 if e == "P" else par["self"]))
-        if o["after"] is not None: s = max(s, fin[o["after"]])
-        block = [(x0 - hop, x1 + hop) for tl in o["ps"] for x0, x1, e2 in held.get(tl, []) if e2 != e]
-        bz = busy[e]; moved = True
-        while moved:
-            moved = False
-            for x0, x1 in bz[max(0, lower(bz, s) - 1):]:
-                if x0 >= s + c: break
-                if x1 > s: s = x1
-            for x0, x1 in block:
-                if x1 > s and x0 < s + c: s = x1; moved = True
-        bz.insert(lower(bz, s), (s, s + c)); start[k] = s; fin[k] = s + c + o["lat"]
-        for tl in o["ps"]: held.setdefault(tl, []).append((s, s + c, e))
-        for x in succ[k]:
-            left[x] -= 1
-            if left[x] == 0: ready.append(x)
-    order = sorted(range(n), key=lambda k: (start[k], k))
-    end = {tl: max(x[1] for x in v) for tl, v in held.items()}
-    bank, last = {}, {}; past = [[] for _ in range(8)]; till = [-1e9] * 8
-    for k in order:
-        o = ops[k]; extra = set()
-        for tl in o["ps"]:
-            if tl not in bank:
-                b = min(range(8), key=lambda j: till[j])
-                if till[b] > start[k]: raise ValueError("no bank")
-                bank[tl] = b; till[b] = end[tl]; extra.update(past[b]); past[b] = []
-            elif ops[last[tl]]["eng"] != o["eng"]: extra.add(last[tl])
-            last[tl] = k; past[bank[tl]].append(k)
-        o["all"] = set(o["deps"]) | extra
-    return order, bank, start, fin
-
-
-def lower(bz, s):
-    a, b = 0, len(bz)
-    while a < b:
-        m = (a + b) // 2
-        if bz[m][0] < s: a = m + 1
-        else: b = m
-    return a
-
-
-def lay_out(ops, par, given=None):
-    n = len(ops); succ = [[] for _ in ops]; left = [0] * n
+def lay_out(ops, par, cost, pr):
+    n = len(ops); pc = price(ops, cost); succ = [[] for _ in ops]; left = [0] * n
+    hop, slf = cost["hop"], cost["self"]
+    eng = [o["eng"] for o in ops]
     for k, o in enumerate(ops):
         pre = set(o["deps"])
         if o["after"] is not None: pre.add(o["after"])
         left[k] = len(pre)
         for d in pre: succ[d].append(k)
-    pr = [0.0] * n
-    for k in range(n - 1, -1, -1):
-        pr[k] = ops[k]["cost"] + ops[k]["lat"] + par["hop"] + max([pr[s] for s in succ[k]] + [0.0])
-    if par.get("T"):
-        rs = [k for k in range(n) if ops[k]["sem"] == "remote"][1::2]
-        dead = {k: (j // NH) * par["T"] + (j % NH) * par["delta"] for j, k in enumerate(rs)}
-        last = max(dead.values()) + par["net"] + 3000.0
-        for k in range(n - 1, -1, -1):
-            pr[k] = ops[k]["cost"] * par["lam"] + ops[k]["lat"] + par["hop"] + (-dead[k] if k in dead else max([pr[s] for s in succ[k]] + [-last]))
-    for k in range(n): pr[k] += par["off"].get(kind(ops[k]), 0) * 100.0 - par["bias"] * ops[k]["h"]
-    if given: pr = given
-    if par["serial"]: return place(ops, par, pr, succ, left)
-    users = {}
-    for k, o in enumerate(ops):
-        for tl in o["ps"]: users.setdefault(tl, []).append(k)
-    rem = {tl: len(u) for tl, u in users.items()}
+    rem = {}
+    for o in ops:
+        for tl in o["ps"]: rem[tl] = rem.get(tl, 0) + 1
     bank, lastacc = {}, {}
     holder = [None] * 8; past = [[] for _ in range(8)]; bfree = [0.0] * 8
-    free = {e: 0.0 for e in "VSPGYN"}; fin = [0.0] * n; start = [0.0] * n
-    ready = [k for k in range(n) if left[k] == 0]; order = []
-
-    def edge(d, k):
-        if ops[d]["eng"] == ops[k]["eng"]:
-            return fin[d] + (0.0 if ops[k]["eng"] == "P" else par["self"])
-        return fin[d] + par["hop"]
+    free = {e: 0.0 for e in "VSPGYN"}; fin = [0.0] * n; start = [0.0] * n; rdy = [0.0] * n
+    ready = [k for k in range(n) if left[k] == 0]; order = []; extras = [()] * n
     while ready:
+        fb = [j for j in range(8) if holder[j] is None]
+        nd = sum(1 for x in holder if x is not None and x[0] == "D")
+        b0 = min(fb, key=lambda j: bfree[j]) if fb else None
         cands = []
         for k in ready:
-            o = ops[k]; s = free[o["eng"]]; b = None
-            for d in o["deps"]: s = max(s, edge(d, k))
-            if o["after"] is not None: s = max(s, fin[o["after"]])
-            ok = True
-            for tl in o["ps"]:
+            s = max(free[eng[k]], rdy[k]); ok = True
+            for tl in ops[k]["ps"]:
                 if tl in bank:
                     d = lastacc[bank[tl]]
-                    if ops[d]["eng"] != o["eng"]: s = max(s, edge(d, k))
-                else:
-                    fb = [j for j in range(8) if holder[j] is None]
-                    nd = sum(1 for x in holder if x is not None and x[0] == "D")
-                    if not fb or (tl[0] == "D" and nd >= par["dmax"]) or (tl[0] in "DKnA" and len(fb) < 2): ok = False; break
-                    b = min(fb, key=lambda j: bfree[j]); s = max(s, bfree[b] + par["hop"])
-            if ok: cands.append((s, k, b))
+                    if eng[d] != eng[k]: s = max(s, fin[d] + hop)
+                elif not fb or (tl[0] == "D" and nd >= par["dmax"]) or (tl[0] in "DKnAfy" and len(fb) < 2): ok = False
+                else: s = max(s, bfree[b0] + hop)
+            if ok: cands.append((s, -pr[k], k))
         if not cands: raise ValueError("no bank")
-        s0, k0, _ = min(cands, key=lambda c: (c[0], -pr[c[1]]))
-        e = ops[k0]["eng"]
-        s, k, b = max([c for c in cands if ops[c[1]]["eng"] == e and c[0] <= s0 + min(par["look"], ops[k0]["cost"])], key=lambda c: (pr[c[1]] - par["beta"] * (c[0] - s0), -c[1]))
-        o = ops[k]; extra = set()
-        for tl in o["ps"]:
+        s0, _, k0 = min(cands); e = eng[k0]; lim = s0 + min(par["look"], pc[k0][0])
+        _, _, s, k = max((-c[1] - par["beta"] * (c[0] - s0), -c[2], c[0], c[2]) for c in cands if eng[c[2]] == e and c[0] <= lim)
+        extra = set()
+        for tl in ops[k]["ps"]:
             if tl not in bank:
-                bank[tl] = b; holder[b] = tl; extra.update(past[b]); past[b] = []
-            elif ops[lastacc[bank[tl]]]["eng"] != e: extra.add(lastacc[bank[tl]])
+                bank[tl] = b0; holder[b0] = tl; extra.update(past[b0]); past[b0] = []
+            elif eng[lastacc[bank[tl]]] != e: extra.add(lastacc[bank[tl]])
             j = bank[tl]; lastacc[j] = k; past[j].append(k); rem[tl] -= 1
-            if rem[tl] == 0: holder[j] = None; bfree[j] = s + o["cost"]
-        o["all"] = set(o["deps"]) | extra
-        start[k] = s; free[e] = s + o["cost"]; fin[k] = s + o["cost"] + o["lat"]
+            if rem[tl] == 0: holder[j] = None; bfree[j] = s + pc[k][0]
+        extras[k] = extra
+        start[k] = s; free[e] = s + pc[k][0]; fin[k] = free[e] + pc[k][1]
         order.append(k); ready.remove(k)
         for x in succ[k]:
+            gap = 0.0 if eng[x] == "N" or eng[x] == e == "P" else slf if eng[x] == e else hop
+            rdy[x] = max(rdy[x], fin[k] + gap)
             left[x] -= 1
             if left[x] == 0: ready.append(x)
-    return order, bank, start, fin
+    return order, bank, extras, start, fin
+
+
+def replay(ops, cost, order, extras):
+    pc = price(ops, cost); free = {e: 0.0 for e in "VSPGYN"}; fin = [0.0] * len(ops); hop, slf = cost["hop"], cost["self"]
+    for k in order:
+        o = ops[k]; e = o["eng"]; s = free[e]
+        for ds in (o["deps"], extras[k]):
+            for d in ds:
+                e2 = ops[d]["eng"]
+                x = fin[d] + (0.0 if e == "N" or e2 == e == "P" else slf if e2 == e else hop)
+                if x > s: s = x
+        if o["after"] is not None and fin[o["after"]] > s: s = fin[o["after"]]
+        free[e] = s + pc[k][0]; fin[k] = free[e] + pc[k][1]
+    return max(fin)
+
+
+def best_order(ops, par, cost, off=None):
+    off = dict(off or {}); kinds = sorted({kind(o) for o in ops if 1 <= o["t"] < V}); x = par["seed"]
+    best = lay_out(ops, par, cost, urgency(ops, par, cost, off)); val = max(best[4])
+    for _ in range(par["rounds"]):
+        x = (x * 1103515245 + 12345) % 2 ** 31; kd = kinds[(x >> 8) % len(kinds)]
+        x = (x * 1103515245 + 12345) % 2 ** 31; step = (-2000.0, -800.0, -300.0, 300.0, 800.0, 2000.0)[(x >> 8) % 6]
+        new = dict(off); new[kd] = new.get(kd, 0.0) + step
+        try:
+            r = lay_out(ops, par, cost, urgency(ops, par, cost, new))
+        except ValueError:
+            continue
+        if max(r[4]) <= val: best, val, off = r, max(r[4]), new
+    return best, off
 
 
 PLAN = []
@@ -583,8 +585,8 @@ def rank_program(g, core, T, topo):
         return
     if not PLAN:
         ops = build_ops(PAR)
-        PLAN.append((ops,) + best_order(ops, PAR))
-    ops, order, bank = PLAN[0][:3]
+        PLAN.append((ops,) + best_order(ops, PAR, COST)[0])
+    ops, order, bank, extras = PLAN[0][:4]
     nxt = T.cores[(rank + 1) % len(T.cores)]; prv = T.cores[(rank - 1) % len(T.cores)]
     rid, pid, _ = topo.addr(nxt)
     env = {"rid": rid, "pid": pid, "mask": topo.mask(core, nxt)}
@@ -600,7 +602,7 @@ def rank_program(g, core, T, topo):
             mark[k] = (o["sem"], n_in, {}); top[o["sem"]] = n_in
             continue
         kn = known[e]
-        pre = set(o["all"])
+        pre = set(o["deps"]) | set(extras[k])
         if e == "V":
             pre.update(drain); drain[:] = [k] if o.get("drain") else []
         need = sorted((mark[d] for d in pre if d in mark and not (e == "P" and ops[d]["eng"] == "P")), key=lambda m: -m[1])

@@ -16,15 +16,15 @@ SEG = 18
 B, F, I32, U16, H16 = "bfloat16", "float32", "int32", "uint16", "float16"
 SCRATCH = {
     "xw": [W, B], "li": [W, I32], "lw": [W, F], "l16": [W, H16],
-    "rin": [V * P, U16], "yin": [(V + 1) * P, B], "rout": [V * P, U16], "yout": [V * P, B], "rfin": [P, F], "rlast": [P, F],
+    "rin": [(V + 1) * P, U16], "yin": [(V + 1) * P, B], "rout": [V * P, U16], "yout": [V * P, B], "rfin": [P, F],
     "wi": [8, I32], "yzf": [256, F], "ci": [8, I32], "cf": [32, F], "rm": [16, F],
     "ioc": [144, F], "iob": [128, F], "iom": [128, F], "ioj": [64, F], "iog": [64, F], "tmp": [256, F],
     "hh": [144, B], "hz": [144, B], "hj": [144, H16], "ba": [16 * 144, H16], "kc": [128 * NH, B], "pen": [128, B],
-    "sel": [128, F], "acc": [8, F], "o16": [16, B], "o512": [8, B], "f0": [192, B], "rs8": [64, F], "rs16": [128, F],
+    "sel": [128, F], "acc": [8, F], "o16": [16, B], "o512": [8, B], "f0": [4 * PW, B], "rs8": [64, F], "rs16": [128, F],
     "thr": [8 * V, F], "ai": [16, I32], "wou": [32, U16], "ws": [2 * P, F], "wp": [128, H16], "wn": [128, H16],
     "lg": [2 * 2048, H16], "dr": [2 * NH * 144, B], "nn": [2 * 2 * P, B], "nt": [2 * 2 * P, B], "qq": [2 * NH * 8, I32],
     "zz": [2 * NH * 128, I32], "zb": [2 * NH * 128, B], "keep": [128, F],
-    "s3": [2 * 3 * P, F], "s3o": [2 * 3 * P, F],
+    "s4": [2 * 4 * P, I32], "s4o": [2 * 4 * P, F],
 }
 for _n in ("idn", "nid", "i16", "n16", "i64", "q25", "nbo", "bo", "tri", "mA", "mB", "w5p", "w5n", "wb", "c1", "c32", "c4096", "cc", "c155", "c2048"):
     SCRATCH[_n] = [128, B]
@@ -47,7 +47,12 @@ PAR = {"xg": ("SS", "SS"), "lg": ("SS", "SS"), "zg": ("SS", "SS"),
        "sg": ("good", "oh"), "split": 1, "fin": "VSVSVSVS",
        "look": 200.0, "beta": 4.0, "dmax": 5, "T": 17000.0, "delta": 7000.0, "lam": 1.3, "rounds": 3500, "seed": 1}
 PAR.update({'zm': (2, 1), 'T': 19000., 'zs': ((0, 0), (0, 1)), 'xs': ((0, 1), (0, 1))})
-COST = {"fix": 70.0, "gam": 1.5, "sca": 3.5, "pe": 0.6, "pfix": 30.0, "hop": 180.0, "self": 110.0, "net": 4500.0, "rem": 900.0}
+COST = {"fix": 70.0, "gam": 1.5, "sca": 3.5, "pe": 0.6, "pfix": 30.0, "hop": 180.0, "self": 110.0, "net": 4500.0, "rem": 900.0, "all": 1.0, "weight": .5,
+        "gfix": 70.0, "sfix": 20.0}
+COSTS = [dict(COST, fix=60.0, sfix=0.0, gfix=60.0, pfix=0.0, hop=200.0, self=200.0, net=3000.0, weight=.4),
+         dict(COST, fix=0.0, sfix=0.0, gfix=60.0, pfix=0.0, pe=.6, hop=260.0, self=260.0, net=2800.0, rem=700.0, weight=.3),
+         dict(COST, fix=30.0, sfix=0.0, gfix=60.0, pfix=0.0, pe=.55, hop=250.0, self=250.0, gam=1.9, sca=5.0, all=1.35, weight=.25)]
+PAR.update({"rounds": 200, "moves": 30000, "heat": 300.0, "aimed": .8, "visits": V, "short": 4, "dq": 1, "reach": 1500.0, "again": 300, "hope": 100.0, "delta": 3000.0, "T": 17000.0})
 
 
 def S(name, a, b, s=1, p0=0, p1=128): return ("s", name, p0, p1, a, b, s)
@@ -95,8 +100,8 @@ def places(x):
 
 
 def build_ops(par):
-    ops, live = [], {}
-    cur = [0, 0]
+    ops, live = [], {}; V = par["visits"]
+    cur = [0, 0]; dry = [False]
 
     def op(eng, size, fn, r, w, nm, sem=None, lat=0.0, after=None, more=()):
         k = len(ops); deps = set(more)
@@ -107,6 +112,7 @@ def build_ops(par):
             deps.update(j for j, m2, isw in live.get(name, []) if isw and m & m2)
         for name, m in wr:
             deps.update(j for j, m2, isw in live.get(name, []) if m & m2)
+        if dry[0]: return {"eng": eng, "size": size, "fn": fn, "deps": deps}
         for name, m in wr:
             live[name] = [(j, m2 & ~m, isw) for j, m2, isw in live.get(name, []) if m2 & ~m] + [(k, m, True)]
         for name, m in rd:
@@ -147,14 +153,26 @@ def build_ops(par):
             return g.scalar.activation(ap(T, Q, out), ap(T, Q, in_), func, bias=ap(T, Q, bias), scale=scale, accum_out=ap(T, Q, acc) if acc else None)
         return op("S", rate(out, in_, 1.0), fn, [in_, bias], [out] + ([acc] if acc else []), nm or out[1])
 
-    def mm(items, first=True, last=True, nm=None):
+    def mm(items, nm=None, closes=False, behind=()):
         def fn(g, T, Q):
-            ins = None
+            ins = None; first, last = Q("ends")
             for j, it in enumerate(items):
                 ins = g.tensor.matmul(ap(T, Q, it[0]), ap(T, Q, it[1]), ap(T, Q, it[2]), first and j == 0, last and j == len(items) - 1)
             return ins
         cols = sum(max(min(64, width(l)), width(r)) * (4 if SCRATCH[r[1]][2] == F else 1) for o, l, r in items)
-        return op("P", ("pe", cols), fn, [x for it in items for x in it[1:]], [items[0][0]], nm or "".join(x for x in items[0][0][1] if x.isalpha()))
+        tl = items[0][0][1]; mine = live.setdefault("ps " + tl, [])
+        k = op("P", ("pe", cols), fn, [x for it in items for x in it[1:]], [], nm or "".join(x for x in tl if x.isalpha()), more=[j for j, m, w in mine] if closes else behind)
+        ops[k]["ps"] = (tl,); mine.append((k, 1, True))
+        return k
+
+    def either(on_s, on_v, first="S"):
+        one, other = (on_s, on_v) if first == "S" else (on_v, on_s)
+        dry[0] = True; alt = other(); dry[0] = False
+        k = one(); ops[k]["deps"] |= alt["deps"]; ops[k]["alt"] = alt
+        return k
+
+    def move(out, in_, add=0.0, first="S"):
+        return either(lambda: act(out, in_, ACT.Identity, add), lambda: ts(out, in_, add, None, ALU.add) if add else cp(out, in_), first)
 
     def col(j): return S("cf", j, j + 1)
 
@@ -230,8 +248,8 @@ def build_ops(par):
     ts(full("keep"), full("iom"), 0.0, None, ALU.not_equal)
     for nme, v in (("c1", M1), ("c32", M32), ("c4096", M4096), ("c155", 15.5), ("c2048", 2048.0)):
         ms(full(nme), v)
-    for j, v in enumerate((0.0, 39.0 / 64, 39.0 / 128)):
-        ms(S("f0", j, 192, 3), v)
+    for j, v in enumerate((0.0, 1.0, 39.0 / 64, 39.0 / 128)):
+        ms(S("f0", j, 4 * PW, 4), v)
     ts(col(17), col(1), 1.0, -0.5, ALU.is_equal, ALU.mult)
     ts(col(22), col(7), 2048.0, col(17), ALU.mult, ALU.add)
     ts(full("cc"), full("iom"), 0.0, col(22), ALU.mult, ALU.add)
@@ -277,7 +295,7 @@ def build_ops(par):
 
             def jc(name, c, i0=0, i1=PW): return S(name, ob + 16 * i0 + c, ob + 16 * i1, NC)
 
-            def s3(j, name="s3"): return S(name, 3 * o + j, 3 * o + 3 * PW, 3)
+            def s4(j, name="s4"): return S(name, 4 * o + j, 4 * o + 4 * PW, 4)
 
             RU, YIN, YN = S("rin", oi, oi + PW), S("yin", oi, oi + PW), S("yout", oi, oi + PW)
             if t:
@@ -289,32 +307,29 @@ def build_ops(par):
                 for j, e in enumerate(who):
                     out = S(name, ob + 16 * pw * j, ob + 16 * pw * (j + 1))
                     src = IND(win, 0, W, S(offs, at + pw * j, at + pw * (j + 1)))
-                    if e == "S": act(out, src, ACT.Identity, add)
-                    elif add: ts(out, src, add, None, ALU.add)
-                    else: cp(out, src)
+                    move(out, src, add, e)
                 return [(pw * j, pw * (j + 1)) for j in range(len(who))]
 
-            def fill(tl, lhs, Y, first, last):
-                mm([(PS(tl, j, 512, KK), lhs, Y) for j in range(KK)], first, last, nm="fill" + tl[:2])
+            def fill(tl, lhs, Y, n=KK):
+                return mm([(PS(tl, j, n * PW, n), lhs, Y) for j in range(n)], "fill" + tl[:2])
 
             def near(out, d): ts(out, d, M4, M4, ALU.add, ALU.is_equal)
 
             def test(out, ab, d, way):
                 if way == 0: return near(out, d)
                 act(ab, d, ACT.Abs)
-                if way == 1: ts(out, ab, 1.0, None, ALU.is_le)
-                else: act(out, ab, ACT.Sigmoid, 384.0, -256.0)
+                either(lambda: act(out, ab, ACT.Sigmoid, 384.0, -256.0), lambda: ts(out, ab, 1.0, None, ALU.is_le), "V" if way == 1 else "S")
 
             xp = gather("xg", "xw", "rin", oi)
-            cp(s3(2), RU, "rf")
+            cp(s4(3), RU, "rf")
             ts(sm("kp"), RU, 32.0, col(5), ALU.mult, ALU.add)
-            if par["xm"][h] == 2: fill("Dx" + v, IDN, YIN, True, True)
+            if par["xm"][h] == 2: fill("Dx" + v, IDN, YIN)
             for c in range(NC):
                 if par["xm"][h] == 1:
                     tl = "Dx%s_%d" % (v, c); d = PS(tl, 0, 512)
-                    fill(tl, NID, YIN, True, False)
-                    for j, (i0, i1) in enumerate(xp):
-                        mm([(PS(tl, KK * i0, KK * i1), IDN, jc("xg", c, i0, i1))], False, j == len(xp) - 1)
+                    k = fill(tl, NID, YIN)
+                    for i0, i1 in xp:
+                        mm([(PS(tl, KK * i0, KK * i1), IDN, jc("xg", c, i0, i1))], behind=[k])
                 else:
                     d = cls("dx", c)
                     tt(d, jc("xg", c), PS("Dx" + v, 0, 512), ALU.subtract)
@@ -325,49 +340,49 @@ def build_ops(par):
             mm([(PS(tl, 0, PW), IDN, cst("c2048"))]
                + [(PS(tl, 0, PW), S("ba", 144 * ((k + t) % 16) + 15 - k, 144 * ((k + t) % 16) + 143 - k), S("lg", ob + k, ob + n16, 16)) for k in range(16)])
             cp(sm("nu"), PS(tl, 0, PW))
-            tt(s3(1), PS(tl, 0, PW), s3(2), ALU.subtract, "nr")
-            act(sm("nm"), PS(tl, 0, PW), ACT.Identity)
+            tt(s4(2), PS(tl, 0, PW), s4(3), ALU.subtract, "nr")
+            ts(s4(1), PS(tl, 0, PW), -1.0, None, ALU.mult, nm="nm")
             zp = gather("zg", "xw", "nu", o)
 
-            def byclass(out, lhs, name, first=True, last=True):
+            def byclass(out, lhs, name, behind=()):
                 for c in range(NC):
-                    mm([(out, lhs(k), ks(name, k)) for k in range(c, 16, NC)], first and c == 0, last and c == NC - 1)
+                    mm([(out, lhs(k), ks(name, k)) for k in range(c, 16, NC)], behind=behind)
             tl = "nb" + v
             byclass(PS(tl, 0, PW), lambda k: IDN, "nx")
-            if "good" in par["sg"]: act(sm("good"), PS(tl, 0, PW), ACT.Sigmoid, -1920.0, 256.0)
-            else: ts(sm("good"), PS(tl, 0, PW), 8.0, None, ALU.is_ge)
+            either(lambda: act(sm("good"), PS(tl, 0, PW), ACT.Sigmoid, -1920.0, 256.0), lambda: ts(sm("good"), PS(tl, 0, PW), 8.0, None, ALU.is_ge))
             tl = "pre" + v
             mm([(PS(tl, 0, PW), full("tri"), sm("good"))])
-            if "oh" in par["sg"]: act(sm("oh"), PS(tl, 0, PW), ACT.Sigmoid, col(14), 256.0)
-            else: ts(sm("oh"), PS(tl, 0, PW), col(9), None, ALU.is_gt)
+            either(lambda: act(sm("oh"), PS(tl, 0, PW), ACT.Sigmoid, col(14), 256.0), lambda: ts(sm("oh"), PS(tl, 0, PW), col(9), None, ALU.is_gt))
             tl = "cnt" + v
             byclass(PS(tl, 0, PW), lambda k: hk("hh", k), "nx")
             act(sm("sa"), PS(tl, 0, PW), ACT.Sign, -11.5)
-            act(sm("cnt"), PS(tl, 0, PW), ACT.Identity)
+            move(sm("cnt"), PS(tl, 0, PW))
             tl = "cT" + v
             mm([(PS(tl, 0, PW), full("bo"), sm("sa"))])
             act(sm("nl"), PS(tl, 0, PW), ACT.Sigmoid, S("thr", 8 * t, 8 * t + 1), 256.0, S("acc", o3, o3 + 1))
             tl = "ya" + v
             mm([(PS(tl, 0, PW), full("i16"), sm("oh")), (PS(tl, 0, PW), full("i64"), sm("nl"))])
             tt(sm("yy"), YIN, PS(tl, 0, PW), ALU.min)
-            if 0 in par["ds"][h]: fill("Dm" + v, full("i16"), sm("oh"), True, True)
+            dq = par["dq"]
+            if 0 in par["ds"][h]: fill("Dm" + v, full("i16"), sm("oh"), KK // dq)
             for c in range(NC):
                 if par["ds"][h][c]:
                     tl = "Dm%s_%d" % (v, c)
-                    mm([(PS(tl, 0, 512), IDN, jc("xg", c))], True, False)
-                    fill(tl, full("n16"), sm("oh"), False, True)
+                    mm([(PS(tl, 0, 512), IDN, jc("xg", c))])
+                    fill(tl, full("n16"), sm("oh"))
                     act(cls("dm", c), PS(tl, 0, 512), ACT.Relu)
                 else:
-                    tt(cls("dm", c), jc("xg", c), PS("Dm" + v, 0, 512), ALU.max)
+                    for j in range(dq):
+                        tt(S("dm", ob + 512 * c + j, ob + 512 * c + 512, dq), S("xg", ob + c + NC * j, ob + n16, NC * dq), PS("Dm" + v, 0, 512 // dq), ALU.max)
             tl = "K" + v
 
             def both(name, j): return S(name, ob + j, ob + n16, KK)
-            mm([(PS(tl, 0, 128), IDN, S("kc", 128 * h, 128 * h + 128))] + [(PS(tl, j, 64, 8), both("ad", j), S("o512", 0, 8)) for j in range(KK)], True, False, "Ka")
-            mm([(PS(tl, 0, 64, 1, PW * c, PW * c + PW), sm("sa"), S("pen", 64 * c, 64 * c + 64)) for c in range(NC)], False, False, "Kp")
-            mm([(PS(tl, j, 128, 8), both("dm", j), S("o16", 0, 16)) for j in range(KK)], False, True, "Kd")
+            k = mm([(PS(tl, 0, 128), IDN, S("kc", 128 * h, 128 * h + 128))] + [(PS(tl, j, 64, 8), both("ad", j), S("o512", 0, 8)) for j in range(KK)], "Ka")
+            mm([(PS(tl, 0, 64, 1, PW * c, PW * c + PW), sm("sa"), S("pen", 64 * c, 64 * c + 64)) for c in range(NC)], "Kp", behind=[k])
+            mm([(PS(tl, j, 128, 8), both("dm", j), S("o16", 0, 16)) for j in range(KK)], "Kd", True)
             scan(sm("sc"), S("rs8", 0, 64), PS(tl, 0, 64), ALU.add, ALU.min)
             od = 144 * o3 + 8; oq = 128 * o3
-            act(S("dr", od, od + 128, 2), PS(tl, 64, 128), ACT.Identity)
+            move(S("dr", od, od + 128, 2), PS(tl, 64, 128))
             least = S("qq", 8 * o3, 8 * o3 + 8, 1, 0, PW)
             k = tt(least, S("sc", o + 7, o + PW, 8, 0, PW), S("sc", o + 7, o + PW, 8, PW, 128), ALU.min)
             ops[k]["drain"] = True
@@ -376,9 +391,9 @@ def build_ops(par):
             scan(ZB, S("keep", 0, 128, 1, 0, PW), S("zz", oq, oq + 128, 1, 0, PW), ALU.mult, ALU.add)
             IW, NW = S("idn", 0, PW, 1, 0, PW), S("nid", 0, PW, 1, 0, PW)
             tl = "del" + v
-            mm([(PS(tl, 0, PW), full("n16"), sm("oh")), (PS(tl, 0, PW), full("n16"), sm("nl"))], True, False)
-            mm([(PS(tl, 0, PW), ZB, IW)], False, True, "delz")
-            tt(YN, sm("yy"), PS(tl, 0, PW), ALU.max)
+            mm([(PS(tl, 0, PW), full("n16"), sm("oh")), (PS(tl, 0, PW), full("n16"), sm("nl"))])
+            mm([(PS(tl, 0, PW), ZB, IW)], "delz")
+            kyn = tt(YN, sm("yy"), PS(tl, 0, PW), ALU.max)
 
             def send(kind, src, dst):
                 def fn(g, T, Q, t=t, h=h):
@@ -389,8 +404,8 @@ def build_ops(par):
 
             def xr(a0):
                 return [(PS(tl, a0, a0 + PW), S("dr", od - c, od - c + 128), S("idn", PW * c, PW * c + PW)) for c in range(NC)] + [(PS(tl, a0, a0 + PW), full("i64"), sm("nl"))]
-            mm(xr(0) + [(PS(tl, 0, PW), full("nbo"), YIN), (PS(tl, 0, PW), full("bo"), sm("yy"))] + xr(PW), True, False)
-            mm([(PS(tl, PW, 2 * PW), ZB, NW)], False, True, "ddz")
+            mm(xr(0) + [(PS(tl, 0, PW), full("nbo"), YIN), (PS(tl, 0, PW), full("bo"), sm("yy"))] + xr(PW))
+            mm([(PS(tl, PW, 2 * PW), ZB, NW)], "ddz")
             on = 2 * o
             test(S("nn", on, on + 2 * PW), S("nt", on, on + 2 * PW), PS(tl, 0, 2 * PW), 2 if "nn" in par["sg"] else 0)
             tl = "c2" + v
@@ -402,33 +417,29 @@ def build_ops(par):
             tl = "u" + v
             its = modulo(PS(tl, 0, PW), full("wn"), full("wp"), YN, (full("bo"), cst("cc")), cst("c4096"))
             mm(its)
-            tt(sm("pi"), s3(2), PS(tl, 0, PW), ALU.mult)
+            tt(sm("pi"), s4(3), PS(tl, 0, PW), ALU.mult)
             tt(sm("pj"), sm("pi"), sm("kp"), ALU.add)
-            ts(sm("far"), sm("pj"), 5, W - 1, ALU.arith_shift_right, ALU.bitwise_and)
-            tt(s3(0), sm("far"), sm("nm"), ALU.subtract, "fn")
-            if par["zm"][h] == 2: fill("Dz" + v, IDN, YN, True, True)
+            ts(s4(0), sm("pj"), 5, W - 1, ALU.arith_shift_right, ALU.bitwise_and, "far")
+            if par["zm"][h] == 2: fill("Dz" + v, IDN, YN)
             for c in range(NC):
                 if par["zm"][h] == 1:
                     tl = "Dz%s_%d" % (v, c); d = PS(tl, 0, 512)
-                    mm([(d, IDN, jc("zg", c))], True, False)
-                    fill(tl, NID, YN, False, True)
+                    mm([(d, IDN, jc("zg", c))])
+                    fill(tl, NID, YN)
                 else:
                     d = cls("dz", c)
                     tt(d, jc("zg", c), PS("Dz" + v, 0, 512), ALU.subtract)
                 test(cls("nz", c), cls("az", c), d, par["zs"][h][c])
             tl = "fin" + v
-            TF, CH = PS(tl, 1, 3 * PW, 3), PS(tl, 2, 3 * PW, 3)
-            mm([(PS(tl, 0, 3 * PW), IDN, S("f0", 0, 3 * PW)), (CH, full("mB"), sm("sa2")), (CH, IDN, cst("c1")), (CH, full("mA"), sm("sa2")), (CH, NID, cst("c1")),
-                (TF, full("q25"), sm("sa2"))], True, False, "finc")
-            byclass(TF, lambda k: hk("hz", k), "nz", False, False)
-            mm([(TF, IDN, cst("c1")), (TF, NID, cst("c1"))], False, True, "finr")
-            scan(S("s3o", 3 * o, 3 * o + 3 * PW), PS(tl, 0, 3 * PW), S("s3", 3 * o, 3 * o + 3 * PW), ALU.mult, ALU.add)
-            if t < V - 1:
-                RN = S("rout", oi, oi + PW); cp(RN, s3(2, "s3o"))
-                send("r", RN, S("rin", oi + P, oi + P + PW))
-            else:
-                RN = S("rlast", h * PW, h * PW + PW); cp(RN, s3(2, "s3o"), "rout")
-                send("r", RN, S("rfin", h * PW, h * PW + PW))
+            TF, CH = PS(tl, 2, 4 * PW, 4), PS(tl, 3, 4 * PW, 4)
+            k = mm([(PS(tl, 0, 4 * PW), IDN, S("f0", 0, 4 * PW))], "fino", behind=[kyn])
+            mm([(CH, full("mB"), sm("sa2")), (CH, IDN, cst("c1")), (CH, full("mA"), sm("sa2")), (CH, NID, cst("c1")), (TF, full("q25"), sm("sa2"))], "finc", behind=[k])
+            byclass(TF, lambda k: hk("hz", k), "nz", [k])
+            mm([(TF, IDN, cst("c1")), (TF, NID, cst("c1"))], "finr", True)
+            scan(S("s4o", 4 * o, 4 * o + 4 * PW), PS(tl, 0, 4 * PW), S("s4", 4 * o, 4 * o + 4 * PW), ALU.mult, ALU.add)
+            RN = S("rout", oi, oi + PW)
+            cp(RN, s4(3, "s4o"))
+            send("r", RN, S("rin", oi + P, oi + P + PW))
         hs = range(NH); cur[0] = 0
         if t < V - 1:
             tl = "A%d" % t
@@ -445,21 +456,21 @@ def build_ops(par):
             offs = S("wou", 16 * a + i0 // 16, 16 * a + (i0 + n) // 16)
             cp(offs, S("ws", a * P + i0 + 15, a * P + i0 + n, 16))
             if t < V - 1: cp(IND("xw", 32 * i0, 32 * (i0 + n), offs), Y, "xw")
-            cp(IND("lw", 32 * i0, 32 * (i0 + n), offs), S("rout", t * P + i0, t * P + i0 + n) if t < V - 1 else S("rlast", i0, i0 + n), "lw")
+            cp(IND("lw", 32 * i0, 32 * (i0 + n), offs), S("rout", t * P + i0, t * P + i0 + n), "lw")
     cur[1] = V
     for h in range(NH):
         cur[0] = h
         v = "%d_%d" % (V, h); oi = V * P + h * PW
-        op("N", (0.0, 0), None, [], [S("rfin", h * PW, h * PW + PW)], "ar", "ar" + v, -1.0, sends["r%d_%d" % (V - 1, h)])
+        op("N", (0.0, 0), None, [], [S("rin", oi, oi + PW)], "ar", "ar" + v, -1.0, sends["r%d_%d" % (V - 1, h)])
+        cp(S("rfin", h * PW, h * PW + PW), S("rin", oi, oi + PW))
         op("N", (0.0, 0), None, [], [S("yin", oi, oi + PW)], "ay", "ay" + v, -1.0, sends["y%d_%d" % (V - 1, h)])
         dma("Y", HBM("yo", h * PW, h * PW + PW), S("yin", oi, oi + PW), "oo%d" % h, 2500)
         dma("Y", HBM("yj", h * PW, h * PW + PW), S("rfin", h * PW, h * PW + PW), "oj%d" % h, 2500)
     n = len(par["fin"]); w = W // n
     for j, e in enumerate(par["fin"]):
         cur[0] = j * NH // n
-        if e == "V": ts(S("l16", w * j, w * j + w), S("lw", w * j, w * j + w), -2048.0, None, ALU.add)
-        else: act(S("l16", w * j, w * j + w), S("lw", w * j, w * j + w), ACT.Identity, -2048.0)
-        mm([(PS("yz", 0, 256), hk("hj", c), S("l16", 256 * c, 256 * c + 256)) for c in range(j * w // 256, (j + 1) * w // 256)], j == 0, j == n - 1)
+        move(S("l16", w * j, w * j + w), S("lw", w * j, w * j + w), -2048.0, e)
+        mm([(PS("yz", 0, 256), hk("hj", c), S("l16", 256 * c, 256 * c + 256)) for c in range(j * w // 256, (j + 1) * w // 256)])
     act(S("yzf", 0, 256), PS("yz", 0, 256), ACT.Identity, 2048.0 * 136)
     dma("Y", HBM("yz"), S("yzf", 0, 256), "oyz", 2500)
     return ops
@@ -473,7 +484,9 @@ def price(ops, cost):
         elif e == "G": x = cost["rem"] if c == "rem" else float(n)
         elif e == "N": x = 0.0
         elif o["sem"]: x = 60.0
-        else: x = max(64.0, cost["fix"] + (20.0 if e == "S" else 0.0) + n * (cost[c] if isinstance(c, str) else c)) + (cost["self"] if o.get("drain") else 0.0)
+        elif isinstance(c, str): x = cost["gfix"] + (20.0 if e == "S" else 0.0) + n * cost[c]
+        else: x = max(64.0, cost["fix"] + (cost["sfix"] if e == "S" else 0.0) + n * c) + (cost["self"] if o.get("drain") else 0.0)
+        if e in "VSP" and not o["sem"]: x *= cost["all"]
         out.append((x, cost["net"] if e == "N" else o["lat"]))
     return out
 
@@ -487,7 +500,7 @@ def urgency(ops, par, cost, off):
     for k, o in enumerate(ops):
         for d in o["deps"]: succ[d].append(k)
         if o["after"] is not None: succ[o["after"]].append(k)
-    last = (V - 1) * par["T"] + par["delta"] + cost["net"] + 3000.0
+    last = (par["visits"] - 1) * par["T"] + par["delta"] + cost["net"] + 3000.0
     pr = [0.0] * n
     for k in range(n - 1, -1, -1):
         o = ops[k]
@@ -576,6 +589,151 @@ def best_order(ops, par, cost, off=None):
     return best, off
 
 
+def prepare(ops, costs):
+    n = len(ops); succ = [[] for _ in ops]; left = [0] * n; sets = []; users = {}
+    pre = [sorted(set(o["deps"]) | ({o["after"]} if o["after"] is not None else set())) for o in ops]
+    above = [0] * n
+    for k, o in enumerate(ops):
+        far = 0
+        for d in pre[k]: far |= above[d]
+        above[k] = far | sum(1 << d for d in pre[k])
+        pre[k] = [d for d in pre[k] if not far >> d & 1]
+        for d in pre[k]: succ[d].append(k)
+        for tl in o["ps"]: users[tl] = users.get(tl, 0) + 1
+    forms = (ops, [dict(o, **{x: o["alt"][x] for x in ("eng", "size", "fn")}) if "alt" in o else o for o in ops])
+    eng = [["VSPGYN".index(o["eng"]) for o in f] for f in forms]
+    for cost in costs:
+        pc = [price(f, cost) for f in forms]
+        gap = [[0.0 if b == 5 or a == b == 2 else cost["self"] if a == b else cost["hop"] for a in range(6)] for b in range(6)]
+        sets.append(([[c[0] for c in p] for p in pc], [c[1] for c in pc[0]], gap))
+    return succ, left, users, eng, sets, [o["ps"][0] if o["ps"] else None for o in ops], pre, forms
+
+
+def arrange(prep, key, eng, dmax):
+    users, ps, pre = prep[2], prep[5], prep[6]
+    n = len(key); rem = dict(users)
+    for k in range(n):
+        x = key[k]
+        for d in pre[k]:
+            if key[d] > x: x = key[d]
+        key[k] = x
+    bank = {}; last = [-1] * 8; fb = list(range(8)); order = []; extras = [-1] * n; held = []; done = [False] * n
+
+    def take(k):
+        if held:
+            for d in pre[k]:
+                if not done[d]: return False
+        tl = ps[k]
+        if tl:
+            b = bank.get(tl)
+            if b is None:
+                if len(fb) < (2 if tl[0] in "DKnAfy" else 1): return False
+                b = bank[tl] = fb.pop(0); extras[k] = last[b]
+            elif eng[last[b]] != eng[k]: extras[k] = last[b]
+            last[b] = k; rem[tl] -= 1
+            if rem[tl] == 0: fb.append(b)
+        order.append(k); done[k] = True
+        return True
+    for k in sorted(range(n), key=lambda k: key[k]):
+        if not take(k):
+            held.append(k)
+            continue
+        j = 0
+        while j < len(held):
+            if take(held[j]):
+                del held[j]; j = 0
+            else: j += 1
+    return None if held else (order, bank, extras)
+
+
+def timing(prep, which, order, extras, eng, form):
+    run, lat, gap = prep[4][which]; pre = prep[6]; n = len(eng)
+    free = [0.0] * 6; prev = [-1] * 6; fin = [0.0] * n; start = [0.0] * n; who = [-1] * n
+    for k in order:
+        e = eng[k]; s = free[e]; w = prev[e]; gp = gap[e]
+        for d in pre[k]:
+            x = fin[d] + gp[eng[d]]
+            if x > s: s = x; w = d
+        d = extras[k]
+        if d >= 0:
+            x = fin[d] + gp[eng[d]]
+            if x > s: s = x; w = d
+        start[k] = s; who[k] = w; prev[e] = k; s += run[form[k]][k]; free[e] = s; fin[k] = s + lat[k]
+    return max(fin), start, fin, who
+
+
+def improve(ops, par, costs, start):
+    prep = prepare(ops, costs); n = len(ops); seen = {}; slot = []; T = par["T"]
+    for o in ops:
+        ph = min(o["t"], 1) if o["t"] < V - 1 else o["t"]
+        kd = (o["t"], kind(o)); seen[kd] = seen.get(kd, 0) + 1; slot.append((ph, kind(o), seen[kd]))
+    names = sorted(set(slot)); num = {s: j for j, s in enumerate(names)}; slot = [num[s] for s in slot]
+    rs = [k for k in range(n) if ops[k]["nm"] == "sendr"]; pre = prep[6]; succ = prep[0]
+
+    def keys(start):
+        T = start[rs[3 * NH]] - start[rs[2 * NH]]; base = [min(o["t"], V - 1) * T for o in ops]; tau = [0.0] * len(names)
+        for k in range(n):
+            if ops[k]["t"] in (0, 3, V - 1, V): tau[slot[k]] = start[k] - base[k] + k * 1e-4
+        return base, tau
+    base, tau = keys(start); pick = [0] * len(names)
+    x = [par["seed"]]; free = [k for k in range(n) if "alt" in ops[k]]
+
+    def rnd():
+        x[0] = (x[0] * 1103515245 + 12345) % 2 ** 31
+        return (x[0] >> 8) / 2.0 ** 23
+
+    def value(base, tau, pick, than=None, slack=0.0):
+        form = [pick[s] for s in slot]; eng = [prep[3][f][k] for k, f in enumerate(form)]
+        a = arrange(prep, [b + tau[s] for b, s in zip(base, slot)], eng, par["dmax"])
+        if a is None or (than and a[0] == than[1][0] and form == than[3]): return None
+        ts = []; worse = 0.0
+        for w, c in enumerate(costs):
+            ts.append(timing(prep, w, a[0], a[2], eng, form))
+            if than:
+                worse += (ts[w][0] - than[2][w][0]) * c["weight"]
+                if worse > slack + par["hope"] * (len(costs) - 1 - w): return None
+        return sum(t[0] * c["weight"] for t, c in zip(ts, costs)), a, ts, form
+
+    def shift(new, k, to, near, sign, depth):
+        new[slot[k]] = to - base[k]
+        for d in near[k] if depth else ():
+            if (base[d] + new[slot[d]] - to) * sign > 0 and ops[d]["t"] == ops[k]["t"]: shift(new, d, to - sign, near, sign, depth - 1)
+    cur = best = value(base, tau, pick); deps = [set(p) for p in pre]
+    for it in range(par["moves"]):
+        heat = par["heat"] * (1.0 - it / par["moves"])
+        if it % par["again"] == 0:
+            b2, t2 = keys(cur[2][0][1]); r = value(b2, t2, pick)
+            if r is not None and r[0] <= cur[0] + heat: base, tau, cur = b2, t2, r
+        new = list(tau); other = pick; z = rnd()
+        if z < par["aimed"]:
+            end, st, fin, who = cur[2][int(rnd() * len(costs))]
+            k = fin.index(end); pairs = []
+            while who[k] >= 0:
+                if who[k] not in deps[k]: pairs.append((who[k], k))
+                k = who[k]
+            if not pairs: continue
+            p, k = pairs[int(rnd() * len(pairs))]; z = rnd()
+            if z < .2 and ("alt" in ops[p] or "alt" in ops[k]):
+                other = list(pick); other[slot[p if "alt" in ops[p] else k]] ^= 1
+            elif z < .6: shift(new, k, base[p] + tau[slot[p]] - 1.0 - 50.0 * rnd(), pre, 1.0, 3)
+            else: shift(new, p, base[k] + tau[slot[k]] + 1.0 + 50.0 * rnd(), succ, -1.0, 3)
+        elif z < par["aimed"] + .05:
+            other = list(pick); other[slot[free[int(rnd() * len(free))]]] ^= 1
+        else:
+            k = int(rnd() * n); z = (rnd() - .5) * par["reach"]
+            shift(new, k, base[k] + tau[slot[k]] + z, pre if z < 0 else succ, 1.0 if z < 0 else -1.0, 3)
+        r = value(base, new, other, cur, heat * rnd())
+        if r is None: continue
+        cur, tau, pick = r, new, other
+        if r[0] < best[0]: best = r
+    return [prep[7][best[3][k]][k] for k in range(n)], best
+
+
+def plan(par, costs):
+    ops = build_ops(par)
+    return improve(ops, par, costs, best_order(ops, par, costs[0])[0][3])
+
+
 PLAN = []
 
 
@@ -584,13 +742,17 @@ def rank_program(g, core, T, topo):
     if rank is None:
         return
     if not PLAN:
-        ops = build_ops(PAR)
-        PLAN.append((ops,) + best_order(ops, PAR, COST)[0])
-    ops, order, bank, extras = PLAN[0][:4]
+        PLAN.append(plan(PAR, COSTS))
+    ops = PLAN[0][0]; order, bank, extras = PLAN[0][1][1]
     nxt = T.cores[(rank + 1) % len(T.cores)]; prv = T.cores[(rank - 1) % len(T.cores)]
     rid, pid, _ = topo.addr(nxt)
     env = {"rid": rid, "pid": pid, "mask": topo.mask(core, nxt)}
     n_out, n_in = len(topo.engines(core, nxt)), len(topo.engines(prv, core))
+
+    todo = {}
+    for o in ops:
+        if o["eng"] == "P": todo[o["ps"][0]] = todo.get(o["ps"][0], 0) + 1
+    opened = set()
 
     def Q(name):
         return env[name] if name in env else T["pb%d" % bank[name]]
@@ -602,7 +764,7 @@ def rank_program(g, core, T, topo):
             mark[k] = (o["sem"], n_in, {}); top[o["sem"]] = n_in
             continue
         kn = known[e]
-        pre = set(o["deps"]) | set(extras[k])
+        pre = set(o["deps"]) | {extras[k]}
         if e == "V":
             pre.update(drain); drain[:] = [k] if o.get("drain") else []
         need = sorted((mark[d] for d in pre if d in mark and not (e == "P" and ops[d]["eng"] == "P")), key=lambda m: -m[1])
@@ -614,6 +776,8 @@ def rank_program(g, core, T, topo):
         for sem, val, clock in need:
             for s2, v2 in list(clock.items()) + [(sem, val)]:
                 if kn.get(s2, 0) < v2: kn[s2] = v2
+        if e == "P":
+            tl = o["ps"][0]; todo[tl] -= 1; env["ends"] = (tl not in opened, todo[tl] == 0); opened.add(tl)
         ins = o["fn"](g, T, Q)
         if o["sem"] == "remote":
             sent += n_out

@@ -8,8 +8,8 @@ PW = P // NH
 NC = 2
 KK = 16 // NC
 M4 = float((2 ** 23 + 1) * 4)
-M1, M32, M4096 = float(3 * 2 ** 22), float(3 * 2 ** 27), float(3 * 2 ** 34)
-PEN = float(2 ** 17)
+M1, M16, M32, M4096 = (float(3 * 2 ** 22 * n) for n in (1, 16, 32, 4096))
+PEN = float(2 ** 18)
 BIG = float(2 ** 22)
 SEG = 18
 
@@ -19,11 +19,12 @@ SCRATCH = {
     "rin": [(V + 1) * P, U16], "yin": [(V + 1) * P, B], "rout": [V * P, U16], "yout": [V * P, B], "rfin": [P, F],
     "wi": [8, I32], "yzf": [256, F], "ci": [8, I32], "cf": [32, F], "rm": [16, F],
     "ioc": [144, F], "iob": [128, F], "iom": [128, F], "ioj": [64, F], "iog": [64, F], "tmp": [256, F],
-    "hh": [144, B], "hz": [144, B], "hj": [144, H16], "ba": [16 * 144, H16], "kc": [128 * NH, B], "pen": [128, B],
-    "sel": [128, F], "acc": [8, F], "o16": [16, B], "o512": [8, B], "f0": [4 * PW, B], "rs8": [64, F], "rs16": [128, F],
+    "hh": [144, B], "hz": [144, B], "hj": [144, H16], "ba": [16 * 144, H16], "kc": [192, B], "pen": [256, B],
+    "sel": [128, F], "acc": [8, F], "o16": [16, B], "o512": [16, B], "f0": [4 * PW, B], "rs8": [128, F], "rs16": [128, F],
+    "cm": [512, B], "c16": [512, B], "sc": [2 * NH * 128, F],
     "thr": [8 * V, F], "ai": [16, I32], "wou": [32, U16], "ws": [2 * P, F], "wp": [128, H16], "wn": [128, H16],
-    "lg": [2 * 2048, H16], "dr": [2 * NH * 144, B], "nn": [2 * 2 * P, B], "nt": [2 * 2 * P, B], "qq": [2 * NH * 8, I32],
-    "zz": [2 * NH * 128, I32], "zb": [2 * NH * 128, B], "keep": [128, F],
+    "lg": [2 * 2048, H16], "dr": [2 * NH * 144, B], "nn": [2 * 2 * P, B], "nt": [2 * 2 * P, B], "qq": [2 * NH * 256, F],
+    "zb": [2 * NH * 128, B],
     "s4": [2 * 4 * P, I32], "s4o": [2 * 4 * P, F],
 }
 for _n in ("idn", "nid", "i16", "n16", "i64", "q25", "nbo", "bo", "tri", "mA", "mB", "w5p", "w5n", "wb", "c1", "c32", "c4096", "cc", "c155", "c2048"):
@@ -31,7 +32,7 @@ for _n in ("idn", "nid", "i16", "n16", "i64", "q25", "nbo", "bo", "tri", "mA", "
 for _n in ("xg", "zg", "ad", "nx", "dm", "az", "nz", "dx", "dz"):
     SCRATCH[_n] = [2 * 2048, B]
 for _n, _d in (("nu", U16), ("nm", F), ("kp", F), ("good", B), ("cnt", B), ("sa", B), ("oh", B), ("yy", B), ("nl", B), ("sa2", B),
-               ("pi", I32), ("pj", I32), ("far", I32), ("sc", F)):
+               ("pi", I32), ("pj", I32)):
     SCRATCH[_n] = [2 * P, _d]
 SCRATCH = {_n: ("sbuf", [128, _v[0]], _v[1]) for _n, _v in SCRATCH.items()}
 for _n in range(8):
@@ -49,10 +50,10 @@ PAR = {"xg": ("SS", "SS"), "lg": ("SS", "SS"), "zg": ("SS", "SS"),
 PAR.update({'zm': (2, 1), 'T': 19000., 'zs': ((0, 0), (0, 1)), 'xs': ((0, 1), (0, 1))})
 COST = {"fix": 70.0, "gam": 1.5, "sca": 3.5, "pe": 0.6, "pfix": 30.0, "hop": 180.0, "self": 110.0, "net": 4500.0, "rem": 900.0, "all": 1.0, "weight": .5,
         "gfix": 70.0, "sfix": 20.0}
-COSTS = [dict(COST, fix=60.0, sfix=0.0, gfix=60.0, pfix=0.0, hop=200.0, self=200.0, net=3000.0, weight=.4),
-         dict(COST, fix=0.0, sfix=0.0, gfix=60.0, pfix=0.0, pe=.6, hop=260.0, self=260.0, net=2800.0, rem=700.0, weight=.3),
-         dict(COST, fix=30.0, sfix=0.0, gfix=60.0, pfix=0.0, pe=.55, hop=250.0, self=250.0, gam=1.9, sca=5.0, all=1.35, weight=.25)]
-PAR.update({"rounds": 200, "moves": 30000, "heat": 300.0, "aimed": .8, "visits": V, "short": 4, "dq": 1, "reach": 1500.0, "again": 300, "hope": 100.0, "delta": 3000.0, "T": 17000.0})
+COST.update({"fix": 0.0, "sfix": 0.0, "gfix": 60.0, "pfix": 0.0, "hop": 260.0, "self": 260.0, "net": 2000.0, "rem": 600.0})
+COSTS = [COST, dict(COST, fix=15.0, hop=300.0, self=300.0, gam=1.9, sca=5.0, all=1.35, net=3500.0, rem=900.0, weight=.35)]
+PAR.update({"rounds": 200, "moves": 30000, "heat": 300.0, "aimed": .8, "visits": V, "short": 4, "dq": 4, "zq": 4, "reach": 1500.0, "again": 300, "hope": 100.0, "delta": 3000.0, "T": 16000.0,
+            "deltas": (2500.0, 3000.0, 3500.0, 4000.0), "few": 5000, "rounds": 100, "moves": 40000, "zm": ((2, 1), (2, 1)), "zs": ((0, 1), (0, 1)), "xs": ((1, 1), (1, 1))})
 
 
 def S(name, a, b, s=1, p0=0, p1=128): return ("s", name, p0, p1, a, b, s)
@@ -216,8 +217,8 @@ def build_ops(par):
     ts(col(7), col(1), 0.0, None, ALU.is_equal)
     ts(col(8), col(7), 17.0, -1.0, ALU.mult, ALU.add)
     tt(col(9), col(7), col(1), ALU.subtract)
-    ts(col(14), col(9), -256.0, -128.0, ALU.mult, ALU.add)
-    for nme, sc in (("idn", 1.0), ("nid", -1.0), ("i16", 16.0), ("n16", -16.0), ("i64", 64.0), ("q25", .25)):
+    ts(col(14), col(9), -.25, 7.875, ALU.mult, ALU.add)
+    for nme, sc in (("idn", 1.0), ("nid", -1.0), ("n16", -16.0), ("i64", 64.0), ("q25", .25)):
         ts(full(nme), full("ioc"), col(0), sc, ALU.is_equal, ALU.mult)
     ts(S("hh", 0, 144), S("ioc", 0, 144), col(3), None, ALU.is_equal)
     ts(S("hz", 0, 144), S("hh", 0, 144), -1.0 / 32, None, ALU.mult)
@@ -230,22 +231,23 @@ def build_ops(par):
     ts(S("tmp", 0, 128), full("iom"), col(1), -1.0, ALU.is_gt, ALU.mult)
     tt(S("tmp", 128, 256), S("tmp", 0, 128), full("idn"), ALU.add)
     ts(S("tmp", 128, 256, 16), S("ioc", 0, 8), 0.0, col(8), ALU.mult, ALU.add)
-    tt(full("tri"), S("tmp", 128, 256), full("bo"), ALU.mult)
+    ts(S("tmp", 0, 128), full("bo"), .25, None, ALU.mult)
+    tt(full("tri"), S("tmp", 128, 256), S("tmp", 0, 128), ALU.mult)
     for a in (0, 8):
         cp(S("o16", a, a + 8), S("bo", 0, 128, 16))
-    ts(S("o512", 0, 8), S("bo", 0, 128, 16), 512.0, None, ALU.mult)
+        ts(S("o512", a, a + 8), S("bo", 0, 128, 16), 512.0, None, ALU.mult)
     for c in range(NC):
         ts(col(15 + c), col(0), -float(c), None, ALU.add)
-        ts(S("pen", 64 * c, 64 * c + 64), S("iog", 0, 64), col(15 + c), PEN, ALU.is_equal, ALU.mult)
-    for h in range(NH):
-        v0, v1 = (0.0 if par["ds"][h][c] else -240.0 for c in range(NC))
-        ts(col(18 + h), col(4), (v1 - v0) / 32, v0, ALU.mult, ALU.add)
-        tt(col(20 + h), col(18 + h), col(4), ALU.add)
-        ts(S("kc", 128 * h, 128 * h + 64), S("ioj", 0, 64), col(20 + h), None, ALU.add)
-        ts(S("kc", 128 * h + 64, 128 * h + 128), S("ioj", 0, 64), 0.0, col(18 + h), ALU.mult, ALU.add)
+        for a in (0, 64):
+            ts(S("pen", 128 * c + a, 128 * c + a + 64), S("iog", 0, 64), col(15 + c), PEN, ALU.is_equal, ALU.mult)
+    ts(S("kc", 0, 64), S("ioj", 0, 64), col(4), None, ALU.add)
+    ts(S("kc", 64, 128), S("ioj", 0, 64), col(4), -240.0, ALU.add, ALU.add)
+    ms(S("kc", 128, 192), -240.0)
     ms(S("dr", 0, 2 * NH * 144), 0.0)
-    ms(S("zz", 0, 2 * NH * 128), 0)
-    ts(full("keep"), full("iom"), 0.0, None, ALU.not_equal)
+    ms(S("qq", 0, 2 * NH * 256), 0.0)
+    n = KK // par["dq"] * PW
+    ts(S("cm", 0, n), S("qq", 0, n), col(14), None, ALU.add)
+    ms(S("c16", 0, n), M16)
     for nme, v in (("c1", M1), ("c32", M32), ("c4096", M4096), ("c155", 15.5), ("c2048", 2048.0)):
         ms(full(nme), v)
     for j, v in enumerate((0.0, 1.0, 39.0 / 64, 39.0 / 128)):
@@ -253,10 +255,11 @@ def build_ops(par):
     ts(col(17), col(1), 1.0, -0.5, ALU.is_equal, ALU.mult)
     ts(col(22), col(7), 2048.0, col(17), ALU.mult, ALU.add)
     ts(full("cc"), full("iom"), 0.0, col(22), ALU.mult, ALU.add)
-    lo, st = 1792.0, -512.0
+    lo, st = -1152.0, -256.0
     ts(full("sel"), full("iom"), 0.0, col(7), ALU.mult, ALU.add)
     ms(S("thr", 0, 1), lo)
-    ts(S("rs8", 0, 64), S("ioj", 0, 64), 0.0, BIG, ALU.is_equal, ALU.mult)
+    for a in (0, 64):
+        ts(S("rs8", a, a + 64), S("ioj", 0, 64), 0.0, BIG, ALU.is_equal, ALU.mult)
     ts(full("rs16"), full("iom"), 0.0, -BIG, ALU.is_equal, ALU.mult)
     ts(S("tmp", 0, 128), full("iom"), col(1), None, ALU.is_equal)
     ts(S("tmp", 128, 256), full("ioc"), 32.0, 32768.0, ALU.mult, ALU.add)
@@ -313,6 +316,11 @@ def build_ops(par):
             def fill(tl, lhs, Y, n=KK):
                 return mm([(PS(tl, j, n * PW, n), lhs, Y) for j in range(n)], "fill" + tl[:2])
 
+            def against(out, src, c, tl, q, o):
+                its = [(S(out, ob + 512 * c + j, ob + 512 * c + 512, q), S(src, ob + c + NC * j, ob + n16, NC * q), PS(tl, 0, 512 // q)) for j in range(q)]
+                op("V", (1.0, 512), lambda g, T, Q: [g.vector.tensor_tensor(ap(T, Q, x), ap(T, Q, y), ap(T, Q, z), o) for x, y, z in its],
+                   [jc(src, c), its[0][2]], [cls(out, c)], out)
+
             def near(out, d): ts(out, d, M4, M4, ALU.add, ALU.is_equal)
 
             def test(out, ab, d, way):
@@ -323,7 +331,7 @@ def build_ops(par):
             xp = gather("xg", "xw", "rin", oi)
             cp(s4(3), RU, "rf")
             ts(sm("kp"), RU, 32.0, col(5), ALU.mult, ALU.add)
-            if par["xm"][h] == 2: fill("Dx" + v, IDN, YIN)
+            if par["xm"][h] == 2: fill("Dx" + v, IDN, YIN, KK // par["zq"])
             for c in range(NC):
                 if par["xm"][h] == 1:
                     tl = "Dx%s_%d" % (v, c); d = PS(tl, 0, 512)
@@ -332,7 +340,7 @@ def build_ops(par):
                         mm([(PS(tl, KK * i0, KK * i1), IDN, jc("xg", c, i0, i1))], behind=[k])
                 else:
                     d = cls("dx", c)
-                    tt(d, jc("xg", c), PS("Dx" + v, 0, 512), ALU.subtract)
+                    against("dx", "xg", c, "Dx" + v, par["zq"], ALU.subtract)
                 test(cls("nx", c), cls("ad", c), d, par["xs"][h][c])
                 if par["xs"][h][c] == 0: act(cls("ad", c), d, ACT.Abs)
             gather("lg", "lw", "rin", oi)
@@ -350,48 +358,38 @@ def build_ops(par):
             tl = "nb" + v
             byclass(PS(tl, 0, PW), lambda k: IDN, "nx")
             either(lambda: act(sm("good"), PS(tl, 0, PW), ACT.Sigmoid, -1920.0, 256.0), lambda: ts(sm("good"), PS(tl, 0, PW), 8.0, None, ALU.is_ge))
-            tl = "pre" + v
-            mm([(PS(tl, 0, PW), full("tri"), sm("good"))])
-            either(lambda: act(sm("oh"), PS(tl, 0, PW), ACT.Sigmoid, col(14), 256.0), lambda: ts(sm("oh"), PS(tl, 0, PW), col(9), None, ALU.is_gt))
+            tl = "Dm" + v; n = KK // par["dq"]
+            mm([(PS(tl, 0, n * PW), IDN, cst("cm", n * PW))] + [(PS(tl, j, n * PW, n), full("tri"), sm("good")) for j in range(n)]
+               + [(PS(tl, 0, n * PW), lhs, cst("c16", n * PW)) for lhs in (IDN, NID)])
+            for c in range(NC):
+                against("dm", "xg", c, tl, par["dq"], ALU.max)
+            either(lambda: act(sm("oh"), PS(tl, 0, n * PW, n), ACT.Identity), lambda: cp(sm("oh"), PS(tl, 0, n * PW, n)))
             tl = "cnt" + v
             byclass(PS(tl, 0, PW), lambda k: hk("hh", k), "nx")
-            act(sm("sa"), PS(tl, 0, PW), ACT.Sign, -11.5)
+            either(lambda: act(sm("sa"), PS(tl, 0, PW), ACT.Sigmoid, -2944.0, 256.0), lambda: ts(sm("sa"), PS(tl, 0, PW), 12.0, None, ALU.is_ge))
             move(sm("cnt"), PS(tl, 0, PW))
             tl = "cT" + v
             mm([(PS(tl, 0, PW), full("bo"), sm("sa"))])
             act(sm("nl"), PS(tl, 0, PW), ACT.Sigmoid, S("thr", 8 * t, 8 * t + 1), 256.0, S("acc", o3, o3 + 1))
             tl = "ya" + v
-            mm([(PS(tl, 0, PW), full("i16"), sm("oh")), (PS(tl, 0, PW), full("i64"), sm("nl"))])
+            mm([(PS(tl, 0, PW), IDN, sm("oh")), (PS(tl, 0, PW), full("i64"), sm("nl"))])
             tt(sm("yy"), YIN, PS(tl, 0, PW), ALU.min)
-            dq = par["dq"]
-            if 0 in par["ds"][h]: fill("Dm" + v, full("i16"), sm("oh"), KK // dq)
-            for c in range(NC):
-                if par["ds"][h][c]:
-                    tl = "Dm%s_%d" % (v, c)
-                    mm([(PS(tl, 0, 512), IDN, jc("xg", c))])
-                    fill(tl, full("n16"), sm("oh"))
-                    act(cls("dm", c), PS(tl, 0, 512), ACT.Relu)
-                else:
-                    for j in range(dq):
-                        tt(S("dm", ob + 512 * c + j, ob + 512 * c + 512, dq), S("xg", ob + c + NC * j, ob + n16, NC * dq), PS("Dm" + v, 0, 512 // dq), ALU.max)
             tl = "K" + v
 
             def both(name, j): return S(name, ob + j, ob + n16, KK)
-            k = mm([(PS(tl, 0, 128), IDN, S("kc", 128 * h, 128 * h + 128))] + [(PS(tl, j, 64, 8), both("ad", j), S("o512", 0, 8)) for j in range(KK)], "Ka")
-            mm([(PS(tl, 0, 64, 1, PW * c, PW * c + PW), sm("sa"), S("pen", 64 * c, 64 * c + 64)) for c in range(NC)], "Kp", behind=[k])
-            mm([(PS(tl, j, 128, 8), both("dm", j), S("o16", 0, 16)) for j in range(KK)], "Kd", True)
-            scan(sm("sc"), S("rs8", 0, 64), PS(tl, 0, 64), ALU.add, ALU.min)
-            od = 144 * o3 + 8; oq = 128 * o3
-            move(S("dr", od, od + 128, 2), PS(tl, 64, 128))
-            least = S("qq", 8 * o3, 8 * o3 + 8, 1, 0, PW)
-            k = tt(least, S("sc", o + 7, o + PW, 8, 0, PW), S("sc", o + 7, o + PW, 8, PW, 128), ALU.min)
+            k = mm([(PS(tl, 0, 192), IDN, S("kc", 0, 192))] + [(PS(tl, j, 128, 8), both("ad", j), S("o512", 0, 16)) for j in range(KK)], "Ka")
+            mm([(PS(tl, 0, 128, 1, PW * c, PW * c + PW), sm("sa"), S("pen", 128 * c, 128 * c + 128)) for c in range(NC)], "Kp", behind=[k])
+            mm([(PS(tl, 64 + j, 192, 8), both("dm", j), S("o16", 0, 16)) for j in range(KK)], "Kd", True)
+            oq = 128 * o3; od = 144 * o3 + 8
+            scan(S("sc", oq, oq + 128), full("rs8"), PS(tl, 0, 128), ALU.add, ALU.min)
+            move(S("dr", od, od + 128, 2), PS(tl, 128, 192))
+            k = tt(S("qq", 2 * oq, 2 * oq + 256, 16, 0, PW), S("sc", oq + 7, oq + 128, 8, 0, PW), S("sc", oq + 7, oq + 128, 8, PW, 128), ALU.min)
             ops[k]["drain"] = True
-            ts(S("zz", oq, oq + 128, 16, 0, PW), least, 31, None, ALU.bitwise_and)
             ZB = S("zb", oq, oq + 128, 1, 0, PW)
-            scan(ZB, S("keep", 0, 128, 1, 0, PW), S("zz", oq, oq + 128, 1, 0, PW), ALU.mult, ALU.add)
+            scan(ZB, S("qq", 2 * oq + 128, 2 * oq + 256, 1, 0, PW), S("qq", 2 * oq, 2 * oq + 128, 1, 0, PW), ALU.max, ALU.subtract)
             IW, NW = S("idn", 0, PW, 1, 0, PW), S("nid", 0, PW, 1, 0, PW)
             tl = "del" + v
-            mm([(PS(tl, 0, PW), full("n16"), sm("oh")), (PS(tl, 0, PW), full("n16"), sm("nl"))])
+            mm([(PS(tl, 0, PW), NID, sm("oh")), (PS(tl, 0, PW), full("n16"), sm("nl"))])
             mm([(PS(tl, 0, PW), ZB, IW)], "delz")
             kyn = tt(YN, sm("yy"), PS(tl, 0, PW), ALU.max)
 
@@ -420,15 +418,15 @@ def build_ops(par):
             tt(sm("pi"), s4(3), PS(tl, 0, PW), ALU.mult)
             tt(sm("pj"), sm("pi"), sm("kp"), ALU.add)
             ts(s4(0), sm("pj"), 5, W - 1, ALU.arith_shift_right, ALU.bitwise_and, "far")
-            if par["zm"][h] == 2: fill("Dz" + v, IDN, YN)
+            if 2 in par["zm"][h]: fill("Dz" + v, IDN, YN, KK // par["zq"])
             for c in range(NC):
-                if par["zm"][h] == 1:
+                if par["zm"][h][c] == 1:
                     tl = "Dz%s_%d" % (v, c); d = PS(tl, 0, 512)
                     mm([(d, IDN, jc("zg", c))])
                     fill(tl, NID, YN)
                 else:
                     d = cls("dz", c)
-                    tt(d, jc("zg", c), PS("Dz" + v, 0, 512), ALU.subtract)
+                    against("dz", "zg", c, "Dz" + v, par["zq"], ALU.subtract)
                 test(cls("nz", c), cls("az", c), d, par["zs"][h][c])
             tl = "fin" + v
             TF, CH = PS(tl, 2, 4 * PW, 4), PS(tl, 3, 4 * PW, 4)
@@ -485,7 +483,7 @@ def price(ops, cost):
         elif e == "N": x = 0.0
         elif o["sem"]: x = 60.0
         elif isinstance(c, str): x = cost["gfix"] + (20.0 if e == "S" else 0.0) + n * cost[c]
-        else: x = max(64.0, cost["fix"] + (cost["sfix"] if e == "S" else 0.0) + n * c) + (cost["self"] if o.get("drain") else 0.0)
+        else: x = max(64.0, cost["fix"] + (cost["sfix"] if e == "S" else 0.0) + n * c)
         if e in "VSP" and not o["sem"]: x *= cost["all"]
         out.append((x, cost["net"] if e == "N" else o["lat"]))
     return out
@@ -605,7 +603,7 @@ def prepare(ops, costs):
     for cost in costs:
         pc = [price(f, cost) for f in forms]
         gap = [[0.0 if b == 5 or a == b == 2 else cost["self"] if a == b else cost["hop"] for a in range(6)] for b in range(6)]
-        sets.append(([[c[0] for c in p] for p in pc], [c[1] for c in pc[0]], gap))
+        sets.append(([[c[0] for c in p] for p in pc], [c[1] for c in pc[0]], gap, [cost["self"] if o.get("drain") else 0.0 for o in ops]))
     return succ, left, users, eng, sets, [o["ps"][0] if o["ps"] else None for o in ops], pre, forms
 
 
@@ -647,7 +645,7 @@ def arrange(prep, key, eng, dmax):
 
 
 def timing(prep, which, order, extras, eng, form):
-    run, lat, gap = prep[4][which]; pre = prep[6]; n = len(eng)
+    run, lat, gap, hold = prep[4][which]; pre = prep[6]; n = len(eng)
     free = [0.0] * 6; prev = [-1] * 6; fin = [0.0] * n; start = [0.0] * n; who = [-1] * n
     for k in order:
         e = eng[k]; s = free[e]; w = prev[e]; gp = gap[e]
@@ -658,11 +656,11 @@ def timing(prep, which, order, extras, eng, form):
         if d >= 0:
             x = fin[d] + gp[eng[d]]
             if x > s: s = x; w = d
-        start[k] = s; who[k] = w; prev[e] = k; s += run[form[k]][k]; free[e] = s; fin[k] = s + lat[k]
+        start[k] = s; who[k] = w; prev[e] = k; s += run[form[k]][k]; free[e] = s + hold[k]; fin[k] = s + lat[k]
     return max(fin), start, fin, who
 
 
-def improve(ops, par, costs, start):
+def improve(ops, par, costs, start, form=()):
     prep = prepare(ops, costs); n = len(ops); seen = {}; slot = []; T = par["T"]
     for o in ops:
         ph = min(o["t"], 1) if o["t"] < V - 1 else o["t"]
@@ -676,6 +674,7 @@ def improve(ops, par, costs, start):
             if ops[k]["t"] in (0, 3, V - 1, V): tau[slot[k]] = start[k] - base[k] + k * 1e-4
         return base, tau
     base, tau = keys(start); pick = [0] * len(names)
+    for k, f in enumerate(form): pick[slot[k]] = f
     x = [par["seed"]]; free = [k for k in range(n) if "alt" in ops[k]]
 
     def rnd():
@@ -730,8 +729,12 @@ def improve(ops, par, costs, start):
 
 
 def plan(par, costs):
-    ops = build_ops(par)
-    return improve(ops, par, costs, best_order(ops, par, costs[0])[0][3])
+    ops = build_ops(par); best = None
+    for seed, delta in enumerate(par["deltas"]):
+        one = dict(par, seed=par["seed"] + seed, delta=delta, moves=par["few"])
+        r = improve(ops, one, costs, best_order(ops, one, costs[0])[0][3])
+        if best is None or r[1][0] < best[1][0]: best = r
+    return improve(ops, dict(par, heat=par["heat"] / 2), costs, best[1][2][0][1], best[1][3])
 
 
 PLAN = []
@@ -784,7 +787,9 @@ def rank_program(g, core, T, topo):
         elif o["sem"]:
             ins.then_inc(T.sem[o["sem"]], 16); mark[k] = (o["sem"], 16, dict(kn)); top[o["sem"]] = 16
         else:
-            count[e] += 1; ins.then_inc(T.sem["c" + e], 1); mark[k] = ("c" + e, count[e], dict(kn)); top["c" + e] = count[e]
+            for x in ins if isinstance(ins, list) else [ins]:
+                count[e] += 1; x.then_inc(T.sem["c" + e], 1)
+            mark[k] = ("c" + e, count[e], dict(kn)); top["c" + e] = count[e]
     g.wait_ge(T.sem.sent, sent)
     for sem, val in top.items():
         if sem[0] in "co": g.wait_ge(T.sem[sem], val)

@@ -1,4 +1,4 @@
-from concourse.mybir import dt, AluOpType, ActivationFunctionType
+from concourse.mybir import AluOpType, ActivationFunctionType, AxisListType
 
 ALU = AluOpType
 ACT = ActivationFunctionType
@@ -16,18 +16,18 @@ SEG = 18
 B, F, I32, U16, H16 = "bfloat16", "float32", "int32", "uint16", "float16"
 SCRATCH = {
     "xw": [W, B], "li": [W, I32], "lw": [W, F], "l16": [W, H16],
-    "rin": [(V + 1) * P, U16], "yin": [(V + 1) * P, B], "rout": [V * P, U16], "yout": [V * P, B], "rfin": [P, F],
+    "rin": [(V + 1) * P, U16], "yin": [(V + 1) * P, B], "rout": [V * P, U16], "yout": [V * P, B], "rfin": [P, F], "rlast": [P, F],
     "wi": [8, I32], "yzf": [256, F], "ci": [8, I32], "cf": [32, F], "rm": [16, F],
-    "ioc": [144, F], "iob": [128, F], "iom": [128, F], "ioj": [64, F], "iog": [64, F], "tmp": [256, F],
-    "hh": [144, B], "hz": [144, B], "hj": [144, H16], "ba": [16 * 144, H16], "kc": [192, B], "pen": [256, B],
-    "sel": [128, F], "acc": [8, F], "o16": [16, B], "o512": [16, B], "f0": [4 * PW, B], "rs8": [128, F], "rs16": [128, F],
+    "ioc": [144, B], "iob": [128, B], "iom": [128, B], "ioj": [64, B], "tmp": [1312, B], "nc": [16 * 144, B], "iok": [288, B], "cm8": [128, B], "tf": [256, F], "ji": [P, I32],
+    "hh": [144, B], "hz": [144, B], "hj": [144, H16], "ba": [16 * 144, B], "kc": [192, B], "pen": [256, B],
+    "sel": [128, B], "acc": [8, F], "o16": [16, B], "o512": [16, B], "f0": [4 * PW, B], "rs8": [128, F], "rs16": [128, F],
     "cm": [512, B], "c16": [512, B], "sc": [2 * NH * 128, F],
     "thr": [8 * V, F], "ai": [16, I32], "wou": [32, U16], "ws": [2 * P, F], "wp": [128, H16], "wn": [128, H16],
     "lg": [2 * 2048, H16], "dr": [2 * NH * 144, B], "nn": [2 * 2 * P, B], "nt": [2 * 2 * P, B], "qq": [2 * NH * 256, F],
     "zb": [2 * NH * 128, B],
     "s4": [2 * 4 * P, I32], "s4o": [2 * 4 * P, F],
 }
-for _n in ("idn", "nid", "i16", "n16", "i64", "q25", "nbo", "bo", "tri", "mA", "mB", "w5p", "w5n", "wb", "c1", "c32", "c4096", "cc", "c155", "c2048"):
+for _n in ("idn", "nid", "n16", "i64", "q25", "nbo", "c32", "bo", "tri", "mA", "mB", "w5p", "w5n", "wb", "c1", "c4096", "cc", "c155", "c2048"):
     SCRATCH[_n] = [128, B]
 for _n in ("xg", "zg", "ad", "nx", "dm", "az", "nz", "dx", "dz"):
     SCRATCH[_n] = [2 * 2048, B]
@@ -37,6 +37,7 @@ for _n, _d in (("nu", U16), ("nm", F), ("kp", F), ("good", B), ("cnt", B), ("sa"
 SCRATCH = {_n: ("sbuf", [128, _v[0]], _v[1]) for _n, _v in SCRATCH.items()}
 for _n in range(8):
     SCRATCH["pb%d" % _n] = ("psum", [128, 512], F)
+CUTS = (0, 1536, 2816, 3712, W)
 LCH = 4
 SEMAPHORES = (["cV", "cS", "cP", "cG", "sent", "ljur", "lown", "lwgt", "lx", "oyz"] + ["ll%d" % j for j in range(LCH)]
               + ["oj%d" % h for h in range(NH)] + ["oo%d" % h for h in range(NH)]
@@ -51,9 +52,11 @@ PAR.update({'zm': (2, 1), 'T': 19000., 'zs': ((0, 0), (0, 1)), 'xs': ((0, 1), (0
 COST = {"fix": 70.0, "gam": 1.5, "sca": 3.5, "pe": 0.6, "pfix": 30.0, "hop": 180.0, "self": 110.0, "net": 4500.0, "rem": 900.0, "all": 1.0, "weight": .5,
         "gfix": 70.0, "sfix": 20.0}
 COST.update({"fix": 0.0, "sfix": 0.0, "gfix": 60.0, "pfix": 0.0, "hop": 260.0, "self": 260.0, "net": 2000.0, "rem": 600.0})
-COSTS = [COST, dict(COST, fix=15.0, hop=300.0, self=300.0, gam=1.9, sca=5.0, all=1.35, net=3500.0, rem=900.0, weight=.35)]
+COSTS = [COST, dict(COST, fix=15.0, hop=300.0, self=300.0, gam=2.0, sca=5.5, all=1.3, net=3500.0, rem=900.0, weight=.35)]
 PAR.update({"rounds": 200, "moves": 30000, "heat": 300.0, "aimed": .8, "visits": V, "short": 4, "dq": 4, "zq": 4, "reach": 1500.0, "again": 300, "hope": 100.0, "delta": 3000.0, "T": 16000.0,
-            "deltas": (2500.0, 3000.0, 3500.0, 4000.0), "few": 5000, "rounds": 100, "moves": 40000, "zm": ((2, 1), (2, 1)), "zs": ((0, 1), (0, 1)), "xs": ((1, 1), (1, 1))})
+            "deltas": (2500.0, 3000.0, 3500.0, 4000.0), "few": 5000, "rounds": 100, "moves": 40000, "zm": ((2, 1), (2, 1)), "zs": ((0, 1), (0, 1)), "xs": ((1, 1), (1, 1)),
+            "conv": 1, "far": .3, "dn": 4, "zn": 4, "xs": ((0, 1), (0, 1)), "heat": 2000.0, "deltas": (3000.0,), "few": 1000,
+            "zm": ((1, 2), (1, 2)), "zs": ((0, 0), (0, 0)), "stages": ((5, 50000, 1000.0, False), (3, 30000, 300.0, True), (V, 10000, 100.0, False))})
 
 
 def S(name, a, b, s=1, p0=0, p1=128): return ("s", name, p0, p1, a, b, s)
@@ -65,7 +68,7 @@ def PS(tile, a, b, s=1, p0=0, p1=128): return ("p", tile, p0, p1, a, b, s)
 def IND(win, a, b, offs): return ("i", win, 0, 128, a, b, offs)
 
 
-def Z3(a, b, c0, c1): return ("3", "zb", 0, PW, a, b, (c0, c1))
+def Y3(a, b, c0, c1): return ("3", "yb", 0, 128, a, b, (c0, c1))
 
 
 def HBM(name, a=None, b=None): return ("d", name, 0, 128, a, b, 1)
@@ -95,7 +98,7 @@ def places(x):
     k, name, p0, p1, a, b, s = x
     if k == "p": return [("ps " + name, 1)]
     if k == "i": return [(name, ((1 << (b - a)) - 1) << a)] + places(s)
-    if k == "3": return [(name, ((1 << (b - a)) - 1) << a)]
+    if k == "3": return [(name, sum(((1 << (s[1] - s[0])) - 1) << (16 * j + s[0]) for j in range(a, b)))]
     if (a, b, s) not in MASKS: MASKS[(a, b, s)] = sum(1 << j for j in range(a, b, s))
     return [(name, MASKS[(a, b, s)])]
 
@@ -151,8 +154,8 @@ def build_ops(par):
 
     def act(out, in_, func, bias=0.0, scale=1.0, acc=None, nm=None):
         def fn(g, T, Q):
-            return g.scalar.activation(ap(T, Q, out), ap(T, Q, in_), func, bias=ap(T, Q, bias), scale=scale, accum_out=ap(T, Q, acc) if acc else None)
-        return op("S", rate(out, in_, 1.0), fn, [in_, bias], [out] + ([acc] if acc else []), nm or out[1])
+            return g.scalar.activation(ap(T, Q, out), ap(T, Q, in_), func, bias=ap(T, Q, bias), scale=ap(T, Q, scale), accum_out=ap(T, Q, acc) if acc else None)
+        return op("S", rate(out, in_, 1.0), fn, [in_, bias, scale], [out] + ([acc] if acc else []), nm or out[1])
 
     def mm(items, nm=None, closes=False, behind=()):
         def fn(g, T, Q):
@@ -181,31 +184,44 @@ def build_ops(par):
         def fn(g, T, Q): return (g.sync if q == "Y" else g.scalar).dma_start(ap(T, Q, out), ap(T, Q, in_))
         return op(q, (0.0, 0), fn, [in_], [out], sem, sem, lat)
 
-    def iota(name, n, pat, cm):
+    def iota(name, n, pat, cm, a=0):
         def fn(g, T, Q):
-            if SCRATCH[name][2] == I32: return g.iota(T[name][:, 0:n], pat, 0, cm)
-            return g.iota(T[name][:, 0:n], pat, 0, cm, allow_small_or_imprecise_dtypes=True)
-        op("G", ("g", 160 + 2 * n), fn, [], [S(name, 0, n)], name)
+            if SCRATCH[name][2] == I32: return g.iota(T[name][:, a:a + n], pat, 0, cm)
+            return g.iota(T[name][:, a:a + n], pat, 0, cm, allow_small_or_imprecise_dtypes=True)
+        op("G", ("g", 160 + 2 * n), fn, [], [S(name, a, a + n)], name)
 
     def full(name): return S(name, 0, 128)
 
-    dma("Y", S("li", 0, P), HBM("jur"), "ljur", 2500)
-    dma("Y", S("xw", 0, W), HBM("xc"), "lx", 5000)
+    def lin(out, in_, scale, bias=0.0):
+        return either(lambda: act(out, in_, ACT.Identity, bias, scale), lambda: ts(out, in_, scale, bias, ALU.mult, ALU.add))
+
+    def const(out, v):
+        return either(lambda: act(out, S("ioc", 0, width(out)), ACT.Identity, v, 0.0), lambda: ms(out, v), "V")
+
+    dma("Y", S("ji", 0, P), HBM("jur"), "ljur", 2500)
     dma("S", S("yin", 0, P), HBM("own"), "lown", 2500)
     dma("S", S("wi", 0, 1), HBM("wgt"), "lwgt", 2500)
+    dma("Y", S("xw", 0, W), HBM("xc"), "lx", 5000)
     for h in range(NH):
-        cp(S("rin", h * PW, h * PW + PW), S("li", h * PW, h * PW + PW), "ru")
-    for j in list(range(1, LCH)) + [0]:
-        a, b = j * W // LCH, (j + 1) * W // LCH
-        dma("Y", S("li", a, b), HBM("lsr", a, b), "ll%d" % j, 5000 + 6000 * ((j - 1) % LCH + 1) / LCH)
-        cp(S("lw", a, b), S("li", a, b), "lw0")
+        cp(S("rin", h * PW, h * PW + PW), S("ji", h * PW, h * PW + PW), "ru")
+    LW = "lw" if par["conv"] else "li"
+    for j in range(LCH):
+        a, b = CUTS[j], CUTS[j + 1]
+        dma("Y", S("li", a, b), HBM("lsr", a, b), "ll%d" % j, 5000 + 6000 * b / W)
+        for x in range(a, b, 512) if par["conv"] else ():
+            cp(S("lw", x, min(b, x + 512)), S("li", x, min(b, x + 512)), "lw0")
 
+    first = len(ops)
     iota("ci", 1, [[0, 1]], 1)
     iota("ioc", 144, [[1, 144]], 0)
     iota("iob", 128, [[16, 8], [0, 16]], 0)
     iota("iom", 128, [[0, 8], [1, 16]], 0)
     iota("ioj", 64, [[0, 8], [64, 8]], 0)
-    iota("iog", 64, [[2, 64]], 0)
+    iota("iok", 144, [[1, 16], [16, 9]], 0)
+    iota("iok", 144, [[0, 16], [16, 9]], 0, 144)
+    iota("qq", NH * 256, [[0, NH * 256]], 0)
+    iota("dr", NH * 144, [[0, NH * 144]], 0)
+    iota("ba", 16 * 144, [[0, 16 * 144]], 0)
     cp(col(0), S("ci", 0, 1))
     ts(S("ci", 4, 5), S("ci", 0, 1), 15, None, ALU.bitwise_and)
     cp(col(1), S("ci", 4, 5))
@@ -214,68 +230,75 @@ def build_ops(par):
     ts(col(4), col(0), float(PW), 32.0, ALU.is_ge, ALU.mult)
     ts(col(5), col(1), 37.0 * 32, -2.0 ** 23, ALU.mult, ALU.add)
     ts(col(6), col(1), 1.0, None, ALU.add)
-    ts(col(7), col(1), 0.0, None, ALU.is_equal)
+    act(col(7), col(1), ACT.Sigmoid, 128.0, -256.0)
     ts(col(8), col(7), 17.0, -1.0, ALU.mult, ALU.add)
     tt(col(9), col(7), col(1), ALU.subtract)
     ts(col(14), col(9), -.25, 7.875, ALU.mult, ALU.add)
-    for nme, sc in (("idn", 1.0), ("nid", -1.0), ("n16", -16.0), ("i64", 64.0), ("q25", .25)):
-        ts(full(nme), full("ioc"), col(0), sc, ALU.is_equal, ALU.mult)
+    ts(full("idn"), full("ioc"), col(0), None, ALU.is_equal)
+    for nme, sc in (("nid", -1.0), ("n16", -16.0), ("i64", 64.0), ("q25", .25)):
+        lin(full(nme), full("idn"), sc)
     ts(S("hh", 0, 144), S("ioc", 0, 144), col(3), None, ALU.is_equal)
-    ts(S("hz", 0, 144), S("hh", 0, 144), -1.0 / 32, None, ALU.mult)
+    lin(S("hz", 0, 144), S("hh", 0, 144), -1.0 / 32)
     ts(full("bo"), full("iob"), col(2), None, ALU.is_equal)
-    ts(full("nbo"), full("bo"), -1.0, None, ALU.mult)
-    for nme, off, dg in (("mA", 1.0 / 64, -39.0 / 64), ("mB", -1.0 / 64, 89.0 / 128)):
-        ts(S("tmp", 0, 128), full("bo"), off, None, ALU.mult)
-        ts(S("tmp", 128, 256), full("idn"), dg, None, ALU.mult)
-        tt(full(nme), S("tmp", 0, 128), S("tmp", 128, 256), ALU.add)
-    ts(S("tmp", 0, 128), full("iom"), col(1), -1.0, ALU.is_gt, ALU.mult)
-    tt(S("tmp", 128, 256), S("tmp", 0, 128), full("idn"), ALU.add)
-    ts(S("tmp", 128, 256, 16), S("ioc", 0, 8), 0.0, col(8), ALU.mult, ALU.add)
-    ts(S("tmp", 0, 128), full("bo"), .25, None, ALU.mult)
-    tt(full("tri"), S("tmp", 128, 256), S("tmp", 0, 128), ALU.mult)
+    lin(full("nbo"), full("bo"), -1.0)
+
+    def tmp(j): return S("tmp", 128 * j, 128 * j + 128)
+    for j, (nme, off, dg) in enumerate((("mA", 1.0 / 64, -39.0 / 64), ("mB", -1.0 / 64, 89.0 / 128))):
+        lin(tmp(j), full("idn"), dg / off, 1.0)
+        lin(tmp(2 + j), full("bo"), off)
+        tt(full(nme), tmp(j), tmp(2 + j), ALU.mult)
+    ts(tmp(4), full("iom"), col(1), -1.0, ALU.is_gt, ALU.mult)
+    tt(tmp(5), tmp(4), full("idn"), ALU.add)
+    ts(S("tmp", 640, 768, 16), S("ioc", 0, 8), 0.0, col(8), ALU.mult, ALU.add)
+    lin(tmp(6), full("bo"), .25)
+    tt(full("tri"), tmp(5), tmp(6), ALU.mult)
+    for k in range(16):
+        lin(S("nc", 143 * k, 143 * k + 128), full("idn"), 32.0)
+    ts(S("tmp", 1024, 1168), S("iok", 0, 144), col(0), 32.0, ALU.is_equal, ALU.mult)
+    ts(S("tmp", 1168, 1312), S("iok", 144, 288), col(2), None, ALU.is_equal)
+    tt(S("nc", 0, 16 * 144, 16), S("tmp", 1024, 1168), S("tmp", 1168, 1312), ALU.add)
+    const(full("cm8"), -8.0)
     for a in (0, 8):
-        cp(S("o16", a, a + 8), S("bo", 0, 128, 16))
-        ts(S("o512", a, a + 8), S("bo", 0, 128, 16), 512.0, None, ALU.mult)
+        lin(S("o16", a, a + 8), S("bo", 0, 128, 16), 1.0)
+        lin(S("o512", a, a + 8), S("bo", 0, 128, 16), 512.0)
     for c in range(NC):
-        ts(col(15 + c), col(0), -float(c), None, ALU.add)
         for a in (0, 64):
-            ts(S("pen", 128 * c + a, 128 * c + a + 64), S("iog", 0, 64), col(15 + c), PEN, ALU.is_equal, ALU.mult)
-    ts(S("kc", 0, 64), S("ioj", 0, 64), col(4), None, ALU.add)
-    ts(S("kc", 64, 128), S("ioj", 0, 64), col(4), -240.0, ALU.add, ALU.add)
-    ms(S("kc", 128, 192), -240.0)
-    ms(S("dr", 0, 2 * NH * 144), 0.0)
-    ms(S("qq", 0, 2 * NH * 256), 0.0)
-    n = KK // par["dq"] * PW
-    ts(S("cm", 0, n), S("qq", 0, n), col(14), None, ALU.add)
-    ms(S("c16", 0, n), M16)
+            lin(S("pen", 128 * c + a, 128 * c + a + 64), S("idn", c, 128, 2), PEN)
+    ts(col(15), col(4), -240.0, None, ALU.add)
+    lin(S("kc", 0, 64), S("ioj", 0, 64), 1.0, col(4))
+    lin(S("kc", 64, 128), S("ioj", 0, 64), 1.0, col(15))
+    const(S("kc", 128, 192), -240.0)
+    lin(full("cm"), full("iom"), 0.0, col(14))
+    const(full("c16"), M16)
     for nme, v in (("c1", M1), ("c32", M32), ("c4096", M4096), ("c155", 15.5), ("c2048", 2048.0)):
-        ms(full(nme), v)
+        const(full(nme), v)
     for j, v in enumerate((0.0, 1.0, 39.0 / 64, 39.0 / 128)):
-        ms(S("f0", j, 4 * PW, 4), v)
+        const(S("f0", j, 4 * PW, 4), v)
     ts(col(17), col(1), 1.0, -0.5, ALU.is_equal, ALU.mult)
     ts(col(22), col(7), 2048.0, col(17), ALU.mult, ALU.add)
-    ts(full("cc"), full("iom"), 0.0, col(22), ALU.mult, ALU.add)
+    lin(full("cc"), full("iom"), 0.0, col(22))
     lo, st = -1152.0, -256.0
-    ts(full("sel"), full("iom"), 0.0, col(7), ALU.mult, ALU.add)
+    lin(full("sel"), full("iom"), 0.0, col(7))
     ms(S("thr", 0, 1), lo)
+    ms(S("thr", 1, 2), -lo)
     for a in (0, 64):
         ts(S("rs8", a, a + 64), S("ioj", 0, 64), 0.0, BIG, ALU.is_equal, ALU.mult)
     ts(full("rs16"), full("iom"), 0.0, -BIG, ALU.is_equal, ALU.mult)
-    ts(S("tmp", 0, 128), full("iom"), col(1), None, ALU.is_equal)
-    ts(S("tmp", 128, 256), full("ioc"), 32.0, 32768.0, ALU.mult, ALU.add)
-    tt(S("tmp", 128, 256), S("tmp", 128, 256), S("tmp", 0, 128), ALU.mult)
-    ts(full("wb"), S("tmp", 128, 256), -32768.0, None, ALU.add)
-    ts(S("rm", 0, 16), S("ioc", 0, 16), col(1), None, ALU.is_equal)
-    for a in range(16):
-        ts(S("ba", 144 * a, 144 * a + 144), S("hh", 0, 144), S("rm", a, a + 1), None, ALU.mult)
-    ts(S("hj", 0, 144), S("hh", 0, 144), col(6), None, ALU.mult)
+    ts(tmp(7), full("iom"), col(1), 32768.0, ALU.not_equal, ALU.mult)
+    lin(S("tf", 0, 128), full("ioc"), 32.0)
+    tt(S("tf", 128, 256), S("tf", 0, 128), tmp(7), ALU.subtract)
+    ts(full("wb"), S("tf", 128, 256), -16384.0, None, ALU.max)
+    ts(S("ba", 15, 16 * 144, 16), S("iok", 0, 144), col(0), None, ALU.is_equal)
+    lin(S("hj", 0, 144), S("hh", 0, 144), col(6))
     ts(S("wi", 4, 5), S("wi", 0, 1), 31, None, ALU.bitwise_and)
     cp(col(10), S("wi", 4, 5))
     ts(col(11), S("wi", 0, 1), 2048.0, -4096.0, ALU.is_ge, ALU.mult)
     tt(col(12), col(11), S("wi", 0, 1), ALU.add)
-    for nme, j, sg in (("w5p", 10, 1.0), ("w5n", 10, -1.0), ("wp", 12, 1.0), ("wn", 12, -1.0)):
-        ts(full(nme), full("bo"), col(j), sg, ALU.mult, ALU.mult)
+    for p, n, j in (("w5p", "w5n", 10), ("wp", "wn", 12)):
+        lin(full(p), full("bo"), col(j))
+        lin(full(n), full("nbo"), col(j))
 
+    for o in ops[first:]: o["const"] = True
     IDN, NID = full("idn"), full("nid")
 
     def hk(name, k): return S(name, 15 - k, 143 - k)
@@ -310,16 +333,19 @@ def build_ops(par):
                 for j, e in enumerate(who):
                     out = S(name, ob + 16 * pw * j, ob + 16 * pw * (j + 1))
                     src = IND(win, 0, W, S(offs, at + pw * j, at + pw * (j + 1)))
-                    move(out, src, add, e)
+                    if win == "li": ts(out, src, add, None, ALU.add)
+                    else: move(out, src, add, e)
                 return [(pw * j, pw * (j + 1)) for j in range(len(who))]
 
             def fill(tl, lhs, Y, n=KK):
                 return mm([(PS(tl, j, n * PW, n), lhs, Y) for j in range(n)], "fill" + tl[:2])
 
-            def against(out, src, c, tl, q, o):
-                its = [(S(out, ob + 512 * c + j, ob + 512 * c + 512, q), S(src, ob + c + NC * j, ob + n16, NC * q), PS(tl, 0, 512 // q)) for j in range(q)]
-                op("V", (1.0, 512), lambda g, T, Q: [g.vector.tensor_tensor(ap(T, Q, x), ap(T, Q, y), ap(T, Q, z), o) for x, y, z in its],
-                   [jc(src, c), its[0][2]], [cls(out, c)], out)
+            def km(name, k0, k1): return S(name, ob + PW * k0, ob + PW * k1)
+
+            def against(out, src, k0, k1, tl, o):
+                its = [(km(out, k, k + 1), S(src, ob + k, ob + n16, 16), PS(tl, 0, PW)) for k in range(k0, k1)]
+                op("V", (1.0, PW * (k1 - k0)), lambda g, T, Q: [g.vector.tensor_tensor(ap(T, Q, x), ap(T, Q, y), ap(T, Q, z), o) for x, y, z in its],
+                   [y for x, y, z in its] + [its[0][2]], [km(out, k0, k1)], out)
 
             def near(out, d): ts(out, d, M4, M4, ALU.add, ALU.is_equal)
 
@@ -331,46 +357,41 @@ def build_ops(par):
             xp = gather("xg", "xw", "rin", oi)
             cp(s4(3), RU, "rf")
             ts(sm("kp"), RU, 32.0, col(5), ALU.mult, ALU.add)
-            if par["xm"][h] == 2: fill("Dx" + v, IDN, YIN, KK // par["zq"])
             for c in range(NC):
-                if par["xm"][h] == 1:
-                    tl = "Dx%s_%d" % (v, c); d = PS(tl, 0, 512)
-                    k = fill(tl, NID, YIN)
-                    for i0, i1 in xp:
-                        mm([(PS(tl, KK * i0, KK * i1), IDN, jc("xg", c, i0, i1))], behind=[k])
-                else:
-                    d = cls("dx", c)
-                    against("dx", "xg", c, "Dx" + v, par["zq"], ALU.subtract)
+                tl = "Dx%s_%d" % (v, c); d = PS(tl, 0, 512)
+                k = fill(tl, NID, YIN)
+                for i0, i1 in xp:
+                    mm([(PS(tl, KK * i0, KK * i1), IDN, jc("xg", c, i0, i1))], behind=[k])
                 test(cls("nx", c), cls("ad", c), d, par["xs"][h][c])
                 if par["xs"][h][c] == 0: act(cls("ad", c), d, ACT.Abs)
-            gather("lg", "lw", "rin", oi)
+            gather("lg", LW if t or par["conv"] == 1 else "li", "rin", oi)
             tl = "n" + v
-            mm([(PS(tl, 0, PW), IDN, cst("c2048"))]
-               + [(PS(tl, 0, PW), S("ba", 144 * ((k + t) % 16) + 15 - k, 144 * ((k + t) % 16) + 143 - k), S("lg", ob + k, ob + n16, 16)) for k in range(16)])
+            for k0 in (0, KK):
+                mm([(PS(tl, 0, PW), S("ba", 144 * ((k + t) % 16) + 15 - k, 144 * ((k + t) % 16) + 143 - k), S("lg", ob + k, ob + n16, 16)) for k in range(k0, k0 + KK)]
+                   + ([] if k0 else [(PS(tl, 0, PW), IDN, cst("c2048"))]))
             cp(sm("nu"), PS(tl, 0, PW))
             tt(s4(2), PS(tl, 0, PW), s4(3), ALU.subtract, "nr")
             ts(s4(1), PS(tl, 0, PW), -1.0, None, ALU.mult, nm="nm")
             zp = gather("zg", "xw", "nu", o)
 
-            def byclass(out, lhs, name, behind=()):
+            def byclass(out, lhs, name, behind=(), head=()):
                 for c in range(NC):
-                    mm([(out, lhs(k), ks(name, k)) for k in range(c, 16, NC)], behind=behind)
+                    mm(list(() if c else head) + [(out, lhs(k), ks(name, k)) for k in range(c, 16, NC)], behind=behind)
             tl = "nb" + v
-            byclass(PS(tl, 0, PW), lambda k: IDN, "nx")
-            either(lambda: act(sm("good"), PS(tl, 0, PW), ACT.Sigmoid, -1920.0, 256.0), lambda: ts(sm("good"), PS(tl, 0, PW), 8.0, None, ALU.is_ge))
-            tl = "Dm" + v; n = KK // par["dq"]
-            mm([(PS(tl, 0, n * PW), IDN, cst("cm", n * PW))] + [(PS(tl, j, n * PW, n), full("tri"), sm("good")) for j in range(n)]
-               + [(PS(tl, 0, n * PW), lhs, cst("c16", n * PW)) for lhs in (IDN, NID)])
-            for c in range(NC):
-                against("dm", "xg", c, tl, par["dq"], ALU.max)
-            either(lambda: act(sm("oh"), PS(tl, 0, n * PW, n), ACT.Identity), lambda: cp(sm("oh"), PS(tl, 0, n * PW, n)))
-            tl = "cnt" + v
-            byclass(PS(tl, 0, PW), lambda k: hk("hh", k), "nx")
-            either(lambda: act(sm("sa"), PS(tl, 0, PW), ACT.Sigmoid, -2944.0, 256.0), lambda: ts(sm("sa"), PS(tl, 0, PW), 12.0, None, ALU.is_ge))
-            move(sm("cnt"), PS(tl, 0, PW))
+            byclass(PS(tl, 0, PW), lambda k: S("nc", 143 * k, 143 * k + 128), "nx", head=[(PS(tl, 0, PW), IDN, cst("cm8"))])
+            either(lambda: act(sm("good"), PS(tl, 0, PW), ACT.Sigmoid, -240.0 * 16, 16.0), lambda: ts(sm("good"), PS(tl, 0, PW), 240.0, None, ALU.is_ge))
+            ts(sm("nm"), PS(tl, 0, PW), M32, M32, ALU.add, ALU.subtract, "nbr")
+            tt(sm("cnt"), PS(tl, 0, PW), sm("nm"), ALU.subtract)
+            either(lambda: act(sm("sa"), sm("cnt"), ACT.Sigmoid, -896.0, 256.0), lambda: ts(sm("sa"), sm("cnt"), 4.0, None, ALU.is_ge))
+            tl = "Dm" + v; dn = par["dn"]
+            mm([(PS(tl, 0, PW), lhs, rhs) for lhs, rhs in ((IDN, cst("cm")), (full("tri"), sm("good")), (IDN, cst("c16")), (NID, cst("c16")))])
+            for k0 in range(0, 16, dn):
+                against("dm", "xg", k0, k0 + dn, tl, ALU.max)
+            move(sm("oh"), PS(tl, 0, PW))
             tl = "cT" + v
             mm([(PS(tl, 0, PW), full("bo"), sm("sa"))])
-            act(sm("nl"), PS(tl, 0, PW), ACT.Sigmoid, S("thr", 8 * t, 8 * t + 1), 256.0, S("acc", o3, o3 + 1))
+            either(lambda: act(sm("nl"), PS(tl, 0, PW), ACT.Sigmoid, S("thr", 8 * t, 8 * t + 1), 256.0),
+                   lambda: ts(sm("nl"), PS(tl, 0, PW), 256.0, S("thr", 8 * t + 1, 8 * t + 2), ALU.mult, ALU.is_ge))
             tl = "ya" + v
             mm([(PS(tl, 0, PW), IDN, sm("oh")), (PS(tl, 0, PW), full("i64"), sm("nl"))])
             tt(sm("yy"), YIN, PS(tl, 0, PW), ALU.min)
@@ -379,8 +400,9 @@ def build_ops(par):
             def both(name, j): return S(name, ob + j, ob + n16, KK)
             k = mm([(PS(tl, 0, 192), IDN, S("kc", 0, 192))] + [(PS(tl, j, 128, 8), both("ad", j), S("o512", 0, 16)) for j in range(KK)], "Ka")
             mm([(PS(tl, 0, 128, 1, PW * c, PW * c + PW), sm("sa"), S("pen", 128 * c, 128 * c + 128)) for c in range(NC)], "Kp", behind=[k])
-            mm([(PS(tl, 64 + j, 192, 8), both("dm", j), S("o16", 0, 16)) for j in range(KK)], "Kd", True)
-            oq = 128 * o3; od = 144 * o3 + 8
+            for k0 in range(0, 16, dn):
+                mm([(PS(tl, 64 + j, 192, 8), km("dm", 2 * j, 2 * j + 2), S("o16", 0, 16)) for j in range(k0 // 2, (k0 + dn) // 2)], "Kd", k0 + dn == 16, [k])
+            oq = 128 * h; od = 144 * h + 8
             scan(S("sc", oq, oq + 128), full("rs8"), PS(tl, 0, 128), ALU.add, ALU.min)
             move(S("dr", od, od + 128, 2), PS(tl, 128, 192))
             k = tt(S("qq", 2 * oq, 2 * oq + 256, 16, 0, PW), S("sc", oq + 7, oq + 128, 8, 0, PW), S("sc", oq + 7, oq + 128, 8, PW, 128), ALU.min)
@@ -408,7 +430,7 @@ def build_ops(par):
             test(S("nn", on, on + 2 * PW), S("nt", on, on + 2 * PW), PS(tl, 0, 2 * PW), 2 if "nn" in par["sg"] else 0)
             tl = "c2" + v
             mm([(PS(tl, 0, PW), IDN, sm("cnt")), (PS(tl, 0, PW), NID, S("nn", on, on + PW)), (PS(tl, 0, PW), IDN, S("nn", on + PW, on + 2 * PW))])
-            act(sm("sa2"), PS(tl, 0, PW), ACT.Sign, -11.5)
+            act(sm("sa2"), PS(tl, 0, PW), ACT.Sign, -3.5)
 
             def modulo(out, neg, pos, Y, half, big):
                 return [(out,) + half, (out, neg, Y), (out, NID, big), (out, IDN, big), (out, pos, Y)]
@@ -418,33 +440,39 @@ def build_ops(par):
             tt(sm("pi"), s4(3), PS(tl, 0, PW), ALU.mult)
             tt(sm("pj"), sm("pi"), sm("kp"), ALU.add)
             ts(s4(0), sm("pj"), 5, W - 1, ALU.arith_shift_right, ALU.bitwise_and, "far")
-            if 2 in par["zm"][h]: fill("Dz" + v, IDN, YN, KK // par["zq"])
+            if 2 in par["zm"][h]: mm([(PS("Dz" + v, 0, PW), IDN, YN)], "fillDz")
+            zn = par["zn"]
             for c in range(NC):
+                tl = "Dz%s_%d" % (v, c)
                 if par["zm"][h][c] == 1:
-                    tl = "Dz%s_%d" % (v, c); d = PS(tl, 0, 512)
-                    mm([(d, IDN, jc("zg", c))])
-                    fill(tl, NID, YN)
-                else:
-                    d = cls("dz", c)
-                    against("dz", "zg", c, "Dz" + v, par["zq"], ALU.subtract)
-                test(cls("nz", c), cls("az", c), d, par["zs"][h][c])
+                    mm([(PS(tl, PW * j, PW * j + PW), IDN, S("zg", ob + KK * c + j, ob + n16, 16)) for j in range(KK)])
+                    mm([(PS(tl, PW * j, PW * j + PW), NID, YN) for j in range(KK)], "fillDz")
+                for j in range(0, KK, zn):
+                    k0 = KK * c + j; d = PS(tl, PW * j, PW * (j + zn))
+                    if par["zm"][h][c] == 2:
+                        d = km("dz", k0, k0 + zn); against("dz", "zg", k0, k0 + zn, "Dz" + v, ALU.subtract)
+                    test(km("nz", k0, k0 + zn), km("az", k0, k0 + zn), d, par["zs"][h][c])
             tl = "fin" + v
             TF, CH = PS(tl, 2, 4 * PW, 4), PS(tl, 3, 4 * PW, 4)
             k = mm([(PS(tl, 0, 4 * PW), IDN, S("f0", 0, 4 * PW))], "fino", behind=[kyn])
             mm([(CH, full("mB"), sm("sa2")), (CH, IDN, cst("c1")), (CH, full("mA"), sm("sa2")), (CH, NID, cst("c1")), (TF, full("q25"), sm("sa2"))], "finc", behind=[k])
-            byclass(TF, lambda k: hk("hz", k), "nz", [k])
+            for k0 in range(0, 16, zn):
+                mm([(TF, hk("hz", j), km("nz", j, j + 1)) for j in range(k0, k0 + zn)], behind=[k])
             mm([(TF, IDN, cst("c1")), (TF, NID, cst("c1"))], "finr", True)
             scan(S("s4o", 4 * o, 4 * o + 4 * PW), PS(tl, 0, 4 * PW), S("s4", 4 * o, 4 * o + 4 * PW), ALU.mult, ALU.add)
-            RN = S("rout", oi, oi + PW)
-            cp(RN, s4(3, "s4o"))
-            send("r", RN, S("rin", oi + P, oi + P + PW))
+            RN = S("rout", oi, oi + PW) if t < V - 1 else S("rlast", h * PW, h * PW + PW)
+            cp(RN, s4(3, "s4o"), "rout")
+            send("r", RN, S("rin", oi + P, oi + P + PW) if t < V - 1 else S("rfin", h * PW, h * PW + PW))
         hs = range(NH); cur[0] = 0
         if t < V - 1:
             tl = "A%d" % t
-            mm([(PS(tl, 0, 1), full("sel"), S("acc", a * NH + h, a * NH + h + 1)) for h in hs])
-            cp(S("ai", 8 * a, 8 * a + 1), PS(tl, 0, 1))
+            mm([(PS(tl, 0, PW), full("sel"), S("nl", a * P + h * PW, a * P + h * PW + PW)) for h in hs])
+            op("V", (1.0, PW), lambda g, T, Q, a=a, tl=tl: g.vector.tensor_reduce(ap(T, Q, S("acc", a, a + 1)), ap(T, Q, PS(tl, 0, PW)), AxisListType.X, ALU.add),
+               [PS(tl, 0, PW)], [S("acc", a, a + 1)], "acc")
+            cp(S("ai", 8 * a, 8 * a + 1), S("acc", a, a + 1))
             ts(S("ai", 8 * a + 4, 8 * a + 5), S("ai", 8 * a, 8 * a + 1), 1, None, ALU.bitwise_and, nm="aj")
             ts(S("thr", 8 * t + 8, 8 * t + 9), S("ai", 8 * a + 4, 8 * a + 5), st, lo, ALU.mult, ALU.add)
+            ts(S("thr", 8 * t + 9, 8 * t + 10), S("ai", 8 * a + 4, 8 * a + 5), -st, -lo, ALU.mult, ALU.add)
         parts = [(h * PW, PW) for h in hs] if par["split"] or t == V - 1 else [(0, P)]
         for i0, n in parts:
             cur[0] = i0 // PW
@@ -454,20 +482,20 @@ def build_ops(par):
             offs = S("wou", 16 * a + i0 // 16, 16 * a + (i0 + n) // 16)
             cp(offs, S("ws", a * P + i0 + 15, a * P + i0 + n, 16))
             if t < V - 1: cp(IND("xw", 32 * i0, 32 * (i0 + n), offs), Y, "xw")
-            cp(IND("lw", 32 * i0, 32 * (i0 + n), offs), S("rout", t * P + i0, t * P + i0 + n), "lw")
+            cp(IND(LW, 32 * i0, 32 * (i0 + n), offs), S("rout", t * P + i0, t * P + i0 + n) if t < V - 1 else S("rlast", i0, i0 + n), "lw")
     cur[1] = V
     for h in range(NH):
         cur[0] = h
         v = "%d_%d" % (V, h); oi = V * P + h * PW
-        op("N", (0.0, 0), None, [], [S("rin", oi, oi + PW)], "ar", "ar" + v, -1.0, sends["r%d_%d" % (V - 1, h)])
-        cp(S("rfin", h * PW, h * PW + PW), S("rin", oi, oi + PW))
+        op("N", (0.0, 0), None, [], [S("rfin", h * PW, h * PW + PW)], "ar", "ar" + v, -1.0, sends["r%d_%d" % (V - 1, h)])
         op("N", (0.0, 0), None, [], [S("yin", oi, oi + PW)], "ay", "ay" + v, -1.0, sends["y%d_%d" % (V - 1, h)])
         dma("Y", HBM("yo", h * PW, h * PW + PW), S("yin", oi, oi + PW), "oo%d" % h, 2500)
         dma("Y", HBM("yj", h * PW, h * PW + PW), S("rfin", h * PW, h * PW + PW), "oj%d" % h, 2500)
     n = len(par["fin"]); w = W // n
     for j, e in enumerate(par["fin"]):
         cur[0] = j * NH // n
-        move(S("l16", w * j, w * j + w), S("lw", w * j, w * j + w), -2048.0, e)
+        if par["conv"]: move(S("l16", w * j, w * j + w), S(LW, w * j, w * j + w), -2048.0, e)
+        else: ts(S("l16", w * j, w * j + w), S(LW, w * j, w * j + w), -2048.0, None, ALU.add)
         mm([(PS("yz", 0, 256), hk("hj", c), S("l16", 256 * c, 256 * c + 256)) for c in range(j * w // 256, (j + 1) * w // 256)])
     act(S("yzf", 0, 256), PS("yz", 0, 256), ACT.Identity, 2048.0 * 136)
     dma("Y", HBM("yz"), S("yzf", 0, 256), "oyz", 2500)
@@ -479,7 +507,7 @@ def price(ops, cost):
     for o in ops:
         c, n = o["size"]; e = o["eng"]
         if e == "P": x = cost["pfix"] + n * cost["pe"]
-        elif e == "G": x = cost["rem"] if c == "rem" else float(n)
+        elif e == "G": x = cost["rem"] if c == "rem" else n * cost["all"]
         elif e == "N": x = 0.0
         elif o["sem"]: x = 60.0
         elif isinstance(c, str): x = cost["gfix"] + (20.0 if e == "S" else 0.0) + n * cost[c]
@@ -660,22 +688,27 @@ def timing(prep, which, order, extras, eng, form):
     return max(fin), start, fin, who
 
 
-def improve(ops, par, costs, start, form=()):
-    prep = prepare(ops, costs); n = len(ops); seen = {}; slot = []; T = par["T"]
+def improve(par, costs, given, moves, heat0, ends=False):
+    ops = build_ops(par); V = par["visits"]
+    prep = prepare(ops, costs); n = len(ops); seen = {}; slot = []
     for o in ops:
-        ph = min(o["t"], 1) if o["t"] < V - 1 else o["t"]
+        ph = min(o["t"], 1) if o["t"] < V - 1 else o["t"] - V + 3
         kd = (o["t"], kind(o)); seen[kd] = seen.get(kd, 0) + 1; slot.append((ph, kind(o), seen[kd]))
     names = sorted(set(slot)); num = {s: j for j, s in enumerate(names)}; slot = [num[s] for s in slot]
     rs = [k for k in range(n) if ops[k]["nm"] == "sendr"]; pre = prep[6]; succ = prep[0]
+    may = [not ends or names[s][0] != 1 for s in slot]; some = [k for k in range(n) if may[k]]
 
     def keys(start):
-        T = start[rs[3 * NH]] - start[rs[2 * NH]]; base = [min(o["t"], V - 1) * T for o in ops]; tau = [0.0] * len(names)
+        T = start[rs[(V - 3) * NH]] - start[rs[(V - 4) * NH]]; base = [min(o["t"], V - 1) * T for o in ops]; tau = [0.0] * len(names)
         for k in range(n):
-            if ops[k]["t"] in (0, 3, V - 1, V): tau[slot[k]] = start[k] - base[k] + k * 1e-4
+            if ops[k]["t"] in (0, V - 3, V - 1, V): tau[slot[k]] = start[k] - base[k] + k * 1e-4
         return base, tau
-    base, tau = keys(start); pick = [0] * len(names)
-    for k, f in enumerate(form): pick[slot[k]] = f
-    x = [par["seed"]]; free = [k for k in range(n) if "alt" in ops[k]]
+    if given:
+        base = [min(o["t"], V - 1) * given[0] for o in ops]; tau = [given[1][s][0] for s in names]; pick = [given[1][s][1] for s in names]
+    else:
+        base, tau = keys(best_order(ops, par, costs[0])[0][3]); pick = [0] * len(names)
+    loads = [k for k in range(n) if ops[k]["sem"] and ops[k]["sem"][0] == "l"]
+    x = [par["seed"] + moves]; free = [k for k in some if "alt" in ops[k]]
 
     def rnd():
         x[0] = (x[0] * 1103515245 + 12345) % 2 ** 31
@@ -683,7 +716,9 @@ def improve(ops, par, costs, start, form=()):
 
     def value(base, tau, pick, than=None, slack=0.0):
         form = [pick[s] for s in slot]; eng = [prep[3][f][k] for k, f in enumerate(form)]
-        a = arrange(prep, [b + tau[s] for b, s in zip(base, slot)], eng, par["dmax"])
+        key = [b + tau[s] for b, s in zip(base, slot)]
+        for k in loads: key[k] = k - 1e9
+        a = arrange(prep, key, eng, par["dmax"])
         if a is None or (than and a[0] == than[1][0] and form == than[3]): return None
         ts = []; worse = 0.0
         for w, c in enumerate(costs):
@@ -697,10 +732,14 @@ def improve(ops, par, costs, start, form=()):
         new[slot[k]] = to - base[k]
         for d in near[k] if depth else ():
             if (base[d] + new[slot[d]] - to) * sign > 0 and ops[d]["t"] == ops[k]["t"]: shift(new, d, to - sign, near, sign, depth - 1)
-    cur = best = value(base, tau, pick); deps = [set(p) for p in pre]
-    for it in range(par["moves"]):
-        heat = par["heat"] * (1.0 - it / par["moves"])
-        if it % par["again"] == 0:
+    if ends:
+        need = value(base, tau, pick)[2][0][1]; fixed = [k for k in range(n) if ops[k].get("const")]
+        for k in reversed(fixed): need[k] = min([need[s] for s in succ[k]] + [1e9]) - 1.0
+        for j, k in enumerate(sorted(fixed, key=lambda k: need[k])): tau[slot[k]] = 30.0 * j - 3000.0
+    cur = best = value(base, tau, pick); deps = [set(p) for p in pre]; kept = (base, tau, pick)
+    for it in range(moves):
+        heat = heat0 * (1.0 - it / moves)
+        if it % par["again"] == 0 and not ends:
             b2, t2 = keys(cur[2][0][1]); r = value(b2, t2, pick)
             if r is not None and r[0] <= cur[0] + heat: base, tau, cur = b2, t2, r
         new = list(tau); other = pick; z = rnd()
@@ -708,10 +747,13 @@ def improve(ops, par, costs, start, form=()):
             end, st, fin, who = cur[2][int(rnd() * len(costs))]
             k = fin.index(end); pairs = []
             while who[k] >= 0:
-                if who[k] not in deps[k]: pairs.append((who[k], k))
+                if who[k] not in deps[k] and may[k] and may[who[k]]: pairs.append((who[k], k))
                 k = who[k]
             if not pairs: continue
-            p, k = pairs[int(rnd() * len(pairs))]; z = rnd()
+            j = int(rnd() * len(pairs)); p, k = pairs[j]
+            while j + 1 < len(pairs) and pairs[j + 1][1] == p and rnd() < par["far"]:
+                j += 1; p = pairs[j][0]
+            z = rnd()
             if z < .2 and ("alt" in ops[p] or "alt" in ops[k]):
                 other = list(pick); other[slot[p if "alt" in ops[p] else k]] ^= 1
             elif z < .6: shift(new, k, base[p] + tau[slot[p]] - 1.0 - 50.0 * rnd(), pre, 1.0, 3)
@@ -719,22 +761,21 @@ def improve(ops, par, costs, start, form=()):
         elif z < par["aimed"] + .05:
             other = list(pick); other[slot[free[int(rnd() * len(free))]]] ^= 1
         else:
-            k = int(rnd() * n); z = (rnd() - .5) * par["reach"]
+            k = some[int(rnd() * len(some))]; z = (rnd() - .5) * par["reach"]
             shift(new, k, base[k] + tau[slot[k]] + z, pre if z < 0 else succ, 1.0 if z < 0 else -1.0, 3)
         r = value(base, new, other, cur, heat * rnd())
         if r is None: continue
         cur, tau, pick = r, new, other
-        if r[0] < best[0]: best = r
-    return [prep[7][best[3][k]][k] for k in range(n)], best
+        if r[0] < best[0]: best = r; kept = (base, tau, pick)
+    state = (kept[0][rs[NH]], {s: (kept[1][j], kept[2][j]) for j, s in enumerate(names)})
+    return [prep[7][best[3][k]][k] for k in range(n)], best, state
 
 
 def plan(par, costs):
-    ops = build_ops(par); best = None
-    for seed, delta in enumerate(par["deltas"]):
-        one = dict(par, seed=par["seed"] + seed, delta=delta, moves=par["few"])
-        r = improve(ops, one, costs, best_order(ops, one, costs[0])[0][3])
-        if best is None or r[1][0] < best[1][0]: best = r
-    return improve(ops, dict(par, heat=par["heat"] / 2), costs, best[1][2][0][1], best[1][3])
+    state = None
+    for visits, moves, heat, ends in par["stages"]:
+        ops, best, state = improve(dict(par, visits=visits), costs, state, moves, heat, ends)
+    return ops, best
 
 
 PLAN = []

@@ -1,4 +1,5 @@
-from concourse.mybir import AluOpType, ActivationFunctionType, AxisListType
+import math
+from concourse.mybir import AluOpType, ActivationFunctionType
 
 ALU = AluOpType
 ACT = ActivationFunctionType
@@ -9,32 +10,33 @@ NC = 2
 KK = 16 // NC
 M4 = float((2 ** 23 + 1) * 4)
 M1, M16, M32, M4096 = (float(3 * 2 ** 22 * n) for n in (1, 16, 32, 4096))
-PEN = float(2 ** 18)
+PEN = float(2 ** 24)
 BIG = float(2 ** 22)
-SEG = 18
+DMS = 16 + 16 * PW + 16
 
 B, F, I32, U16, H16 = "bfloat16", "float32", "int32", "uint16", "float16"
 SCRATCH = {
     "xw": [W, B], "li": [W, I32], "lw": [W, F], "l16": [W, H16],
     "rin": [(V + 1) * P, U16], "yin": [(V + 1) * P, B], "rout": [V * P, U16], "yout": [V * P, B], "rfin": [P, F], "rlast": [P, F],
-    "wi": [8, I32], "yzf": [256, F], "ci": [8, I32], "cf": [32, F], "rm": [16, F],
+    "wi": [8, I32], "yzf": [256, F], "ci": [8, I32], "cf": [32, F],
     "ioc": [144, B], "iob": [128, B], "iom": [128, B], "ioj": [64, B], "tmp": [1312, B], "nc": [16 * 144, B], "iok": [288, B], "cm8": [128, B], "tf": [256, F], "ji": [P, I32],
-    "hh": [144, B], "hz": [144, B], "hj": [144, H16], "ba": [16 * 144, B], "kc": [192, B], "pen": [256, B],
-    "sel": [128, B], "acc": [8, F], "o16": [16, B], "o512": [16, B], "f0": [4 * PW, B], "rs8": [128, F], "rs16": [128, F],
-    "cm": [512, B], "c16": [512, B], "sc": [2 * NH * 128, F],
-    "thr": [8 * V, F], "ai": [16, I32], "wou": [32, U16], "ws": [2 * P, F], "wp": [128, H16], "wn": [128, H16],
-    "lg": [2 * 2048, H16], "dr": [2 * NH * 144, B], "nn": [2 * 2 * P, B], "nt": [2 * 2 * P, B], "qq": [2 * NH * 256, F],
-    "zb": [2 * NH * 128, B],
-    "s4": [2 * 4 * P, I32], "s4o": [2 * 4 * P, F],
+    "hh": [144, B], "hz": [144, B], "hp": [144, B], "hs": [144, B], "hj": [144, H16], "ba": [16 * 144, B], "kb": [PW, H16],
+    "o8": [16, B], "f0": [4 * PW, B], "rsk": [PW, F], "rs16": [128, F], "td": [256, F], "ca": [8, B], "da": [8, F],
+    "wou": [32, U16], "ws": [2 * P, F], "wp": [128, H16], "wn": [128, H16],
+    "lg": [2 * 2048, H16], "dr": [2 * NH * 144, B], "nn": [2 * 2 * P, B], "nt": [2 * 2 * P, B], "y2": [2 * 2 * P, B], "dm": [2 * NH * DMS, B],
+    "s4o": [2 * 4 * P, F], "pi": [2 * 2 * P, I32], "ka": [32, I32], "kt": [32, F], "ko": [32, U16], "lf": [32, B],
 }
-for _n in ("idn", "nid", "n16", "i64", "q25", "nbo", "c32", "bo", "tri", "mA", "mB", "w5p", "w5n", "wb", "c1", "c4096", "cc", "c155", "c2048"):
+for _n in ("idn", "nid", "q25", "nbo", "c32", "bo", "tri", "mA", "mB", "w5p", "w5n", "wb", "c1", "c4096", "cc", "c155", "c2048",
+           "cm", "ck", "cp", "c4", "one", "non"):
     SCRATCH[_n] = [128, B]
-for _n in ("xg", "zg", "ad", "nx", "dm", "az", "nz", "dx", "dz"):
+for _n in ("xd", "yb", "zg", "az", "nz", "dz"):
     SCRATCH[_n] = [2 * 2048, B]
-for _n, _d in (("nu", U16), ("nm", F), ("kp", F), ("good", B), ("cnt", B), ("sa", B), ("oh", B), ("yy", B), ("nl", B), ("sa2", B),
-               ("pi", I32), ("pj", I32)):
+for _n, _d in (("nu", U16), ("good", B), ("nbv", H16), ("sa2", B), ("pj", I32), ("km", I32), ("kv", F)):
     SCRATCH[_n] = [2 * P, _d]
 SCRATCH = {_n: ("sbuf", [128, _v[0]], _v[1]) for _n, _v in SCRATCH.items()}
+for _n in ("ad", "nx"):
+    SCRATCH[_n] = ("sbuf", [128, 2 * P // 16, 16, 16], B)
+SCRATCH["s4"] = ("sbuf", [128, 2 * NH * (4 * PW + 4) + 4], I32)
 for _n in range(8):
     SCRATCH["pb%d" % _n] = ("psum", [128, 512], F)
 CUTS = (0, 1536, 2816, 3712, W)
@@ -57,6 +59,20 @@ PAR.update({"rounds": 200, "moves": 30000, "heat": 300.0, "aimed": .8, "visits":
             "deltas": (2500.0, 3000.0, 3500.0, 4000.0), "few": 5000, "rounds": 100, "moves": 40000, "zm": ((2, 1), (2, 1)), "zs": ((0, 1), (0, 1)), "xs": ((1, 1), (1, 1)),
             "conv": 1, "far": .3, "dn": 4, "zn": 4, "xs": ((0, 1), (0, 1)), "heat": 2000.0, "deltas": (3000.0,), "few": 1000,
             "zm": ((1, 2), (1, 2)), "zs": ((0, 0), (0, 0)), "stages": ((5, 50000, 1000.0, False), (3, 30000, 300.0, True), (V, 10000, 100.0, False))})
+PAR.update({"xd": ("VV", "VV"), "bn": 4, "nx": 2, "ad": 2, "pn": 8, "perq": 0, "usc": 1, "zm": ((1, 1), (1, 1)),
+            "cycle": (100000, 200.0), "lead": 0.0, "rounds": 10, "settle": 4, "rounds2": 2, "ahead": ("c",), "cool": 1.0,
+            "zm": ((2, 2), (1, 2)), "cycle": ((50000, 130.0), (50000, 70.0)), "stay": ("lg", "zg"), "sweep": .03, "yb": ("EE", "EE"), "ahead": ("c", "Dm", "u", "wo"), "stages": ((3, 25000, 200.0, True), (V, 5000, 60.0, False))})
+PAR.update({"yb": ("SS", "SS"), "via": (0, 1), "xat": 0, "cuts": CUTS, "cycle": (), "sweep": .06, "stages": ((3, 45000, 120.0, True), (V, 200, 20.0, False))})
+ROUND = """
+Nay0a PKd1a' Vdz0a' Vdz0d' Pu00a' Pc00a' Vkv1a' Vkm1a' PKd1b' Vnz0a' Vdz0b' Pfino0a' Szg1b' Pddz0a' Vka1a' PKd1c' Pdd0a' Pwo00a' Pwo0a' Vdz0c' Pu0a' Vkt1a' Vnn0a'
+Pfin0a' Vnz0d' Pc01a' Vko1a' Vnz0b' Pc0a' Vnz0c' PKd1d' Pfin0d' Vyout1a' Pfin0b' Ssa20a' Vpi0a' Sdr1a' Pfin0c' Vkp1a' Syb0a Vnr1a' Gsendy1a' Vws0a' PfillDz1a' Pfinc0a'
+Pfinr0a' Vfar0a' Vnm0a' Pdd1a' Pddz1a' Pwo01a' Vdz1b' Syb0b Vs4o0a' PDz1a' Nay1a Vnn1a' PfillDz1b' Vnz1d' Vrout0a' Vdz1a' Pu01a' Pc1a' Pu1a' Vwou0a' Gsendr0a' Vnz1a'
+Pwo1a' Ssa21a' Vnz1b' Vnz1c' Pfino1a' Vpi1a' Pfin1d' Pfinc1a' Nar0a Pfin1a' Pfin1b' Pfin1c' Vws1a' Vxw0a' Vfar1a' Pfinr1a' Vnm1a' PDm00a Vlw0a' Syb1a Vs4o1a' Vwou1a'
+Vrout1a' Vxw1a' Gsendr1a' Vlw1a' Syb1b Slf1a' Vxd0a Slg0a Slg0b Nar1a Vlf0a' Vxd0b PA0a' Vnx0a Sad0a Vnx0b Pn0a Vtd0a' Sad0b Vrf0a Vxd1a PKn0b PKn0a Slg1b Pnb0b Vxd1b
+Pnb0a Slg1a PKr0a Pn0b Vgood0a PKa0b Vnx1a Vnx1b Sad1a PDm0a PKa0a Vkp0a Vnu0a Vdm0b PDm01a Sad1b Vdm0d Pnb1b Pnb1a Vkm0a Vdm0a Szg0b Szg0a Pn1a Vkv0a Vka0a Vgood1a
+Vnr0a Vrf1a PKd0d PKd0b PKd0a Vkt0a Vdm0c PDm1a Pn1b Vko0a Snbv1a Vdm1d PKn1a Vyout0a PKn1b PKd0c Vnu1a Vdm1c Gsendy0a Vdm1b PfillDz0a PKr1a PKa1a Snbv0a Vdm1a Sdr0a
+Szg1a PKa1b
+"""
 
 
 def S(name, a, b, s=1, p0=0, p1=128): return ("s", name, p0, p1, a, b, s)
@@ -68,15 +84,22 @@ def PS(tile, a, b, s=1, p0=0, p1=128): return ("p", tile, p0, p1, a, b, s)
 def IND(win, a, b, offs): return ("i", win, 0, 128, a, b, offs)
 
 
-def Y3(a, b, c0, c1): return ("3", "yb", 0, 128, a, b, (c0, c1))
+def ND(name, *ix): return ("n", name, 0, 128, ix, None, None)
 
 
 def HBM(name, a=None, b=None): return ("d", name, 0, 128, a, b, 1)
 
 
+def spots(x):
+    out = [0]
+    for n, i in zip(SCRATCH[x[1]][1][1:], x[4]):
+        out = [n * o + j for o in out for j in (range(*i) if isinstance(i, tuple) else (i,))]
+    return out
+
+
 def width(x):
     if x[0] == "i": return 16 * width(x[6])
-    if x[0] == "3": return (x[5] - x[4]) * (x[6][1] - x[6][0])
+    if x[0] == "n": return math.prod(i[1] - i[0] for i in x[4] if isinstance(i, tuple))
     return len(range(x[4], x[5], x[6]))
 
 
@@ -84,7 +107,7 @@ def ap(T, Q, x):
     if not isinstance(x, tuple): return x
     k, name, p0, p1, a, b, s = x
     if k == "i": return T[name][:, a:b].indirect(ap(T, Q, s))
-    if k == "3": return T[name][p0:p1, a:b, s[0]:s[1]]
+    if k == "n": return T[name][(slice(p0, p1),) + tuple(slice(*i) if isinstance(i, tuple) else i for i in a)]
     if k == "d": return T[name][:, a:b]
     t = Q(name) if k == "p" else T[name]
     return t[p0:p1, a:b:s] if s > 1 else t[p0:p1, a:b]
@@ -98,14 +121,16 @@ def places(x):
     k, name, p0, p1, a, b, s = x
     if k == "p": return [("ps " + name, 1)]
     if k == "i": return [(name, ((1 << (b - a)) - 1) << a)] + places(s)
-    if k == "3": return [(name, sum(((1 << (s[1] - s[0])) - 1) << (16 * j + s[0]) for j in range(a, b)))]
+    if k == "n":
+        if x not in MASKS: MASKS[x] = sum(1 << j for j in spots(x))
+        return [(name, MASKS[x])]
     if (a, b, s) not in MASKS: MASKS[(a, b, s)] = sum(1 << j for j in range(a, b, s))
     return [(name, MASKS[(a, b, s)])]
 
 
 def build_ops(par):
     ops, live = [], {}; V = par["visits"]
-    cur = [0, 0]; dry = [False]
+    cur = [0, 0]; dry = [0]
 
     def op(eng, size, fn, r, w, nm, sem=None, lat=0.0, after=None, more=()):
         k = len(ops); deps = set(more)
@@ -116,7 +141,7 @@ def build_ops(par):
             deps.update(j for j, m2, isw in live.get(name, []) if isw and m & m2)
         for name, m in wr:
             deps.update(j for j, m2, isw in live.get(name, []) if m & m2)
-        if dry[0]: return {"eng": eng, "size": size, "fn": fn, "deps": deps}
+        if dry[0]: return {"eng": eng, "size": size, "fn": fn, "deps": deps, "r": r, "w": w}
         for name, m in wr:
             live[name] = [(j, m2 & ~m, isw) for j, m2, isw in live.get(name, []) if m2 & ~m] + [(k, m, True)]
         for name, m in rd:
@@ -126,7 +151,7 @@ def build_ops(par):
         ops.append({"eng": eng, "size": size, "fn": fn, "deps": deps, "ps": ps, "sem": sem, "lat": lat, "after": after, "h": cur[0], "t": cur[1], "nm": nm})
         return k
 
-    def two(*xs): return all(x[0] in "s3" and SCRATCH[x[1]][2] in (B, H16, U16) for x in xs)
+    def two(*xs): return all(x[0] in "sn" and SCRATCH[x[1]][2] in (B, H16, U16) for x in xs)
 
     def rate(out, in0, other):
         if in0[0] == "i": return ("gam", width(in0))
@@ -146,8 +171,13 @@ def build_ops(par):
     def cp(out, in_, nm=None, more=()):
         return op("V", rate(out, in_, .5 if two(out, in_) else 1.0), lambda g, T, Q: g.vector.tensor_copy(ap(T, Q, out), ap(T, Q, in_)), [in_], [out], nm or out[1], more=more)
 
-    def scan(out, d0, d1, o0, o1):
-        return op("V", (1.0, width(d0)), lambda g, T, Q: g.vector.tensor_tensor_scan(ap(T, Q, out), ap(T, Q, d0), ap(T, Q, d1), 0.0, o0, o1), [d0, d1], [out], out[1])
+    def scan(out, d0, d1, o0, o1, first=0.0):
+        return op("V", (1.0, width(d0)), lambda g, T, Q: g.vector.tensor_tensor_scan(ap(T, Q, out), ap(T, Q, d0), ap(T, Q, d1), first, o0, o1), [d0, d1], [out], out[1])
+
+    def many(e, calls, nm):
+        dry[0] += 1; its = [c() for c in calls]; dry[0] -= 1
+        size = ("g", sum(x["size"][1] for x in its)) if e == "G" else (1.0, sum(max(64.0, x["size"][0] * x["size"][1]) for x in its))
+        return op(e, size, lambda g, T, Q: [x["fn"](g, T, Q) for x in its], [y for x in its for y in x["r"]], [y for x in its for y in x["w"]], nm)
 
     def ms(out, val):
         return op("V", (.5 if two(out) else 1.0, width(out)), lambda g, T, Q: g.vector.memset(ap(T, Q, out), val), [], [out], out[1])
@@ -169,9 +199,14 @@ def build_ops(par):
         ops[k]["ps"] = (tl,); mine.append((k, 1, True))
         return k
 
+    def steps(n, items):
+        nm = "".join(x for x in items[0][0][1] if x.isalpha())
+        if nm not in par["ahead"]: return mm(items)
+        return mm(items[n:], behind=[mm(items[:n], nm + "0")])
+
     def either(on_s, on_v, first="S"):
         one, other = (on_s, on_v) if first == "S" else (on_v, on_s)
-        dry[0] = True; alt = other(); dry[0] = False
+        dry[0] += 1; alt = other(); dry[0] -= 1
         k = one(); ops[k]["deps"] |= alt["deps"]; ops[k]["alt"] = alt
         return k
 
@@ -190,7 +225,13 @@ def build_ops(par):
             return g.iota(T[name][:, a:a + n], pat, 0, cm, allow_small_or_imprecise_dtypes=True)
         op("G", ("g", 160 + 2 * n), fn, [], [S(name, a, a + n)], name)
 
+    def hand(out, in_):
+        n = width(in_)
+        return op("G", ("g", 205 + 2 * n), lambda g, T, Q: g.affine_select(ap(T, Q, out), ap(T, Q, in_), [[0, n]], ALU.is_ge, 0.0, 0, 0), [in_], [out], out[1])
+
     def full(name): return S(name, 0, 128)
+
+    def cst(name, n=PW): return S(name, 0, n)
 
     def lin(out, in_, scale, bias=0.0):
         return either(lambda: act(out, in_, ACT.Identity, bias, scale), lambda: ts(out, in_, scale, bias, ALU.mult, ALU.add))
@@ -201,13 +242,13 @@ def build_ops(par):
     dma("Y", S("ji", 0, P), HBM("jur"), "ljur", 2500)
     dma("S", S("yin", 0, P), HBM("own"), "lown", 2500)
     dma("S", S("wi", 0, 1), HBM("wgt"), "lwgt", 2500)
-    dma("Y", S("xw", 0, W), HBM("xc"), "lx", 5000)
     for h in range(NH):
         cp(S("rin", h * PW, h * PW + PW), S("ji", h * PW, h * PW + PW), "ru")
-    LW = "lw" if par["conv"] else "li"
+    LW = "lw" if par["conv"] else "li"; CUTS = par["cuts"]
     for j in range(LCH):
         a, b = CUTS[j], CUTS[j + 1]
-        dma("Y", S("li", a, b), HBM("lsr", a, b), "ll%d" % j, 5000 + 6000 * b / W)
+        if j == par["xat"]: dma("Y", S("xw", 0, W), HBM("xc"), "lx", 5000 + 6000 * a / W)
+        dma("Y", S("li", a, b), HBM("lsr", a, b), "ll%d" % j, (5000 if j >= par["xat"] else 2500) + 6000 * b / W)
         for x in range(a, b, 512) if par["conv"] else ():
             cp(S("lw", x, min(b, x + 512)), S("li", x, min(b, x + 512)), "lw0")
 
@@ -216,29 +257,30 @@ def build_ops(par):
     iota("ioc", 144, [[1, 144]], 0)
     iota("iob", 128, [[16, 8], [0, 16]], 0)
     iota("iom", 128, [[0, 8], [1, 16]], 0)
-    iota("ioj", 64, [[0, 8], [64, 8]], 0)
+    iota("ioj", PW, [[16, PW // 16], [PW, 16]], 0)
     iota("iok", 144, [[1, 16], [16, 9]], 0)
     iota("iok", 144, [[0, 16], [16, 9]], 0, 144)
-    iota("qq", NH * 256, [[0, NH * 256]], 0)
     iota("dr", NH * 144, [[0, NH * 144]], 0)
     iota("ba", 16 * 144, [[0, 16 * 144]], 0)
+    for j in range(2 * NH):
+        iota("dm", 16, [[0, 16]], 0, DMS * j)
     cp(col(0), S("ci", 0, 1))
     ts(S("ci", 4, 5), S("ci", 0, 1), 15, None, ALU.bitwise_and)
     cp(col(1), S("ci", 4, 5))
     tt(col(2), col(0), col(1), ALU.subtract)
     ts(col(3), col(2), 15.0, None, ALU.add)
-    ts(col(4), col(0), float(PW), 32.0, ALU.is_ge, ALU.mult)
     ts(col(5), col(1), 37.0 * 32, -2.0 ** 23, ALU.mult, ALU.add)
     ts(col(6), col(1), 1.0, None, ALU.add)
     act(col(7), col(1), ACT.Sigmoid, 128.0, -256.0)
     ts(col(8), col(7), 17.0, -1.0, ALU.mult, ALU.add)
     tt(col(9), col(7), col(1), ALU.subtract)
-    ts(col(14), col(9), -.25, 7.875, ALU.mult, ALU.add)
+    ts(col(14), col(9), 1.0 / 64, 65.0 / 128, ALU.mult, ALU.add)
     ts(full("idn"), full("ioc"), col(0), None, ALU.is_equal)
-    for nme, sc in (("nid", -1.0), ("n16", -16.0), ("i64", 64.0), ("q25", .25)):
+    for nme, sc in (("nid", -1.0), ("q25", .25)):
         lin(full(nme), full("idn"), sc)
     ts(S("hh", 0, 144), S("ioc", 0, 144), col(3), None, ALU.is_equal)
-    lin(S("hz", 0, 144), S("hh", 0, 144), -1.0 / 32)
+    for nme, sc in (("hz", -1.0 / 32), ("hp", PEN * 89 / 2048), ("hs", 16.0 * PW)):
+        lin(S(nme, 0, 144), S("hh", 0, 144), sc)
     ts(full("bo"), full("iob"), col(2), None, ALU.is_equal)
     lin(full("nbo"), full("bo"), -1.0)
 
@@ -250,39 +292,31 @@ def build_ops(par):
     ts(tmp(4), full("iom"), col(1), -1.0, ALU.is_gt, ALU.mult)
     tt(tmp(5), tmp(4), full("idn"), ALU.add)
     ts(S("tmp", 640, 768, 16), S("ioc", 0, 8), 0.0, col(8), ALU.mult, ALU.add)
-    lin(tmp(6), full("bo"), .25)
+    lin(tmp(6), full("bo"), -1.0 / 64)
     tt(full("tri"), tmp(5), tmp(6), ALU.mult)
     for k in range(16):
         lin(S("nc", 143 * k, 143 * k + 128), full("idn"), 32.0)
     ts(S("tmp", 1024, 1168), S("iok", 0, 144), col(0), 32.0, ALU.is_equal, ALU.mult)
     ts(S("tmp", 1168, 1312), S("iok", 144, 288), col(2), None, ALU.is_equal)
     tt(S("nc", 0, 16 * 144, 16), S("tmp", 1024, 1168), S("tmp", 1168, 1312), ALU.add)
-    const(full("cm8"), -8.0)
-    for a in (0, 8):
-        lin(S("o16", a, a + 8), S("bo", 0, 128, 16), 1.0)
-        lin(S("o512", a, a + 8), S("bo", 0, 128, 16), 512.0)
-    for c in range(NC):
-        for a in (0, 64):
-            lin(S("pen", 128 * c + a, 128 * c + a + 64), S("idn", c, 128, 2), PEN)
-    ts(col(15), col(4), -240.0, None, ALU.add)
-    lin(S("kc", 0, 64), S("ioj", 0, 64), 1.0, col(4))
-    lin(S("kc", 64, 128), S("ioj", 0, 64), 1.0, col(15))
-    const(S("kc", 128, 192), -240.0)
-    lin(full("cm"), full("iom"), 0.0, col(14))
-    const(full("c16"), M16)
-    for nme, v in (("c1", M1), ("c32", M32), ("c4096", M4096), ("c155", 15.5), ("c2048", 2048.0)):
-        const(full(nme), v)
+    lin(S("kb", 0, PW), S("ioj", 0, PW), 1.0, col(1))
+    lin(cst("cm"), cst("iom"), 0.0, col(14))
+    for nme, v, n in (("c1", M1, PW), ("c32", M32, PW), ("c4096", M4096, PW), ("c155", 15.5, PW), ("c2048", 2048.0, PW),
+                      ("cp", M1 * PEN, PW), ("c4", 4 * M1, 4), ("one", 1.0, 128), ("non", -1.0, 128)):
+        const(cst(nme, n), v)
     for j, v in enumerate((0.0, 1.0, 39.0 / 64, 39.0 / 128)):
         const(S("f0", j, 4 * PW, 4), v)
     ts(col(17), col(1), 1.0, -0.5, ALU.is_equal, ALU.mult)
     ts(col(22), col(7), 2048.0, col(17), ALU.mult, ALU.add)
-    lin(full("cc"), full("iom"), 0.0, col(22))
-    lo, st = -1152.0, -256.0
-    lin(full("sel"), full("iom"), 0.0, col(7))
-    ms(S("thr", 0, 1), lo)
-    ms(S("thr", 1, 2), -lo)
-    for a in (0, 64):
-        ts(S("rs8", a, a + 64), S("ioj", 0, 64), 0.0, BIG, ALU.is_equal, ALU.mult)
+    const(S("cc", 0, 128, 2), 0.0)
+    lin(S("cc", 1, 128, 2), cst("iom"), 0.0, col(22))
+    for a in (0, 128):
+        const(S("td", a, a + 128), -64 * PEN)
+    const(S("td", PW, 2 * PW, 16), 5 * PEN)
+    for a, b, v, w in ((0, 4, -1.0, 0.0), (4, 5, -PEN / 2, 5.5 * PEN), (5, 8, 1.0, 0.0)):
+        const(S("ca", a, b), v)
+        const(S("da", a, b), w)
+    ts(cst("rsk"), cst("iom"), 0.0, 4 * PEN, ALU.is_equal, ALU.mult)
     ts(full("rs16"), full("iom"), 0.0, -BIG, ALU.is_equal, ALU.mult)
     ts(tmp(7), full("iom"), col(1), 32768.0, ALU.not_equal, ALU.mult)
     lin(S("tf", 0, 128), full("ioc"), 32.0)
@@ -303,8 +337,6 @@ def build_ops(par):
 
     def hk(name, k): return S(name, 15 - k, 143 - k)
 
-    def cst(name, n=PW): return S(name, 0, n)
-
     sends = {}
     for t in range(V):
         a = t & 1; cur[1] = t
@@ -315,13 +347,11 @@ def build_ops(par):
 
             def sm(name): return S(name, o, o + PW)
 
-            def cls(name, c): return S(name, ob + 512 * c, ob + 512 * c + 512)
+            def four(name): return S(name, 8 * o3, 8 * o3 + PW // 16)
 
-            def ks(name, k): return S(name, ob + 512 * (k % NC) + k // NC, ob + 512 * (k % NC) + 512, KK)
+            def cube(name, r=(0, 16), k=(0, 16), i0=0, i1=PW): return ND(name, ((o + i0) // 16, (o + i1) // 16), r, k)
 
-            def jc(name, c, i0=0, i1=PW): return S(name, ob + 16 * i0 + c, ob + 16 * i1, NC)
-
-            def s4(j, name="s4"): return S(name, 4 * o + j, 4 * o + 4 * PW, 4)
+            def s4(j, s=4): return S("s4", (4 * PW + 4) * o3 + j, (4 * PW + 4) * o3 + j + 4 * PW, s)
 
             RU, YIN, YN = S("rin", oi, oi + PW), S("yin", oi, oi + PW), S("yout", oi, oi + PW)
             if t:
@@ -333,14 +363,13 @@ def build_ops(par):
                 for j, e in enumerate(who):
                     out = S(name, ob + 16 * pw * j, ob + 16 * pw * (j + 1))
                     src = IND(win, 0, W, S(offs, at + pw * j, at + pw * (j + 1)))
-                    if win == "li": ts(out, src, add, None, ALU.add)
+                    if name == "xd": tt(out, src, S("yb", ob + 16 * pw * j, ob + 16 * pw * (j + 1)), ALU.subtract)
+                    elif win == "li": ts(out, src, add, None, ALU.add)
                     else: move(out, src, add, e)
-                return [(pw * j, pw * (j + 1)) for j in range(len(who))]
 
-            def fill(tl, lhs, Y, n=KK):
-                return mm([(PS(tl, j, n * PW, n), lhs, Y) for j in range(n)], "fill" + tl[:2])
-
-            def km(name, k0, k1): return S(name, ob + PW * k0, ob + PW * k1)
+            def km(name, k0, k1):
+                at = DMS * o3 + 16 if name == "dm" else ob
+                return S(name, at + PW * k0, at + PW * k1)
 
             def against(out, src, k0, k1, tl, o):
                 its = [(km(out, k, k + 1), S(src, ob + k, ob + n16, 16), PS(tl, 0, PW)) for k in range(k0, k1)]
@@ -354,16 +383,35 @@ def build_ops(par):
                 act(ab, d, ACT.Abs)
                 either(lambda: act(out, ab, ACT.Sigmoid, 384.0, -256.0), lambda: ts(out, ab, 1.0, None, ALU.is_le), "V" if way == 1 else "S")
 
-            xp = gather("xg", "xw", "rin", oi)
+            Y2 = S("y2", 2 * o, 2 * o + 2 * PW)
+            via = not t and par["via"][h]
+            who = "" if via else par["yb"][h]; bn = 8 // max(1, len(who))
+            if "E" in who: many("V", [lambda c=c: cp(S("y2", 2 * o + c, 2 * o + 2 * PW, 2), YIN) for c in range(2)], "y2")
+            for j, e in enumerate(who):
+                cs = range(bn * j, bn * j + bn); outs = [S("yb", ob + k, ob + n16, 16) for c in cs for k in (c, c + 8)]
+
+                def on_s(): return many("S", [lambda x=x: act(x, YIN, ACT.Identity) for x in outs], "yb")
+                if e == "S": on_s()
+                elif e == "G": many("G", [lambda x=x: hand(x, YIN) for x in outs], "yb")
+                else: either(on_s, lambda: many("V", [lambda c=c: cp(S("yb", ob + c, ob + n16, 8), Y2) for c in cs], "yb"))
+            if via:
+                for j in range(2):
+                    move(S("yb", ob + 512 * j, ob + 512 * j + 512), IND("xw", 0, W, S("rin", oi + PW // 2 * j, oi + PW // 2 * (j + 1))))
+                for c in range(NC):
+                    tl = "Dx%s_%d" % (v, c)
+                    k = mm([(PS(tl, j, 512, KK), NID, YIN) for j in range(KK)], "fillDx")
+                    for j in range(2):
+                        mm([(PS(tl, 256 * j, 256 * j + 256), IDN, S("yb", ob + 512 * j + c, ob + 512 * j + 512, NC))], behind=[k])
+                    move(S("xd", ob + c, ob + n16, NC), PS(tl, 0, 512))
+            else: gather("xd", "xw", "rin", oi)
             cp(s4(3), RU, "rf")
-            ts(sm("kp"), RU, 32.0, col(5), ALU.mult, ALU.add)
-            for c in range(NC):
-                tl = "Dx%s_%d" % (v, c); d = PS(tl, 0, 512)
-                k = fill(tl, NID, YIN)
-                for i0, i1 in xp:
-                    mm([(PS(tl, KK * i0, KK * i1), IDN, jc("xg", c, i0, i1))], behind=[k])
-                test(cls("nx", c), cls("ad", c), d, par["xs"][h][c])
-                if par["xs"][h][c] == 0: act(cls("ad", c), d, ACT.Abs)
+            ts(s4(5), RU, 32.0, col(5), ALU.mult, ALU.add, "kp")
+            for name in ("nx", "ad"):
+                pw = PW // par[name]
+                for i0 in range(0, PW, pw):
+                    out, d = cube(name, i0=i0, i1=i0 + pw), S("xd", ob + 16 * i0, ob + 16 * (i0 + pw))
+                    if name == "nx": near(out, d)
+                    else: act(out, d, ACT.Abs)
             gather("lg", LW if t or par["conv"] == 1 else "li", "rin", oi)
             tl = "n" + v
             for k0 in (0, KK):
@@ -371,49 +419,37 @@ def build_ops(par):
                    + ([] if k0 else [(PS(tl, 0, PW), IDN, cst("c2048"))]))
             cp(sm("nu"), PS(tl, 0, PW))
             tt(s4(2), PS(tl, 0, PW), s4(3), ALU.subtract, "nr")
-            ts(s4(1), PS(tl, 0, PW), -1.0, None, ALU.mult, nm="nm")
-            zp = gather("zg", "xw", "nu", o)
-
-            def byclass(out, lhs, name, behind=(), head=()):
-                for c in range(NC):
-                    mm(list(() if c else head) + [(out, lhs(k), ks(name, k)) for k in range(c, 16, NC)], behind=behind)
-            tl = "nb" + v
-            byclass(PS(tl, 0, PW), lambda k: S("nc", 143 * k, 143 * k + 128), "nx", head=[(PS(tl, 0, PW), IDN, cst("cm8"))])
-            either(lambda: act(sm("good"), PS(tl, 0, PW), ACT.Sigmoid, -240.0 * 16, 16.0), lambda: ts(sm("good"), PS(tl, 0, PW), 240.0, None, ALU.is_ge))
-            ts(sm("nm"), PS(tl, 0, PW), M32, M32, ALU.add, ALU.subtract, "nbr")
-            tt(sm("cnt"), PS(tl, 0, PW), sm("nm"), ALU.subtract)
-            either(lambda: act(sm("sa"), sm("cnt"), ACT.Sigmoid, -896.0, 256.0), lambda: ts(sm("sa"), sm("cnt"), 4.0, None, ALU.is_ge))
+            gather("zg", "xw", "nu", o)
+            tl = "nb" + v; out = PS(tl, 0, PW); pn = par["pn"]
+            for k0 in range(0, 16, pn):
+                mm([(out, S("nc", 143 * k, 143 * k + 128), cube("nx", k=k)) for k in range(k0, k0 + pn)])
+            either(lambda: act(sm("good"), out, ACT.Sigmoid, -248.0 * 16, 16.0), lambda: ts(sm("good"), out, 248.0, None, ALU.is_ge))
+            move(sm("nbv"), out, -8.0)
             tl = "Dm" + v; dn = par["dn"]
-            mm([(PS(tl, 0, PW), lhs, rhs) for lhs, rhs in ((IDN, cst("cm")), (full("tri"), sm("good")), (IDN, cst("c16")), (NID, cst("c16")))])
+            steps(1, [(PS(tl, 0, PW), lhs, rhs) for lhs, rhs in ((IDN, cst("cm")), (full("tri"), sm("good")), (IDN, cst("c1")), (NID, cst("c1")))])
             for k0 in range(0, 16, dn):
-                against("dm", "xg", k0, k0 + dn, tl, ALU.max)
-            move(sm("oh"), PS(tl, 0, PW))
-            tl = "cT" + v
-            mm([(PS(tl, 0, PW), full("bo"), sm("sa"))])
-            either(lambda: act(sm("nl"), PS(tl, 0, PW), ACT.Sigmoid, S("thr", 8 * t, 8 * t + 1), 256.0),
-                   lambda: ts(sm("nl"), PS(tl, 0, PW), 256.0, S("thr", 8 * t + 1, 8 * t + 2), ALU.mult, ALU.is_ge))
-            tl = "ya" + v
-            mm([(PS(tl, 0, PW), IDN, sm("oh")), (PS(tl, 0, PW), full("i64"), sm("nl"))])
-            tt(sm("yy"), YIN, PS(tl, 0, PW), ALU.min)
-            tl = "K" + v
-
-            def both(name, j): return S(name, ob + j, ob + n16, KK)
-            k = mm([(PS(tl, 0, 192), IDN, S("kc", 0, 192))] + [(PS(tl, j, 128, 8), both("ad", j), S("o512", 0, 16)) for j in range(KK)], "Ka")
-            mm([(PS(tl, 0, 128, 1, PW * c, PW * c + PW), sm("sa"), S("pen", 128 * c, 128 * c + 128)) for c in range(NC)], "Kp", behind=[k])
+                against("dm", "xd", k0, k0 + dn, tl, ALU.mult)
+            tl = "K" + v; out = PS(tl, 0, PW)
+            ks = [mm([(out, hk("hp", r), cube("nx", r=r)) for r in range(r0, r0 + pn)], "Kn") for r0 in range(0, 16, pn)]
+            k = mm([(out, IDN, cst("cp")), (out, NID, cst("cp")), (out, IDN, cst("kb"))], "Kr", behind=ks)
+            for r0 in range(0, 16, pn):
+                mm([(out, hk("hs", r), cube("ad", r=r)) for r in range(r0, r0 + pn)], "Ka", behind=[k])
+            KM, KV = S("km", o + 15, o + PW, 16), S("kv", o + 15, o + PW, 16)
+            scan(sm("km"), cst("rsk"), out, ALU.add, ALU.min)
+            scan(sm("kv"), S("td", 128 * a + PW, 128 * a + 2 * PW), out, ALU.max, ALU.subtract)
+            ts(four("ka"), KM, 16 * PW - 1, None, ALU.bitwise_and)
+            if par["perq"]:
+                many("V", [lambda q=q: ts(S("ko", 8 * o3 + q, 8 * o3 + q + 1), S("ka", 8 * o3 + q, 8 * o3 + q + 1), S("kv", o + 16 * q + 15, o + 16 * q + 16), 16.0, ALU.min, ALU.add)
+                           for q in range(PW // 16)], "ko")
+            else:
+                tt(four("kt"), four("ka"), KV, ALU.min)
+                ts(four("ko"), four("kt"), 16.0, None, ALU.add)
+            kyn = tt(YN, IND("dm", DMS * o3, DMS * o3 + 16 + n16, four("ko")), YIN, ALU.add)
+            if t < V - 1: either(lambda: act(four("lf"), KV, ACT.Sign), lambda: ts(four("lf"), KV, 0.0, 2.0, ALU.is_gt, ALU.mult))
+            tl = "Kd" + v; od = 144 * h + 8
             for k0 in range(0, 16, dn):
-                mm([(PS(tl, 64 + j, 192, 8), km("dm", 2 * j, 2 * j + 2), S("o16", 0, 16)) for j in range(k0 // 2, (k0 + dn) // 2)], "Kd", k0 + dn == 16, [k])
-            oq = 128 * h; od = 144 * h + 8
-            scan(S("sc", oq, oq + 128), full("rs8"), PS(tl, 0, 128), ALU.add, ALU.min)
-            move(S("dr", od, od + 128, 2), PS(tl, 128, 192))
-            k = tt(S("qq", 2 * oq, 2 * oq + 256, 16, 0, PW), S("sc", oq + 7, oq + 128, 8, 0, PW), S("sc", oq + 7, oq + 128, 8, PW, 128), ALU.min)
-            ops[k]["drain"] = True
-            ZB = S("zb", oq, oq + 128, 1, 0, PW)
-            scan(ZB, S("qq", 2 * oq + 128, 2 * oq + 256, 1, 0, PW), S("qq", 2 * oq, 2 * oq + 128, 1, 0, PW), ALU.max, ALU.subtract)
-            IW, NW = S("idn", 0, PW, 1, 0, PW), S("nid", 0, PW, 1, 0, PW)
-            tl = "del" + v
-            mm([(PS(tl, 0, PW), NID, sm("oh")), (PS(tl, 0, PW), full("n16"), sm("nl"))])
-            mm([(PS(tl, 0, PW), ZB, IW)], "delz")
-            kyn = tt(YN, sm("yy"), PS(tl, 0, PW), ALU.max)
+                mm([(PS(tl, j, PW, 8), km("dm", 2 * j, 2 * j + 2), S("bo", 0, 128, 16)) for j in range(k0 // 2, (k0 + dn) // 2)], "Kd")
+            move(S("dr", od, od + 128, 2), PS(tl, 0, PW))
 
             def send(kind, src, dst):
                 def fn(g, T, Q, t=t, h=h):
@@ -423,23 +459,22 @@ def build_ops(par):
             tl = "dd" + v
 
             def xr(a0):
-                return [(PS(tl, a0, a0 + PW), S("dr", od - c, od - c + 128), S("idn", PW * c, PW * c + PW)) for c in range(NC)] + [(PS(tl, a0, a0 + PW), full("i64"), sm("nl"))]
-            mm(xr(0) + [(PS(tl, 0, PW), full("nbo"), YIN), (PS(tl, 0, PW), full("bo"), sm("yy"))] + xr(PW))
-            mm([(PS(tl, PW, 2 * PW), ZB, NW)], "ddz")
+                return [(PS(tl, a0, a0 + PW), S("dr", od - c, od - c + 128), S("idn", PW * c, PW * c + PW)) for c in range(NC)]
+            mm(xr(0) + xr(PW))
+            mm([(PS(tl, PW, 2 * PW), full("bo"), YIN), (PS(tl, PW, 2 * PW), full("nbo"), YN)], "ddz")
             on = 2 * o
             test(S("nn", on, on + 2 * PW), S("nt", on, on + 2 * PW), PS(tl, 0, 2 * PW), 2 if "nn" in par["sg"] else 0)
-            tl = "c2" + v
-            mm([(PS(tl, 0, PW), IDN, sm("cnt")), (PS(tl, 0, PW), NID, S("nn", on, on + PW)), (PS(tl, 0, PW), IDN, S("nn", on + PW, on + 2 * PW))])
-            act(sm("sa2"), PS(tl, 0, PW), ACT.Sign, -3.5)
+            tl = "c2" + v; out = PS(tl, 0, PW)
+            steps(4, [(out, NID, sm("nbv")), (out, IDN, cst("c32")), (out, NID, cst("c32")), (out, IDN, sm("nbv")), (out, NID, S("nn", on, on + PW)), (out, IDN, S("nn", on + PW, on + 2 * PW))])
+            act(sm("sa2"), out, ACT.Sign, -3.5)
 
-            def modulo(out, neg, pos, Y, half, big):
-                return [(out,) + half, (out, neg, Y), (out, NID, big), (out, IDN, big), (out, pos, Y)]
+            def modulo(out, neg, pos, Y, big):
+                return [(out, neg, Y), (out, NID, big), (out, IDN, big), (out, pos, Y)]
             tl = "u" + v
-            its = modulo(PS(tl, 0, PW), full("wn"), full("wp"), YN, (full("bo"), cst("cc")), cst("c4096"))
-            mm(its)
-            tt(sm("pi"), s4(3), PS(tl, 0, PW), ALU.mult)
-            tt(sm("pj"), sm("pi"), sm("kp"), ALU.add)
-            ts(s4(0), sm("pj"), 5, W - 1, ALU.arith_shift_right, ALU.bitwise_and, "far")
+            steps(1, [(PS(tl, 0, 2 * PW), full("bo"), full("cc"))] + modulo(PS(tl, 1, 2 * PW, 2), full("wn"), full("wp"), YN, cst("c4096")))
+            scan(S("pi", on, on + 2 * PW), PS(tl, 0, 2 * PW), s4(3, 2), ALU.mult, ALU.add)
+            ts(s4(0), S("pi", on + 1, on + 2 * PW, 2), 5, W - 1, ALU.arith_shift_right, ALU.bitwise_and, "far")
+            ts(s4(1), sm("nu"), -1.0, None, ALU.mult, nm="nm")
             if 2 in par["zm"][h]: mm([(PS("Dz" + v, 0, PW), IDN, YN)], "fillDz")
             zn = par["zn"]
             for c in range(NC):
@@ -454,30 +489,25 @@ def build_ops(par):
                     test(km("nz", k0, k0 + zn), km("az", k0, k0 + zn), d, par["zs"][h][c])
             tl = "fin" + v
             TF, CH = PS(tl, 2, 4 * PW, 4), PS(tl, 3, 4 * PW, 4)
-            k = mm([(PS(tl, 0, 4 * PW), IDN, S("f0", 0, 4 * PW))], "fino", behind=[kyn])
+            k = mm([(PS(tl, 0, 4 * PW), IDN, S("f0", 0, 4 * PW))], "fino", behind=[] if "fin" in par["ahead"] else [kyn])
             mm([(CH, full("mB"), sm("sa2")), (CH, IDN, cst("c1")), (CH, full("mA"), sm("sa2")), (CH, NID, cst("c1")), (TF, full("q25"), sm("sa2"))], "finc", behind=[k])
             for k0 in range(0, 16, zn):
                 mm([(TF, hk("hz", j), km("nz", j, j + 1)) for j in range(k0, k0 + zn)], behind=[k])
             mm([(TF, IDN, cst("c1")), (TF, NID, cst("c1"))], "finr", True)
-            scan(S("s4o", 4 * o, 4 * o + 4 * PW), PS(tl, 0, 4 * PW), S("s4", 4 * o, 4 * o + 4 * PW), ALU.mult, ALU.add)
+            scan(S("s4o", 4 * o, 4 * o + 4 * PW), PS(tl, 0, 4 * PW), s4(0, 1), ALU.mult, ALU.add)
             RN = S("rout", oi, oi + PW) if t < V - 1 else S("rlast", h * PW, h * PW + PW)
-            cp(RN, s4(3, "s4o"), "rout")
+            cp(RN, S("s4o", 4 * o + 3, 4 * o + 4 * PW, 4), "rout")
             send("r", RN, S("rin", oi + P, oi + P + PW) if t < V - 1 else S("rfin", h * PW, h * PW + PW))
         hs = range(NH); cur[0] = 0
         if t < V - 1:
-            tl = "A%d" % t
-            mm([(PS(tl, 0, PW), full("sel"), S("nl", a * P + h * PW, a * P + h * PW + PW)) for h in hs])
-            op("V", (1.0, PW), lambda g, T, Q, a=a, tl=tl: g.vector.tensor_reduce(ap(T, Q, S("acc", a, a + 1)), ap(T, Q, PS(tl, 0, PW)), AxisListType.X, ALU.add),
-               [PS(tl, 0, PW)], [S("acc", a, a + 1)], "acc")
-            cp(S("ai", 8 * a, 8 * a + 1), S("acc", a, a + 1))
-            ts(S("ai", 8 * a + 4, 8 * a + 5), S("ai", 8 * a, 8 * a + 1), 1, None, ALU.bitwise_and, nm="aj")
-            ts(S("thr", 8 * t + 8, 8 * t + 9), S("ai", 8 * a + 4, 8 * a + 5), st, lo, ALU.mult, ALU.add)
-            ts(S("thr", 8 * t + 9, 8 * t + 10), S("ai", 8 * a + 4, 8 * a + 5), -st, -lo, ALU.mult, ALU.add)
-        parts = [(h * PW, PW) for h in hs] if par["split"] or t == V - 1 else [(0, P)]
-        for i0, n in parts:
+            tl = "A%d" % t; out = PS(tl, 0, 4); lfs = [S("lf", 8 * (a * NH + h), 8 * (a * NH + h) + 4) for h in hs]
+            mm([(PS(tl, 0, 8), IDN, cst("ca", 8))] + [(out, full("one"), x) for x in lfs] + [(out, IDN, cst("c4", 4)), (out, NID, cst("c4", 4))]
+               + [(out, full("non"), x) for x in lfs] + [(out, IDN, cst("one", 4))])
+            scan(S("td", 128 * (1 - a), 128 * (1 - a) + 128, 16), PS(tl, 0, 8), cst("da", 8), ALU.mult, ALU.add, 1.0)
+        for i0, n in [(h * PW, PW) for h in hs]:
             cur[0] = i0 // PW
             tl = "wo%d_%d" % (t, i0); Y = S("yout", t * P + i0, t * P + i0 + n); out = PS(tl, 0, n)
-            mm(modulo(out, full("w5n"), full("w5p"), Y, (IDN, cst("c155", n)), cst("c32", n)) + [(out, IDN, cst("wb", n))])
+            steps(1, [(out, IDN, cst("c155", n))] + modulo(out, full("w5n"), full("w5p"), Y, cst("c32", n)) + [(out, IDN, cst("wb", n))])
             scan(S("ws", a * P + i0, a * P + i0 + n), cst("rs16", n), out, ALU.add, ALU.max)
             offs = S("wou", 16 * a + i0 // 16, 16 * a + (i0 + n) // 16)
             cp(offs, S("ws", a * P + i0 + 15, a * P + i0 + n, 16))
@@ -631,7 +661,7 @@ def prepare(ops, costs):
     for cost in costs:
         pc = [price(f, cost) for f in forms]
         gap = [[0.0 if b == 5 or a == b == 2 else cost["self"] if a == b else cost["hop"] for a in range(6)] for b in range(6)]
-        sets.append(([[c[0] for c in p] for p in pc], [c[1] for c in pc[0]], gap, [cost["self"] if o.get("drain") else 0.0 for o in ops]))
+        sets.append(([[c[0] for c in p] for p in pc], [c[1] for c in pc[0]], gap, [-1e9 if o["eng"] == "N" else 0.0 for o in ops]))
     return succ, left, users, eng, sets, [o["ps"][0] if o["ps"] else None for o in ops], pre, forms
 
 
@@ -653,7 +683,7 @@ def arrange(prep, key, eng, dmax):
         if tl:
             b = bank.get(tl)
             if b is None:
-                if len(fb) < (2 if tl[0] in "DKnAfy" else 1): return False
+                if not fb: return False
                 b = bank[tl] = fb.pop(0); extras[k] = last[b]
             elif eng[last[b]] != eng[k]: extras[k] = last[b]
             last[b] = k; rem[tl] -= 1
@@ -690,10 +720,7 @@ def timing(prep, which, order, extras, eng, form):
 
 def improve(par, costs, given, moves, heat0, ends=False):
     ops = build_ops(par); V = par["visits"]
-    prep = prepare(ops, costs); n = len(ops); seen = {}; slot = []
-    for o in ops:
-        ph = min(o["t"], 1) if o["t"] < V - 1 else o["t"] - V + 3
-        kd = (o["t"], kind(o)); seen[kd] = seen.get(kd, 0) + 1; slot.append((ph, kind(o), seen[kd]))
+    prep = prepare(ops, costs); n = len(ops); slot = slots(ops, V)
     names = sorted(set(slot)); num = {s: j for j, s in enumerate(names)}; slot = [num[s] for s in slot]
     rs = [k for k in range(n) if ops[k]["nm"] == "sendr"]; pre = prep[6]; succ = prep[0]
     may = [not ends or names[s][0] != 1 for s in slot]; some = [k for k in range(n) if may[k]]
@@ -736,9 +763,52 @@ def improve(par, costs, given, moves, heat0, ends=False):
         need = value(base, tau, pick)[2][0][1]; fixed = [k for k in range(n) if ops[k].get("const")]
         for k in reversed(fixed): need[k] = min([need[s] for s in succ[k]] + [1e9]) - 1.0
         for j, k in enumerate(sorted(fixed, key=lambda k: need[k])): tau[slot[k]] = 30.0 * j - 3000.0
+    def sweep(cur, c, part):
+        order, bank, extras = cur[1]; end, st, fin, who = cur[2][c]; form = cur[3]; run, lat, gap, hold = prep[4][c]
+        eng = [prep[3][f][k] for k, f in enumerate(form)]; rn = [run[f][k] for k, f in enumerate(form)]; s = list(st)
+        up = [[] for _ in s]; down = [[] for _ in s]; on = [[] for _ in range(6)]
+        for k in order:
+            on[eng[k]].append(k)
+            for d in pre[k] + ([extras[k]] if extras[k] >= 0 else []):
+                y = rn[d] + lat[d] + gap[eng[k]][eng[d]]; up[k].append((d, y)); down[d].append((k, y))
+        for sign, links in ((-1.0, down), (1.0, up)):
+            for k in sorted(some, key=lambda k: sign * s[k]):
+                e = eng[k]; r = rn[k]
+                if e != 5 and (rnd() > part or k in loads): continue
+                to = max([s[d] + y for d, y in links[k]] + [0.0]) if sign > 0 else min([s[d] - y for d, y in links[k]] + [end - r - lat[k]])
+                if e != 5:
+                    line = on[e]; j = line.index(k); del line[j]
+                    if sign > 0:
+                        while j and s[line[j - 1]] + rn[line[j - 1]] > to: j -= 1
+                        while j < len(line) and s[line[j]] < to + r - 1e-6: to = max(to, s[line[j]] + rn[line[j]]); j += 1
+                    else:
+                        while j < len(line) and s[line[j]] < to + r: j += 1
+                        while j and s[line[j - 1]] + rn[line[j - 1]] > to + 1e-6: to = min(to, s[line[j - 1]] - r); j -= 1
+                    line.insert(j, k)
+                s[k] = to
+        new = list(tau); key = [b + tau[x] for b, x in zip(base, slot)]; z = -1e18; mark = []
+        for k in sorted(range(n), key=lambda k: s[k]):
+            if may[k]: mark.append((k, z))
+            elif key[k] - s[k] * 1e-3 > z: z = key[k] - s[k] * 1e-3
+        first = min(key[k] - s[k] for k in range(n) if not may[k])
+        for k, z in mark: new[slot[k]] = (s[k] + first - 2e4 if z < -1e17 else z + s[k] * 1e-3) - base[k]
+        for line in on[:5]:
+            z = 1e18
+            for k in reversed(line):
+                if not may[k]: z = key[k]
+                elif base[k] + new[slot[k]] >= z:
+                    z -= 1e-3; new[slot[k]] = z - base[k]
+                else: z = base[k] + new[slot[k]]
+        return new
     cur = best = value(base, tau, pick); deps = [set(p) for p in pre]; kept = (base, tau, pick)
     for it in range(moves):
         heat = heat0 * (1.0 - it / moves)
+        if ends and rnd() < par["sweep"]:
+            new = sweep(cur, int(rnd() * len(costs)), rnd()); r = value(base, new, pick, cur, heat * rnd())
+            if r is not None:
+                cur, tau = r, new
+                if r[0] < best[0]: best = r; kept = (base, tau, pick)
+            continue
         if it % par["again"] == 0 and not ends:
             b2, t2 = keys(cur[2][0][1]); r = value(b2, t2, pick)
             if r is not None and r[0] <= cur[0] + heat: base, tau, cur = b2, t2, r
@@ -771,8 +841,204 @@ def improve(par, costs, given, moves, heat0, ends=False):
     return [prep[7][best[3][k]][k] for k in range(n)], best, state
 
 
+def slots(ops, V):
+    seen = {}; out = []
+    for o in ops:
+        ph = min(o["t"], 1) if o["t"] < V - 1 else o["t"] - V + 3
+        kd = (o["t"], kind(o)); seen[kd] = seen.get(kd, 0) + 1; out.append((ph, kind(o), seen[kd]))
+    return out
+
+
+def cycle(par, costs, given, moves, heat0):
+    ops = build_ops(par); prep = prepare(ops, costs); name = slots(ops, par["visits"])
+    mid = [k for k, o in enumerate(ops) if o["t"] == 3]; n = len(mid); num = {name[k]: j for j, k in enumerate(mid)}
+    pre = [[(num[name[d]], 3 - ops[d]["t"]) for d in prep[6][k] if ops[d]["t"]] for k in mid]
+    near = ([[d for d, l in p if not l] for p in pre], [[] for _ in mid]); tiles = {}
+    for j, k in enumerate(mid):
+        for d in near[0][j]: near[1][d].append(j)
+        if prep[5][k]: tiles.setdefault(prep[5][k], []).append(j)
+    tiles = list(tiles.values()); late = [(j, d, l) for j in range(n) for d, l in pre[j] if l]
+    engs = [[prep[3][f][k] for k in mid] for f in (0, 1)]
+    runs = [[[s[0][f][k] for k in mid] for f in (0, 1)] for s in prep[4]]
+    lats = [[s[1][k] + (0.0 if ops[k]["nm"][:4] == "send" else c["hop"]) for k in mid] for s, c in zip(prep[4], costs)]
+    rs = [j for j, k in enumerate(mid) if ops[k]["nm"] == "sendr"]; free = [j for j, k in enumerate(mid) if "alt" in ops[k] and ops[k]["nm"] not in par["stay"]]
+    data = [{d for d, l in p} for p in pre]
+    T0 = given[0]; tau = [given[1][name[k]][0] for k in mid]; pick = [given[1][name[k]][1] for k in mid]
+    x = [par["seed"] + moves]; M = par["rounds2"]
+
+    def rnd():
+        x[0] = (x[0] * 1103515245 + 12345) % 2 ** 31
+        return (x[0] >> 8) / 2.0 ** 23
+
+    def program(tau, pick):
+        key = list(tau)
+        for again in range(4):
+            for j in range(n):
+                y = key[j]
+                for d in near[0][j]:
+                    if key[d] >= y: y = key[d] + 1e-3
+                key[j] = y
+            bad = False
+            for j, d, l in late:
+                if key[d] - l * T0 >= key[j]: key[j] = key[d] - l * T0 + 1e-3; bad = True
+            if not bad: break
+        if bad: return None
+        w = [int(y // T0) for y in key]; pos = [y - a * T0 for y, a in zip(key, w)]; eng = [engs[f][j] for j, f in enumerate(pick)]
+        order = sorted(range(n), key=lambda j: pos[j]); extra = {}; ev = []; live = 0
+        for us in tiles:
+            us = sorted(us, key=lambda j: key[j]); a = us[0]
+            for b in us[1:]:
+                if eng[a] != eng[b]: extra[b] = a - (w[b] - w[a]) * n
+                a = b
+            live += w[a] - w[us[0]]; ev.append((pos[us[0]], 1, us[0])); ev.append((pos[a], -1, a))
+        ev.sort(); top = y = live
+        for p, s, j in ev:
+            y += s
+            if y > top: top = y
+        idle = max(8, top) - live; rel = [j for p, s, j in ev if s < 0]; i = -idle
+        for p, s, j in ev:
+            if s > 0:
+                extra[j] = rel[i] - n if i < 0 else rel[i]; i += 1
+        prog = []
+        for j in order:
+            e = eng[j]; a = w[j]
+            dl = [d - (a + l - w[d]) * n for d, l in pre[j] if e != 2 or eng[d] != 2]
+            if j in extra and (e != 2 or eng[extra[j] % n] != 2): dl.append(extra[j])
+            prog.append((j, e, 6 if e == 5 else e, dl))
+        return key, w, prog, max(0, top - 8), pick
+
+    def run(pg, c, state, rounds, trace=False):
+        key, w, prog, over, pick = pg; f0, T = state; lat = lats[c]; rn = runs[c]
+        av = [f - (3 + a) * T for f, a in zip(f0, w)]; av += [y + T for y in av]; av += [y + T for y in av[n:]]; av += [0.0] * (n * rounds)
+        fr = [-1e18] * 7; who = [-1] * len(av); last = [-1] * 7; full = []
+        for j, e, e2, dl in prog:
+            fr[e2] = av[2 * n + j] - lat[j]; full.append((j, e, e2, dl, rn[pick[j]][j], lat[j]))
+        for b in range(3 * n, (3 + rounds) * n, n):
+            if trace:
+                for j, e, e2, dl, r, l in full:
+                    s = fr[e]; p = last[e]
+                    for d in dl:
+                        if av[b + d] > s: s = av[b + d]; p = b + d
+                    s += r; fr[e2] = s; last[e2] = b + j; av[b + j] = s + l; who[b + j] = p
+            else:
+                for j, e, e2, dl, r, l in full:
+                    s = fr[e]
+                    for d in dl:
+                        y = av[b + d]
+                        if y > s: s = y
+                    s += r; fr[e2] = s; av[b + j] = s + l
+        b = (2 + rounds) * n
+        if not trace: return sum(av[b + j] - av[2 * n + j] for j in rs) / (len(rs) * rounds) + 2000.0 * over
+        T = sum(av[b + j] - av[b - 2 * n + j] for j in rs) / (2 * len(rs)); z = av[b + rs[0]]; pairs = []
+        k = b + rs[-1]
+        while who[k] >= b - 2 * n:
+            p = who[k]
+            if p % n not in data[k % n]: pairs.append((p % n, k % n, (k // n - w[k % n]) - (p // n - w[p % n])))
+            k = p
+        return ([av[b + j] - z + w[j] * T for j in range(n)], T), pairs
+
+    def settle(pg, states): return [run(pg, c, s, par["settle"], True) for c, s in enumerate(states)]
+
+    def worth(pg, got): return sum(g[0][1] * c["weight"] for g, c in zip(got, costs)) + 2000.0 * pg[3]
+
+    def shift(new, k, to, side, sign, depth):
+        new[k] = to
+        for d in side[k] if depth else ():
+            if (new[d] - to) * sign > 0: shift(new, d, to - sign, side, sign, depth - 1)
+    def sweep(pg, c, state, part):
+        key, w, prog, over, pick = pg; f0, T = state; lat = lats[c]; rn = [runs[c][f][j] for j, f in enumerate(pick)]
+        s = [f0[j] - lat[j] - rn[j] for j in range(n)]; up = [[] for _ in s]; down = [[] for _ in s]; on = [[] for _ in range(7)]; eng = [0] * n
+        for j, e, e2, dl in prog:
+            on[e].append(j); eng[j] = e
+            for d, gap in [(x % n, rn[x % n] + lat[x % n] - (-(x // n) - w[j] + w[x % n]) * T) for x in dl] + [(d, rn[d] - l * T) for d, l in pre[j]]:
+                up[j].append((d, gap)); down[d].append((j, gap))
+        for sign, links in ((-1.0, down), (1.0, up)):
+            for j in sorted(range(n), key=lambda j: sign * s[j]):
+                if not links[j] or (eng[j] != 5 and rnd() > part): continue
+                to = sign * max(sign * s[d] + gap for d, gap in links[j]); r = rn[j]
+                if eng[j] != 5:
+                    a = to if sign > 0 else -to - r
+                    for b, y in sorted(((((s[x] if sign > 0 else -s[x] - rn[x]) + rn[x] - a) % T - rn[x], rn[x]) for x in on[eng[j]] if x != j)):
+                        at = to if sign > 0 else -to - r
+                        if a + b >= at + r - 1e-6: break
+                        if a + b + y > at: to = a + b + y if sign > 0 else -(a + b + y) - r
+                if sign * (s[j] - to) > 0: s[j] = to
+        return [y + 2 * T + j * 1e-4 for j, y in enumerate(s)], T
+    pg = program(tau, pick); got = settle(pg, [(pg[0], T0)] * len(costs)); got = settle(pg, [g[0] for g in got])
+    best = (worth(pg, got), T0, pg[0], pick, [g[0][1] for g in got])
+    for it in range(moves):
+        heat = heat0 * (1.0 - it / moves) ** par["cool"]
+        if par.get("log") and it % (moves // 10) == 0: par["log"](it, round(worth(pg, got)), round(best[0]))
+        if it % par["again"] == 0:
+            f0, T = got[0][0]; keep = T0; T0 = T
+            p2 = program([f0[j] - lats[0][j] - runs[0][pick[j]][j] + 2 * T + j * 1e-4 for j in range(n)], pick)
+            g2 = p2 and settle(p2, [g[0] for g in got])
+            if p2 and worth(p2, g2) <= worth(pg, got) + heat: pg, got = p2, g2
+            else: T0 = keep
+        if rnd() < par["sweep"]:
+            c = int(rnd() * len(costs)); keep = T0; new, T0 = sweep(pg, c, got[c][0], rnd()); p2 = program(new, pick)
+            g2 = p2 and settle(p2, [g[0] for g in got])
+            if p2 and worth(p2, g2) <= worth(pg, got) + heat * rnd():
+                pg, got = p2, g2
+                if worth(pg, got) < best[0]: best = (worth(pg, got), T0, pg[0], pick, [g[0][1] for g in got])
+            else: T0 = keep
+            continue
+        tau = pg[0]; new = list(tau); other = pick; z = rnd()
+        if z < par["aimed"]:
+            pairs = got[int(rnd() * len(costs))][1]
+            if not pairs: continue
+            j = int(rnd() * len(pairs)); p, k, l = pairs[j]
+            while j + 1 < len(pairs) and pairs[j + 1][1] == p and rnd() < par["far"]:
+                j += 1; p = pairs[j][0]; l += pairs[j][2]
+            z = rnd()
+            if z < .2 and (p in free or k in free):
+                other = list(pick); other[p if p in free else k] ^= 1
+            elif z < .6: shift(new, k, tau[p] - l * T0 - 1.0 - 50.0 * rnd(), near[0], 1.0, 3)
+            else: shift(new, p, tau[k] + l * T0 + 1.0 + 50.0 * rnd(), near[1], -1.0, 3)
+        elif z < par["aimed"] + .05:
+            other = list(pick); other[free[int(rnd() * len(free))]] ^= 1
+        else:
+            k = int(rnd() * n); z = (rnd() - .5) * par["reach"]
+            shift(new, k, tau[k] + z, near[z > 0], 1.0 if z < 0 else -1.0, 3)
+        p2 = program(new, other)
+        if p2 is None or p2[2] == pg[2]: continue
+        worse = -2000.0 * pg[3]; slack = heat * rnd()
+        for c, g in enumerate(got):
+            worse += (run(p2, c, g[0], M) - g[0][1]) * costs[c]["weight"]
+            if worse > slack + par["hope"] * (len(costs) - 1 - c): break
+        if worse > slack: continue
+        if abs(worse) >= 1e-3:
+            g2 = settle(p2, [g[0] for g in got])
+            if worth(p2, g2) > worth(pg, got) + slack: continue
+            got = g2
+        pg, pick = p2, other
+        if worth(pg, got) < best[0]: best = (worth(pg, got), T0, pg[0], pick, [g[0][1] for g in got])
+    out = dict(given[1]); low = min(best[2])
+    for s in out:
+        j = num.get((1,) + s[1:])
+        if j is not None and s[0] < 3: out[s] = (best[2][j] - low, best[3][j])
+    return (best[1], out), best
+
+
+def words(ops, V):
+    return [(s, [e + s[1][1:] + "abcdefghijklmnopqrstuvwxyz"[s[2] - 1] for e in [o["eng"]] + ([o["alt"]["eng"]] if "alt" in o else [])])
+            for o, s in zip(ops, slots(ops, V)) if o["t"] == 3]
+
+
+def read(par, text):
+    ops = build_ops(par); its = text.split(); at = {x.rstrip("'"): 80.0 * (j + len(its) * x.count("'")) for j, x in enumerate(its)}
+    mid = {s[1:]: [(at[x], f) for f, x in enumerate(ws) if x in at][0] for s, ws in words(ops, par["visits"])}
+    out = {}
+    for o, s in zip(ops, slots(ops, par["visits"])):
+        out[s] = mid[s[1:]] if s[0] < 3 and s[1:] in mid and (s[0] or s[1][1:-1] not in ("yb", "xd")) else (
+            160.0 * len(its) if s[0] > 1 else max([ops[d]["lat"] for d in o["deps"]] + [0.0]), 0)
+    return 80.0 * len(its), out
+
+
 def plan(par, costs):
-    state = None
+    state = read(par, ROUND)
+    for moves, heat in par["cycle"]:
+        state = cycle(par, costs, state, moves, heat)[0]
     for visits, moves, heat, ends in par["stages"]:
         ops, best, state = improve(dict(par, visits=visits), costs, state, moves, heat, ends)
     return ops, best

@@ -10,6 +10,7 @@ NC = 2
 KK = 16 // NC
 M4 = float((2 ** 23 + 1) * 4)
 M1, M16, M32, M4096 = (float(3 * 2 ** 22 * n) for n in (1, 16, 32, 4096))
+AN = 192.0
 PEN = float(2 ** 24)
 BIG = float(2 ** 22)
 DMS = 16 + 16 * PW + 16
@@ -19,23 +20,25 @@ SCRATCH = {
     "xw": [W, B], "li": [W, I32], "lw": [W, F], "l16": [W, H16],
     "rin": [(V + 1) * P, U16], "yin": [(V + 1) * P, B], "rout": [V * P, U16], "yout": [V * P, B], "rfin": [P, F], "rlast": [P, F],
     "wi": [8, I32], "yzf": [256, F], "ci": [8, I32], "cf": [32, F],
-    "ioc": [144, B], "iob": [128, B], "iom": [128, B], "ioj": [64, B], "tmp": [1312, B], "nc": [16 * 144, B], "iok": [288, B], "cm8": [128, B], "tf": [256, F], "ji": [P, I32],
-    "hh": [144, B], "hz": [144, B], "hp": [144, B], "hs": [144, B], "hj": [144, H16], "ba": [16 * 144, B], "kb": [PW, H16],
-    "o8": [16, B], "f0": [4 * PW, B], "rsk": [PW, F], "rs16": [128, F], "td": [256, F], "ca": [8, B], "da": [8, F],
+    "ioc": [144, B], "iob": [128, B], "iom": [128, B], "ioj": [64, B], "tmp": [1312, B], "nc": [16 * 144, B], "iok": [288, B], "iox": [256, B], "idx": [256, B], "cm8": [128, B], "tf": [256, F], "ji": [P, I32],
+    "hh": [144, B], "hz": [144, B], "hy": [144, B], "hp": [144, B], "hs": [144, B], "hj": [144, H16], "ba": [16 * 144, B], "kb": [PW, H16],
+    "o8": [16, B], "b16": [16, B], "ni": [NH * 272, B], "nbr": [2 * P, B], "f0": [4 * PW, B], "rsk": [PW, F], "rs16": [128, F], "td": [256, F], "ca": [8, B], "da": [8, F],
     "wou": [32, U16], "ws": [2 * P, F], "wp": [128, H16], "wn": [128, H16],
-    "lg": [2 * 2048, H16], "dr": [2 * NH * 144, B], "nn": [2 * 2 * P, B], "nt": [2 * 2 * P, B], "y2": [2 * 2 * P, B], "dm": [2 * NH * DMS, B],
+    "lg": [2 * 2048, H16], "dr": [2 * NH * 144, B], "nn": [2 * 2 * P, B], "yd": [2 * 2 * P, B], "y2": [2 * 2 * P, B], "dm": [2 * NH * DMS, B],
     "s4o": [2 * 4 * P, F], "pi": [2 * 2 * P, I32], "ka": [32, I32], "kt": [32, F], "ko": [32, U16], "lf": [32, B],
 }
 for _n in ("idn", "nid", "q25", "nbo", "c32", "bo", "tri", "mA", "mB", "w5p", "w5n", "wb", "c1", "c4096", "cc", "c155", "c2048",
-           "cm", "ck", "cp", "c4", "one", "non"):
+           "cm", "cp", "c4", "one", "non", "ida", "nia", "boa", "nba", "by", "i32"):
     SCRATCH[_n] = [128, B]
-for _n in ("xd", "yb", "zg", "az", "nz", "dz"):
+for _n in ("xd", "yb", "zg", "dz"):
     SCRATCH[_n] = [2 * 2048, B]
 for _n, _d in (("nu", U16), ("good", B), ("nbv", H16), ("sa2", B), ("pj", I32), ("km", I32), ("kv", F)):
     SCRATCH[_n] = [2 * P, _d]
 SCRATCH = {_n: ("sbuf", [128, _v[0]], _v[1]) for _n, _v in SCRATCH.items()}
 for _n in ("ad", "nx"):
     SCRATCH[_n] = ("sbuf", [128, 2 * P // 16, 16, 16], B)
+SCRATCH["nl"] = ("sbuf", [128, 32 * NH, KK], H16)
+SCRATCH["zr"] = ("sbuf", [128, 18 * NH, KK], H16)
 SCRATCH["s4"] = ("sbuf", [128, 2 * NH * (4 * PW + 4) + 4], I32)
 for _n in range(8):
     SCRATCH["pb%d" % _n] = ("psum", [128, 512], F)
@@ -63,6 +66,8 @@ PAR.update({"xd": ("VV", "VV"), "bn": 4, "nx": 2, "ad": 2, "pn": 8, "perq": 0, "
             "cycle": (100000, 200.0), "lead": 0.0, "rounds": 10, "settle": 4, "rounds2": 2, "ahead": ("c",), "cool": 1.0,
             "zm": ((2, 2), (1, 2)), "cycle": ((50000, 130.0), (50000, 70.0)), "stay": ("lg", "zg"), "sweep": .03, "yb": ("EE", "EE"), "ahead": ("c", "Dm", "u", "wo"), "stages": ((3, 25000, 200.0, True), (V, 5000, 60.0, False))})
 PAR.update({"yb": ("SS", "SS"), "via": (0, 1), "xat": 0, "cuts": CUTS, "cycle": (), "sweep": .06, "stages": ((3, 45000, 120.0, True), (V, 200, 20.0, False))})
+PAR.update({"zm": ("VVVV", "VVVV"), "nx": ("VV", "VV"), "ad": ("SS", "SS"), "first": "VV", "conv": "S", "whole": 0, "yb": ("SS", "SS"), "ns": (1, 1), "fs": (1, 1)})
+FIRST = LAST = ""
 ROUND = """
 Nay0a PKd1a' Vdz0a' Vdz0d' Pu00a' Pc00a' Vkv1a' Vkm1a' PKd1b' Vnz0a' Vdz0b' Pfino0a' Szg1b' Pddz0a' Vka1a' PKd1c' Pdd0a' Pwo00a' Pwo0a' Vdz0c' Pu0a' Vkt1a' Vnn0a'
 Pfin0a' Vnz0d' Pc01a' Vko1a' Vnz0b' Pc0a' Vnz0c' PKd1d' Pfin0d' Vyout1a' Pfin0b' Ssa20a' Vpi0a' Sdr1a' Pfin0c' Vkp1a' Syb0a Vnr1a' Gsendy1a' Vws0a' PfillDz1a' Pfinc0a'
@@ -72,6 +77,129 @@ Vrout1a' Vxw1a' Gsendr1a' Vlw1a' Syb1b Slf1a' Vxd0a Slg0a Slg0b Nar1a Vlf0a' Vxd
 Pnb0a Slg1a PKr0a Pn0b Vgood0a PKa0b Vnx1a Vnx1b Sad1a PDm0a PKa0a Vkp0a Vnu0a Vdm0b PDm01a Sad1b Vdm0d Pnb1b Pnb1a Vkm0a Vdm0a Szg0b Szg0a Pn1a Vkv0a Vka0a Vgood1a
 Vnr0a Vrf1a PKd0d PKd0b PKd0a Vkt0a Vdm0c PDm1a Pn1b Vko0a Snbv1a Vdm1d PKn1a Vyout0a PKn1b PKd0c Vnu1a Vdm1c Gsendy0a Vdm1b PfillDz0a PKr1a PKa1a Snbv0a Vdm1a Sdr0a
 Szg1a PKa1b
+"""
+
+
+PAR.update({"ns": (1, 1), "fs": (2, 2), "im": 1, "re": 0, "ahead": ("c", "Dm", "u", "wo", "fin")})
+FIRST = """
+Yljur0a Slown0a Slwgt0a Ylx0a Yll00a Yll10a Yll20a Yll30a Gci0a Gioc0a Vci0b Vcf0a Giom0a Vcf0b Vidn0a Stf0a Vc10a Vc20480a Gdm0d Vcf0c Scf0g Vnl0a Sc1550a Vnc0e Giob0a Sca0b
+Vtmp0k Snc0a Vnc0b Vcf0i Szr0a Vnc0f Pwo00a Vcf0h Snid0a Vnc0d Gdm0b Vcf0d Stmp0c Vtf0b Giok0a Sda0a Snc0l Vbo0a Sone0a Vnc0m Giok0b Gdr0a Vru0b Syb0a PfillDx1a Vhh0a Vcf0e
+Vtmp0e PfillDx1b Vcf0n Vrsk0a Vrf1a Vru0a Syb0b Vnc0n Vnc0j Gdm0a Vtmp0f Giox0a Vcf0j Vrf0a Snc0g Vf00c Vcf0f Snc0p Vtmp0a Vtmp0j Gdm0c Stmp0b Vnc0o Vwi0a Snon0a Vwb0a Gioj0a
+Snc0h Vtmp0i Vnc0k Scm0a Vnc0i Sca0a Snc0c Sca0c PDm00a PDm01a Vxd0b Syb1b Vcf0o Syb1a Vtmp0d Vxd0a PDx1d PDx1b Sby0a Vnc0q Stmp0h Sda0c PDx1a Sq250a Vnx0a PDx1c Scp0a Shz0a
+Glw0c Vidx0a Sxd1a Vcf0k Vnx0b Vtmp0g Vkp0a Vcf0m Sxd1b VmA0a Pnb0b Vcc0a Vcf0l Pnb0a Vrs160a Shj0a Vtri0a Glw0a Vkp1a Vnx1b Sgood0a Sad0b Vnx1a PDm0a Shp0a Vdm0f Sc40a Std0b
+Sf00d Vdm0g Si320a PKn0a Sad0a Vdm0h PKn0b Vdm0e PKn1a Shy0a Pnb1a Sw5p0a Glw0g Sad1b PKd0b PKd0c Pnb1b PKd0a Shs0a PKn1b Vlg0b Skb0a Sc320a PKd0d Snbv0a Sad1a PKr0a PKa0a
+Glw0f PKa0b Sf00a Vlg0a Sda0b Std0a PKr1a Snia0a PKa1a Sida0a Glw0e Snba0a PKa1b Snbo0a Sdr0b Std0c Vkm0a Sboa0a Vlg1b Scc0b PNt0a Pdd0a Snl0b Vka0a Glw0d Swn0a Vkv0a Vkm1a
+Sw5n0a Vkv1a Vc40960a Sgood1a Pn0a Swp0a Vkt0a Sf00b Slf0a Slf1a PDm1a Vnu0a Snbv1a Pc00a Vlg1a Szg0a Glw0b Vko0a VmB0a PNt1a Szg0b Vyout0a Vdm1a Vka1a Pddz0a Vnl1a Pwo0a Vdm1b
+Gsendy0a PfillDz0a Pcy0a Nay0a:1 Snn0a Vdm1c Pn1a Vdm1d Pc0a Glw0i Pfino0a Vnu1a Pfinz0b Vkt1a Vdz0c Ssa20a Pfinz0a Szg1a Vdz0a Pfinc0a Vdz0b Pu00a Pu0a PKd1d Vko1a Pfin0c
+Vdz0d Pfin0a Szg1b Pfin0b Vpi0a PKd1a Vyout1a PKd1b PKd1c Vnr0a Pfiny0a Pfin0d Vnm0a Vfar0a Pfinr0a Vws0a Pu01a Gsendy1a Syb0a:1 Vdr1a Pddz1a PfillDz1a Pu1a Vs4o0a Pc01a Pdd1a
+Pfino1a Vpi1a Nay1a:1 Pfinz1b Vrout0a Vdz1c Snn1a Pcy1a Pwo01a Pfiny1a Pfinz1a Vdz1d Gsendr0a Pc1a Vdz1a Pwo1a Vdz1b Pfin1d Ssa21a Glw0h Pfin1c Syb0b:1 Vwou0a Pfin1a Vfar1a
+Vnr1a Pfinc1a Vws1a Vnm1a Pfin1b Vlw0j Pfinr1a Pwo00a:1 PA0a Vwou1a Vs4o1a PDm00a:1 Vxw0a Syb1b:1 Vrout1a Vxw1a Syb1a:1 Gsendr1a Vlw1a Vtd0d
+"""
+ROUND = """
+Nay0a Vkv1a' Pdd0a' Vkm1a' Vnu1a' Pcy0a' Vdm1b' PfillDz0a' Pwo0a' Pfino0a' Vnn0a' Szg1b' Pfiny0a' Vka1a' Pfinz0b' Vdz0b' PKd1b' Vkt1a' Pc0a' Vdz0c' Pu00a' Pu0a' Pfinz0a' Vdz0a'
+Ssa20a' Szg1a' PKd1c' Vko1a' Pfin0c' Vdz0d' Pfin0b' PKd1d' Vpi0a' Pfinc0a' Vyout1a' PKd1a' Pfin0a' Vws0a' Pfin0d' Vnm0a' Vfar0a' Pfinr0a' Sdr1a' Vkp1a' Gsendy1a' Pu01a' Syb0a
+Vwou0a' Pc01a' PfillDz1a' Pfino1a' Vs4o0a' Pddz1a' Pdd1a' Vdz1a' Pu1a' Nay1a Pfinz1b' Vrout0a' Snn1a' Vdz1b' Pfinz1a' Slf1a' Vrf1a' Gsendr0a' Vdz1d' Pcy1a' Pc1a' Pwo01a'
+Pfin1b' Vpi1a' Pwo1a' Vdz1c' Ssa21a' Pfin1a' Slf0a' Nar0a Syb0b Pfin1d' Vnr1a' Pfiny1a' Vws1a' Pfinc1a' Vfar1a' Vnm1a' Pfin1c' Vlw0a' Pfinr1a' PDm01a Pwo00a PA0a' Vwou1a'
+Vs4o1a' PDm00a Vxw0a' Syb1b Vrout1a' Vxw1a' Syb1a Gsendr1a' Vlw1a' Vtd0a' Vxd0a Slg0b Nar1a Vxd0b Slg0a Vnx0a Sad0a Vrf0a Vnx0b PNt0a Vkp0a Sad0b Vxd1a PKn0b PKn0a Snl0a Slg1b
+PKr0a Pnb0b Vxd1b Pnb0a Pn0a PKa0a Sgood0a Snbv0a PKa0b Vnx1a Slg1a PDm0a Vnx1b Vnu0a Vkm0a Vkv0a Vdm0c Pnb1b Sad1b Vka0a Vdm0a Pnb1a Vdm0d PKn1a Sad1a Vkt0a PNt1a Vgood1a
+Vdm0b PKn1b Szg0a Vko0a Vnr0a PDm1a Vnl1a PKr1a Vnbv1a PKd0d Vyout0a PKd0a PKd0c Vdm1d PKd0b PKa1b Gsendy0a Vdm1a Szg0b PKa1a Vdr0a Vdm1c Pn1a Pddz0a Pc00a
+"""
+LAST = """
+Pwo00a Pc00a:4 Nay0a Pu1a:4 Nay1a Pc1a:4 Syb0b Slf0a:4 Nar0a Pfinr1a:4 Syb0a Vwou1a:4 PDm00a Vs4o1a:4 Pu00a PDm01a Vxw0a:4 Syb1a Vxw1a:4 Syb1b Vtd0a:4 Vkp0a Vxd0a Nar1a Vxd0b
+Slg0a Slg0b PNt0a Vnx0a Sad0a Vnx0b Vxd1a Sad0b PKn0b Vxd1b Slg1b PKn0a Snl0a Pnb0b Pnb0a PKr0a PKa0a PKa0b Vgood0a Vnx1a Vnx1b PDm0a Vkm0a Vnbv0a Slg1a Sad1a Sad1b Vdm0d Vkv0a
+Pn0a Vka0a Pnb1b Pnb1a PNt1a Sgood1a Vnu0a Vrf1a Vdm0b Vkt0a PKn1a Vkp1a Vdm0c Vdm0a PDm1a PKn1b Vko0a Vnbv1a Vrf0a PKr1a Vdm1c PKd0b PKd0c Vyout0a PKd0a PKd0d Vdm1b Vdm1a
+PKa1b Szg0b Snl1a Pn1a Szg0a Gsendy0a PKa1a Pddz0a Vdr0a Pu0a Vnu1a Vnr1a Pwo0a Nay0a! Vdm1d Vkm1a PfillDz0a Vpi0a Pfino0a Vkv1a Pdd0a Vws0a PKd1b Pfinz0a Vka1a Vdz0d PKd1a
+Pc00a Vkt1a Szg1a PKd1c Vdz0c PKd1d Szg1b Pcy0a Pfinz0b Vko1a Vnn0a Vdr1a Vwou0a Pfin0d Vyout1a Pc01a Pu01a Pdd1a Vnr0a Vdz0b Pc0a Gsendy1a Pu1a Pfiny0a Vdz0a PfillDz1a Ssa20a
+Vfar0a Pddz1a Vnm0a Vpi1a Pfin0c Yoo00a! Vdz1c Pfin0b Nay1a! Pfin0a Snn1a Pfinc0a Pcy1a Pfinr0a Pfino1a Vdz1d Pc1a Vdz1a Pfin1c Vs4o0a Ssa21a Vdz1b Pfinz1b Pfinz1a Pfiny1a
+Vrout0a Vnm1a Pfin1d Vfar1a Pfinc1a Gsendr0a Vlw0a Pfin1a Pfin1b Pfinr1a Pwo01a Pwo1a Nar0a! Vs4o1a Vws1a Vrout1a Vwou1a Sl160a! Sl160b! Pyz0a! Sl160c! Gsendr1a Vlw1a Vl160d!
+Pyz0b! Nar1a! Sl161d! Yoo11a! Vl161a! Sl161c! Pyz0c! Pyz0d! Vl161b! Pyz1d! Yoj00a! Pyz1a! Pyz1c! Pyz1b! Syzf1a! Yoj11a! Yoyz1a!
+"""
+
+
+FIRST = """
+Yljur0a Slown0a Slwgt0a Ylx0a Yll00a Yll10a Yll20a Yll30a Gci0a Gioc0a Vci0b Vcf0a Giom0a Vcf0b Vidn0a Sf00c Sc1550a Vc40a Giob0a Vcf0c Scf0g Vcf0k Giok0b Snc0a Vc10a Vc320a
+Vnc0b Sda0a Pwo00a Snc0d Vtmp0e Giok0a Vone0a Snid0a Vf00d Si320a Vcf0i Sf00b Vnc0f Snc0m Gdm0d Vtmp0f Snc0j Vnc0l Vcf0j Gioj0a Snc0i Vtmp0k Vnc0n Vca0b Gdm0a Gdm0c Vq250a
+Vnon0a Giox0a Vru0a Syb0b Vcm0a Vcf0d Vcf0n Vwi0a Vru0b Giox0b Vtmp0i PDm01a PfillDx1b Vbo0a Std0b Vrs160a Stf0a Vcf0h PfillDx1a Vcf0e Syb0a Vnc0g Vnc0c PDm00a Vtf0b Gdr0a
+Vnc0e Snc0h Vcf0f Vnc0k Snl0a Vtmp0c Snc0p Vhh0a Stmp0d Syb1a Vidx0a Vxd0b Vxd0a Syb1b PDx1c PDx1a Vtmp0j Vnx0b Snc0o Sda0b Scp0a Shz0a PDx1b PDx1d Stmp0h Sda0c Vnx0a Vnc0q
+Vrf0a Glw0b Vidx0b Vcf0m Sxd1a Vcf0l Vtmp0g Vwb0a VmB0a Pnb0a Sxd1b Pnb0b Vrsk0a Snba0a Vtri0a Sc40960a Glw0a Sc20480a Sgood0a Sad1a Vnx1b Vnx1a Vcf0o PDm0a Sad0a Vdm0g Vdm0e
+Pnb1b Sf00a Glw0c Shp0a PKn0a Sida0a Skb0a Scc0a PKn1a Stmp0b Sad0b PKn0b PKn1b Sca0a Shy0a Glw0d Vdm0f Vdm0h Shs0a PKr0a Std0a PKd0b Sw5p0a PKd0d PKr1a Sad1b PKd0a PKa0b PKa0a
+Vlg0b Snbv0a Sboa0a Sby0a Pnb1a Snbo0a Glw0f Vlg0a Std0c Snia0a Scc0b Szr0a Sgood1a Sca0c Vkm0a Glw0i Vlg1a PNt0a PKa1b Snl0c Stmp0a PKa1a Vka0a Vkv0a Snl0b PKd0c Glw0e Sw5n0a
+Swn0a Pn0a Pc00a Vkv1a Vkm1a PDm1a Sdr0b Swp0a Vnu0a Vkt0a Snbv1a Vlg1b Glw0h Vko0a Vka1a Vdm1d PNt1a Vnr0a Vyout0a Szg0b Vkt1a Szg0a Pdd0a VmA0a Gdm0b Pddz0a Pcy0a PfillDz0a
+Gsendy0a Vdm1c Pwo0a Snl1a Vkp0a Nay0a:1 Snn0a Pfino0a Vko1a Shj0a Vdz0b Pn1a Slf1a Glw0g Pu00a Vdz0c Pc0a Pfinz0b Vnu1a Pfin0b Ssa20a Slf0a Pfinz0a Szg1b Pu0a Vdm1a Pfinc0a
+Vdm1b Vdz0a Vdz0d Pfiny0a PKd1c Pfin0c PKd1a Vpi0a PKd1d Pfin0a Szg1a Vyout1a PKd1b Pfin0d Vrf1a Pfinr0a Vfar0a Pu01a Vnm0a Vws0a Gsendy1a Vkp1a Syb0a:1 Vdr1a Pu1a Pfino1a
+Vs4o0a Pc01a PfillDz1a Pddz1a Vpi1a Pdd1a Nay1a:1 Vwou0a Pfinz1a Pfinz1b Vrout0a Snn1a Pcy1a Gsendr0a Vdz1b Vdz1c Pwo01a Pfiny1a Pc1a Vdz1a Pwo1a Pfin1b Pfin1c Vdz1d Ssa21a
+Syb0b:1 Vnm1a Pfin1a Vws1a Vnr1a Pfinc1a Vfar1a Vlw0j Pfin1d Pfinr1a PDm01a:1 PA0a Pwo00a:1 Vwou1a Vs4o1a PDm00a:1 Vxw0a Syb1b:1 Vrout1a Vxw1a Syb1a:1 Gsendr1a Vlw1a Sad0a:1
+Vtd0d
+"""
+
+
+FIRST = """
+Yljur0a Slown0a Slwgt0a Ylx0a Yll00a Yll10a Yll20a Yll30a Gci0a Vcf0a Gioc0a Vci0b Giom0a Giob0a Vcf0b Giox0b Vidn0a Vnl0b Sc10a Sc20480a Sc40a Scf0g Sc40960a Vzr0a Stmp0a
+Vcf0c Vda0a Snid0a Std0a Vc1550a Pwo00a Vnc0f Snc0e Snc0k Snc0b Vtmp0k Sf00a Vcf0i Vnc0h Vnon0a Sf00c Vbo0a Stmp0h Scc0a Gdm0a Vcf0d Stf0a Vtd0b Vone0a Vtmp0e Stmp0d Sb160b
+Gioj0a Vnc0l Vca0a Vru0a Syb0b Snc0d Giox0a Vcf0k Vtmp0f Vcf0h Vca0b Giok0a Vcf0j Sb160a Vf00b Vf00d Vrs160a Vcf0m Vtmp0g Syb0a Vnc0n Vtf0b Scp0a Vru0b Giok0b Vcf0f Grf0a
+Vtri0a Snc0m Sca0c Vcm0a Sboa0a Vcf0e Gdm0d PfillDx1b Grf1a Vhh0a Vwb0a Snc0c Gdm0c Snc0i Gdm0b Vtmp0j Vhj0a Vxd0b Gni0a Vq250a Snc0p Syb1b PfillDx1a Syb1a Vtmp0i PDm01a PDx1c
+Snc0g Vxd0a PDx1d Vnc0a Snc0j Stmp0b Stmp0c PDx1a Vnc0o Vnx0b Vrsk0a Vnx0a PDm00a Vnc0q PDx1b Vcf0n Sxd1b Pnb0b Sxd1a VmA0a Vkp1a Sc320a Vidx0b Pnb0a Vhp0a Vkp0a Sad0b Sda0b
+VmB0a Vcf0l Snba0a Skb0a Si320a Glw0c Vgood0a Vidx0a PDm0a Sad0a Vnx1a Scc0b Vnx1b Sby0a Std0c PKn0b Shs0a Swp0a Snbo0a Glw0f PKn0a Glw0a Vdm0f Vdm0h Sad1b Pnb1b PKr0a Pnb1a
+PKn1a Snbr0a PKn1b PKa0b Snl0a Vdm0g Snbr1a Sda0c Sida0a So80a PKd0d Sad1a PKd0b PKd0c Glw0b Sgood1a PKa0a Vlg0b Vlg0a Glw0d Vkm0a PNt0a Vkv0a PKr1a Vlg1b Glw0g Glw0e Swn0a
+Snl0c Vka0a Vlg1a Shz0a PKa1a PDm1a Pn0a Slf0a Pc00a Vnu0a Vkt0a Pc01a Vnr0a PKa1b Vdm0e PNt1a Vko0a Vdm1c Pu00a PKd0a Vkm1a Vyout0a Gsendy0a Vnl1a Pddz0b Vka1a Pddz0a Szg0b
+Pn1a Vkv1a PfillDz0a Vdm1d Szg0a Sni0b Vdm1a Vnu1a Vdm1b Nay0a:1 Glw0i Pu0a Vpi0a Vkt1a Szg1a Pwo0a Vdz0c Pcy0a Vdz0a Pc0a PZz0a Vdz0b Pfino0a Vko1a Pfin0d PKd1d Pfin0b Ssa20a
+Pfiny0a Szr0b Szg1b Vdz0d Vnm0a Vfar0a Vyout1a Pfin0c Pfinc0a Gsendy1a Pfin0a Pfin0e Vlw0h Vws0a Pfinr0a Vs4o0a Pfino1a Pwo01a Vnr1a PKd1a PKd1c PfillDz1a PKd1b Pddz1a Vlf1a
+Nay1a:1 Pddz1b Sni1a Pu01a Vwou0a Vrout0a Pu1a Gsendr0a PZz1a Vdz1b Szr1a Vdz1c Pwo1a Pc1a Pcy1a Ssa21a Vdz1a Pfin1c Nar0a:1 Pfiny1a Vdz1d Pfin1a Pfin1d Pfin1b Vpi1a Vws1a
+Pfinc1a Syb0b:1 Pfin1e Vfar1a Vnm1a Pfinr1a Gwou1a PDm01a:1 Vxw0a PDm00a:1 PA0a Vs4o1a Syb1a:1 Vlw0j Vrout1a Gsendr1a Vxw1a Syb1b:1 Vlw1a PNt0a:1 Vtd0d
+"""
+ROUND = """
+Nay0a Pwo0a' Sni0a' Vka1a' Pfino0a' Vdz0a' Szg1b' PZz0a' Vkt1a' Vdz0d' Pc0a' Pu00a' Pu0a' Vdz0c' PKd1a' Pfin0b' Vko1a' Pfiny0a' Ssa20a' Vdz0b' Pfin0e' Szr0a' Szg1a' Pfin0d'
+Vpi0a' Pfinc0a' Vyout1a' Pfin0a' Pfin0c' Vfar0a' Pfinr0a' Vnm0a' Pu01a' Vkp1a' Gsendy1a' PKd1d' Vws0a' PKd1c' PKd1b' Snbr1a' Slf0a' Pddz1b' Vs4o0a' Slf1a' Pddz1a' PfillDz1a'
+PZz1a' Gwou0a' Nay1a Sni1a' Pc01a' Pfino1a' Vrout0a' Vdz1a' Pfiny1a' Pu1a' Szr1a' Pcy1a' Vdz1b' Gsendr0a' Pc1a' Pwo01a' Pwo1a' Vdz1d' Pfin1b' Ssa21a' Syb0a Vdz1c' Pfin1c' Nar0a
+Pfin1a' Pfinc1a' Vpi1a' Vws1a' Pfin1e' Syb0b Pfin1d' Vfar1a' Pfinr1a' Vnm1a' Gwou1a' Pwo00a PDm01a Vlw0a' PDm00a PA0a' Vs4o1a' Syb1a Vxw1a' Vrout1a' Vxw0a' Syb1b Gsendr1a'
+Vlw1a' Vtd0a' Vxd0b Slg0a Grf0a Nar1a Vxd0a Slg0b Vnx0b Sad0b Vnx0a PNt0a Vkp0a Sad0a Vxd1b Grf1a Pnb0a Pnb0b Slg1a PKn0a PKn0b Vxd1a PKr0a PKa0a Sgood0a Snl0a PKa0b Slg1b
+Vnx1b Pn0a PDm0a Vnx1a Vnu0a Vkm0a Vdm0d Sad1a Pnb1b Vka0a Vkv0a Vdm0b Pnb1a Sad1b Vdm0a PNt1a Vgood1a PKn1b Vkt0a Szg0b Vdm0c PDm1a Vnr0a PKn1a Vnl1a Vko0a Vnbr0a PKr1a Vdm1b
+PKa1a Vyout0a Szg0a PKa1b Vdm1a PKd0d Vdm1c Gsendy0a Pn1a PKd0a PKd0c PKd0b Vkv1a Pc00a Vkm1a Pddz0b Vnu1a Pddz0a Vnr1a PfillDz0a Vdm1d Pcy0a
+"""
+LAST = """
+Pcy0a:4 Nay0a Gwou0a:4 Nay1a Ssa21a:4 Syb0a Pfin1c:4 Nar0a Pfin1e:4 Syb0b PA0a:4 PDm00a Pwo00a Vs4o1a:4 PDm01a Syb1b Vxw0a:4 Syb1a Vtd0a:4 Vxd0a Slg0a Grf0a Nar1a Vxd0b Slg0b
+Vkp0a Vnx0a Sad0a Vnx0b PNt0a Sad0b Vxd1b Grf1a PKn0b Pnb0b Slg1b PKn0a Vnl0a Pnb0a Vxd1a Pn0a Slg1a PKr0a PKa0b PKa0a Vgood0a Vnx1b Vnx1a PDm0a Sad1b Vnu0a PNt1a Vkv0a Vdm0c
+Sad1a Pnb1b Vkm0a Vdm0b Pnb1a Vnr0a Vka0a Szg0a PKn1b Vnl1a Vdm0d PKn1a Vgood1a Vkt0a Vnbr1a Pn1a Vdm0a PKr1a PDm1a Szg0b PKa1b Vko0a Vkp1a Vnu1a Vnr1a Vnbr0a PKa1a Vyout0a
+Vdm1a PKd0b PKd0d PKd0a PKd0c Gsendy0a Vkm1a Pddz0b Szg1a Vkv1a Pc00a Pddz0a Vdm1b Pu00a Pcy0a PfillDz0a Vka1a Pfino0a Vni0a Pc01a Pwo0a Nay0a! Vdm1c Vkt1a Pc0a Vdm1d Pfiny0a
+PZz0a Vdz0b Ssa20a Pu0a Szg1b Vko1a PKd1a Vdz0a PKd1b PKd1c Pfin0c Vpi0a Pfinc0a Vyout1a Pu01a Vdz0c Pfin0b Szr0a PKd1d Pddz1a Vfar0a Gsendy1a PfillDz1a Vnm0a Pddz1b Vdz0d
+Pcy1a Pfin0d Vws0a PZz1a Sni1a Vdz1b Yoo00a! Nay1a! Pfin0a Vdz1c Gwou0a Pfin0e Pfinr0a Szr1a Pu1a Vdz1a Pc1a Pfino1a Vs4o0a Pfin1d Ssa21a Pfin1c Vdz1d Pfin1a Pfin1b Vpi1a
+Pfinc1a Vrout0a Pfiny1a Pfin1e Vfar1a Pwo01a Pfinr1a Gsendr0a Vnm1a Pwo1a Vlw0a Vs4o1a Nar0a! Vws1a Sl160c! Yoo11a! Vrout1a Gwou1a Vl160d! Sl160b! Gsendr1a Pyz0c! Vlw1a Pyz0d!
+Vl160a! Nar1a! Pyz0b! Sl161d! Vl161a! Pyz0a! Sl161b! Vl161c! Pyz1d! Yoj00a! Pyz1a! Pyz1b! Pyz1c! Yoj11a! Syzf1a! Yoyz1a!
+"""
+
+
+FIRST = """
+Yljur0a Slown0a Slwgt0a Ylx0a Yll00a Yll10a Yll20a Yll30a Gci0a Gioc0a Sc1550a Sca0c Vci0b Giom0a Vcf0a Gdm0c Sca0b Vcf0b Vidn0a Vnl0b Vcf0c Scf0g Vzr0a Vc320a Sda0a Gdm0b
+Vcf0e Giox0a Vnc0b Stmp0c Sf00d Sca0a Vnl0a Vtmp0a Sc40960a Vnc0l Vrs160a Pwo00a Giok0b Vtmp0e Vnc0n Snid0a Giob0a Vnc0m Vcf0d Vtmp0k Snc0d Snc0e Sida0a Vcf0i Gioj0a Vcp0a
+Vtmp0f Stf0a Sf00b Vcf0f Vtf0b Vhh0a Vcf0m Giok0a Snon0a Vnc0a Vq250a Syb0b Snc0h Snc0g Giox0b Syb0a Vcf0j PfillDx1b Sc40a Vru0b Sc20480a PfillDx1a Scm0a Vcf0k Vnc0j Shp0a
+Snc0k Vcf0h Vbo0a Sb160b Snc0o Vru0a Vnc0i Gdm0d Shz0a Sf00c Vnc0p Vcf0l Vb160a PDm00a Vtd0b Vrsk0a Snc0f Vnc0c Syb1a Vtmp0d Syb1b Vcf0n Scc0a Vtmp0j Grf0a Vidx0a Vtmp0b Vtmp0i
+Stmp0h Vc10a Vwb0a Grf1a Gdm0a Skb0a PDm01a Std0a Sda0b Sf00a Vi320a Vxd0b Vxd0a PDx1c Vtmp0g Vnc0q Gni0a Snba0a Vnx0a Vnx0b PDx1d Sxd1b PDx1b PDx1a Vo80a Sxd1a Pnb0b Vidx0b
+Glw0b Vtri0a VmA0a Pnb0a Sgood0a Vone0a PKn0b VmB0a Sda0c Scc0b PDm0a Glw0a Shs0a PKn0a Vkp0a Vnx1a Glw0c Snbv0a Snbo0a Vnx1b Pnb1a Pnb1b PKn1b Sad0b Vdm0h Vdm0g Swn0a PKr0a
+Sad0a PKd0d Vdm0f Pc00a PKa0b Vdm0e PKd0b Std0c Sgood1a Snbv1a PKd0a Pfino0a Glw0i PDm1a Shj0a Sad1a Glw0g PKd0c PKa0a Glw0d Sboa0a Pddz0a Sad1b Sby0a PKn1a PKr1a Vlg0a Vlg0b
+PNt0a PKa1b Snl0c Swp0a PKa1a Vkm0a Pn0a Vlg1a Vlg1b Vnu0a Vkv0a Glw0e Vkm1a PNt1a Vka0a Vdm1d Vkt0a Pu00a Vdm1a Vko0a Vnl1a Vnr0a Vkv1a Vyout0a Vdm1c Vka1a Gsendy0a Vdm1b Pn1a
+Glw0f Pddz0b Vnu1a PfillDz0a Nay0a:1 Pwo0a Vni0b Vkt1a Szg0b Pu0a Szg0a PKd1a PKd1c Vdz0a Vdz0c Pcy0a Vdz0b Szg1a Pc0a PZz0a PKd1b Pfin0b Szr0b Ssa20a Vko1a PKd1d Pfiny0a Vdz0d
+Pfin0d Pfin0c Szg1b Vpi0a Pfin0a Pfinc0a Vyout1a Pfin0e Pfinr0a Vnr1a Pwo01a Vnm0a Vfar0a Gsendy1a PfillDz1a Vws0a Gwou0a Pddz1b Pddz1a Pc01a Pu01a Vs4o0a Pu1a Nay1a:1 PZz1a
+Sni1a Vdz1a Vrout0a Gsendr0a Pc1a Szr1a Pcy1a Ssa21a Pwo1a Vkp1a Pfino1a Syb0a:1 Pfin1a Nar0a:1 Pfin1b Vdz1b Pfin1c Vdz1d Slf1a Vpi1a Vdz1c Syb0b:1 Slf0a Pfinc1a Pfin1e Vlw0j
+Vnm1a Glw0h Pfiny1a Pfin1d Pfinr1a PDm01a:1 Vfar1a Vws1a Gwou1a Syb1a:1 PA0a Vxw0a Vs4o1a Vrout1a Gsendr1a Vxw1a Syb1b:1 Vlw1a Vtd0d
+"""
+ROUND = """
+Nay0a Pddz0b' Vkv1a' Pwo0a' Vdm1a' Pcy0a' Sni0a' Vka1a' PZz0a' Vdz0b' Szg1b' PKd1b' Vkt1a' Pfiny0a' Pu00a' Vdz0a' Pc0a' PKd1a' Vdz0d' PKd1c' Pu0a' Pfin0c' Vko1a' Ssa20a' Vdz0c'
+Pfin0b' Szr0a' Szg1a' Pfin0e' Vpi0a' Pfinc0a' Vyout1a' Pfin0a' Pfin0d' Vnm0a' Pfinr0a' Vfar0a' PKd1d' Vnr1a' Gsendy1a' Pc01a' Vkp1a' Vws0a' Pddz1a' Pddz1b' Vs4o0a' Pcy1a'
+PfillDz1a' Pu01a' Vlf0a' Pu1a' Sni1a' Nay1a PZz1a' Slf1a' Vrout0a' Vdz1a' Pc1a' Vdz1c' Gsendr0a' Pwo01a' Pwo1a' Szr1a' Pfino1a' Vdz1d' Ssa21a' Syb0a Pfin1b' Pfiny1a' Vdz1b'
+Pfin1d' Gwou0a' Nar0a Pfinc1a' Vpi1a' Pfin1e' Syb0b Vws1a' Pfin1a' Pfin1c' Vfar1a' Pfinr1a' Vnm1a' Gwou1a' PA0a' Vxw0a' Pwo00a PDm00a Pfino0a Vs4o1a' PDm01a Syb1a Vxw1a'
+Vrout1a' Vlw0a' Syb1b Gsendr1a' Vlw1a' Vtd0a' Vkp0a Vxd0b Slg0b Grf0a Nar1a Vxd0a Slg0a Vnx0b Sad0b Vnx0a PNt0a Sad0a Vxd1b Grf1a Pnb0a PKn0b Slg1a Pnb0b Vxd1a PKn0a PKr0a
+PKa0b Snl0a Sgood0a Snbv0a PKa0a Slg1b Vnx1b Pn0a PDm0a Vnx1a Pc00a Vkv0a Vkm0a Vnu0a Vnr0a Sad1b Vdm0c Pnb1a Vka0a Pnb1b Vdm0b Sad1a PKn1a Vdm0a PNt1a Vkt0a Vgood1a Vdm0d
+Szg0a PKn1b Vko0a Vnbv1a PDm1a Vnl1a PKr1a PKa1a Vyout0a Vdm1b Pn1a Szg0b PKd0d Vdm1c Gsendy0a PKa1b Vnu1a PfillDz0a Vdm1d PKd0a PKd0c PKd0b Pddz0a Vkm1a
+"""
+LAST = """
+Vkm1a:4 Nay0a Sni1a:4 Nay1a Ssa21a:4 Syb0b Gwou0a:4 Nar0a Pfin1e:4 Syb0a Vxw0a:4 PDm01a Pu00a Vs4o1a:4 PDm00a Syb1a Vlw0a:4 Syb1b Vtd0a:4 Vxd0a Slg0b Grf0a Nar1a Vxd0b Slg0a
+Vnx0a Sad0a Vnx0b PNt0a Vkp0a Sad0b Vxd1b Grf1a Pnb0a PKn0a Slg1a PKn0b PKr0a Vxd1a Pnb0b PKa0a Slg1b PKa0b Vgood0a Vnl0a Vnx1b PDm0a Vnx1a Pn0a Sad1b Vdm0a PNt1a Vkm0a Sad1a
+Pnb1b Vnbv0a Vnu0a Vdm0c Pnb1a Vka0a Vkv0a Szg0b PKn1a Vdm0b Vgood1a PKn1b Vnl1a Vkt0a Vdm0d PKd0a PDm1a PKr1a Vkp1a PKa1b Snbv1a Vko0a Szg0a Vnr0a Vdm1c PKa1a Vyout0a Pn1a
+Vdm1a PKd0b PKd0d Pwo00a PKd0c Vkm1a Gsendy0a Pddz0a Vnu1a Pc00a Vdm1b Pddz0b Pcy0a Pu0a Vka1a Szg1b Vnr1a Pwo0a Vkv1a Vdm1d Nay0a! PKd1a PKd1c PKd1b Vkt1a PfillDz0a Vpi0a
+Pfino0a Vws0a Vni0a PZz0a Vko1a Szg1a Vdz0a Gwou0a PKd1d Pddz1a Pfiny0a Pc01a Vyout1a Pfino1a Vdz0c Pc0a Pfin0b Vdz0b Gsendy1a Pddz1b Pcy1a Ssa20a PfillDz1a Vnm0a Pfin0d Vdz0d
+Sni1a Pfiny1a Pfin0c Szr0a Vfar0a Nay1a! Vdz1a Pu01a Pfinc0a Pc1a Vdz1d Yoo00a! Pfin0e Pfin0a Vdz1b Pfinr0a Ssa21a PZz1a Vdz1c Pu1a Vs4o0a Pfin1b Szr1a Pfin1e Vpi1a Pfin1d
+Pfin1c Vrout0a Pfin1a Pfinc1a Vfar1a Vnm1a Pfinr1a Gsendr0a Vlw0a Pwo01a Pwo1a Vs4o1a Yoo11a! Vws1a Sl160b! Nar0a! Vrout1a Gwou1a Vl160a! Sl160c! Gsendr1a Pyz0b! Vlw1a Sl160d!
+Nar1a! Pyz0c! Vl161c! Sl161d! Pyz0a! Pyz0d! Vl161a! Sl161b! Pyz1c! Yoj00a! Pyz1d! Pyz1a! Pyz1b! Yoj11a! Syzf1a! Yoyz1a!
 """
 
 
@@ -99,7 +227,7 @@ def spots(x):
 
 def width(x):
     if x[0] == "i": return 16 * width(x[6])
-    if x[0] == "n": return math.prod(i[1] - i[0] for i in x[4] if isinstance(i, tuple))
+    if x[0] == "n": return math.prod(len(range(*i)) for i in x[4] if isinstance(i, tuple))
     return len(range(x[4], x[5], x[6]))
 
 
@@ -187,16 +315,16 @@ def build_ops(par):
             return g.scalar.activation(ap(T, Q, out), ap(T, Q, in_), func, bias=ap(T, Q, bias), scale=ap(T, Q, scale), accum_out=ap(T, Q, acc) if acc else None)
         return op("S", rate(out, in_, 1.0), fn, [in_, bias, scale], [out] + ([acc] if acc else []), nm or out[1])
 
-    def mm(items, nm=None, closes=False, behind=()):
+    def mm(items, nm=None, closes=False, behind=(), grp=0):
         def fn(g, T, Q):
             ins = None; first, last = Q("ends")
             for j, it in enumerate(items):
-                ins = g.tensor.matmul(ap(T, Q, it[0]), ap(T, Q, it[1]), ap(T, Q, it[2]), first and j == 0, last and j == len(items) - 1)
+                ins = g.tensor.matmul(ap(T, Q, it[0]), ap(T, Q, it[1]), ap(T, Q, it[2]), first and j == 0, last and all(x[0][2] != it[0][2] for x in items[j + 1:]))
             return ins
         cols = sum(max(min(64, width(l)), width(r)) * (4 if SCRATCH[r[1]][2] == F else 1) for o, l, r in items)
         tl = items[0][0][1]; mine = live.setdefault("ps " + tl, [])
         k = op("P", ("pe", cols), fn, [x for it in items for x in it[1:]], [], nm or "".join(x for x in tl if x.isalpha()), more=[j for j, m, w in mine] if closes else behind)
-        ops[k]["ps"] = (tl,); mine.append((k, 1, True))
+        ops[k]["ps"] = (tl,); ops[k]["grp"] = (tl, grp); mine.append((k, 1, True))
         return k
 
     def steps(n, items):
@@ -237,7 +365,7 @@ def build_ops(par):
         return either(lambda: act(out, in_, ACT.Identity, bias, scale), lambda: ts(out, in_, scale, bias, ALU.mult, ALU.add))
 
     def const(out, v):
-        return either(lambda: act(out, S("ioc", 0, width(out)), ACT.Identity, v, 0.0), lambda: ms(out, v), "V")
+        return lin(out, S("ioc", 0, width(out)), 0.0, v)
 
     dma("Y", S("ji", 0, P), HBM("jur"), "ljur", 2500)
     dma("S", S("yin", 0, P), HBM("own"), "lown", 2500)
@@ -250,7 +378,7 @@ def build_ops(par):
         if j == par["xat"]: dma("Y", S("xw", 0, W), HBM("xc"), "lx", 5000 + 6000 * a / W)
         dma("Y", S("li", a, b), HBM("lsr", a, b), "ll%d" % j, (5000 if j >= par["xat"] else 2500) + 6000 * b / W)
         for x in range(a, b, 512) if par["conv"] else ():
-            cp(S("lw", x, min(b, x + 512)), S("li", x, min(b, x + 512)), "lw0")
+            either(lambda: hand(S("lw", x, min(b, x + 512)), S("li", x, min(b, x + 512))), lambda: cp(S("lw", x, min(b, x + 512)), S("li", x, min(b, x + 512))), par["conv"])
 
     first = len(ops)
     iota("ci", 1, [[0, 1]], 1)
@@ -260,8 +388,9 @@ def build_ops(par):
     iota("ioj", PW, [[16, PW // 16], [PW, 16]], 0)
     iota("iok", 144, [[1, 16], [16, 9]], 0)
     iota("iok", 144, [[0, 16], [16, 9]], 0, 144)
-    iota("dr", NH * 144, [[0, NH * 144]], 0)
-    iota("ba", 16 * 144, [[0, 16 * 144]], 0)
+    if par["im"]: iota("ni", NH * 272, [[0, NH * 272]], 0)
+    else: iota("dr", NH * 144, [[0, NH * 144]], 0)
+    if not all(par["ns"]): iota("ba", 16 * 144, [[0, 16 * 144]], 0)
     for j in range(2 * NH):
         iota("dm", 16, [[0, 16]], 0, DMS * j)
     cp(col(0), S("ci", 0, 1))
@@ -276,13 +405,21 @@ def build_ops(par):
     tt(col(9), col(7), col(1), ALU.subtract)
     ts(col(14), col(9), 1.0 / 64, 65.0 / 128, ALU.mult, ALU.add)
     ts(full("idn"), full("ioc"), col(0), None, ALU.is_equal)
-    for nme, sc in (("nid", -1.0), ("q25", .25)):
-        lin(full(nme), full("idn"), sc)
+    for nme, sc in (("nid", -1.0), ("q25", .25), ("ida", AN), ("nia", -AN), ("i32", 2.0 if 2 in par["fs"] else 1.0 / 32)):
+        if (nme != "nia" or "T" in "".join(par["zm"])) and (nme != "i32" or any(par["fs"])): lin(full(nme), full("idn"), sc)
+    for c in range(2):
+        iota("iox", 128, [[1, 8], [8 - 16 * c, 2], [16, 8]], -1, 128 * c)
+        ts(S("idx", 128 * c, 128 * c + 128), S("iox", 128 * c, 128 * c + 128), -8.0 * c, None, ALU.is_equal)
+        const(ND("nl", (32 * c + 1, 32 * c + 32, 2), (0, KK)), 0.0)
+    if any(par["fs"]): const(ND("zr", (0, 18 * NH, 2), (0, KK)), 0.0)
     ts(S("hh", 0, 144), S("ioc", 0, 144), col(3), None, ALU.is_equal)
-    for nme, sc in (("hz", -1.0 / 32), ("hp", PEN * 89 / 2048), ("hs", 16.0 * PW)):
-        lin(S(nme, 0, 144), S("hh", 0, 144), sc)
+    for nme, sc in (("hz", -1.0 / 32), ("hy", 1.0 / 32), ("hp", PEN * 89 / 2048), ("hs", 16.0 * PW)):
+        if (nme != "hy" or 0 in par["fs"]) and (nme != "hz" or par["fs"] != (1, 1)): lin(S(nme, 0, 144), S("hh", 0, 144), sc)
     ts(full("bo"), full("iob"), col(2), None, ALU.is_equal)
-    lin(full("nbo"), full("bo"), -1.0)
+    if 2 in par["fs"]: lin(cst("o8", 8), S("bo", 0, 128, 16), 1.0 / 64)
+    for c in range(2) if par["im"] else (): lin(S("b16", 8 * c, 8 * c + 8), S("bo", 0, 128, 16), 1.0)
+    for nme, sc in (("nbo", -1.0), ("boa", AN), ("nba", -AN), ("by", -AN / 32)):
+        lin(full(nme), full("bo"), sc)
 
     def tmp(j): return S("tmp", 128 * j, 128 * j + 128)
     for j, (nme, off, dg) in enumerate((("mA", 1.0 / 64, -39.0 / 64), ("mB", -1.0 / 64, 89.0 / 128))):
@@ -301,7 +438,7 @@ def build_ops(par):
     tt(S("nc", 0, 16 * 144, 16), S("tmp", 1024, 1168), S("tmp", 1168, 1312), ALU.add)
     lin(S("kb", 0, PW), S("ioj", 0, PW), 1.0, col(1))
     lin(cst("cm"), cst("iom"), 0.0, col(14))
-    for nme, v, n in (("c1", M1, PW), ("c32", M32, PW), ("c4096", M4096, PW), ("c155", 15.5, PW), ("c2048", 2048.0, PW),
+    for nme, v, n in (("c1", M1, PW), ("c32", M32, P), ("c4096", M4096, PW), ("c155", 15.5, P), ("c2048", 2048.0, PW),
                       ("cp", M1 * PEN, PW), ("c4", 4 * M1, 4), ("one", 1.0, 128), ("non", -1.0, 128)):
         const(cst(nme, n), v)
     for j, v in enumerate((0.0, 1.0, 39.0 / 64, 39.0 / 128)):
@@ -322,13 +459,11 @@ def build_ops(par):
     lin(S("tf", 0, 128), full("ioc"), 32.0)
     tt(S("tf", 128, 256), S("tf", 0, 128), tmp(7), ALU.subtract)
     ts(full("wb"), S("tf", 128, 256), -16384.0, None, ALU.max)
-    ts(S("ba", 15, 16 * 144, 16), S("iok", 0, 144), col(0), None, ALU.is_equal)
+    if not all(par["ns"]): ts(S("ba", 15, 16 * 144, 16), S("iok", 0, 144), col(0), None, ALU.is_equal)
     lin(S("hj", 0, 144), S("hh", 0, 144), col(6))
-    ts(S("wi", 4, 5), S("wi", 0, 1), 31, None, ALU.bitwise_and)
-    cp(col(10), S("wi", 4, 5))
     ts(col(11), S("wi", 0, 1), 2048.0, -4096.0, ALU.is_ge, ALU.mult)
     tt(col(12), col(11), S("wi", 0, 1), ALU.add)
-    for p, n, j in (("w5p", "w5n", 10), ("wp", "wn", 12)):
+    for p, n, j in (("wp", "wn", 12),):
         lin(full(p), full("bo"), col(j))
         lin(full(n), full("nbo"), col(j))
 
@@ -364,6 +499,7 @@ def build_ops(par):
                     out = S(name, ob + 16 * pw * j, ob + 16 * pw * (j + 1))
                     src = IND(win, 0, W, S(offs, at + pw * j, at + pw * (j + 1)))
                     if name == "xd": tt(out, src, S("yb", ob + 16 * pw * j, ob + 16 * pw * (j + 1)), ALU.subtract)
+                    elif name == "zg": either(lambda: act(out, src, ACT.Identity, 0.0, AN), lambda: ts(out, src, AN, None, ALU.mult), e)
                     elif win == "li": ts(out, src, add, None, ALU.add)
                     else: move(out, src, add, e)
 
@@ -371,10 +507,10 @@ def build_ops(par):
                 at = DMS * o3 + 16 if name == "dm" else ob
                 return S(name, at + PW * k0, at + PW * k1)
 
-            def against(out, src, k0, k1, tl, o):
-                its = [(km(out, k, k + 1), S(src, ob + k, ob + n16, 16), PS(tl, 0, PW)) for k in range(k0, k1)]
-                op("V", (1.0, PW * (k1 - k0)), lambda g, T, Q: [g.vector.tensor_tensor(ap(T, Q, x), ap(T, Q, y), ap(T, Q, z), o) for x, y, z in its],
-                   [y for x, y, z in its] + [its[0][2]], [km(out, k0, k1)], out)
+            def against(its, out, tl, o):
+                z = PS(tl, 0, PW)
+                op("V", (1.0, PW * len(its)), lambda g, T, Q: [g.vector.tensor_tensor(ap(T, Q, x), ap(T, Q, y), ap(T, Q, z), o) for x, y in its],
+                   [y for x, y in its] + [z], [out], out[1])
 
             def near(out, d): ts(out, d, M4, M4, ALU.add, ALU.is_equal)
 
@@ -386,13 +522,17 @@ def build_ops(par):
             Y2 = S("y2", 2 * o, 2 * o + 2 * PW)
             via = not t and par["via"][h]
             who = "" if via else par["yb"][h]; bn = 8 // max(1, len(who))
-            if "E" in who: many("V", [lambda c=c: cp(S("y2", 2 * o + c, 2 * o + 2 * PW, 2), YIN) for c in range(2)], "y2")
+            def twice(name, Y):
+                outs = [S(name, 2 * o + c, 2 * o + 2 * PW, 2) for c in range(2)]
+                either(lambda: many("S", [lambda x=x: act(x, Y, ACT.Identity) for x in outs], name), lambda: many("V", [lambda x=x: cp(x, Y) for x in outs], name))
+            if "E" in who or "H" in who: twice("y2", YIN)
             for j, e in enumerate(who):
                 cs = range(bn * j, bn * j + bn); outs = [S("yb", ob + k, ob + n16, 16) for c in cs for k in (c, c + 8)]
 
                 def on_s(): return many("S", [lambda x=x: act(x, YIN, ACT.Identity) for x in outs], "yb")
                 if e == "S": on_s()
                 elif e == "G": many("G", [lambda x=x: hand(x, YIN) for x in outs], "yb")
+                elif e == "H": either(on_s, lambda: many("G", [lambda c=c: hand(S("yb", ob + c, ob + n16, 8), Y2) for c in cs], "yb"), "G")
                 else: either(on_s, lambda: many("V", [lambda c=c: cp(S("yb", ob + c, ob + n16, 8), Y2) for c in cs], "yb"))
             if via:
                 for j in range(2):
@@ -404,17 +544,22 @@ def build_ops(par):
                         mm([(PS(tl, 256 * j, 256 * j + 256), IDN, S("yb", ob + 512 * j + c, ob + 512 * j + 512, NC))], behind=[k])
                     move(S("xd", ob + c, ob + n16, NC), PS(tl, 0, 512))
             else: gather("xd", "xw", "rin", oi)
-            cp(s4(3), RU, "rf")
+            ops[either(lambda: hand(s4(3), RU), lambda: cp(s4(3), RU), "V")]["nm"] = "rf"
             ts(s4(5), RU, 32.0, col(5), ALU.mult, ALU.add, "kp")
-            for name in ("nx", "ad"):
-                pw = PW // par[name]
-                for i0 in range(0, PW, pw):
+            for name in ("ad", "nx"):
+                pw = PW // len(par[name][h])
+                for i0, e in zip(range(0, PW, pw), par[name][h]):
                     out, d = cube(name, i0=i0, i1=i0 + pw), S("xd", ob + 16 * i0, ob + 16 * (i0 + pw))
-                    if name == "nx": near(out, d)
-                    else: act(out, d, ACT.Abs)
-            gather("lg", LW if t or par["conv"] == 1 else "li", "rin", oi)
+                    if name == "ad": act(out, d, ACT.Abs)
+                    elif e == "V": near(out, d)
+                    else: act(out, cube("ad", i0=i0, i1=i0 + pw), ACT.Sigmoid, 384.0, -256.0)
+            gather("lg", LW if t or par["first"][h] == "S" else "li", "rin", oi)
             tl = "n" + v
-            for k0 in (0, KK):
+            if par["ns"][h]:
+                mm([(PS("Nt" + v, j, 2 * PW, KK), S("lg", ob + j, ob + n16, KK), S("idx", 16 * ((j + t) % 16), 16 * ((j + t) % 16) + 16)) for j in range(KK)])
+                move(ND("nl", (32 * h, 32 * h + 32, 2), (0, KK)), PS("Nt" + v, 0, 2 * PW))
+                mm([(PS(tl, 0, PW), IDN, cst("c2048"))] + [(PS(tl, 0, PW), ND("nl", (32 * h + 15 * c, 32 * h + 15 * c + 16), (0, KK)), S("idn", c, 128, 2)) for c in range(2)])
+            for k0 in (0, KK) if not par["ns"][h] else ():
                 mm([(PS(tl, 0, PW), S("ba", 144 * ((k + t) % 16) + 15 - k, 144 * ((k + t) % 16) + 143 - k), S("lg", ob + k, ob + n16, 16)) for k in range(k0, k0 + KK)]
                    + ([] if k0 else [(PS(tl, 0, PW), IDN, cst("c2048"))]))
             cp(sm("nu"), PS(tl, 0, PW))
@@ -424,11 +569,12 @@ def build_ops(par):
             for k0 in range(0, 16, pn):
                 mm([(out, S("nc", 143 * k, 143 * k + 128), cube("nx", k=k)) for k in range(k0, k0 + pn)])
             either(lambda: act(sm("good"), out, ACT.Sigmoid, -248.0 * 16, 16.0), lambda: ts(sm("good"), out, 248.0, None, ALU.is_ge))
-            move(sm("nbv"), out, -8.0)
+            move(sm("nbr" if par["re"] else "nbv"), out, 4088.0 if par["re"] else -8.0)
+            reads = [j for j, m, w in live["ps " + tl]]
             tl = "Dm" + v; dn = par["dn"]
             steps(1, [(PS(tl, 0, PW), lhs, rhs) for lhs, rhs in ((IDN, cst("cm")), (full("tri"), sm("good")), (IDN, cst("c1")), (NID, cst("c1")))])
             for k0 in range(0, 16, dn):
-                against("dm", "xd", k0, k0 + dn, tl, ALU.mult)
+                against([(km("dm", k, k + 1), S("xd", ob + k, ob + n16, 16)) for k in range(k0, k0 + dn)], km("dm", k0, k0 + dn), tl, ALU.mult)
             tl = "K" + v; out = PS(tl, 0, PW)
             ks = [mm([(out, hk("hp", r), cube("nx", r=r)) for r in range(r0, r0 + pn)], "Kn") for r0 in range(0, 16, pn)]
             k = mm([(out, IDN, cst("cp")), (out, NID, cst("cp")), (out, IDN, cst("kb"))], "Kr", behind=ks)
@@ -447,9 +593,16 @@ def build_ops(par):
             kyn = tt(YN, IND("dm", DMS * o3, DMS * o3 + 16 + n16, four("ko")), YIN, ALU.add)
             if t < V - 1: either(lambda: act(four("lf"), KV, ACT.Sign), lambda: ts(four("lf"), KV, 0.0, 2.0, ALU.is_gt, ALU.mult))
             tl = "Kd" + v; od = 144 * h + 8
-            for k0 in range(0, 16, dn):
-                mm([(PS(tl, j, PW, 8), km("dm", 2 * j, 2 * j + 2), S("bo", 0, 128, 16)) for j in range(k0 // 2, (k0 + dn) // 2)], "Kd")
-            move(S("dr", od, od + 128, 2), PS(tl, 0, PW))
+            def kd(k0, **kw): return mm([(PS(tl, j, 2 * PW, 8), km("dm", 2 * j, 2 * j + 2), cst("b16", 16)) for j in range(k0 // 2, (k0 + dn) // 2)], "Kd", **kw)
+            if par["im"]:
+                ks = [kd(k0) for k0 in range(0, 16, dn)]
+                for Y, b in ((YIN, "bo"), (YN, "nbo")):
+                    mm([(PS(tl, PW, 2 * PW, 1, PW * c, PW * c + PW), Y, S(b, 0, 128, 2)) for c in range(2)], "ddz", behind=ks)
+                lin(S("ni", 272 * h + 8, 272 * h + 264, 2), PS(tl, 0, 2 * PW), AN, 1.0)
+            else:
+                for k0 in range(0, 16, dn):
+                    mm([(PS(tl, j, PW, 8), km("dm", 2 * j, 2 * j + 2), S("bo", 0, 128, 16)) for j in range(k0 // 2, (k0 + dn) // 2)], "Kd")
+                move(S("dr", od, od + 128, 2), PS(tl, 0, PW))
 
             def send(kind, src, dst):
                 def fn(g, T, Q, t=t, h=h):
@@ -460,13 +613,18 @@ def build_ops(par):
 
             def xr(a0):
                 return [(PS(tl, a0, a0 + PW), S("dr", od - c, od - c + 128), S("idn", PW * c, PW * c + PW)) for c in range(NC)]
-            mm(xr(0) + xr(PW))
-            mm([(PS(tl, PW, 2 * PW), full("bo"), YIN), (PS(tl, PW, 2 * PW), full("nbo"), YN)], "ddz")
             on = 2 * o
-            test(S("nn", on, on + 2 * PW), S("nt", on, on + 2 * PW), PS(tl, 0, 2 * PW), 2 if "nn" in par["sg"] else 0)
-            tl = "c2" + v; out = PS(tl, 0, PW)
-            steps(4, [(out, NID, sm("nbv")), (out, IDN, cst("c32")), (out, NID, cst("c32")), (out, IDN, sm("nbv")), (out, NID, S("nn", on, on + PW)), (out, IDN, S("nn", on + PW, on + 2 * PW))])
-            act(sm("sa2"), out, ACT.Sign, -3.5)
+            if not par["im"]:
+                mm(xr(0) + xr(PW))
+                mm([(PS(tl, PW, 2 * PW), full("bo"), YIN), (PS(tl, PW, 2 * PW), full("nbo"), YN)], "ddz")
+                lin(S("nn", on, on + 2 * PW), PS(tl, 0, 2 * PW), AN, 1.0)
+            tl = ("nb" if par["re"] else "c2") + v; out = PS(tl, 0, PW)
+            if par["re"]: k = mm([(out, NID, sm("nbr"))], "c0", behind=reads, grp=1)
+            else: k = mm([(out, NID, sm("nbv")), (out, IDN, cst("c32")), (out, NID, cst("c32")), (out, IDN, sm("nbv"))], "c0")
+            mm([(out, full("nba"), YIN), (out, full("boa"), YN)], "cy", behind=[k], grp=par["re"])
+            if par["im"]: mm([(out, S("ni", 272 * h + 8 + 128 * s - c, 272 * h + 136 + 128 * s - c), S(b, PW * c, PW * c + PW)) for s, b in enumerate(("nid", "idn")) for c in range(2)], "c", behind=[k], grp=par["re"])
+            else: mm([(out, NID, S("nn", on, on + PW)), (out, IDN, S("nn", on + PW, on + 2 * PW))], "c", behind=[k], grp=par["re"])
+            act(sm("sa2"), out, ACT.Sign, 4096 - 11.5 if par["re"] else -3.5)
 
             def modulo(out, neg, pos, Y, big):
                 return [(out, neg, Y), (out, NID, big), (out, IDN, big), (out, pos, Y)]
@@ -475,24 +633,39 @@ def build_ops(par):
             scan(S("pi", on, on + 2 * PW), PS(tl, 0, 2 * PW), s4(3, 2), ALU.mult, ALU.add)
             ts(s4(0), S("pi", on + 1, on + 2 * PW, 2), 5, W - 1, ALU.arith_shift_right, ALU.bitwise_and, "far")
             ts(s4(1), sm("nu"), -1.0, None, ALU.mult, nm="nm")
-            if 2 in par["zm"][h]: mm([(PS("Dz" + v, 0, PW), IDN, YN)], "fillDz")
-            zn = par["zn"]
-            for c in range(NC):
-                tl = "Dz%s_%d" % (v, c)
-                if par["zm"][h][c] == 1:
-                    mm([(PS(tl, PW * j, PW * j + PW), IDN, S("zg", ob + KK * c + j, ob + n16, 16)) for j in range(KK)])
-                    mm([(PS(tl, PW * j, PW * j + PW), NID, YN) for j in range(KK)], "fillDz")
-                for j in range(0, KK, zn):
-                    k0 = KK * c + j; d = PS(tl, PW * j, PW * (j + zn))
-                    if par["zm"][h][c] == 2:
-                        d = km("dz", k0, k0 + zn); against("dz", "zg", k0, k0 + zn, "Dz" + v, ALU.subtract)
-                    test(km("nz", k0, k0 + zn), km("az", k0, k0 + zn), d, par["zs"][h][c])
+            zm = par["zm"][h]; zn = KK // len(zm)
+            if "V" in zm: mm([(PS("Dz" + v, 0, PW), IDN, cst("non")), (PS("Dz" + v, 0, PW), full("ida"), YN)], "fillDz")
+
+            def pair(j, c=0, s=1, n=1): return S("dz", ob + 2 * PW * j + c, ob + 2 * PW * (j + n), s)
+            for j0, e in zip(range(0, KK, zn), zm):
+                tl = "Dz%s_%d" % (v, j0); js = range(j0, j0 + zn)
+                if e == "V": against([(pair(j, c, 2), S("zg", ob + j + KK * c, ob + n16, 16)) for j in js for c in range(2)], pair(j0, n=zn), "Dz" + v, ALU.subtract)
+                else:
+                    mm([(PS(tl, P * (j - j0), P * (j - j0 + 1)), IDN, S("zg", ob + j, ob + n16, KK)) for j in js])
+                    mm([(PS(tl, P * (j - j0) + c, P * (j - j0 + 1), 2), full("nia"), YN) for j in js for c in range(2)], "subDz")
+                    move(pair(j0, n=zn), PS(tl, 0, P * zn), 1.0)
+            if par["fs"][h] == 2:
+                mm([(PS("Zt" + v, j, PW, KK), S("zg", ob + j, ob + n16, KK), cst("o8", 8)) for j in range(KK)], "Zz")
+                move(ND("zr", (18 * h + 1, 18 * h + 17, 2), (0, KK)), PS("Zt" + v, 0, PW))
+            if par["fs"][h] == 1:
+                tl = "Zt" + v; twice("yd", YN)
+                k = mm([(PS(tl, j, PW, KK), S("zg", ob + j, ob + n16, KK), S("bo", 0, 128, 16)) for j in range(KK)], "Zz")
+                mm([(PS(tl, 0, PW), S("yd", 2 * o, 2 * o + 2 * PW), S("nba", 0, 128, 2))], "Zy", behind=[k])
+                for j0 in range(0, KK, zn):
+                    mm([(PS(tl, j, PW, KK), pair(j), S("nbo", 0, 128, 16)) for j in range(j0, j0 + zn)], "Zd", behind=[k])
+                move(ND("zr", (18 * h + 1, 18 * h + 17, 2), (0, KK)), PS(tl, 0, PW))
             tl = "fin" + v
             TF, CH = PS(tl, 2, 4 * PW, 4), PS(tl, 3, 4 * PW, 4)
             k = mm([(PS(tl, 0, 4 * PW), IDN, S("f0", 0, 4 * PW))], "fino", behind=[] if "fin" in par["ahead"] else [kyn])
             mm([(CH, full("mB"), sm("sa2")), (CH, IDN, cst("c1")), (CH, full("mA"), sm("sa2")), (CH, NID, cst("c1")), (TF, full("q25"), sm("sa2"))], "finc", behind=[k])
-            for k0 in range(0, 16, zn):
-                mm([(TF, hk("hz", j), km("nz", j, j + 1)) for j in range(k0, k0 + zn)], behind=[k])
+            if par["fs"][h]:
+                mm([(TF, ND("zr", (18 * h + 1 - c, 18 * h + 17 - c), (0, KK)), S("i32", c, 128, 2)) for c in range(2)], behind=[k])
+            if par["fs"][h] != 1:
+                for k0 in range(0, 16, pn) if not par["fs"][h] else ():
+                    mm([(TF, hk("hy", j), S("zg", ob + j, ob + n16, 16)) for j in range(k0, k0 + pn)], "finz", behind=[k])
+                mm([(TF, full("by"), YN)], "finy", behind=[k])
+                for j0 in range(0, KK, zn):
+                    mm([(TF, hk("hz", j + KK * c), pair(j, c, 2)) for j in range(j0, j0 + zn) for c in range(2)], behind=[k])
             mm([(TF, IDN, cst("c1")), (TF, NID, cst("c1"))], "finr", True)
             scan(S("s4o", 4 * o, 4 * o + 4 * PW), PS(tl, 0, 4 * PW), s4(0, 1), ALU.mult, ALU.add)
             RN = S("rout", oi, oi + PW) if t < V - 1 else S("rlast", h * PW, h * PW + PW)
@@ -504,13 +677,13 @@ def build_ops(par):
             mm([(PS(tl, 0, 8), IDN, cst("ca", 8))] + [(out, full("one"), x) for x in lfs] + [(out, IDN, cst("c4", 4)), (out, NID, cst("c4", 4))]
                + [(out, full("non"), x) for x in lfs] + [(out, IDN, cst("one", 4))])
             scan(S("td", 128 * (1 - a), 128 * (1 - a) + 128, 16), PS(tl, 0, 8), cst("da", 8), ALU.mult, ALU.add, 1.0)
-        for i0, n in [(h * PW, PW) for h in hs]:
-            cur[0] = i0 // PW
+        for i0, n in [(h * PW, PW) for h in hs] if t == V - 1 or not par["whole"] else [(0, P)]:
+            cur[0] = (i0 + n - 1) // PW
             tl = "wo%d_%d" % (t, i0); Y = S("yout", t * P + i0, t * P + i0 + n); out = PS(tl, 0, n)
-            steps(1, [(out, IDN, cst("c155", n))] + modulo(out, full("w5n"), full("w5p"), Y, cst("c32", n)) + [(out, IDN, cst("wb", n))])
+            steps(1, [(out, IDN, cst("c155", n))] + modulo(out, full("wn"), full("wp"), Y, cst("c32", n)) + [(out, IDN, cst("wb", n))])
             scan(S("ws", a * P + i0, a * P + i0 + n), cst("rs16", n), out, ALU.add, ALU.max)
             offs = S("wou", 16 * a + i0 // 16, 16 * a + (i0 + n) // 16)
-            cp(offs, S("ws", a * P + i0 + 15, a * P + i0 + n, 16))
+            either(lambda: hand(offs, S("ws", a * P + i0 + 15, a * P + i0 + n, 16)), lambda: cp(offs, S("ws", a * P + i0 + 15, a * P + i0 + n, 16)), "V")
             if t < V - 1: cp(IND("xw", 32 * i0, 32 * (i0 + n), offs), Y, "xw")
             cp(IND(LW, 32 * i0, 32 * (i0 + n), offs), S("rout", t * P + i0, t * P + i0 + n) if t < V - 1 else S("rlast", i0, i0 + n), "lw")
     cur[1] = V
@@ -548,7 +721,7 @@ def price(ops, cost):
 
 
 def kind(o):
-    return o["eng"] + o["nm"] + str(o["h"])
+    return "-" + o["nm"] + str(o["h"])
 
 
 def urgency(ops, par, cost, off):
@@ -1027,7 +1200,7 @@ def words(ops, V):
 
 def read(par, text):
     ops = build_ops(par); its = text.split(); at = {x.rstrip("'"): 80.0 * (j + len(its) * x.count("'")) for j, x in enumerate(its)}
-    mid = {s[1:]: [(at[x], f) for f, x in enumerate(ws) if x in at][0] for s, ws in words(ops, par["visits"])}
+    mid = {s[1:]: ([(at[x], f) for f, x in enumerate(ws) if x in at] + [(at[x], 0) for x in at if x[1:] == ws[0][1:]] + [(0.0, 0)])[0] for s, ws in words(ops, par["visits"])}
     out = {}
     for o, s in zip(ops, slots(ops, par["visits"])):
         out[s] = mid[s[1:]] if s[0] < 3 and s[1:] in mid and (s[0] or s[1][1:-1] not in ("yb", "xd")) else (
@@ -1044,6 +1217,29 @@ def plan(par, costs):
     return ops, best
 
 
+def places_of(ops, succ, lists):
+    name = slots(ops, V); its = lists[1].split(); n = len(its); key = [0.0] * len(ops); form = [0] * len(ops)
+    at = {x.rstrip("'")[1:]: (j + n * x.count("'"), x[0]) for j, x in enumerate(its)}
+    for ph, text in ((0, lists[0]), (2, lists[2])):
+        base = -1e5
+        for j, x in enumerate(text.split()):
+            if ":" in x: base = at[x[1:-2]][0] + n * int(x[-1])
+            else: at[ph, x[1:]] = (base + j * 1e-3, x[0])
+    for k, o in enumerate(ops):
+        w = name[k][1][1:] + "abcdefghijklmnopqrstuvwxyz"[name[k][2] - 1]
+        key[k], e = at[w] if name[k][0] == 1 else at[min(name[k][0], 2), w + "!" * (name[k][0] == 3)]
+        key[k] += n * o["t"] * (name[k][0] == 1); form[k] = int(e != o["eng"])
+    for k, o in enumerate(ops):
+        if o["sem"] and o["sem"][0] == "l": key[k] = k - 1e9
+    return key, form
+
+
+def plan2(par, costs, lists):
+    ops = build_ops(par); prep = prepare(ops, costs); key, form = places_of(ops, prep[0], lists)
+    eng = [prep[3][f][k] for k, f in enumerate(form)]; a = arrange(prep, key, eng, 0)
+    return [prep[7][f][k] for k, f in enumerate(form)], (0, a, [timing(prep, c, a[0], a[2], eng, form) for c in range(len(costs))])
+
+
 PLAN = []
 
 
@@ -1052,7 +1248,7 @@ def rank_program(g, core, T, topo):
     if rank is None:
         return
     if not PLAN:
-        PLAN.append(plan(PAR, COSTS))
+        PLAN.append(plan2(PAR, COSTS, (FIRST, ROUND, LAST)) if FIRST else plan(PAR, COSTS))
     ops = PLAN[0][0]; order, bank, extras = PLAN[0][1][1]
     nxt = T.cores[(rank + 1) % len(T.cores)]; prv = T.cores[(rank - 1) % len(T.cores)]
     rid, pid, _ = topo.addr(nxt)
@@ -1061,7 +1257,7 @@ def rank_program(g, core, T, topo):
 
     todo = {}
     for o in ops:
-        if o["eng"] == "P": todo[o["ps"][0]] = todo.get(o["ps"][0], 0) + 1
+        if o["eng"] == "P": todo[o["grp"]] = todo.get(o["grp"], 0) + 1
     opened = set()
 
     def Q(name):
@@ -1087,7 +1283,7 @@ def rank_program(g, core, T, topo):
             for s2, v2 in list(clock.items()) + [(sem, val)]:
                 if kn.get(s2, 0) < v2: kn[s2] = v2
         if e == "P":
-            tl = o["ps"][0]; todo[tl] -= 1; env["ends"] = (tl not in opened, todo[tl] == 0); opened.add(tl)
+            tl = o["ps"][0]; todo[o["grp"]] -= 1; env["ends"] = (tl not in opened, todo[o["grp"]] == 0); opened.add(tl)
         ins = o["fn"](g, T, Q)
         if o["sem"] == "remote":
             sent += n_out

@@ -6,10 +6,9 @@ ACT = ActivationFunctionType
 V, W, P = 6, 4096, 128
 NH = 2
 PW = P // NH
-NC = 2
-KK = 16 // NC
+KK = 8
 M4 = float((2 ** 23 + 1) * 4)
-M1, M16, M32, M4096 = (float(3 * 2 ** 22 * n) for n in (1, 16, 32, 4096))
+M1, M32, M4096 = (float(3 * 2 ** 22 * n) for n in (1, 32, 4096))
 AN = 192.0
 PEN = float(2 ** 24)
 BIG = float(2 ** 22)
@@ -17,193 +16,69 @@ DMS = 16 + 16 * PW + 16
 
 B, F, I32, U16, H16 = "bfloat16", "float32", "int32", "uint16", "float16"
 SCRATCH = {
-    "xw": [W, B], "li": [W, I32], "lw": [W, F], "l16": [W, H16],
+    "xw": [W, B], "li": [W, I32], "l16": [W, H16], "ji": [P, I32], "wi": [8, I32], "ci": [8, I32], "cf": [32, F], "yzf": [256, F],
     "rin": [(V + 1) * P, U16], "yin": [(V + 1) * P, B], "rout": [V * P, U16], "yout": [V * P, B], "rfin": [P, F], "rlast": [P, F],
-    "wi": [8, I32], "yzf": [256, F], "ci": [8, I32], "cf": [32, F],
-    "ioc": [144, B], "iob": [128, B], "iom": [128, B], "ioj": [64, B], "tmp": [1312, B], "nc": [16 * 144, B], "iok": [288, B], "iox": [256, B], "idx": [256, B], "cm8": [128, B], "tf": [256, F], "ji": [P, I32],
-    "hh": [144, B], "hz": [144, B], "hy": [144, B], "hp": [144, B], "hs": [144, B], "hj": [144, H16], "ba": [16 * 144, B], "kb": [PW, H16],
-    "o8": [16, B], "b16": [16, B], "ni": [NH * 272, B], "nbr": [2 * P, B], "f0": [4 * PW, B], "rsk": [PW, F], "rs16": [128, F], "td": [256, F], "ca": [8, B], "da": [8, F],
-    "wou": [32, U16], "ws": [2 * P, F], "wp": [128, H16], "wn": [128, H16],
-    "lg": [2 * 2048, H16], "dr": [2 * NH * 144, B], "nn": [2 * 2 * P, B], "yd": [2 * 2 * P, B], "y2": [2 * 2 * P, B], "dm": [2 * NH * DMS, B],
-    "s4o": [2 * 4 * P, F], "pi": [2 * 2 * P, I32], "ka": [32, I32], "kt": [32, F], "ko": [32, U16], "lf": [32, B],
+    "ioj": [PW, B], "iox": [256, B], "idx": [256, B], "tmp": [800, B], "nc": [16 * 144, B], "hj": [144, H16], "kb": [PW, H16],
+    "o8": [16, B], "b16": [16, B], "f0": [4 * PW, B], "rsk": [PW, F], "rs16": [128, F], "td": [256, F], "ca": [8, B], "da": [8, F],
+    "wp": [128, H16], "wn": [128, H16], "wou": [32, U16], "ws": [2 * P, F], "ni": [NH * 272, B], "dm": [2 * NH * DMS, B], "lg": [2 * 2048, H16],
+    "s4": [2 * NH * (4 * PW + 4) + 4, F], "s4o": [2 * 4 * P, F], "pi": [2 * 2 * P, I32], "ka": [32, I32], "kt": [32, F], "ko": [32, U16], "lf": [32, B],
 }
-for _n in ("idn", "nid", "q25", "nbo", "c32", "bo", "tri", "mA", "mB", "w5p", "w5n", "wb", "c1", "c4096", "cc", "c155", "c2048",
-           "cm", "cp", "c4", "one", "non", "ida", "nia", "boa", "nba", "by", "i32"):
+for _n in ("ioc", "iok", "one", "hh", "hz", "hp", "hs"):
+    SCRATCH[_n] = [144, B]
+for _n in ("iob", "iom", "idn", "nid", "q25", "ida", "i32", "bo", "nbo", "boa", "nba", "by", "tri", "mA", "mB", "wb", "c1", "c32", "c4096", "cc", "c155",
+           "c2048", "cm", "cn", "th", "cp", "c4", "non"):
     SCRATCH[_n] = [128, B]
 for _n in ("xd", "yb", "zg", "dz"):
     SCRATCH[_n] = [2 * 2048, B]
-for _n, _d in (("nu", U16), ("good", B), ("nbv", H16), ("sa2", B), ("pj", I32), ("km", I32), ("kv", F)):
+for _n, _d in (("nu", U16), ("good", B), ("mk", B), ("nbv", H16), ("sa2", B), ("pj", I32), ("km", I32), ("kv", F)):
     SCRATCH[_n] = [2 * P, _d]
 SCRATCH = {_n: ("sbuf", [128, _v[0]], _v[1]) for _n, _v in SCRATCH.items()}
 for _n in ("ad", "nx"):
     SCRATCH[_n] = ("sbuf", [128, 2 * P // 16, 16, 16], B)
-SCRATCH["nl"] = ("sbuf", [128, 32 * NH, KK], H16)
-SCRATCH["zr"] = ("sbuf", [128, 18 * NH, KK], H16)
-SCRATCH["s4"] = ("sbuf", [128, 2 * NH * (4 * PW + 4) + 4], I32)
+for _n, _r in (("nl", 32), ("zr", 18)):
+    SCRATCH[_n] = ("sbuf", [128, _r * NH, KK], H16)
 for _n in range(8):
     SCRATCH["pb%d" % _n] = ("psum", [128, 512], F)
-CUTS = (0, 1536, 2816, 3712, W)
-LCH = 4
-SEMAPHORES = (["cV", "cS", "cP", "cG", "sent", "ljur", "lown", "lwgt", "lx", "oyz"] + ["ll%d" % j for j in range(LCH)]
-              + ["oj%d" % h for h in range(NH)] + ["oo%d" % h for h in range(NH)]
+SEMAPHORES = (["cV", "cS", "cP", "cG", "sent", "ljur", "lown", "lwgt", "lx", "ll0", "oyz"] + ["o%s%d" % (k, h) for k in "jo" for h in range(NH)]
               + ["a%s%d_%d" % (k, t, h) for k in "ry" for t in range(1, V + 1) for h in range(NH)])
 
-PAR = {"xg": ("SS", "SS"), "lg": ("SS", "SS"), "zg": ("SS", "SS"),
-       "xm": (1, 1), "zm": (1, 1),
-       "xs": ((1, 1), (1, 1)), "zs": ((0, 0), (0, 0)), "ds": ((0, 0), (0, 0)),
-       "sg": ("good", "oh"), "split": 1, "fin": "VSVSVSVS",
-       "look": 200.0, "beta": 4.0, "dmax": 5, "T": 17000.0, "delta": 7000.0, "lam": 1.3, "rounds": 3500, "seed": 1}
-PAR.update({'zm': (2, 1), 'T': 19000., 'zs': ((0, 0), (0, 1)), 'xs': ((0, 1), (0, 1))})
-COST = {"fix": 70.0, "gam": 1.5, "sca": 3.5, "pe": 0.6, "pfix": 30.0, "hop": 180.0, "self": 110.0, "net": 4500.0, "rem": 900.0, "all": 1.0, "weight": .5,
-        "gfix": 70.0, "sfix": 20.0}
-COST.update({"fix": 0.0, "sfix": 0.0, "gfix": 60.0, "pfix": 0.0, "hop": 260.0, "self": 260.0, "net": 2000.0, "rem": 600.0})
-COSTS = [COST, dict(COST, fix=15.0, hop=300.0, self=300.0, gam=2.0, sca=5.5, all=1.3, net=3500.0, rem=900.0, weight=.35)]
-PAR.update({"rounds": 200, "moves": 30000, "heat": 300.0, "aimed": .8, "visits": V, "short": 4, "dq": 4, "zq": 4, "reach": 1500.0, "again": 300, "hope": 100.0, "delta": 3000.0, "T": 16000.0,
-            "deltas": (2500.0, 3000.0, 3500.0, 4000.0), "few": 5000, "rounds": 100, "moves": 40000, "zm": ((2, 1), (2, 1)), "zs": ((0, 1), (0, 1)), "xs": ((1, 1), (1, 1)),
-            "conv": 1, "far": .3, "dn": 4, "zn": 4, "xs": ((0, 1), (0, 1)), "heat": 2000.0, "deltas": (3000.0,), "few": 1000,
-            "zm": ((1, 2), (1, 2)), "zs": ((0, 0), (0, 0)), "stages": ((5, 50000, 1000.0, False), (3, 30000, 300.0, True), (V, 10000, 100.0, False))})
-PAR.update({"xd": ("VV", "VV"), "bn": 4, "nx": 2, "ad": 2, "pn": 8, "perq": 0, "usc": 1, "zm": ((1, 1), (1, 1)),
-            "cycle": (100000, 200.0), "lead": 0.0, "rounds": 10, "settle": 4, "rounds2": 2, "ahead": ("c",), "cool": 1.0,
-            "zm": ((2, 2), (1, 2)), "cycle": ((50000, 130.0), (50000, 70.0)), "stay": ("lg", "zg"), "sweep": .03, "yb": ("EE", "EE"), "ahead": ("c", "Dm", "u", "wo"), "stages": ((3, 25000, 200.0, True), (V, 5000, 60.0, False))})
-PAR.update({"yb": ("SS", "SS"), "via": (0, 1), "xat": 0, "cuts": CUTS, "cycle": (), "sweep": .06, "stages": ((3, 45000, 120.0, True), (V, 200, 20.0, False))})
-PAR.update({"zm": ("VVVV", "VVVV"), "nx": ("VV", "VV"), "ad": ("SS", "SS"), "first": "VV", "conv": "S", "whole": 0, "yb": ("SS", "SS"), "ns": (1, 1), "fs": (1, 1)})
-FIRST = LAST = ""
-ROUND = """
-Nay0a PKd1a' Vdz0a' Vdz0d' Pu00a' Pc00a' Vkv1a' Vkm1a' PKd1b' Vnz0a' Vdz0b' Pfino0a' Szg1b' Pddz0a' Vka1a' PKd1c' Pdd0a' Pwo00a' Pwo0a' Vdz0c' Pu0a' Vkt1a' Vnn0a'
-Pfin0a' Vnz0d' Pc01a' Vko1a' Vnz0b' Pc0a' Vnz0c' PKd1d' Pfin0d' Vyout1a' Pfin0b' Ssa20a' Vpi0a' Sdr1a' Pfin0c' Vkp1a' Syb0a Vnr1a' Gsendy1a' Vws0a' PfillDz1a' Pfinc0a'
-Pfinr0a' Vfar0a' Vnm0a' Pdd1a' Pddz1a' Pwo01a' Vdz1b' Syb0b Vs4o0a' PDz1a' Nay1a Vnn1a' PfillDz1b' Vnz1d' Vrout0a' Vdz1a' Pu01a' Pc1a' Pu1a' Vwou0a' Gsendr0a' Vnz1a'
-Pwo1a' Ssa21a' Vnz1b' Vnz1c' Pfino1a' Vpi1a' Pfin1d' Pfinc1a' Nar0a Pfin1a' Pfin1b' Pfin1c' Vws1a' Vxw0a' Vfar1a' Pfinr1a' Vnm1a' PDm00a Vlw0a' Syb1a Vs4o1a' Vwou1a'
-Vrout1a' Vxw1a' Gsendr1a' Vlw1a' Syb1b Slf1a' Vxd0a Slg0a Slg0b Nar1a Vlf0a' Vxd0b PA0a' Vnx0a Sad0a Vnx0b Pn0a Vtd0a' Sad0b Vrf0a Vxd1a PKn0b PKn0a Slg1b Pnb0b Vxd1b
-Pnb0a Slg1a PKr0a Pn0b Vgood0a PKa0b Vnx1a Vnx1b Sad1a PDm0a PKa0a Vkp0a Vnu0a Vdm0b PDm01a Sad1b Vdm0d Pnb1b Pnb1a Vkm0a Vdm0a Szg0b Szg0a Pn1a Vkv0a Vka0a Vgood1a
-Vnr0a Vrf1a PKd0d PKd0b PKd0a Vkt0a Vdm0c PDm1a Pn1b Vko0a Snbv1a Vdm1d PKn1a Vyout0a PKn1b PKd0c Vnu1a Vdm1c Gsendy0a Vdm1b PfillDz0a PKr1a PKa1a Snbv0a Vdm1a Sdr0a
-Szg1a PKa1b
-"""
-
-
-PAR.update({"ns": (1, 1), "fs": (2, 2), "im": 1, "re": 0, "ahead": ("c", "Dm", "u", "wo", "fin")})
 FIRST = """
-Yljur0a Slown0a Slwgt0a Ylx0a Yll00a Yll10a Yll20a Yll30a Gci0a Gioc0a Vci0b Vcf0a Giom0a Vcf0b Vidn0a Stf0a Vc10a Vc20480a Gdm0d Vcf0c Scf0g Vnl0a Sc1550a Vnc0e Giob0a Sca0b
-Vtmp0k Snc0a Vnc0b Vcf0i Szr0a Vnc0f Pwo00a Vcf0h Snid0a Vnc0d Gdm0b Vcf0d Stmp0c Vtf0b Giok0a Sda0a Snc0l Vbo0a Sone0a Vnc0m Giok0b Gdr0a Vru0b Syb0a PfillDx1a Vhh0a Vcf0e
-Vtmp0e PfillDx1b Vcf0n Vrsk0a Vrf1a Vru0a Syb0b Vnc0n Vnc0j Gdm0a Vtmp0f Giox0a Vcf0j Vrf0a Snc0g Vf00c Vcf0f Snc0p Vtmp0a Vtmp0j Gdm0c Stmp0b Vnc0o Vwi0a Snon0a Vwb0a Gioj0a
-Snc0h Vtmp0i Vnc0k Scm0a Vnc0i Sca0a Snc0c Sca0c PDm00a PDm01a Vxd0b Syb1b Vcf0o Syb1a Vtmp0d Vxd0a PDx1d PDx1b Sby0a Vnc0q Stmp0h Sda0c PDx1a Sq250a Vnx0a PDx1c Scp0a Shz0a
-Glw0c Vidx0a Sxd1a Vcf0k Vnx0b Vtmp0g Vkp0a Vcf0m Sxd1b VmA0a Pnb0b Vcc0a Vcf0l Pnb0a Vrs160a Shj0a Vtri0a Glw0a Vkp1a Vnx1b Sgood0a Sad0b Vnx1a PDm0a Shp0a Vdm0f Sc40a Std0b
-Sf00d Vdm0g Si320a PKn0a Sad0a Vdm0h PKn0b Vdm0e PKn1a Shy0a Pnb1a Sw5p0a Glw0g Sad1b PKd0b PKd0c Pnb1b PKd0a Shs0a PKn1b Vlg0b Skb0a Sc320a PKd0d Snbv0a Sad1a PKr0a PKa0a
-Glw0f PKa0b Sf00a Vlg0a Sda0b Std0a PKr1a Snia0a PKa1a Sida0a Glw0e Snba0a PKa1b Snbo0a Sdr0b Std0c Vkm0a Sboa0a Vlg1b Scc0b PNt0a Pdd0a Snl0b Vka0a Glw0d Swn0a Vkv0a Vkm1a
-Sw5n0a Vkv1a Vc40960a Sgood1a Pn0a Swp0a Vkt0a Sf00b Slf0a Slf1a PDm1a Vnu0a Snbv1a Pc00a Vlg1a Szg0a Glw0b Vko0a VmB0a PNt1a Szg0b Vyout0a Vdm1a Vka1a Pddz0a Vnl1a Pwo0a Vdm1b
-Gsendy0a PfillDz0a Pcy0a Nay0a:1 Snn0a Vdm1c Pn1a Vdm1d Pc0a Glw0i Pfino0a Vnu1a Pfinz0b Vkt1a Vdz0c Ssa20a Pfinz0a Szg1a Vdz0a Pfinc0a Vdz0b Pu00a Pu0a PKd1d Vko1a Pfin0c
-Vdz0d Pfin0a Szg1b Pfin0b Vpi0a PKd1a Vyout1a PKd1b PKd1c Vnr0a Pfiny0a Pfin0d Vnm0a Vfar0a Pfinr0a Vws0a Pu01a Gsendy1a Syb0a:1 Vdr1a Pddz1a PfillDz1a Pu1a Vs4o0a Pc01a Pdd1a
-Pfino1a Vpi1a Nay1a:1 Pfinz1b Vrout0a Vdz1c Snn1a Pcy1a Pwo01a Pfiny1a Pfinz1a Vdz1d Gsendr0a Pc1a Vdz1a Pwo1a Vdz1b Pfin1d Ssa21a Glw0h Pfin1c Syb0b:1 Vwou0a Pfin1a Vfar1a
-Vnr1a Pfinc1a Vws1a Vnm1a Pfin1b Vlw0j Pfinr1a Pwo00a:1 PA0a Vwou1a Vs4o1a PDm00a:1 Vxw0a Syb1b:1 Vrout1a Vxw1a Syb1a:1 Gsendr1a Vlw1a Vtd0d
+Yljur0a Slown0a Ylx0a Yll00a Ylwgt0a Vone0a Gci0a Gioc0a Sc10a Vnon0a Sda0b Vci0b Scc0a Vcf0a Sca0c Vc20480a Sf00a Giom0a Vzr0a Sda0c Sca0a Vcf0b Sc320a Vnl0b Vidn0a Std0a
+Vtmp0f Vc1550a Giob0a Std0b Vcf0g Vcf0c Scp0a Vnc0j Snc0b Vnc0f Vnc0k Std0c Vcf0i Snid0a Giok0a Vcf0k Vnc0n Snc0p Vcf0h Vnc0m Sda0a Vnl0a Syb0a Vrs160a PfillDx1a Gdm0c Vf00d
+Vnc0g Vcf0e PfillDx1b Gni0a Vcf0j Vtmp0d Vnc0l Sru0b Vcf0l Syb0b Pwo00a Vnc0c Vnc0i Vtmp0e Vbo0a Vnc0d Vru0a Vnc0e Vida0a Sc40960a Vca0b Sf00b Vcf0d Scm0a Vnc0h Sb160b Vth0a
+Vxd0a Syb1b PDm01a Gdm0d Grf0a Gioj0a Vnc0o Syb1a Vxd0b Giox0a PDx1b PDx1d Pwb0a Sad0a Vnc0a Vnx0a PDx1a Vnx0b Gnc0q PDx1c So80a Vrsk0a Sad1a Vwb0b Vhh0a Gtmp0c Vidx0a Vcf0f
+Vtmp0a Pnb0b Vcf0o Sad1b Vcc0b Vhz0a Vhp0a Pnb0a Vkb0a Vb160a Vf00c Vhs0a Gtri0a Vnx1a PKn0a Sad0b Vtmp0b Vcn0a PKn0b Vnba0a Grf1a Vnx1b PKr0a Snbv0a Sgood0a PDm00a Vtri0b
+Slg0b Vby0a Vlg0a Giox0b PKa0b PKa0a Gdm0a PDm0a Pnb1b GmB0a Slg1a Vcf0m Vkm0a Pnb1a Vkv0a Vdm0h GmA0a PNt0a Vka0a Vdm0e PKn1a Vgood1a Vdm0g Snl0c PKn1b Slg1b Vkt0a PDm1a Vdm0f
+Pn0a PKr1a Vboa0a PKa1b Vko0a Vmk1a Vnu0a Vnr0a Vq250a Vdm1b Snbv1a Szg0a PKd0b PKa1a Vyout0a PNt1a Vcf0n Vnbo0a PKd0a Vkm1a PKd0c Vdm1d PKd0d Gsendy0a Pddz0a Pddz0b Pu00a
+Vkv1a Pc00a Szg0b Vwn0a Vnl1a Pcy0a Vka1a Vni0b Pfino0a Vwp0a Vdm1c Pn1a PfillDz0a Nay0a:1 Vkt1a Pc0a Vi320a Vdm1a Pu0a Snu1a Skp0a Pwo0a Sko1a Ssa20a Vdz0c PZz0a Szg1b Vdz0a
+Pc01a PKd1c PKd1a Vdz0b Pfiny0a Pfin0d Gdm0b Pfinc0a Vpi0a PKd1d Vdz0d Szr0b Szg1a Pfin0c Vfar0a Pfin0b Vyout1a Pfin0a Vnm0a Pfin0e Vfa0a Vnr1a Pfinr0a Vws0a PKd1b Gsendy1a
+Pu01a Pddz1b PfillDz1a Vs4o0a Pddz1a Pfino1a Vdz1d PZz1a Sni1a Nay1a:1 Srout0a Vdz1b Pu1a Skp1a Swou0a Pwo01a Slf0a Pc1a Vdz1a Szr1a Gsendr0a Pfiny1a Pcy1a Pwo1a Vidx0b Pfin1c
+Vpi1a Ssa21a Vdz1c Pfin1e Syb0a:1 Pfin1b Nar0a:1 Vfar1a Pfinc1a Vnm1a Vws1a Pfin1a Pfin1d Vfa1a Vxw0a Syb0b:1 Pfinr1a Vs4o1a Pfino0a:1 Vc40a Vwou1a Slf1a Vrout1a Vlw0a PA0a
+Gsendr1a Vxw1a Syb1b:1 Vlw1a Nar1a:1 Vhj0a Syb1a:1 Vtd0d
 """
 ROUND = """
-Nay0a Vkv1a' Pdd0a' Vkm1a' Vnu1a' Pcy0a' Vdm1b' PfillDz0a' Pwo0a' Pfino0a' Vnn0a' Szg1b' Pfiny0a' Vka1a' Pfinz0b' Vdz0b' PKd1b' Vkt1a' Pc0a' Vdz0c' Pu00a' Pu0a' Pfinz0a' Vdz0a'
-Ssa20a' Szg1a' PKd1c' Vko1a' Pfin0c' Vdz0d' Pfin0b' PKd1d' Vpi0a' Pfinc0a' Vyout1a' PKd1a' Pfin0a' Vws0a' Pfin0d' Vnm0a' Vfar0a' Pfinr0a' Sdr1a' Vkp1a' Gsendy1a' Pu01a' Syb0a
-Vwou0a' Pc01a' PfillDz1a' Pfino1a' Vs4o0a' Pddz1a' Pdd1a' Vdz1a' Pu1a' Nay1a Pfinz1b' Vrout0a' Snn1a' Vdz1b' Pfinz1a' Slf1a' Vrf1a' Gsendr0a' Vdz1d' Pcy1a' Pc1a' Pwo01a'
-Pfin1b' Vpi1a' Pwo1a' Vdz1c' Ssa21a' Pfin1a' Slf0a' Nar0a Syb0b Pfin1d' Vnr1a' Pfiny1a' Vws1a' Pfinc1a' Vfar1a' Vnm1a' Pfin1c' Vlw0a' Pfinr1a' PDm01a Pwo00a PA0a' Vwou1a'
-Vs4o1a' PDm00a Vxw0a' Syb1b Vrout1a' Vxw1a' Syb1a Gsendr1a' Vlw1a' Vtd0a' Vxd0a Slg0b Nar1a Vxd0b Slg0a Vnx0a Sad0a Vrf0a Vnx0b PNt0a Vkp0a Sad0b Vxd1a PKn0b PKn0a Snl0a Slg1b
-PKr0a Pnb0b Vxd1b Pnb0a Pn0a PKa0a Sgood0a Snbv0a PKa0b Vnx1a Slg1a PDm0a Vnx1b Vnu0a Vkm0a Vkv0a Vdm0c Pnb1b Sad1b Vka0a Vdm0a Pnb1a Vdm0d PKn1a Sad1a Vkt0a PNt1a Vgood1a
-Vdm0b PKn1b Szg0a Vko0a Vnr0a PDm1a Vnl1a PKr1a Vnbv1a PKd0d Vyout0a PKd0a PKd0c Vdm1d PKd0b PKa1b Gsendy0a Vdm1a Szg0b PKa1a Vdr0a Vdm1c Pn1a Pddz0a Pc00a
+Nay0a PfillDz0a' Vnu1a' Pu00a' Vdm1b' Pu0a' Sni0a' Pwo0a' Vka1a' Szg1b' Pfiny0a' Vdz0a' Pc00a' Pcy0a' PKd1a' Vdz0b' PKd1d' Pc0a' PZz0a' Vkt1a' Vdz0d' Pfin0b' Vpi0a' Ssa20a'
+PKd1c' Sko1a' Vdz0c' Pfin0c' Szr0a' Szg1a' Pfin0e' Vfar0a' Pfinc0a' Vyout1a' Pfin0a' Slf1a' Pfin0d' Vnm0a' Vfa0a' Pfinr0a' Vws0a' Pwo01a' Vnr1a' Gsendy1a' PKd1b' Vlf0a' Pddz1b'
+PfillDz1a' Pddz1a' Vs4o0a' Pc01a' Pu01a' Pcy1a' Vdz1a' Sni1a' Nay1a Srout0a' Vdz1d' Pu1a' Skp1a' PZz1a' Pwo1a' Gsendr0a' Vdz1c' Szr1a' Pc1a' Pfino1a' Vpi1a' Pfin1b' Vws1a'
+Vdz1b' Ssa21a' Pfin1e' Syb0a Pfiny1a' Pfin1d' Swou0a' Nar0a Vwou1a' Vfar1a' Pfin1a' Vnm1a' Pfinc1a' Pfin1c' Syb0b Vfa1a' Pfinr1a' PA0a' Vs4o1a' PDm01a Pwo00a PDm00a Pfino0a
+Vxw1a' Srout1a' Vxw0a' Gsendr1a' Vlw1a' Syb1b Vlw0a' Nar1a Vtd0a' Syb1a Vxd0a Grf0a Slg0a Vxd0b Slg0b Vkp0a Sad0a Vnx0a PNt0a Vnx0b Grf1a Sad0b Vxd1b PKn0b Snl0a Pnb0a Slg1a
+Pnb0b Vxd1a PKn0a PKr0a PKa0b Sgood0a Slg1b PKa0a Vnx1b PDm0a Vnx1a Pn0a Vnbv0a Vkm0a Vkv0a Vdm0d Sad1b Pnb1a Vka0a Vnu0a Pnb1b Vdm0b Sad1a PNt1a Vdm0a PKn1b PKn1a Vkt0a
+Vgood1a Vdm0c Szg0b Vko0a Vnbv1a PDm1a Vnr0a Vnl1a PKr1a PKa1a Vyout0a Vdm1d PKd0a Szg0a Vdm1a Gsendy0a PKd0d PKa1b Pn1a Vdm1c PKd0b PKd0c Pddz0a Vkm1a Pddz0b Vkv1a
 """
 LAST = """
-Pwo00a Pc00a:4 Nay0a Pu1a:4 Nay1a Pc1a:4 Syb0b Slf0a:4 Nar0a Pfinr1a:4 Syb0a Vwou1a:4 PDm00a Vs4o1a:4 Pu00a PDm01a Vxw0a:4 Syb1a Vxw1a:4 Syb1b Vtd0a:4 Vkp0a Vxd0a Nar1a Vxd0b
-Slg0a Slg0b PNt0a Vnx0a Sad0a Vnx0b Vxd1a Sad0b PKn0b Vxd1b Slg1b PKn0a Snl0a Pnb0b Pnb0a PKr0a PKa0a PKa0b Vgood0a Vnx1a Vnx1b PDm0a Vkm0a Vnbv0a Slg1a Sad1a Sad1b Vdm0d Vkv0a
-Pn0a Vka0a Pnb1b Pnb1a PNt1a Sgood1a Vnu0a Vrf1a Vdm0b Vkt0a PKn1a Vkp1a Vdm0c Vdm0a PDm1a PKn1b Vko0a Vnbv1a Vrf0a PKr1a Vdm1c PKd0b PKd0c Vyout0a PKd0a PKd0d Vdm1b Vdm1a
-PKa1b Szg0b Snl1a Pn1a Szg0a Gsendy0a PKa1a Pddz0a Vdr0a Pu0a Vnu1a Vnr1a Pwo0a Nay0a! Vdm1d Vkm1a PfillDz0a Vpi0a Pfino0a Vkv1a Pdd0a Vws0a PKd1b Pfinz0a Vka1a Vdz0d PKd1a
-Pc00a Vkt1a Szg1a PKd1c Vdz0c PKd1d Szg1b Pcy0a Pfinz0b Vko1a Vnn0a Vdr1a Vwou0a Pfin0d Vyout1a Pc01a Pu01a Pdd1a Vnr0a Vdz0b Pc0a Gsendy1a Pu1a Pfiny0a Vdz0a PfillDz1a Ssa20a
-Vfar0a Pddz1a Vnm0a Vpi1a Pfin0c Yoo00a! Vdz1c Pfin0b Nay1a! Pfin0a Snn1a Pfinc0a Pcy1a Pfinr0a Pfino1a Vdz1d Pc1a Vdz1a Pfin1c Vs4o0a Ssa21a Vdz1b Pfinz1b Pfinz1a Pfiny1a
-Vrout0a Vnm1a Pfin1d Vfar1a Pfinc1a Gsendr0a Vlw0a Pfin1a Pfin1b Pfinr1a Pwo01a Pwo1a Nar0a! Vs4o1a Vws1a Vrout1a Vwou1a Sl160a! Sl160b! Pyz0a! Sl160c! Gsendr1a Vlw1a Vl160d!
-Pyz0b! Nar1a! Sl161d! Yoo11a! Vl161a! Sl161c! Pyz0c! Pyz0d! Vl161b! Pyz1d! Yoj00a! Pyz1a! Pyz1c! Pyz1b! Syzf1a! Yoj11a! Yoyz1a!
+Vkv1a:4 Nay0a Pu1a:4 Nay1a Pfin1e:4 Syb0a Swou0a:4 Nar0a Pfin1c:4 Syb0b Vs4o1a:4 Pfino0a Pwo00a PDm00a PDm01a Vlw1a:4 Syb1b Vlw0a:4 Nar1a Vtd0a:4 Syb1a Vxd0a Grf0a Slg0a Vxd0b
+Slg0b Vnx0a Sad0a Vnx0b PNt0a Vxd1b Grf1a Sad0b PKn0b PKn0a Snl0a Slg1a Pnb0a Vxd1a Pnb0b PKr0a PKa0b Sgood0a Slg1b PKa0a Vnx1b Pn0a Vnx1a PDm0a Vkv0a Vkm0a Vdm0a Pnb1a Sad1a
+Vnu0a Vka0a Pnb1b Vnbv0a Vdm0d Sad1b PNt1a Vkp0a Vkt0a Vgood1a PKn1b Vdm0c Sko0a Szg0a Vnl1a PDm1a PKn1a Vdm0b PKr1a Vnbv1a Vdm1d PKa1a Vyout0a PKa1b Szg0b Vdm1b PKd0b Pn1a
+Vdm1c Gsendy0a PKd0c PKd0d Pwo0a Vkm1a Vnr0a PKd0a Vnu1a Pddz0a Vkv1a Pu00a Vnr1a Pfiny0a Vka1a Pddz0b Nay0a! Vdm1a PfillDz0a Szg1a Pu0a PKd1d Vkt1a PKd1c Vdz0b PKd1b PZz0a
+Vni0a PKd1a Vko1a Pc00a Vdz0d Pcy0a Pfin0c Szg1b Vzr0a Pc0a Vws0a Vyout1a Pc01a Vpi0a Pfin0e Vdz0c Pfin0a Pu01a Gsendy1a PfillDz1a Pddz1b Vfar0a Pcy1a Vdz0a Pu1a Ssa20a Pddz1a
+Pfin0d Sfa0a Vdz1a PZz1a Swou0a Nay1a! Sni1a Vdz1d Pfin0b Pfinc0a Vdz1c Szr1a Pfinr0a Skp1a Pc1a Snm0a Vdz1b Pfino1a Yoo00a! Pfin1b Vpi1a Ssa21a Pfin1a Vs4o0a Pfin1d Pfin1c
+Vfar1a Snm1a Pfinc1a Pfiny1a Pfin1e Vlw0a Sfa1a Pfinr1a Srout0a Pwo01a Pwo1a Vs4o1a Gsendr0a Sl160b! Vws1a Vl160f! Srout1a Vwou1a Sl160e! Nar0a! Vl160d! Pyz0b! Pyz0f! Sl160h!
+Gsendr1a Vlw1a Yoo11a! Sl160a! Pyz0d! Vl160g! Sl160c! Pyz0h! Nar1a! Vl161f! Pyz0e! Sl161e! Pyz0a! Vl161h! Pyz0g! Sl161g! Pyz0c! Vl161c! Pyz1f! Sl161b! Pyz1e! Vl161a! Pyz1h!
+Pyz1g! Vl161d! Pyz1c! Pyz1a! Pyz1b! Pyz1d! Syzf1a! Yoj00a! Yoyz1a! Yoj11a!
 """
 
 
-FIRST = """
-Yljur0a Slown0a Slwgt0a Ylx0a Yll00a Yll10a Yll20a Yll30a Gci0a Gioc0a Vci0b Vcf0a Giom0a Vcf0b Vidn0a Sf00c Sc1550a Vc40a Giob0a Vcf0c Scf0g Vcf0k Giok0b Snc0a Vc10a Vc320a
-Vnc0b Sda0a Pwo00a Snc0d Vtmp0e Giok0a Vone0a Snid0a Vf00d Si320a Vcf0i Sf00b Vnc0f Snc0m Gdm0d Vtmp0f Snc0j Vnc0l Vcf0j Gioj0a Snc0i Vtmp0k Vnc0n Vca0b Gdm0a Gdm0c Vq250a
-Vnon0a Giox0a Vru0a Syb0b Vcm0a Vcf0d Vcf0n Vwi0a Vru0b Giox0b Vtmp0i PDm01a PfillDx1b Vbo0a Std0b Vrs160a Stf0a Vcf0h PfillDx1a Vcf0e Syb0a Vnc0g Vnc0c PDm00a Vtf0b Gdr0a
-Vnc0e Snc0h Vcf0f Vnc0k Snl0a Vtmp0c Snc0p Vhh0a Stmp0d Syb1a Vidx0a Vxd0b Vxd0a Syb1b PDx1c PDx1a Vtmp0j Vnx0b Snc0o Sda0b Scp0a Shz0a PDx1b PDx1d Stmp0h Sda0c Vnx0a Vnc0q
-Vrf0a Glw0b Vidx0b Vcf0m Sxd1a Vcf0l Vtmp0g Vwb0a VmB0a Pnb0a Sxd1b Pnb0b Vrsk0a Snba0a Vtri0a Sc40960a Glw0a Sc20480a Sgood0a Sad1a Vnx1b Vnx1a Vcf0o PDm0a Sad0a Vdm0g Vdm0e
-Pnb1b Sf00a Glw0c Shp0a PKn0a Sida0a Skb0a Scc0a PKn1a Stmp0b Sad0b PKn0b PKn1b Sca0a Shy0a Glw0d Vdm0f Vdm0h Shs0a PKr0a Std0a PKd0b Sw5p0a PKd0d PKr1a Sad1b PKd0a PKa0b PKa0a
-Vlg0b Snbv0a Sboa0a Sby0a Pnb1a Snbo0a Glw0f Vlg0a Std0c Snia0a Scc0b Szr0a Sgood1a Sca0c Vkm0a Glw0i Vlg1a PNt0a PKa1b Snl0c Stmp0a PKa1a Vka0a Vkv0a Snl0b PKd0c Glw0e Sw5n0a
-Swn0a Pn0a Pc00a Vkv1a Vkm1a PDm1a Sdr0b Swp0a Vnu0a Vkt0a Snbv1a Vlg1b Glw0h Vko0a Vka1a Vdm1d PNt1a Vnr0a Vyout0a Szg0b Vkt1a Szg0a Pdd0a VmA0a Gdm0b Pddz0a Pcy0a PfillDz0a
-Gsendy0a Vdm1c Pwo0a Snl1a Vkp0a Nay0a:1 Snn0a Pfino0a Vko1a Shj0a Vdz0b Pn1a Slf1a Glw0g Pu00a Vdz0c Pc0a Pfinz0b Vnu1a Pfin0b Ssa20a Slf0a Pfinz0a Szg1b Pu0a Vdm1a Pfinc0a
-Vdm1b Vdz0a Vdz0d Pfiny0a PKd1c Pfin0c PKd1a Vpi0a PKd1d Pfin0a Szg1a Vyout1a PKd1b Pfin0d Vrf1a Pfinr0a Vfar0a Pu01a Vnm0a Vws0a Gsendy1a Vkp1a Syb0a:1 Vdr1a Pu1a Pfino1a
-Vs4o0a Pc01a PfillDz1a Pddz1a Vpi1a Pdd1a Nay1a:1 Vwou0a Pfinz1a Pfinz1b Vrout0a Snn1a Pcy1a Gsendr0a Vdz1b Vdz1c Pwo01a Pfiny1a Pc1a Vdz1a Pwo1a Pfin1b Pfin1c Vdz1d Ssa21a
-Syb0b:1 Vnm1a Pfin1a Vws1a Vnr1a Pfinc1a Vfar1a Vlw0j Pfin1d Pfinr1a PDm01a:1 PA0a Pwo00a:1 Vwou1a Vs4o1a PDm00a:1 Vxw0a Syb1b:1 Vrout1a Vxw1a Syb1a:1 Gsendr1a Vlw1a Sad0a:1
-Vtd0d
-"""
-
-
-FIRST = """
-Yljur0a Slown0a Slwgt0a Ylx0a Yll00a Yll10a Yll20a Yll30a Gci0a Vcf0a Gioc0a Vci0b Giom0a Giob0a Vcf0b Giox0b Vidn0a Vnl0b Sc10a Sc20480a Sc40a Scf0g Sc40960a Vzr0a Stmp0a
-Vcf0c Vda0a Snid0a Std0a Vc1550a Pwo00a Vnc0f Snc0e Snc0k Snc0b Vtmp0k Sf00a Vcf0i Vnc0h Vnon0a Sf00c Vbo0a Stmp0h Scc0a Gdm0a Vcf0d Stf0a Vtd0b Vone0a Vtmp0e Stmp0d Sb160b
-Gioj0a Vnc0l Vca0a Vru0a Syb0b Snc0d Giox0a Vcf0k Vtmp0f Vcf0h Vca0b Giok0a Vcf0j Sb160a Vf00b Vf00d Vrs160a Vcf0m Vtmp0g Syb0a Vnc0n Vtf0b Scp0a Vru0b Giok0b Vcf0f Grf0a
-Vtri0a Snc0m Sca0c Vcm0a Sboa0a Vcf0e Gdm0d PfillDx1b Grf1a Vhh0a Vwb0a Snc0c Gdm0c Snc0i Gdm0b Vtmp0j Vhj0a Vxd0b Gni0a Vq250a Snc0p Syb1b PfillDx1a Syb1a Vtmp0i PDm01a PDx1c
-Snc0g Vxd0a PDx1d Vnc0a Snc0j Stmp0b Stmp0c PDx1a Vnc0o Vnx0b Vrsk0a Vnx0a PDm00a Vnc0q PDx1b Vcf0n Sxd1b Pnb0b Sxd1a VmA0a Vkp1a Sc320a Vidx0b Pnb0a Vhp0a Vkp0a Sad0b Sda0b
-VmB0a Vcf0l Snba0a Skb0a Si320a Glw0c Vgood0a Vidx0a PDm0a Sad0a Vnx1a Scc0b Vnx1b Sby0a Std0c PKn0b Shs0a Swp0a Snbo0a Glw0f PKn0a Glw0a Vdm0f Vdm0h Sad1b Pnb1b PKr0a Pnb1a
-PKn1a Snbr0a PKn1b PKa0b Snl0a Vdm0g Snbr1a Sda0c Sida0a So80a PKd0d Sad1a PKd0b PKd0c Glw0b Sgood1a PKa0a Vlg0b Vlg0a Glw0d Vkm0a PNt0a Vkv0a PKr1a Vlg1b Glw0g Glw0e Swn0a
-Snl0c Vka0a Vlg1a Shz0a PKa1a PDm1a Pn0a Slf0a Pc00a Vnu0a Vkt0a Pc01a Vnr0a PKa1b Vdm0e PNt1a Vko0a Vdm1c Pu00a PKd0a Vkm1a Vyout0a Gsendy0a Vnl1a Pddz0b Vka1a Pddz0a Szg0b
-Pn1a Vkv1a PfillDz0a Vdm1d Szg0a Sni0b Vdm1a Vnu1a Vdm1b Nay0a:1 Glw0i Pu0a Vpi0a Vkt1a Szg1a Pwo0a Vdz0c Pcy0a Vdz0a Pc0a PZz0a Vdz0b Pfino0a Vko1a Pfin0d PKd1d Pfin0b Ssa20a
-Pfiny0a Szr0b Szg1b Vdz0d Vnm0a Vfar0a Vyout1a Pfin0c Pfinc0a Gsendy1a Pfin0a Pfin0e Vlw0h Vws0a Pfinr0a Vs4o0a Pfino1a Pwo01a Vnr1a PKd1a PKd1c PfillDz1a PKd1b Pddz1a Vlf1a
-Nay1a:1 Pddz1b Sni1a Pu01a Vwou0a Vrout0a Pu1a Gsendr0a PZz1a Vdz1b Szr1a Vdz1c Pwo1a Pc1a Pcy1a Ssa21a Vdz1a Pfin1c Nar0a:1 Pfiny1a Vdz1d Pfin1a Pfin1d Pfin1b Vpi1a Vws1a
-Pfinc1a Syb0b:1 Pfin1e Vfar1a Vnm1a Pfinr1a Gwou1a PDm01a:1 Vxw0a PDm00a:1 PA0a Vs4o1a Syb1a:1 Vlw0j Vrout1a Gsendr1a Vxw1a Syb1b:1 Vlw1a PNt0a:1 Vtd0d
-"""
-ROUND = """
-Nay0a Pwo0a' Sni0a' Vka1a' Pfino0a' Vdz0a' Szg1b' PZz0a' Vkt1a' Vdz0d' Pc0a' Pu00a' Pu0a' Vdz0c' PKd1a' Pfin0b' Vko1a' Pfiny0a' Ssa20a' Vdz0b' Pfin0e' Szr0a' Szg1a' Pfin0d'
-Vpi0a' Pfinc0a' Vyout1a' Pfin0a' Pfin0c' Vfar0a' Pfinr0a' Vnm0a' Pu01a' Vkp1a' Gsendy1a' PKd1d' Vws0a' PKd1c' PKd1b' Snbr1a' Slf0a' Pddz1b' Vs4o0a' Slf1a' Pddz1a' PfillDz1a'
-PZz1a' Gwou0a' Nay1a Sni1a' Pc01a' Pfino1a' Vrout0a' Vdz1a' Pfiny1a' Pu1a' Szr1a' Pcy1a' Vdz1b' Gsendr0a' Pc1a' Pwo01a' Pwo1a' Vdz1d' Pfin1b' Ssa21a' Syb0a Vdz1c' Pfin1c' Nar0a
-Pfin1a' Pfinc1a' Vpi1a' Vws1a' Pfin1e' Syb0b Pfin1d' Vfar1a' Pfinr1a' Vnm1a' Gwou1a' Pwo00a PDm01a Vlw0a' PDm00a PA0a' Vs4o1a' Syb1a Vxw1a' Vrout1a' Vxw0a' Syb1b Gsendr1a'
-Vlw1a' Vtd0a' Vxd0b Slg0a Grf0a Nar1a Vxd0a Slg0b Vnx0b Sad0b Vnx0a PNt0a Vkp0a Sad0a Vxd1b Grf1a Pnb0a Pnb0b Slg1a PKn0a PKn0b Vxd1a PKr0a PKa0a Sgood0a Snl0a PKa0b Slg1b
-Vnx1b Pn0a PDm0a Vnx1a Vnu0a Vkm0a Vdm0d Sad1a Pnb1b Vka0a Vkv0a Vdm0b Pnb1a Sad1b Vdm0a PNt1a Vgood1a PKn1b Vkt0a Szg0b Vdm0c PDm1a Vnr0a PKn1a Vnl1a Vko0a Vnbr0a PKr1a Vdm1b
-PKa1a Vyout0a Szg0a PKa1b Vdm1a PKd0d Vdm1c Gsendy0a Pn1a PKd0a PKd0c PKd0b Vkv1a Pc00a Vkm1a Pddz0b Vnu1a Pddz0a Vnr1a PfillDz0a Vdm1d Pcy0a
-"""
-LAST = """
-Pcy0a:4 Nay0a Gwou0a:4 Nay1a Ssa21a:4 Syb0a Pfin1c:4 Nar0a Pfin1e:4 Syb0b PA0a:4 PDm00a Pwo00a Vs4o1a:4 PDm01a Syb1b Vxw0a:4 Syb1a Vtd0a:4 Vxd0a Slg0a Grf0a Nar1a Vxd0b Slg0b
-Vkp0a Vnx0a Sad0a Vnx0b PNt0a Sad0b Vxd1b Grf1a PKn0b Pnb0b Slg1b PKn0a Vnl0a Pnb0a Vxd1a Pn0a Slg1a PKr0a PKa0b PKa0a Vgood0a Vnx1b Vnx1a PDm0a Sad1b Vnu0a PNt1a Vkv0a Vdm0c
-Sad1a Pnb1b Vkm0a Vdm0b Pnb1a Vnr0a Vka0a Szg0a PKn1b Vnl1a Vdm0d PKn1a Vgood1a Vkt0a Vnbr1a Pn1a Vdm0a PKr1a PDm1a Szg0b PKa1b Vko0a Vkp1a Vnu1a Vnr1a Vnbr0a PKa1a Vyout0a
-Vdm1a PKd0b PKd0d PKd0a PKd0c Gsendy0a Vkm1a Pddz0b Szg1a Vkv1a Pc00a Pddz0a Vdm1b Pu00a Pcy0a PfillDz0a Vka1a Pfino0a Vni0a Pc01a Pwo0a Nay0a! Vdm1c Vkt1a Pc0a Vdm1d Pfiny0a
-PZz0a Vdz0b Ssa20a Pu0a Szg1b Vko1a PKd1a Vdz0a PKd1b PKd1c Pfin0c Vpi0a Pfinc0a Vyout1a Pu01a Vdz0c Pfin0b Szr0a PKd1d Pddz1a Vfar0a Gsendy1a PfillDz1a Vnm0a Pddz1b Vdz0d
-Pcy1a Pfin0d Vws0a PZz1a Sni1a Vdz1b Yoo00a! Nay1a! Pfin0a Vdz1c Gwou0a Pfin0e Pfinr0a Szr1a Pu1a Vdz1a Pc1a Pfino1a Vs4o0a Pfin1d Ssa21a Pfin1c Vdz1d Pfin1a Pfin1b Vpi1a
-Pfinc1a Vrout0a Pfiny1a Pfin1e Vfar1a Pwo01a Pfinr1a Gsendr0a Vnm1a Pwo1a Vlw0a Vs4o1a Nar0a! Vws1a Sl160c! Yoo11a! Vrout1a Gwou1a Vl160d! Sl160b! Gsendr1a Pyz0c! Vlw1a Pyz0d!
-Vl160a! Nar1a! Pyz0b! Sl161d! Vl161a! Pyz0a! Sl161b! Vl161c! Pyz1d! Yoj00a! Pyz1a! Pyz1b! Pyz1c! Yoj11a! Syzf1a! Yoyz1a!
-"""
-
-
-FIRST = """
-Yljur0a Slown0a Slwgt0a Ylx0a Yll00a Yll10a Yll20a Yll30a Gci0a Gioc0a Sc1550a Sca0c Vci0b Giom0a Vcf0a Gdm0c Sca0b Vcf0b Vidn0a Vnl0b Vcf0c Scf0g Vzr0a Vc320a Sda0a Gdm0b
-Vcf0e Giox0a Vnc0b Stmp0c Sf00d Sca0a Vnl0a Vtmp0a Sc40960a Vnc0l Vrs160a Pwo00a Giok0b Vtmp0e Vnc0n Snid0a Giob0a Vnc0m Vcf0d Vtmp0k Snc0d Snc0e Sida0a Vcf0i Gioj0a Vcp0a
-Vtmp0f Stf0a Sf00b Vcf0f Vtf0b Vhh0a Vcf0m Giok0a Snon0a Vnc0a Vq250a Syb0b Snc0h Snc0g Giox0b Syb0a Vcf0j PfillDx1b Sc40a Vru0b Sc20480a PfillDx1a Scm0a Vcf0k Vnc0j Shp0a
-Snc0k Vcf0h Vbo0a Sb160b Snc0o Vru0a Vnc0i Gdm0d Shz0a Sf00c Vnc0p Vcf0l Vb160a PDm00a Vtd0b Vrsk0a Snc0f Vnc0c Syb1a Vtmp0d Syb1b Vcf0n Scc0a Vtmp0j Grf0a Vidx0a Vtmp0b Vtmp0i
-Stmp0h Vc10a Vwb0a Grf1a Gdm0a Skb0a PDm01a Std0a Sda0b Sf00a Vi320a Vxd0b Vxd0a PDx1c Vtmp0g Vnc0q Gni0a Snba0a Vnx0a Vnx0b PDx1d Sxd1b PDx1b PDx1a Vo80a Sxd1a Pnb0b Vidx0b
-Glw0b Vtri0a VmA0a Pnb0a Sgood0a Vone0a PKn0b VmB0a Sda0c Scc0b PDm0a Glw0a Shs0a PKn0a Vkp0a Vnx1a Glw0c Snbv0a Snbo0a Vnx1b Pnb1a Pnb1b PKn1b Sad0b Vdm0h Vdm0g Swn0a PKr0a
-Sad0a PKd0d Vdm0f Pc00a PKa0b Vdm0e PKd0b Std0c Sgood1a Snbv1a PKd0a Pfino0a Glw0i PDm1a Shj0a Sad1a Glw0g PKd0c PKa0a Glw0d Sboa0a Pddz0a Sad1b Sby0a PKn1a PKr1a Vlg0a Vlg0b
-PNt0a PKa1b Snl0c Swp0a PKa1a Vkm0a Pn0a Vlg1a Vlg1b Vnu0a Vkv0a Glw0e Vkm1a PNt1a Vka0a Vdm1d Vkt0a Pu00a Vdm1a Vko0a Vnl1a Vnr0a Vkv1a Vyout0a Vdm1c Vka1a Gsendy0a Vdm1b Pn1a
-Glw0f Pddz0b Vnu1a PfillDz0a Nay0a:1 Pwo0a Vni0b Vkt1a Szg0b Pu0a Szg0a PKd1a PKd1c Vdz0a Vdz0c Pcy0a Vdz0b Szg1a Pc0a PZz0a PKd1b Pfin0b Szr0b Ssa20a Vko1a PKd1d Pfiny0a Vdz0d
-Pfin0d Pfin0c Szg1b Vpi0a Pfin0a Pfinc0a Vyout1a Pfin0e Pfinr0a Vnr1a Pwo01a Vnm0a Vfar0a Gsendy1a PfillDz1a Vws0a Gwou0a Pddz1b Pddz1a Pc01a Pu01a Vs4o0a Pu1a Nay1a:1 PZz1a
-Sni1a Vdz1a Vrout0a Gsendr0a Pc1a Szr1a Pcy1a Ssa21a Pwo1a Vkp1a Pfino1a Syb0a:1 Pfin1a Nar0a:1 Pfin1b Vdz1b Pfin1c Vdz1d Slf1a Vpi1a Vdz1c Syb0b:1 Slf0a Pfinc1a Pfin1e Vlw0j
-Vnm1a Glw0h Pfiny1a Pfin1d Pfinr1a PDm01a:1 Vfar1a Vws1a Gwou1a Syb1a:1 PA0a Vxw0a Vs4o1a Vrout1a Gsendr1a Vxw1a Syb1b:1 Vlw1a Vtd0d
-"""
-ROUND = """
-Nay0a Pddz0b' Vkv1a' Pwo0a' Vdm1a' Pcy0a' Sni0a' Vka1a' PZz0a' Vdz0b' Szg1b' PKd1b' Vkt1a' Pfiny0a' Pu00a' Vdz0a' Pc0a' PKd1a' Vdz0d' PKd1c' Pu0a' Pfin0c' Vko1a' Ssa20a' Vdz0c'
-Pfin0b' Szr0a' Szg1a' Pfin0e' Vpi0a' Pfinc0a' Vyout1a' Pfin0a' Pfin0d' Vnm0a' Pfinr0a' Vfar0a' PKd1d' Vnr1a' Gsendy1a' Pc01a' Vkp1a' Vws0a' Pddz1a' Pddz1b' Vs4o0a' Pcy1a'
-PfillDz1a' Pu01a' Vlf0a' Pu1a' Sni1a' Nay1a PZz1a' Slf1a' Vrout0a' Vdz1a' Pc1a' Vdz1c' Gsendr0a' Pwo01a' Pwo1a' Szr1a' Pfino1a' Vdz1d' Ssa21a' Syb0a Pfin1b' Pfiny1a' Vdz1b'
-Pfin1d' Gwou0a' Nar0a Pfinc1a' Vpi1a' Pfin1e' Syb0b Vws1a' Pfin1a' Pfin1c' Vfar1a' Pfinr1a' Vnm1a' Gwou1a' PA0a' Vxw0a' Pwo00a PDm00a Pfino0a Vs4o1a' PDm01a Syb1a Vxw1a'
-Vrout1a' Vlw0a' Syb1b Gsendr1a' Vlw1a' Vtd0a' Vkp0a Vxd0b Slg0b Grf0a Nar1a Vxd0a Slg0a Vnx0b Sad0b Vnx0a PNt0a Sad0a Vxd1b Grf1a Pnb0a PKn0b Slg1a Pnb0b Vxd1a PKn0a PKr0a
-PKa0b Snl0a Sgood0a Snbv0a PKa0a Slg1b Vnx1b Pn0a PDm0a Vnx1a Pc00a Vkv0a Vkm0a Vnu0a Vnr0a Sad1b Vdm0c Pnb1a Vka0a Pnb1b Vdm0b Sad1a PKn1a Vdm0a PNt1a Vkt0a Vgood1a Vdm0d
-Szg0a PKn1b Vko0a Vnbv1a PDm1a Vnl1a PKr1a PKa1a Vyout0a Vdm1b Pn1a Szg0b PKd0d Vdm1c Gsendy0a PKa1b Vnu1a PfillDz0a Vdm1d PKd0a PKd0c PKd0b Pddz0a Vkm1a
-"""
-LAST = """
-Vkm1a:4 Nay0a Sni1a:4 Nay1a Ssa21a:4 Syb0b Gwou0a:4 Nar0a Pfin1e:4 Syb0a Vxw0a:4 PDm01a Pu00a Vs4o1a:4 PDm00a Syb1a Vlw0a:4 Syb1b Vtd0a:4 Vxd0a Slg0b Grf0a Nar1a Vxd0b Slg0a
-Vnx0a Sad0a Vnx0b PNt0a Vkp0a Sad0b Vxd1b Grf1a Pnb0a PKn0a Slg1a PKn0b PKr0a Vxd1a Pnb0b PKa0a Slg1b PKa0b Vgood0a Vnl0a Vnx1b PDm0a Vnx1a Pn0a Sad1b Vdm0a PNt1a Vkm0a Sad1a
-Pnb1b Vnbv0a Vnu0a Vdm0c Pnb1a Vka0a Vkv0a Szg0b PKn1a Vdm0b Vgood1a PKn1b Vnl1a Vkt0a Vdm0d PKd0a PDm1a PKr1a Vkp1a PKa1b Snbv1a Vko0a Szg0a Vnr0a Vdm1c PKa1a Vyout0a Pn1a
-Vdm1a PKd0b PKd0d Pwo00a PKd0c Vkm1a Gsendy0a Pddz0a Vnu1a Pc00a Vdm1b Pddz0b Pcy0a Pu0a Vka1a Szg1b Vnr1a Pwo0a Vkv1a Vdm1d Nay0a! PKd1a PKd1c PKd1b Vkt1a PfillDz0a Vpi0a
-Pfino0a Vws0a Vni0a PZz0a Vko1a Szg1a Vdz0a Gwou0a PKd1d Pddz1a Pfiny0a Pc01a Vyout1a Pfino1a Vdz0c Pc0a Pfin0b Vdz0b Gsendy1a Pddz1b Pcy1a Ssa20a PfillDz1a Vnm0a Pfin0d Vdz0d
-Sni1a Pfiny1a Pfin0c Szr0a Vfar0a Nay1a! Vdz1a Pu01a Pfinc0a Pc1a Vdz1d Yoo00a! Pfin0e Pfin0a Vdz1b Pfinr0a Ssa21a PZz1a Vdz1c Pu1a Vs4o0a Pfin1b Szr1a Pfin1e Vpi1a Pfin1d
-Pfin1c Vrout0a Pfin1a Pfinc1a Vfar1a Vnm1a Pfinr1a Gsendr0a Vlw0a Pwo01a Pwo1a Vs4o1a Yoo11a! Vws1a Sl160b! Nar0a! Vrout1a Gwou1a Vl160a! Sl160c! Gsendr1a Pyz0b! Vlw1a Sl160d!
-Nar1a! Pyz0c! Vl161c! Sl161d! Pyz0a! Pyz0d! Vl161a! Sl161b! Pyz1c! Yoj00a! Pyz1d! Pyz1a! Pyz1b! Yoj11a! Syzf1a! Yoyz1a!
-"""
-
-
-def S(name, a, b, s=1, p0=0, p1=128): return ("s", name, p0, p1, a, b, s)
+def S(name, a, b, s=1): return ("s", name, 0, 128, a, b, s)
 
 
 def PS(tile, a, b, s=1, p0=0, p1=128): return ("p", tile, p0, p1, a, b, s)
@@ -216,13 +91,6 @@ def ND(name, *ix): return ("n", name, 0, 128, ix, None, None)
 
 
 def HBM(name, a=None, b=None): return ("d", name, 0, 128, a, b, 1)
-
-
-def spots(x):
-    out = [0]
-    for n, i in zip(SCRATCH[x[1]][1][1:], x[4]):
-        out = [n * o + j for o in out for j in (range(*i) if isinstance(i, tuple) else (i,))]
-    return out
 
 
 def width(x):
@@ -249,18 +117,19 @@ def places(x):
     k, name, p0, p1, a, b, s = x
     if k == "p": return [("ps " + name, 1)]
     if k == "i": return [(name, ((1 << (b - a)) - 1) << a)] + places(s)
-    if k == "n":
-        if x not in MASKS: MASKS[x] = sum(1 << j for j in spots(x))
-        return [(name, MASKS[x])]
-    if (a, b, s) not in MASKS: MASKS[(a, b, s)] = sum(1 << j for j in range(a, b, s))
-    return [(name, MASKS[(a, b, s)])]
+    if x[1:] not in MASKS:
+        cols = [0] if k == "n" else range(a, b, s)
+        for n, i in zip(SCRATCH[name][1][1:], a) if k == "n" else ():
+            cols = [n * o + j for o in cols for j in (range(*i) if isinstance(i, tuple) else (i,))]
+        MASKS[x[1:]] = sum(1 << j for j in cols)
+    return [(name, MASKS[x[1:]])]
 
 
-def build_ops(par):
-    ops, live = [], {}; V = par["visits"]
+def build_ops():
+    ops, live = [], {}
     cur = [0, 0]; dry = [0]
 
-    def op(eng, size, fn, r, w, nm, sem=None, lat=0.0, after=None, more=()):
+    def op(eng, size, fn, r, w, nm, sem=None, more=()):
         k = len(ops); deps = set(more)
         rd = [y for x in r for y in places(x)]
         wr = [places(x)[0] for x in w if places(x)]
@@ -274,78 +143,72 @@ def build_ops(par):
             live[name] = [(j, m2 & ~m, isw) for j, m2, isw in live.get(name, []) if m2 & ~m] + [(k, m, True)]
         for name, m in rd:
             live.setdefault(name, []).append((k, m, False))
-        deps.discard(k)
-        ps = tuple(sorted({x[1] for x in list(r) + list(w) if isinstance(x, tuple) and x[0] == "p"}))
-        ops.append({"eng": eng, "size": size, "fn": fn, "deps": deps, "ps": ps, "sem": sem, "lat": lat, "after": after, "h": cur[0], "t": cur[1], "nm": nm})
+        ps = [x[1] for x in list(r) + list(w) if isinstance(x, tuple) and x[0] == "p"]
+        ops.append({"eng": eng, "size": size, "fn": fn, "deps": deps - {k}, "ps": ps[0] if ps else None, "sem": sem, "h": cur[0], "t": cur[1], "nm": nm})
         return k
-
-    def two(*xs): return all(x[0] in "sn" and SCRATCH[x[1]][2] in (B, H16, U16) for x in xs)
 
     def rate(out, in0, other):
         if in0[0] == "i": return ("gam", width(in0))
         if out[0] == "i": return ("sca", width(in0))
-        return (other, width(in0))
+        return (other or (.5 if all(x[0] in "sn" and SCRATCH[x[1]][2] in (B, H16, U16) for x in (out, in0)) else 1.0), width(in0))
 
     def ts(out, in0, s1, s2, o0, o1=None, nm=None):
         def fn(g, T, Q):
             if o1 is None: return g.vector.tensor_scalar(ap(T, Q, out), ap(T, Q, in0), ap(T, Q, s1), None, o0)
             return g.vector.tensor_scalar(ap(T, Q, out), ap(T, Q, in0), ap(T, Q, s1), ap(T, Q, s2), o0, o1)
-        return op("V", rate(out, in0, .5 if two(out, in0) else 1.0), fn, [in0, s1, s2], [out], nm or out[1])
+        return op("V", rate(out, in0, 0), fn, [in0, s1, s2], [out], nm or out[1])
 
     def tt(out, in0, in1, o, nm=None):
-        c = 1.0 if "p" in (in0[0], in1[0]) else 2.0
-        return op("V", rate(out, in0, c), lambda g, T, Q: g.vector.tensor_tensor(ap(T, Q, out), ap(T, Q, in0), ap(T, Q, in1), o), [in0, in1], [out], nm or out[1])
+        return op("V", rate(out, in0, 1.0 if "p" in (in0[0], in1[0]) else 2.0), lambda g, T, Q: g.vector.tensor_tensor(ap(T, Q, out), ap(T, Q, in0), ap(T, Q, in1), o), [in0, in1], [out], nm or out[1])
 
-    def cp(out, in_, nm=None, more=()):
-        return op("V", rate(out, in_, .5 if two(out, in_) else 1.0), lambda g, T, Q: g.vector.tensor_copy(ap(T, Q, out), ap(T, Q, in_)), [in_], [out], nm or out[1], more=more)
+    def cp(out, in_, nm=None):
+        return op("V", rate(out, in_, 0), lambda g, T, Q: g.vector.tensor_copy(ap(T, Q, out), ap(T, Q, in_)), [in_], [out], nm or out[1])
 
     def scan(out, d0, d1, o0, o1, first=0.0):
         return op("V", (1.0, width(d0)), lambda g, T, Q: g.vector.tensor_tensor_scan(ap(T, Q, out), ap(T, Q, d0), ap(T, Q, d1), first, o0, o1), [d0, d1], [out], out[1])
 
     def many(e, calls, nm):
         dry[0] += 1; its = [c() for c in calls]; dry[0] -= 1
-        size = ("g", sum(x["size"][1] for x in its)) if e == "G" else (1.0, sum(max(64.0, x["size"][0] * x["size"][1]) for x in its))
-        return op(e, size, lambda g, T, Q: [x["fn"](g, T, Q) for x in its], [y for x in its for y in x["r"]], [y for x in its for y in x["w"]], nm)
+        return op(e, (1.0, 64 * len(its)), lambda g, T, Q: [x["fn"](g, T, Q) for x in its], [y for x in its for y in x["r"]], [y for x in its for y in x["w"]], nm)
 
     def ms(out, val):
-        return op("V", (.5 if two(out) else 1.0, width(out)), lambda g, T, Q: g.vector.memset(ap(T, Q, out), val), [], [out], out[1])
+        return op("V", rate(out, out, 0), lambda g, T, Q: g.vector.memset(ap(T, Q, out), val), [], [out], out[1])
 
-    def act(out, in_, func, bias=0.0, scale=1.0, acc=None, nm=None):
-        def fn(g, T, Q):
-            return g.scalar.activation(ap(T, Q, out), ap(T, Q, in_), func, bias=ap(T, Q, bias), scale=ap(T, Q, scale), accum_out=ap(T, Q, acc) if acc else None)
-        return op("S", rate(out, in_, 1.0), fn, [in_, bias, scale], [out] + ([acc] if acc else []), nm or out[1])
+    def act(out, in_, func, bias=0.0, scale=1.0, nm=None):
+        return op("S", rate(out, in_, 1.0), lambda g, T, Q: g.scalar.activation(ap(T, Q, out), ap(T, Q, in_), func, bias=ap(T, Q, bias), scale=ap(T, Q, scale)), [in_, bias, scale], [out], nm or out[1])
 
-    def mm(items, nm=None, closes=False, behind=(), grp=0):
+    def mm(items, nm=None, closes=False, behind=()):
         def fn(g, T, Q):
             ins = None; first, last = Q("ends")
             for j, it in enumerate(items):
                 ins = g.tensor.matmul(ap(T, Q, it[0]), ap(T, Q, it[1]), ap(T, Q, it[2]), first and j == 0, last and all(x[0][2] != it[0][2] for x in items[j + 1:]))
             return ins
-        cols = sum(max(min(64, width(l)), width(r)) * (4 if SCRATCH[r[1]][2] == F else 1) for o, l, r in items)
         tl = items[0][0][1]; mine = live.setdefault("ps " + tl, [])
-        k = op("P", ("pe", cols), fn, [x for it in items for x in it[1:]], [], nm or "".join(x for x in tl if x.isalpha()), more=[j for j, m, w in mine] if closes else behind)
-        ops[k]["ps"] = (tl,); ops[k]["grp"] = (tl, grp); mine.append((k, 1, True))
+        k = op("P", ("pe", sum(max(min(64, width(l)), width(r)) for o, l, r in items)), fn, [x for it in items for x in it[1:]], [],
+               nm or "".join(x for x in tl if x.isalpha()), more=[j for j, m, w in mine] if closes else behind)
+        ops[k]["ps"] = tl; mine.append((k, 1, True))
         return k
 
-    def steps(n, items):
-        nm = "".join(x for x in items[0][0][1] if x.isalpha())
-        if nm not in par["ahead"]: return mm(items)
-        return mm(items[n:], behind=[mm(items[:n], nm + "0")])
+    def steps(items):
+        return mm(items[1:], behind=[mm(items[:1], "".join(x for x in items[0][0][1] if x.isalpha()) + "0")])
 
-    def either(on_s, on_v, first="S"):
-        one, other = (on_s, on_v) if first == "S" else (on_v, on_s)
+    def either(one, other, nm=None):
         dry[0] += 1; alt = other(); dry[0] -= 1
-        k = one(); ops[k]["deps"] |= alt["deps"]; ops[k]["alt"] = alt
+        k = one(); ops[k]["deps"] |= alt["deps"]; ops[k]["alt"] = alt; ops[k]["nm"] = nm or ops[k]["nm"]
         return k
 
-    def move(out, in_, add=0.0, first="S"):
-        return either(lambda: act(out, in_, ACT.Identity, add), lambda: ts(out, in_, add, None, ALU.add) if add else cp(out, in_), first)
+    def move(out, in_, add=0.0, nm=None):
+        return either(lambda: act(out, in_, ACT.Identity, add), lambda: ts(out, in_, add, None, ALU.add) if add else cp(out, in_), nm)
 
-    def col(j): return S("cf", j, j + 1)
+    def lin(out, in_, scale, bias=0.0, nm=None):
+        return either(lambda: act(out, in_, ACT.Identity, bias, scale), lambda: ts(out, in_, scale, bias, ALU.mult, ALU.add), nm)
 
-    def dma(q, out, in_, sem, lat):
-        def fn(g, T, Q): return (g.sync if q == "Y" else g.scalar).dma_start(ap(T, Q, out), ap(T, Q, in_))
-        return op(q, (0.0, 0), fn, [in_], [out], sem, sem, lat)
+    def const(out, v):
+        if SCRATCH[out[1]][2] == H16: return lin(out, S("one", 0, width(out)), 0.0, v)
+        return either(lambda: act(out, S("one", 0, width(out)), ACT.Identity, v, 0.0), lambda: ms(out, v))
+
+    def dma(q, out, in_, sem):
+        return op(q, (0.0, 0), lambda g, T, Q: (g.sync if q == "Y" else g.scalar).dma_start(ap(T, Q, out), ap(T, Q, in_)), [in_], [out], sem, sem)
 
     def iota(name, n, pat, cm, a=0):
         def fn(g, T, Q):
@@ -353,44 +216,37 @@ def build_ops(par):
             return g.iota(T[name][:, a:a + n], pat, 0, cm, allow_small_or_imprecise_dtypes=True)
         op("G", ("g", 160 + 2 * n), fn, [], [S(name, a, a + n)], name)
 
-    def hand(out, in_):
+    def hand(out, in_, pat=None, cm=0, how=ALU.is_ge, fill=0.0):
         n = width(in_)
-        return op("G", ("g", 205 + 2 * n), lambda g, T, Q: g.affine_select(ap(T, Q, out), ap(T, Q, in_), [[0, n]], ALU.is_ge, 0.0, 0, 0), [in_], [out], out[1])
+        return op("G", ("g", 205 + 2 * n), lambda g, T, Q: g.affine_select(ap(T, Q, out), ap(T, Q, in_), pat or [[0, n]], how, fill, 0, cm), [in_], [out], out[1])
+
+    def col(j): return S("cf", j, j + 1)
 
     def full(name): return S(name, 0, 128)
 
     def cst(name, n=PW): return S(name, 0, n)
 
-    def lin(out, in_, scale, bias=0.0):
-        return either(lambda: act(out, in_, ACT.Identity, bias, scale), lambda: ts(out, in_, scale, bias, ALU.mult, ALU.add))
+    def tmp(j): return S("tmp", 128 * j, 128 * j + 128)
 
-    def const(out, v):
-        return lin(out, S("ioc", 0, width(out)), 0.0, v)
+    def hk(name, k): return S(name, 15 - k, 143 - k)
 
-    dma("Y", S("ji", 0, P), HBM("jur"), "ljur", 2500)
-    dma("S", S("yin", 0, P), HBM("own"), "lown", 2500)
-    dma("S", S("wi", 0, 1), HBM("wgt"), "lwgt", 2500)
+    dma("Y", S("ji", 0, P), HBM("jur"), "ljur")
+    dma("S", S("yin", 0, P), HBM("own"), "lown")
     for h in range(NH):
-        cp(S("rin", h * PW, h * PW + PW), S("ji", h * PW, h * PW + PW), "ru")
-    LW = "lw" if par["conv"] else "li"; CUTS = par["cuts"]
-    for j in range(LCH):
-        a, b = CUTS[j], CUTS[j + 1]
-        if j == par["xat"]: dma("Y", S("xw", 0, W), HBM("xc"), "lx", 5000 + 6000 * a / W)
-        dma("Y", S("li", a, b), HBM("lsr", a, b), "ll%d" % j, (5000 if j >= par["xat"] else 2500) + 6000 * b / W)
-        for x in range(a, b, 512) if par["conv"] else ():
-            either(lambda: hand(S("lw", x, min(b, x + 512)), S("li", x, min(b, x + 512))), lambda: cp(S("lw", x, min(b, x + 512)), S("li", x, min(b, x + 512))), par["conv"])
+        move(S("rin", h * PW, h * PW + PW), S("ji", h * PW, h * PW + PW), nm="ru")
+    dma("Y", S("xw", 0, W), HBM("xc"), "lx")
+    dma("Y", S("li", 0, W), HBM("lsr"), "ll0")
+    dma("Y", S("wi", 0, 1), HBM("wgt"), "lwgt")
 
     first = len(ops)
+    ms(S("one", 0, 144), 1.0)
     iota("ci", 1, [[0, 1]], 1)
     iota("ioc", 144, [[1, 144]], 0)
     iota("iob", 128, [[16, 8], [0, 16]], 0)
     iota("iom", 128, [[0, 8], [1, 16]], 0)
     iota("ioj", PW, [[16, PW // 16], [PW, 16]], 0)
-    iota("iok", 144, [[1, 16], [16, 9]], 0)
-    iota("iok", 144, [[0, 16], [16, 9]], 0, 144)
-    if par["im"]: iota("ni", NH * 272, [[0, NH * 272]], 0)
-    else: iota("dr", NH * 144, [[0, NH * 144]], 0)
-    if not all(par["ns"]): iota("ba", 16 * 144, [[0, 16 * 144]], 0)
+    iota("iok", 144, [[0, 16], [16, 9]], 0)
+    iota("ni", NH * 272, [[0, NH * 272]], 0)
     for j in range(2 * NH):
         iota("dm", 16, [[0, 16]], 0, DMS * j)
     cp(col(0), S("ci", 0, 1))
@@ -400,48 +256,43 @@ def build_ops(par):
     ts(col(3), col(2), 15.0, None, ALU.add)
     ts(col(5), col(1), 37.0 * 32, -2.0 ** 23, ALU.mult, ALU.add)
     ts(col(6), col(1), 1.0, None, ALU.add)
-    act(col(7), col(1), ACT.Sigmoid, 128.0, -256.0)
-    ts(col(8), col(7), 17.0, -1.0, ALU.mult, ALU.add)
+    ts(col(7), col(1), 0.0, None, ALU.is_equal)
+    ts(col(8), col(7), -17.0 / 128, 1.0 / 128, ALU.mult, ALU.add)
     tt(col(9), col(7), col(1), ALU.subtract)
     ts(col(14), col(9), 1.0 / 64, 65.0 / 128, ALU.mult, ALU.add)
     ts(full("idn"), full("ioc"), col(0), None, ALU.is_equal)
-    for nme, sc in (("nid", -1.0), ("q25", .25), ("ida", AN), ("nia", -AN), ("i32", 2.0 if 2 in par["fs"] else 1.0 / 32)):
-        if (nme != "nia" or "T" in "".join(par["zm"])) and (nme != "i32" or any(par["fs"])): lin(full(nme), full("idn"), sc)
+    for nme, sc in (("nid", -1.0), ("q25", -.25), ("ida", AN), ("i32", -2.0)):
+        lin(full(nme), full("idn"), sc)
     for c in range(2):
         iota("iox", 128, [[1, 8], [8 - 16 * c, 2], [16, 8]], -1, 128 * c)
         ts(S("idx", 128 * c, 128 * c + 128), S("iox", 128 * c, 128 * c + 128), -8.0 * c, None, ALU.is_equal)
         const(ND("nl", (32 * c + 1, 32 * c + 32, 2), (0, KK)), 0.0)
-    if any(par["fs"]): const(ND("zr", (0, 18 * NH, 2), (0, KK)), 0.0)
+    const(ND("zr", (0, 18 * NH, 2), (0, KK)), 0.0)
     ts(S("hh", 0, 144), S("ioc", 0, 144), col(3), None, ALU.is_equal)
-    for nme, sc in (("hz", -1.0 / 32), ("hy", 1.0 / 32), ("hp", PEN * 89 / 2048), ("hs", 16.0 * PW)):
-        if (nme != "hy" or 0 in par["fs"]) and (nme != "hz" or par["fs"] != (1, 1)): lin(S(nme, 0, 144), S("hh", 0, 144), sc)
+    for nme, sc in (("hz", 1.0 / 32), ("hp", PEN * 89 / 2048), ("hs", 32.0 * PW)):
+        lin(S(nme, 0, 144), S("hh", 0, 144), sc)
     ts(full("bo"), full("iob"), col(2), None, ALU.is_equal)
-    if 2 in par["fs"]: lin(cst("o8", 8), S("bo", 0, 128, 16), 1.0 / 64)
-    for c in range(2) if par["im"] else (): lin(S("b16", 8 * c, 8 * c + 8), S("bo", 0, 128, 16), 1.0)
-    for nme, sc in (("nbo", -1.0), ("boa", AN), ("nba", -AN), ("by", -AN / 32)):
+    lin(cst("o8", 8), S("bo", 0, 128, 16), 1.0 / 64)
+    for c in range(2):
+        lin(S("b16", 8 * c, 8 * c + 8), S("bo", 0, 128, 16), 1.0)
+    for nme, sc in (("nbo", -1.0), ("boa", AN), ("nba", -AN), ("by", AN / 32)):
         lin(full(nme), full("bo"), sc)
-
-    def tmp(j): return S("tmp", 128 * j, 128 * j + 128)
     for j, (nme, off, dg) in enumerate((("mA", 1.0 / 64, -39.0 / 64), ("mB", -1.0 / 64, 89.0 / 128))):
-        lin(tmp(j), full("idn"), dg / off, 1.0)
-        lin(tmp(2 + j), full("bo"), off)
-        tt(full(nme), tmp(j), tmp(2 + j), ALU.mult)
-    ts(tmp(4), full("iom"), col(1), -1.0, ALU.is_gt, ALU.mult)
-    tt(tmp(5), tmp(4), full("idn"), ALU.add)
-    ts(S("tmp", 640, 768, 16), S("ioc", 0, 8), 0.0, col(8), ALU.mult, ALU.add)
-    lin(tmp(6), full("bo"), -1.0 / 64)
-    tt(full("tri"), tmp(5), tmp(6), ALU.mult)
+        lin(tmp(j), full("bo"), off)
+        hand(full(nme), tmp(j), [[1, 128]], -1, ALU.not_equal, off + dg)
+    lin(full("th"), full("bo"), 1.0 / 128)
+    hand(tmp(2), full("th"), [[1, 128]], -1, ALU.is_gt)
+    hand(full("tri"), tmp(2), [[1, 128]], -1, ALU.not_equal, -1.0 / 128)
+    lin(S("tri", 0, 128, 16), S("bo", 0, 128, 16), col(8))
     for k in range(16):
         lin(S("nc", 143 * k, 143 * k + 128), full("idn"), 32.0)
-    ts(S("tmp", 1024, 1168), S("iok", 0, 144), col(0), 32.0, ALU.is_equal, ALU.mult)
-    ts(S("tmp", 1168, 1312), S("iok", 144, 288), col(2), None, ALU.is_equal)
-    tt(S("nc", 0, 16 * 144, 16), S("tmp", 1024, 1168), S("tmp", 1168, 1312), ALU.add)
-    lin(S("kb", 0, PW), S("ioj", 0, PW), 1.0, col(1))
-    lin(cst("cm"), cst("iom"), 0.0, col(14))
-    for nme, v, n in (("c1", M1, PW), ("c32", M32, P), ("c4096", M4096, PW), ("c155", 15.5, P), ("c2048", 2048.0, PW),
-                      ("cp", M1 * PEN, PW), ("c4", 4 * M1, 4), ("one", 1.0, 128), ("non", -1.0, 128)):
+    ts(S("tmp", 640, 784), S("iok", 0, 144), col(2), None, ALU.is_equal)
+    hand(S("nc", 0, 16 * 144, 16), S("tmp", 640, 784), [[1, 16], [16, 9]], -1, ALU.not_equal, 33.0)
+    ts(S("kb", 0, PW), S("ioj", 0, PW), 16.0, col(1), ALU.add, ALU.add)
+    lin(cst("cm"), cst("one"), 0.0, col(14))
+    for nme, v, n in (("c1", M1, PW), ("c32", M32, P), ("c4096", M4096, PW), ("c155", 15.5, P), ("c2048", 2048.0, PW), ("cp", M1 * PEN, PW), ("c4", 4 * M1, 4), ("non", -1.0, 128)):
         const(cst(nme, n), v)
-    for j, v in enumerate((0.0, 1.0, 39.0 / 64, 39.0 / 128)):
+    for j, v in enumerate((0.0, -1.0, -39.0 / 64, 39.0 / 128)):
         const(S("f0", j, 4 * PW, 4), v)
     ts(col(17), col(1), 1.0, -0.5, ALU.is_equal, ALU.mult)
     ts(col(22), col(7), 2048.0, col(17), ALU.mult, ALU.add)
@@ -455,22 +306,22 @@ def build_ops(par):
         const(S("da", a, b), w)
     ts(cst("rsk"), cst("iom"), 0.0, 4 * PEN, ALU.is_equal, ALU.mult)
     ts(full("rs16"), full("iom"), 0.0, -BIG, ALU.is_equal, ALU.mult)
-    ts(tmp(7), full("iom"), col(1), 32768.0, ALU.not_equal, ALU.mult)
-    lin(S("tf", 0, 128), full("ioc"), 32.0)
-    tt(S("tf", 128, 256), S("tf", 0, 128), tmp(7), ALU.subtract)
-    ts(full("wb"), S("tf", 128, 256), -16384.0, None, ALU.max)
-    if not all(par["ns"]): ts(S("ba", 15, 16 * 144, 16), S("iok", 0, 144), col(0), None, ALU.is_equal)
+    ts(tmp(3), full("iom"), col(1), -16384.0, ALU.not_equal, ALU.mult)
+    lin(tmp(4), full("ioc"), 32.0)
+    mm([(PS("wb", 0, P), full("idn"), tmp(j)) for j in (3, 4)])
+    move(full("wb"), PS("wb", 0, P))
     lin(S("hj", 0, 144), S("hh", 0, 144), col(6))
     ts(col(11), S("wi", 0, 1), 2048.0, -4096.0, ALU.is_ge, ALU.mult)
     tt(col(12), col(11), S("wi", 0, 1), ALU.add)
-    for p, n, j in (("wp", "wn", 12),):
-        lin(full(p), full("bo"), col(j))
-        lin(full(n), full("nbo"), col(j))
-
+    ts(col(15), col(1), 1.0 / 128, col(14), ALU.mult, ALU.add)
+    lin(cst("cn"), cst("one"), -1.0 / 128, col(15))
+    lin(full("wp"), full("bo"), col(12))
+    lin(full("wn"), full("nbo"), col(12))
     for o in ops[first:]: o["const"] = True
     IDN, NID = full("idn"), full("nid")
 
-    def hk(name, k): return S(name, 15 - k, 143 - k)
+    def modulo(out, Y, big):
+        return [(out, full("wn"), Y), (out, NID, big), (out, IDN, big), (out, full("wp"), Y)]
 
     sends = {}
     for t in range(V):
@@ -478,7 +329,7 @@ def build_ops(par):
         for h in range(NH):
             cur[0] = h
             v = "%d_%d" % (t, h)
-            o = a * P + h * PW; ob = a * 2048 + h * 16 * PW; oi = t * P + h * PW; o3 = a * NH + h; n16 = 16 * PW
+            o = a * P + h * PW; ob = a * 2048 + h * 16 * PW; oi = t * P + h * PW; o3 = a * NH + h; n16 = 16 * PW; on = 2 * o
 
             def sm(name): return S(name, o, o + PW)
 
@@ -488,382 +339,192 @@ def build_ops(par):
 
             def s4(j, s=4): return S("s4", (4 * PW + 4) * o3 + j, (4 * PW + 4) * o3 + j + 4 * PW, s)
 
+            def half(name, j): return S(name, ob + 512 * j, ob + 512 * j + 512)
+
+            def picks(win, offs, at, j): return IND(win, 0, W, S(offs, at + PW // 2 * j, at + PW // 2 * (j + 1)))
+
+            def juror(name, k, s=16): return S(name, ob + k, ob + n16, s)
+
+            def km(k0, k1): return S("dm", DMS * o3 + 16 + PW * k0, DMS * o3 + 16 + PW * k1)
+
             RU, YIN, YN = S("rin", oi, oi + PW), S("yin", oi, oi + PW), S("yout", oi, oi + PW)
             if t:
-                op("N", (0.0, 0), None, [], [RU], "ar", "ar" + v, -1.0, sends["r%d_%d" % (t - 1, h)])
-                op("N", (0.0, 0), None, [], [YIN], "ay", "ay" + v, -1.0, sends["y%d_%d" % (t - 1, h)])
-
-            def gather(name, win, offs, at):
-                who = par[name][h]; pw = PW // len(who); add = -2048.0 if name == "lg" else 0.0
-                for j, e in enumerate(who):
-                    out = S(name, ob + 16 * pw * j, ob + 16 * pw * (j + 1))
-                    src = IND(win, 0, W, S(offs, at + pw * j, at + pw * (j + 1)))
-                    if name == "xd": tt(out, src, S("yb", ob + 16 * pw * j, ob + 16 * pw * (j + 1)), ALU.subtract)
-                    elif name == "zg": either(lambda: act(out, src, ACT.Identity, 0.0, AN), lambda: ts(out, src, AN, None, ALU.mult), e)
-                    elif win == "li": ts(out, src, add, None, ALU.add)
-                    else: move(out, src, add, e)
-
-            def km(name, k0, k1):
-                at = DMS * o3 + 16 if name == "dm" else ob
-                return S(name, at + PW * k0, at + PW * k1)
-
-            def against(its, out, tl, o):
-                z = PS(tl, 0, PW)
-                op("V", (1.0, PW * len(its)), lambda g, T, Q: [g.vector.tensor_tensor(ap(T, Q, x), ap(T, Q, y), ap(T, Q, z), o) for x, y in its],
-                   [y for x, y in its] + [z], [out], out[1])
-
-            def near(out, d): ts(out, d, M4, M4, ALU.add, ALU.is_equal)
-
-            def test(out, ab, d, way):
-                if way == 0: return near(out, d)
-                act(ab, d, ACT.Abs)
-                either(lambda: act(out, ab, ACT.Sigmoid, 384.0, -256.0), lambda: ts(out, ab, 1.0, None, ALU.is_le), "V" if way == 1 else "S")
-
-            Y2 = S("y2", 2 * o, 2 * o + 2 * PW)
-            via = not t and par["via"][h]
-            who = "" if via else par["yb"][h]; bn = 8 // max(1, len(who))
-            def twice(name, Y):
-                outs = [S(name, 2 * o + c, 2 * o + 2 * PW, 2) for c in range(2)]
-                either(lambda: many("S", [lambda x=x: act(x, Y, ACT.Identity) for x in outs], name), lambda: many("V", [lambda x=x: cp(x, Y) for x in outs], name))
-            if "E" in who or "H" in who: twice("y2", YIN)
-            for j, e in enumerate(who):
-                cs = range(bn * j, bn * j + bn); outs = [S("yb", ob + k, ob + n16, 16) for c in cs for k in (c, c + 8)]
-
-                def on_s(): return many("S", [lambda x=x: act(x, YIN, ACT.Identity) for x in outs], "yb")
-                if e == "S": on_s()
-                elif e == "G": many("G", [lambda x=x: hand(x, YIN) for x in outs], "yb")
-                elif e == "H": either(on_s, lambda: many("G", [lambda c=c: hand(S("yb", ob + c, ob + n16, 8), Y2) for c in cs], "yb"), "G")
-                else: either(on_s, lambda: many("V", [lambda c=c: cp(S("yb", ob + c, ob + n16, 8), Y2) for c in cs], "yb"))
+                op("N", (0.0, 0), None, [], [RU], "ar", "ar" + v, [sends["r%d_%d" % (t - 1, h)]])
+                op("N", (0.0, 0), None, [], [YIN], "ay", "ay" + v, [sends["y%d_%d" % (t - 1, h)]])
+            via = not t and h
             if via:
                 for j in range(2):
-                    move(S("yb", ob + 512 * j, ob + 512 * j + 512), IND("xw", 0, W, S("rin", oi + PW // 2 * j, oi + PW // 2 * (j + 1))))
-                for c in range(NC):
+                    move(half("yb", j), picks("xw", "rin", oi, j))
+                for c in range(2):
                     tl = "Dx%s_%d" % (v, c)
                     k = mm([(PS(tl, j, 512, KK), NID, YIN) for j in range(KK)], "fillDx")
                     for j in range(2):
-                        mm([(PS(tl, 256 * j, 256 * j + 256), IDN, S("yb", ob + 512 * j + c, ob + 512 * j + 512, NC))], behind=[k])
-                    move(S("xd", ob + c, ob + n16, NC), PS(tl, 0, 512))
-            else: gather("xd", "xw", "rin", oi)
-            ops[either(lambda: hand(s4(3), RU), lambda: cp(s4(3), RU), "V")]["nm"] = "rf"
-            ts(s4(5), RU, 32.0, col(5), ALU.mult, ALU.add, "kp")
-            for name in ("ad", "nx"):
-                pw = PW // len(par[name][h])
-                for i0, e in zip(range(0, PW, pw), par[name][h]):
-                    out, d = cube(name, i0=i0, i1=i0 + pw), S("xd", ob + 16 * i0, ob + 16 * (i0 + pw))
-                    if name == "ad": act(out, d, ACT.Abs)
-                    elif e == "V": near(out, d)
-                    else: act(out, cube("ad", i0=i0, i1=i0 + pw), ACT.Sigmoid, 384.0, -256.0)
-            gather("lg", LW if t or par["first"][h] == "S" else "li", "rin", oi)
-            tl = "n" + v
-            if par["ns"][h]:
-                mm([(PS("Nt" + v, j, 2 * PW, KK), S("lg", ob + j, ob + n16, KK), S("idx", 16 * ((j + t) % 16), 16 * ((j + t) % 16) + 16)) for j in range(KK)])
-                move(ND("nl", (32 * h, 32 * h + 32, 2), (0, KK)), PS("Nt" + v, 0, 2 * PW))
-                mm([(PS(tl, 0, PW), IDN, cst("c2048"))] + [(PS(tl, 0, PW), ND("nl", (32 * h + 15 * c, 32 * h + 15 * c + 16), (0, KK)), S("idn", c, 128, 2)) for c in range(2)])
-            for k0 in (0, KK) if not par["ns"][h] else ():
-                mm([(PS(tl, 0, PW), S("ba", 144 * ((k + t) % 16) + 15 - k, 144 * ((k + t) % 16) + 143 - k), S("lg", ob + k, ob + n16, 16)) for k in range(k0, k0 + KK)]
-                   + ([] if k0 else [(PS(tl, 0, PW), IDN, cst("c2048"))]))
-            cp(sm("nu"), PS(tl, 0, PW))
-            tt(s4(2), PS(tl, 0, PW), s4(3), ALU.subtract, "nr")
-            gather("zg", "xw", "nu", o)
-            tl = "nb" + v; out = PS(tl, 0, PW); pn = par["pn"]
-            for k0 in range(0, 16, pn):
-                mm([(out, S("nc", 143 * k, 143 * k + 128), cube("nx", k=k)) for k in range(k0, k0 + pn)])
-            either(lambda: act(sm("good"), out, ACT.Sigmoid, -248.0 * 16, 16.0), lambda: ts(sm("good"), out, 248.0, None, ALU.is_ge))
-            move(sm("nbr" if par["re"] else "nbv"), out, 4088.0 if par["re"] else -8.0)
-            reads = [j for j, m, w in live["ps " + tl]]
-            tl = "Dm" + v; dn = par["dn"]
-            steps(1, [(PS(tl, 0, PW), lhs, rhs) for lhs, rhs in ((IDN, cst("cm")), (full("tri"), sm("good")), (IDN, cst("c1")), (NID, cst("c1")))])
-            for k0 in range(0, 16, dn):
-                against([(km("dm", k, k + 1), S("xd", ob + k, ob + n16, 16)) for k in range(k0, k0 + dn)], km("dm", k0, k0 + dn), tl, ALU.mult)
-            tl = "K" + v; out = PS(tl, 0, PW)
-            ks = [mm([(out, hk("hp", r), cube("nx", r=r)) for r in range(r0, r0 + pn)], "Kn") for r0 in range(0, 16, pn)]
+                        mm([(PS(tl, 256 * j, 256 * j + 256), IDN, S("yb", ob + 512 * j + c, ob + 512 * j + 512, 2))], behind=[k])
+                    act(cube("ad", k=(c, 16, 2)), PS(tl, 0, 512), ACT.Abs)
+            else:
+                for j in range(2):
+                    many("S", [lambda k=k: act(juror("yb", k), YIN, ACT.Identity) for c in range(4 * j, 4 * j + 4) for k in (c, c + 8)], "yb")
+                for j in range(2):
+                    tt(half("xd", j), picks("xw", "rin", oi, j), half("yb", j), ALU.subtract)
+            either(lambda: cp(s4(3), RU), lambda: hand(s4(3), RU), "rf")
+            lin(s4(5), s4(3), 32.0, col(5), "kp")
+            for c in range(2):
+                if via: ts(cube("nx", k=(c, 16, 2)), cube("ad", k=(c, 16, 2)), 1.0, None, ALU.is_le)
+                else: act(cube("ad", i0=32 * c, i1=32 * c + 32), half("xd", c), ACT.Abs)
+            for c in range(2) if not via else ():
+                ts(cube("nx", i0=32 * c, i1=32 * c + 32), half("xd", c), M4, M4, ALU.add, ALU.is_equal)
+            for j in range(2):
+                move(half("lg", j), picks("li", "rin", oi, j), -2048.0)
+            mm([(PS("Nt" + v, j, 2 * PW, KK), juror("lg", j, KK), S("idx", 16 * ((j + t) % 16), 16 * ((j + t) % 16) + 16)) for j in range(KK)])
+            move(ND("nl", (32 * h, 32 * h + 32, 2), (0, KK)), PS("Nt" + v, 0, 2 * PW))
+            out = PS("n" + v, 0, PW)
+            mm([(out, IDN, cst("c2048"))] + [(out, ND("nl", (32 * h + 15 * c, 32 * h + 15 * c + 16), (0, KK)), S("idn", c, 128, 2)) for c in range(2)])
+            move(sm("nu"), out)
+            tt(s4(2), out, s4(3), ALU.subtract, "nr")
+            for j in range(2):
+                either(lambda: act(half("zg", j), picks("xw", "nu", o, j), ACT.Identity, 0.0, AN), lambda: ts(half("zg", j), picks("xw", "nu", o, j), AN, None, ALU.mult))
+            out = PS("nb" + v, 0, PW)
+            for c in range(2):
+                mm([(out, S("nc", 143 * k, 143 * k + 128), cube("nx", k=k)) for k in (range(c, 16, 2) if via else range(KK * c, KK * c + KK))])
+            if h: ts(sm("good"), out, 248.0, 2.0, ALU.is_ge, ALU.mult)
+            else: act(sm("good"), out, ACT.Sign, -247.5)
+            move(sm("nbv"), out, -8.0)
+            out = PS("Dm" + v, 0, PW)
+            steps([(out, lhs, rhs) for lhs, rhs in ((IDN, cst("cm" if h else "cn")), (full("tri"), sm("good")), (IDN, cst("c1")), (NID, cst("c1")))])
+            if via: move(sm("mk"), out)
+            for q in range(4):
+                if via: many("V", [lambda j=j: tt(km(2 * j + q // 2, 2 * j + q // 2 + 1), PS("Dx%s_%d" % (v, q // 2), j, 512, KK), sm("mk"), ALU.mult) for j in range(q % 2 * 4, q % 2 * 4 + 4)], "dm")
+                else: many("V", [lambda k=k: tt(km(k, k + 1), juror("xd", k), out, ALU.mult) for k in range(4 * q, 4 * q + 4)], "dm")
+            out = PS("K" + v, 0, PW)
+            ks = [mm([(out, hk("hp", r), cube("nx", r=r)) for r in range(r0, r0 + KK)], "Kn") for r0 in (0, KK)]
             k = mm([(out, IDN, cst("cp")), (out, NID, cst("cp")), (out, IDN, cst("kb"))], "Kr", behind=ks)
-            for r0 in range(0, 16, pn):
-                mm([(out, hk("hs", r), cube("ad", r=r)) for r in range(r0, r0 + pn)], "Ka", behind=[k])
-            KM, KV = S("km", o + 15, o + PW, 16), S("kv", o + 15, o + PW, 16)
+            for r0 in (0, KK):
+                mm([(out, hk("hs", r), cube("ad", r=r)) for r in range(r0, r0 + KK)], "Ka", behind=[k])
+            KV = S("kv", o + 15, o + PW, 16)
             scan(sm("km"), cst("rsk"), out, ALU.add, ALU.min)
             scan(sm("kv"), S("td", 128 * a + PW, 128 * a + 2 * PW), out, ALU.max, ALU.subtract)
-            ts(four("ka"), KM, 16 * PW - 1, None, ALU.bitwise_and)
-            if par["perq"]:
-                many("V", [lambda q=q: ts(S("ko", 8 * o3 + q, 8 * o3 + q + 1), S("ka", 8 * o3 + q, 8 * o3 + q + 1), S("kv", o + 16 * q + 15, o + 16 * q + 16), 16.0, ALU.min, ALU.add)
-                           for q in range(PW // 16)], "ko")
-            else:
-                tt(four("kt"), four("ka"), KV, ALU.min)
-                ts(four("ko"), four("kt"), 16.0, None, ALU.add)
-            kyn = tt(YN, IND("dm", DMS * o3, DMS * o3 + 16 + n16, four("ko")), YIN, ALU.add)
+            ts(four("ka"), S("km", o + 15, o + PW, 16), 32 * PW - 1, None, ALU.bitwise_and)
+            tt(four("kt"), four("ka"), KV, ALU.min)
+            move(four("ko"), four("kt"))
+            tt(YN, IND("dm", DMS * o3, DMS * o3 + 16 + n16, four("ko")), YIN, ALU.add)
             if t < V - 1: either(lambda: act(four("lf"), KV, ACT.Sign), lambda: ts(four("lf"), KV, 0.0, 2.0, ALU.is_gt, ALU.mult))
-            tl = "Kd" + v; od = 144 * h + 8
-            def kd(k0, **kw): return mm([(PS(tl, j, 2 * PW, 8), km("dm", 2 * j, 2 * j + 2), cst("b16", 16)) for j in range(k0 // 2, (k0 + dn) // 2)], "Kd", **kw)
-            if par["im"]:
-                ks = [kd(k0) for k0 in range(0, 16, dn)]
-                for Y, b in ((YIN, "bo"), (YN, "nbo")):
-                    mm([(PS(tl, PW, 2 * PW, 1, PW * c, PW * c + PW), Y, S(b, 0, 128, 2)) for c in range(2)], "ddz", behind=ks)
-                lin(S("ni", 272 * h + 8, 272 * h + 264, 2), PS(tl, 0, 2 * PW), AN, 1.0)
-            else:
-                for k0 in range(0, 16, dn):
-                    mm([(PS(tl, j, PW, 8), km("dm", 2 * j, 2 * j + 2), S("bo", 0, 128, 16)) for j in range(k0 // 2, (k0 + dn) // 2)], "Kd")
-                move(S("dr", od, od + 128, 2), PS(tl, 0, PW))
+            tl = "Kd" + v; at = 272 * h + 8
+            ks = [mm([(PS(tl, j, 2 * PW, 8), km(2 * j, 2 * j + 2), cst("b16", 16)) for j in (j0, j0 + 1)]) for j0 in range(0, KK, 2)]
+            for Y, b in ((YIN, "bo"), (YN, "nbo")):
+                mm([(PS(tl, PW, 2 * PW, 1, PW * c, PW * c + PW), Y, S(b, 0, 128, 2)) for c in range(2)], "ddz", behind=ks)
+            lin(S("ni", at, at + 256, 2), PS(tl, 0, 2 * PW), AN, 1.0)
 
             def send(kind, src, dst):
                 def fn(g, T, Q, t=t, h=h):
                     return g.remote_dma(ap(T, Q, dst), ap(T, Q, src), T.sem["a%s%d_%d" % (kind, t + 1, h)], T.sem.sent, Q("pid"), Q("rid"), Q("mask"))
                 sends["%s%d_%d" % (kind, t, h)] = op("G", ("rem", 1), fn, [src], [], "send" + kind, "remote")
             send("y", YN, S("yin", oi + P, oi + P + PW))
-            tl = "dd" + v
-
-            def xr(a0):
-                return [(PS(tl, a0, a0 + PW), S("dr", od - c, od - c + 128), S("idn", PW * c, PW * c + PW)) for c in range(NC)]
-            on = 2 * o
-            if not par["im"]:
-                mm(xr(0) + xr(PW))
-                mm([(PS(tl, PW, 2 * PW), full("bo"), YIN), (PS(tl, PW, 2 * PW), full("nbo"), YN)], "ddz")
-                lin(S("nn", on, on + 2 * PW), PS(tl, 0, 2 * PW), AN, 1.0)
-            tl = ("nb" if par["re"] else "c2") + v; out = PS(tl, 0, PW)
-            if par["re"]: k = mm([(out, NID, sm("nbr"))], "c0", behind=reads, grp=1)
-            else: k = mm([(out, NID, sm("nbv")), (out, IDN, cst("c32")), (out, NID, cst("c32")), (out, IDN, sm("nbv"))], "c0")
-            mm([(out, full("nba"), YIN), (out, full("boa"), YN)], "cy", behind=[k], grp=par["re"])
-            if par["im"]: mm([(out, S("ni", 272 * h + 8 + 128 * s - c, 272 * h + 136 + 128 * s - c), S(b, PW * c, PW * c + PW)) for s, b in enumerate(("nid", "idn")) for c in range(2)], "c", behind=[k], grp=par["re"])
-            else: mm([(out, NID, S("nn", on, on + PW)), (out, IDN, S("nn", on + PW, on + 2 * PW))], "c", behind=[k], grp=par["re"])
-            act(sm("sa2"), out, ACT.Sign, 4096 - 11.5 if par["re"] else -3.5)
-
-            def modulo(out, neg, pos, Y, big):
-                return [(out, neg, Y), (out, NID, big), (out, IDN, big), (out, pos, Y)]
+            out = PS("c2" + v, 0, PW)
+            k = mm([(out, NID, sm("nbv")), (out, IDN, cst("c32")), (out, NID, cst("c32")), (out, IDN, sm("nbv"))], "c0")
+            mm([(out, full("nba"), YIN), (out, full("boa"), YN)], "cy", behind=[k])
+            mm([(out, S("ni", at + 128 * s - c, at + 128 * s + 128 - c), S(b, PW * c, PW * c + PW)) for s, b in enumerate(("nid", "idn")) for c in range(2)], behind=[k])
+            act(sm("sa2"), out, ACT.Sign, -3.5)
             tl = "u" + v
-            steps(1, [(PS(tl, 0, 2 * PW), full("bo"), full("cc"))] + modulo(PS(tl, 1, 2 * PW, 2), full("wn"), full("wp"), YN, cst("c4096")))
+            steps([(PS(tl, 0, 2 * PW), full("bo"), full("cc"))] + modulo(PS(tl, 1, 2 * PW, 2), YN, cst("c4096")))
             scan(S("pi", on, on + 2 * PW), PS(tl, 0, 2 * PW), s4(3, 2), ALU.mult, ALU.add)
-            ts(s4(0), S("pi", on + 1, on + 2 * PW, 2), 5, W - 1, ALU.arith_shift_right, ALU.bitwise_and, "far")
-            ts(s4(1), sm("nu"), -1.0, None, ALU.mult, nm="nm")
-            zm = par["zm"][h]; zn = KK // len(zm)
-            if "V" in zm: mm([(PS("Dz" + v, 0, PW), IDN, cst("non")), (PS("Dz" + v, 0, PW), full("ida"), YN)], "fillDz")
+            ts(sm("pj"), S("pi", on + 1, on + 2 * PW, 2), 5, W - 1, ALU.arith_shift_right, ALU.bitwise_and, "far")
+            move(s4(0), sm("pj"), nm="fa")
+            move(s4(1), sm("nu"), nm="nm")
+            out = PS("Dz" + v, 0, PW)
+            mm([(out, IDN, cst("non")), (out, full("ida"), YN)], "fillDz")
 
-            def pair(j, c=0, s=1, n=1): return S("dz", ob + 2 * PW * j + c, ob + 2 * PW * (j + n), s)
-            for j0, e in zip(range(0, KK, zn), zm):
-                tl = "Dz%s_%d" % (v, j0); js = range(j0, j0 + zn)
-                if e == "V": against([(pair(j, c, 2), S("zg", ob + j + KK * c, ob + n16, 16)) for j in js for c in range(2)], pair(j0, n=zn), "Dz" + v, ALU.subtract)
-                else:
-                    mm([(PS(tl, P * (j - j0), P * (j - j0 + 1)), IDN, S("zg", ob + j, ob + n16, KK)) for j in js])
-                    mm([(PS(tl, P * (j - j0) + c, P * (j - j0 + 1), 2), full("nia"), YN) for j in js for c in range(2)], "subDz")
-                    move(pair(j0, n=zn), PS(tl, 0, P * zn), 1.0)
-            if par["fs"][h] == 2:
-                mm([(PS("Zt" + v, j, PW, KK), S("zg", ob + j, ob + n16, KK), cst("o8", 8)) for j in range(KK)], "Zz")
-                move(ND("zr", (18 * h + 1, 18 * h + 17, 2), (0, KK)), PS("Zt" + v, 0, PW))
-            if par["fs"][h] == 1:
-                tl = "Zt" + v; twice("yd", YN)
-                k = mm([(PS(tl, j, PW, KK), S("zg", ob + j, ob + n16, KK), S("bo", 0, 128, 16)) for j in range(KK)], "Zz")
-                mm([(PS(tl, 0, PW), S("yd", 2 * o, 2 * o + 2 * PW), S("nba", 0, 128, 2))], "Zy", behind=[k])
-                for j0 in range(0, KK, zn):
-                    mm([(PS(tl, j, PW, KK), pair(j), S("nbo", 0, 128, 16)) for j in range(j0, j0 + zn)], "Zd", behind=[k])
-                move(ND("zr", (18 * h + 1, 18 * h + 17, 2), (0, KK)), PS(tl, 0, PW))
+            def pair(j, c): return S("dz", ob + P * j + c, ob + P * j + P, 2)
+            for j0 in range(0, KK, 2):
+                many("V", [lambda j=j, c=c: tt(pair(j, c), juror("zg", j + KK * c), out, ALU.subtract) for j in (j0, j0 + 1) for c in range(2)], "dz")
+            mm([(PS("Zt" + v, j, PW, KK), juror("zg", j, KK), cst("o8", 8)) for j in range(KK)], "Zz")
+            move(ND("zr", (18 * h + 1, 18 * h + 17, 2), (0, KK)), PS("Zt" + v, 0, PW))
             tl = "fin" + v
             TF, CH = PS(tl, 2, 4 * PW, 4), PS(tl, 3, 4 * PW, 4)
-            k = mm([(PS(tl, 0, 4 * PW), IDN, S("f0", 0, 4 * PW))], "fino", behind=[] if "fin" in par["ahead"] else [kyn])
+            k = mm([(PS(tl, 0, 4 * PW), IDN, S("f0", 0, 4 * PW))], "fino")
             mm([(CH, full("mB"), sm("sa2")), (CH, IDN, cst("c1")), (CH, full("mA"), sm("sa2")), (CH, NID, cst("c1")), (TF, full("q25"), sm("sa2"))], "finc", behind=[k])
-            if par["fs"][h]:
-                mm([(TF, ND("zr", (18 * h + 1 - c, 18 * h + 17 - c), (0, KK)), S("i32", c, 128, 2)) for c in range(2)], behind=[k])
-            if par["fs"][h] != 1:
-                for k0 in range(0, 16, pn) if not par["fs"][h] else ():
-                    mm([(TF, hk("hy", j), S("zg", ob + j, ob + n16, 16)) for j in range(k0, k0 + pn)], "finz", behind=[k])
-                mm([(TF, full("by"), YN)], "finy", behind=[k])
-                for j0 in range(0, KK, zn):
-                    mm([(TF, hk("hz", j + KK * c), pair(j, c, 2)) for j in range(j0, j0 + zn) for c in range(2)], behind=[k])
+            mm([(TF, ND("zr", (18 * h + 1 - c, 18 * h + 17 - c), (0, KK)), S("i32", c, 128, 2)) for c in range(2)], behind=[k])
+            mm([(TF, full("by"), YN)], "finy", behind=[k])
+            for j0 in range(0, KK, 2):
+                mm([(TF, hk("hz", j + KK * c), pair(j, c)) for j in (j0, j0 + 1) for c in range(2)], behind=[k])
             mm([(TF, IDN, cst("c1")), (TF, NID, cst("c1"))], "finr", True)
             scan(S("s4o", 4 * o, 4 * o + 4 * PW), PS(tl, 0, 4 * PW), s4(0, 1), ALU.mult, ALU.add)
             RN = S("rout", oi, oi + PW) if t < V - 1 else S("rlast", h * PW, h * PW + PW)
-            cp(RN, S("s4o", 4 * o + 3, 4 * o + 4 * PW, 4), "rout")
+            move(RN, S("s4o", 4 * o + 3, 4 * o + 4 * PW, 4), nm="rout")
             send("r", RN, S("rin", oi + P, oi + P + PW) if t < V - 1 else S("rfin", h * PW, h * PW + PW))
-        hs = range(NH); cur[0] = 0
+        cur[0] = 0
         if t < V - 1:
-            tl = "A%d" % t; out = PS(tl, 0, 4); lfs = [S("lf", 8 * (a * NH + h), 8 * (a * NH + h) + 4) for h in hs]
+            tl = "A%d" % t; out = PS(tl, 0, 4); lfs = [S("lf", 8 * (a * NH + h), 8 * (a * NH + h) + 4) for h in range(NH)]
             mm([(PS(tl, 0, 8), IDN, cst("ca", 8))] + [(out, full("one"), x) for x in lfs] + [(out, IDN, cst("c4", 4)), (out, NID, cst("c4", 4))]
                + [(out, full("non"), x) for x in lfs] + [(out, IDN, cst("one", 4))])
             scan(S("td", 128 * (1 - a), 128 * (1 - a) + 128, 16), PS(tl, 0, 8), cst("da", 8), ALU.mult, ALU.add, 1.0)
-        for i0, n in [(h * PW, PW) for h in hs] if t == V - 1 or not par["whole"] else [(0, P)]:
-            cur[0] = (i0 + n - 1) // PW
-            tl = "wo%d_%d" % (t, i0); Y = S("yout", t * P + i0, t * P + i0 + n); out = PS(tl, 0, n)
-            steps(1, [(out, IDN, cst("c155", n))] + modulo(out, full("wn"), full("wp"), Y, cst("c32", n)) + [(out, IDN, cst("wb", n))])
-            scan(S("ws", a * P + i0, a * P + i0 + n), cst("rs16", n), out, ALU.add, ALU.max)
-            offs = S("wou", 16 * a + i0 // 16, 16 * a + (i0 + n) // 16)
-            either(lambda: hand(offs, S("ws", a * P + i0 + 15, a * P + i0 + n, 16)), lambda: cp(offs, S("ws", a * P + i0 + 15, a * P + i0 + n, 16)), "V")
-            if t < V - 1: cp(IND("xw", 32 * i0, 32 * (i0 + n), offs), Y, "xw")
-            cp(IND(LW, 32 * i0, 32 * (i0 + n), offs), S("rout", t * P + i0, t * P + i0 + n) if t < V - 1 else S("rlast", i0, i0 + n), "lw")
+        for h in range(NH):
+            cur[0] = h; o = a * P + h * PW
+            Y = S("yout", t * P + h * PW, t * P + h * PW + PW); out = PS("wo%d_%d" % (t, h), 0, PW)
+            steps([(out, IDN, cst("c155"))] + modulo(out, Y, cst("c32")) + [(out, IDN, cst("wb"))])
+            scan(S("ws", o, o + PW), cst("rs16"), out, ALU.add, ALU.max)
+            offs = S("wou", 16 * a + 4 * h, 16 * a + 4 * h + 4)
+            move(offs, S("ws", o + 15, o + PW, 16))
+            if t < V - 1: cp(IND("xw", 32 * PW * h, 32 * PW * (h + 1), offs), Y, "xw")
+            cp(IND("li", 32 * PW * h, 32 * PW * (h + 1), offs), S("s4o", 4 * o + 3, 4 * o + 4 * PW, 4), "lw")
     cur[1] = V
     for h in range(NH):
         cur[0] = h
         v = "%d_%d" % (V, h); oi = V * P + h * PW
-        op("N", (0.0, 0), None, [], [S("rfin", h * PW, h * PW + PW)], "ar", "ar" + v, -1.0, sends["r%d_%d" % (V - 1, h)])
-        op("N", (0.0, 0), None, [], [S("yin", oi, oi + PW)], "ay", "ay" + v, -1.0, sends["y%d_%d" % (V - 1, h)])
-        dma("Y", HBM("yo", h * PW, h * PW + PW), S("yin", oi, oi + PW), "oo%d" % h, 2500)
-        dma("Y", HBM("yj", h * PW, h * PW + PW), S("rfin", h * PW, h * PW + PW), "oj%d" % h, 2500)
-    n = len(par["fin"]); w = W // n
-    for j, e in enumerate(par["fin"]):
-        cur[0] = j * NH // n
-        if par["conv"]: move(S("l16", w * j, w * j + w), S(LW, w * j, w * j + w), -2048.0, e)
-        else: ts(S("l16", w * j, w * j + w), S(LW, w * j, w * j + w), -2048.0, None, ALU.add)
-        mm([(PS("yz", 0, 256), hk("hj", c), S("l16", 256 * c, 256 * c + 256)) for c in range(j * w // 256, (j + 1) * w // 256)])
+        op("N", (0.0, 0), None, [], [S("rfin", h * PW, h * PW + PW)], "ar", "ar" + v, [sends["r%d_%d" % (V - 1, h)]])
+        op("N", (0.0, 0), None, [], [S("yin", oi, oi + PW)], "ay", "ay" + v, [sends["y%d_%d" % (V - 1, h)]])
+        dma("Y", HBM("yo", h * PW, h * PW + PW), S("yin", oi, oi + PW), "oo%d" % h)
+        dma("Y", HBM("yj", h * PW, h * PW + PW), S("rfin", h * PW, h * PW + PW), "oj%d" % h)
+    for c in range(16):
+        cur[0] = c // KK
+        move(S("l16", 256 * c, 256 * c + 256), S("li", 256 * c, 256 * c + 256), -2048.0)
+        mm([(PS("yz", 0, 256), hk("hj", c), S("l16", 256 * c, 256 * c + 256))])
     act(S("yzf", 0, 256), PS("yz", 0, 256), ACT.Identity, 2048.0 * 136)
-    dma("Y", HBM("yz"), S("yzf", 0, 256), "oyz", 2500)
+    dma("Y", HBM("yz"), S("yzf", 0, 256), "oyz")
     return ops
 
 
-def price(ops, cost):
-    out = []
+def slots(ops):
+    seen = {}; out = []
     for o in ops:
-        c, n = o["size"]; e = o["eng"]
-        if e == "P": x = cost["pfix"] + n * cost["pe"]
-        elif e == "G": x = cost["rem"] if c == "rem" else n * cost["all"]
-        elif e == "N": x = 0.0
-        elif o["sem"]: x = 60.0
-        elif isinstance(c, str): x = cost["gfix"] + (20.0 if e == "S" else 0.0) + n * cost[c]
-        else: x = max(64.0, cost["fix"] + (cost["sfix"] if e == "S" else 0.0) + n * c)
-        if e in "VSP" and not o["sem"]: x *= cost["all"]
-        out.append((x, cost["net"] if e == "N" else o["lat"]))
+        kd = (o["t"], "-" + o["nm"] + str(o["h"])); seen[kd] = seen.get(kd, 0) + 1
+        out.append((min(o["t"], 1) if o["t"] < V - 1 else o["t"] - V + 3, kd[1], seen[kd]))
     return out
 
 
-def kind(o):
-    return "-" + o["nm"] + str(o["h"])
+def places_of(ops, lists):
+    name = slots(ops); its = lists[1].split(); n = len(its); key = []; form = []
+    at = {x.rstrip("'")[1:]: (j + n * x.count("'"), x[0]) for j, x in enumerate(its)}
+    for ph in (0, 2):
+        base = -1e5
+        for j, x in enumerate(lists[ph].split()):
+            if ":" in x: base = at[x[1:-2]][0] + n * int(x[-1])
+            else: at[ph, x[1:]] = (base + j * 1e-3, x[0])
+    for (ph, nm, piece), o in zip(name, ops):
+        w = nm[1:] + "abcdefghijklmnopqrstuvwxyz"[piece - 1]
+        x, e = at[w] if ph == 1 else at[min(ph, 2), w + "!" * (ph == 3)]
+        key.append(x + n * o["t"] * (ph == 1)); form.append(int(e != o["eng"]))
+    return key, form
 
 
-def urgency(ops, par, cost, off):
-    n = len(ops); pc = price(ops, cost); succ = [[] for _ in ops]
-    for k, o in enumerate(ops):
-        for d in o["deps"]: succ[d].append(k)
-        if o["after"] is not None: succ[o["after"]].append(k)
-    last = (par["visits"] - 1) * par["T"] + par["delta"] + cost["net"] + 3000.0
-    pr = [0.0] * n
-    for k in range(n - 1, -1, -1):
-        o = ops[k]
-        base = -(o["t"] * par["T"] + o["h"] * par["delta"]) if o["nm"] == "sendr" else max([pr[s] for s in succ[k]] + [-last])
-        pr[k] = pc[k][0] * par["lam"] + pc[k][1] + cost["hop"] + base
-    return [pr[k] + off.get(kind(ops[k]), 0.0) for k in range(n)]
-
-
-def lay_out(ops, par, cost, pr):
-    n = len(ops); pc = price(ops, cost); succ = [[] for _ in ops]; left = [0] * n
-    hop, slf = cost["hop"], cost["self"]
-    eng = [o["eng"] for o in ops]
-    for k, o in enumerate(ops):
-        pre = set(o["deps"])
-        if o["after"] is not None: pre.add(o["after"])
-        left[k] = len(pre)
-        for d in pre: succ[d].append(k)
+def arrange(ops, key):
     rem = {}
-    for o in ops:
-        for tl in o["ps"]: rem[tl] = rem.get(tl, 0) + 1
-    bank, lastacc = {}, {}
-    holder = [None] * 8; past = [[] for _ in range(8)]; bfree = [0.0] * 8
-    free = {e: 0.0 for e in "VSPGYN"}; fin = [0.0] * n; start = [0.0] * n; rdy = [0.0] * n
-    ready = [k for k in range(n) if left[k] == 0]; order = []; extras = [()] * n
-    while ready:
-        fb = [j for j in range(8) if holder[j] is None]
-        nd = sum(1 for x in holder if x is not None and x[0] == "D")
-        b0 = min(fb, key=lambda j: bfree[j]) if fb else None
-        cands = []
-        for k in ready:
-            s = max(free[eng[k]], rdy[k]); ok = True
-            for tl in ops[k]["ps"]:
-                if tl in bank:
-                    d = lastacc[bank[tl]]
-                    if eng[d] != eng[k]: s = max(s, fin[d] + hop)
-                elif not fb or (tl[0] == "D" and nd >= par["dmax"]) or (tl[0] in "DKnAfy" and len(fb) < 2): ok = False
-                else: s = max(s, bfree[b0] + hop)
-            if ok: cands.append((s, -pr[k], k))
-        if not cands: raise ValueError("no bank")
-        s0, _, k0 = min(cands); e = eng[k0]; lim = s0 + min(par["look"], pc[k0][0])
-        _, _, s, k = max((-c[1] - par["beta"] * (c[0] - s0), -c[2], c[0], c[2]) for c in cands if eng[c[2]] == e and c[0] <= lim)
-        extra = set()
-        for tl in ops[k]["ps"]:
-            if tl not in bank:
-                bank[tl] = b0; holder[b0] = tl; extra.update(past[b0]); past[b0] = []
-            elif eng[lastacc[bank[tl]]] != e: extra.add(lastacc[bank[tl]])
-            j = bank[tl]; lastacc[j] = k; past[j].append(k); rem[tl] -= 1
-            if rem[tl] == 0: holder[j] = None; bfree[j] = s + pc[k][0]
-        extras[k] = extra
-        start[k] = s; free[e] = s + pc[k][0]; fin[k] = free[e] + pc[k][1]
-        order.append(k); ready.remove(k)
-        for x in succ[k]:
-            gap = 0.0 if eng[x] == "N" or eng[x] == e == "P" else slf if eng[x] == e else hop
-            rdy[x] = max(rdy[x], fin[k] + gap)
-            left[x] -= 1
-            if left[x] == 0: ready.append(x)
-    return order, bank, extras, start, fin
-
-
-def replay(ops, cost, order, extras):
-    pc = price(ops, cost); free = {e: 0.0 for e in "VSPGYN"}; fin = [0.0] * len(ops); hop, slf = cost["hop"], cost["self"]
-    for k in order:
-        o = ops[k]; e = o["eng"]; s = free[e]
-        for ds in (o["deps"], extras[k]):
-            for d in ds:
-                e2 = ops[d]["eng"]
-                x = fin[d] + (0.0 if e == "N" or e2 == e == "P" else slf if e2 == e else hop)
-                if x > s: s = x
-        if o["after"] is not None and fin[o["after"]] > s: s = fin[o["after"]]
-        free[e] = s + pc[k][0]; fin[k] = free[e] + pc[k][1]
-    return max(fin)
-
-
-def best_order(ops, par, cost, off=None):
-    off = dict(off or {}); kinds = sorted({kind(o) for o in ops if 1 <= o["t"] < V}); x = par["seed"]
-    best = lay_out(ops, par, cost, urgency(ops, par, cost, off)); val = max(best[4])
-    for _ in range(par["rounds"]):
-        x = (x * 1103515245 + 12345) % 2 ** 31; kd = kinds[(x >> 8) % len(kinds)]
-        x = (x * 1103515245 + 12345) % 2 ** 31; step = (-2000.0, -800.0, -300.0, 300.0, 800.0, 2000.0)[(x >> 8) % 6]
-        new = dict(off); new[kd] = new.get(kd, 0.0) + step
-        try:
-            r = lay_out(ops, par, cost, urgency(ops, par, cost, new))
-        except ValueError:
-            continue
-        if max(r[4]) <= val: best, val, off = r, max(r[4]), new
-    return best, off
-
-
-def prepare(ops, costs):
-    n = len(ops); succ = [[] for _ in ops]; left = [0] * n; sets = []; users = {}
-    pre = [sorted(set(o["deps"]) | ({o["after"]} if o["after"] is not None else set())) for o in ops]
-    above = [0] * n
     for k, o in enumerate(ops):
-        far = 0
-        for d in pre[k]: far |= above[d]
-        above[k] = far | sum(1 << d for d in pre[k])
-        pre[k] = [d for d in pre[k] if not far >> d & 1]
-        for d in pre[k]: succ[d].append(k)
-        for tl in o["ps"]: users[tl] = users.get(tl, 0) + 1
-    forms = (ops, [dict(o, **{x: o["alt"][x] for x in ("eng", "size", "fn")}) if "alt" in o else o for o in ops])
-    eng = [["VSPGYN".index(o["eng"]) for o in f] for f in forms]
-    for cost in costs:
-        pc = [price(f, cost) for f in forms]
-        gap = [[0.0 if b == 5 or a == b == 2 else cost["self"] if a == b else cost["hop"] for a in range(6)] for b in range(6)]
-        sets.append(([[c[0] for c in p] for p in pc], [c[1] for c in pc[0]], gap, [-1e9 if o["eng"] == "N" else 0.0 for o in ops]))
-    return succ, left, users, eng, sets, [o["ps"][0] if o["ps"] else None for o in ops], pre, forms
-
-
-def arrange(prep, key, eng, dmax):
-    users, ps, pre = prep[2], prep[5], prep[6]
-    n = len(key); rem = dict(users)
-    for k in range(n):
-        x = key[k]
-        for d in pre[k]:
-            if key[d] > x: x = key[d]
-        key[k] = x
-    bank = {}; last = [-1] * 8; fb = list(range(8)); order = []; extras = [-1] * n; held = []; done = [False] * n
+        key[k] = max([key[k]] + [key[d] for d in o["deps"]])
+        rem[o["ps"]] = rem.get(o["ps"], 0) + 1
+    bank = {}; last = [-1] * 8; free = list(range(8)); order = []; extras = [-1] * len(ops); held = []; done = set()
 
     def take(k):
-        if held:
-            for d in pre[k]:
-                if not done[d]: return False
-        tl = ps[k]
+        tl = ops[k]["ps"]
+        if not ops[k]["deps"] <= done or (tl and tl not in bank and not free): return False
         if tl:
-            b = bank.get(tl)
-            if b is None:
-                if not fb: return False
-                b = bank[tl] = fb.pop(0); extras[k] = last[b]
-            elif eng[last[b]] != eng[k]: extras[k] = last[b]
-            last[b] = k; rem[tl] -= 1
-            if rem[tl] == 0: fb.append(b)
-        order.append(k); done[k] = True
+            if tl not in bank:
+                bank[tl] = free.pop(0); extras[k] = last[bank[tl]]
+            elif ops[last[bank[tl]]]["eng"] != ops[k]["eng"]: extras[k] = last[bank[tl]]
+            last[bank[tl]] = k; rem[tl] -= 1
+            if rem[tl] == 0: free.append(bank[tl])
+        order.append(k); done.add(k)
         return True
-    for k in sorted(range(n), key=lambda k: key[k]):
+    for k in sorted(range(len(ops)), key=lambda k: key[k]):
         if not take(k):
             held.append(k)
             continue
@@ -872,372 +533,7 @@ def arrange(prep, key, eng, dmax):
             if take(held[j]):
                 del held[j]; j = 0
             else: j += 1
-    return None if held else (order, bank, extras)
-
-
-def timing(prep, which, order, extras, eng, form):
-    run, lat, gap, hold = prep[4][which]; pre = prep[6]; n = len(eng)
-    free = [0.0] * 6; prev = [-1] * 6; fin = [0.0] * n; start = [0.0] * n; who = [-1] * n
-    for k in order:
-        e = eng[k]; s = free[e]; w = prev[e]; gp = gap[e]
-        for d in pre[k]:
-            x = fin[d] + gp[eng[d]]
-            if x > s: s = x; w = d
-        d = extras[k]
-        if d >= 0:
-            x = fin[d] + gp[eng[d]]
-            if x > s: s = x; w = d
-        start[k] = s; who[k] = w; prev[e] = k; s += run[form[k]][k]; free[e] = s + hold[k]; fin[k] = s + lat[k]
-    return max(fin), start, fin, who
-
-
-def improve(par, costs, given, moves, heat0, ends=False):
-    ops = build_ops(par); V = par["visits"]
-    prep = prepare(ops, costs); n = len(ops); slot = slots(ops, V)
-    names = sorted(set(slot)); num = {s: j for j, s in enumerate(names)}; slot = [num[s] for s in slot]
-    rs = [k for k in range(n) if ops[k]["nm"] == "sendr"]; pre = prep[6]; succ = prep[0]
-    may = [not ends or names[s][0] != 1 for s in slot]; some = [k for k in range(n) if may[k]]
-
-    def keys(start):
-        T = start[rs[(V - 3) * NH]] - start[rs[(V - 4) * NH]]; base = [min(o["t"], V - 1) * T for o in ops]; tau = [0.0] * len(names)
-        for k in range(n):
-            if ops[k]["t"] in (0, V - 3, V - 1, V): tau[slot[k]] = start[k] - base[k] + k * 1e-4
-        return base, tau
-    if given:
-        base = [min(o["t"], V - 1) * given[0] for o in ops]; tau = [given[1][s][0] for s in names]; pick = [given[1][s][1] for s in names]
-    else:
-        base, tau = keys(best_order(ops, par, costs[0])[0][3]); pick = [0] * len(names)
-    loads = [k for k in range(n) if ops[k]["sem"] and ops[k]["sem"][0] == "l"]
-    x = [par["seed"] + moves]; free = [k for k in some if "alt" in ops[k]]
-
-    def rnd():
-        x[0] = (x[0] * 1103515245 + 12345) % 2 ** 31
-        return (x[0] >> 8) / 2.0 ** 23
-
-    def value(base, tau, pick, than=None, slack=0.0):
-        form = [pick[s] for s in slot]; eng = [prep[3][f][k] for k, f in enumerate(form)]
-        key = [b + tau[s] for b, s in zip(base, slot)]
-        for k in loads: key[k] = k - 1e9
-        a = arrange(prep, key, eng, par["dmax"])
-        if a is None or (than and a[0] == than[1][0] and form == than[3]): return None
-        ts = []; worse = 0.0
-        for w, c in enumerate(costs):
-            ts.append(timing(prep, w, a[0], a[2], eng, form))
-            if than:
-                worse += (ts[w][0] - than[2][w][0]) * c["weight"]
-                if worse > slack + par["hope"] * (len(costs) - 1 - w): return None
-        return sum(t[0] * c["weight"] for t, c in zip(ts, costs)), a, ts, form
-
-    def shift(new, k, to, near, sign, depth):
-        new[slot[k]] = to - base[k]
-        for d in near[k] if depth else ():
-            if (base[d] + new[slot[d]] - to) * sign > 0 and ops[d]["t"] == ops[k]["t"]: shift(new, d, to - sign, near, sign, depth - 1)
-    if ends:
-        need = value(base, tau, pick)[2][0][1]; fixed = [k for k in range(n) if ops[k].get("const")]
-        for k in reversed(fixed): need[k] = min([need[s] for s in succ[k]] + [1e9]) - 1.0
-        for j, k in enumerate(sorted(fixed, key=lambda k: need[k])): tau[slot[k]] = 30.0 * j - 3000.0
-    def sweep(cur, c, part):
-        order, bank, extras = cur[1]; end, st, fin, who = cur[2][c]; form = cur[3]; run, lat, gap, hold = prep[4][c]
-        eng = [prep[3][f][k] for k, f in enumerate(form)]; rn = [run[f][k] for k, f in enumerate(form)]; s = list(st)
-        up = [[] for _ in s]; down = [[] for _ in s]; on = [[] for _ in range(6)]
-        for k in order:
-            on[eng[k]].append(k)
-            for d in pre[k] + ([extras[k]] if extras[k] >= 0 else []):
-                y = rn[d] + lat[d] + gap[eng[k]][eng[d]]; up[k].append((d, y)); down[d].append((k, y))
-        for sign, links in ((-1.0, down), (1.0, up)):
-            for k in sorted(some, key=lambda k: sign * s[k]):
-                e = eng[k]; r = rn[k]
-                if e != 5 and (rnd() > part or k in loads): continue
-                to = max([s[d] + y for d, y in links[k]] + [0.0]) if sign > 0 else min([s[d] - y for d, y in links[k]] + [end - r - lat[k]])
-                if e != 5:
-                    line = on[e]; j = line.index(k); del line[j]
-                    if sign > 0:
-                        while j and s[line[j - 1]] + rn[line[j - 1]] > to: j -= 1
-                        while j < len(line) and s[line[j]] < to + r - 1e-6: to = max(to, s[line[j]] + rn[line[j]]); j += 1
-                    else:
-                        while j < len(line) and s[line[j]] < to + r: j += 1
-                        while j and s[line[j - 1]] + rn[line[j - 1]] > to + 1e-6: to = min(to, s[line[j - 1]] - r); j -= 1
-                    line.insert(j, k)
-                s[k] = to
-        new = list(tau); key = [b + tau[x] for b, x in zip(base, slot)]; z = -1e18; mark = []
-        for k in sorted(range(n), key=lambda k: s[k]):
-            if may[k]: mark.append((k, z))
-            elif key[k] - s[k] * 1e-3 > z: z = key[k] - s[k] * 1e-3
-        first = min(key[k] - s[k] for k in range(n) if not may[k])
-        for k, z in mark: new[slot[k]] = (s[k] + first - 2e4 if z < -1e17 else z + s[k] * 1e-3) - base[k]
-        for line in on[:5]:
-            z = 1e18
-            for k in reversed(line):
-                if not may[k]: z = key[k]
-                elif base[k] + new[slot[k]] >= z:
-                    z -= 1e-3; new[slot[k]] = z - base[k]
-                else: z = base[k] + new[slot[k]]
-        return new
-    cur = best = value(base, tau, pick); deps = [set(p) for p in pre]; kept = (base, tau, pick)
-    for it in range(moves):
-        heat = heat0 * (1.0 - it / moves)
-        if ends and rnd() < par["sweep"]:
-            new = sweep(cur, int(rnd() * len(costs)), rnd()); r = value(base, new, pick, cur, heat * rnd())
-            if r is not None:
-                cur, tau = r, new
-                if r[0] < best[0]: best = r; kept = (base, tau, pick)
-            continue
-        if it % par["again"] == 0 and not ends:
-            b2, t2 = keys(cur[2][0][1]); r = value(b2, t2, pick)
-            if r is not None and r[0] <= cur[0] + heat: base, tau, cur = b2, t2, r
-        new = list(tau); other = pick; z = rnd()
-        if z < par["aimed"]:
-            end, st, fin, who = cur[2][int(rnd() * len(costs))]
-            k = fin.index(end); pairs = []
-            while who[k] >= 0:
-                if who[k] not in deps[k] and may[k] and may[who[k]]: pairs.append((who[k], k))
-                k = who[k]
-            if not pairs: continue
-            j = int(rnd() * len(pairs)); p, k = pairs[j]
-            while j + 1 < len(pairs) and pairs[j + 1][1] == p and rnd() < par["far"]:
-                j += 1; p = pairs[j][0]
-            z = rnd()
-            if z < .2 and ("alt" in ops[p] or "alt" in ops[k]):
-                other = list(pick); other[slot[p if "alt" in ops[p] else k]] ^= 1
-            elif z < .6: shift(new, k, base[p] + tau[slot[p]] - 1.0 - 50.0 * rnd(), pre, 1.0, 3)
-            else: shift(new, p, base[k] + tau[slot[k]] + 1.0 + 50.0 * rnd(), succ, -1.0, 3)
-        elif z < par["aimed"] + .05:
-            other = list(pick); other[slot[free[int(rnd() * len(free))]]] ^= 1
-        else:
-            k = some[int(rnd() * len(some))]; z = (rnd() - .5) * par["reach"]
-            shift(new, k, base[k] + tau[slot[k]] + z, pre if z < 0 else succ, 1.0 if z < 0 else -1.0, 3)
-        r = value(base, new, other, cur, heat * rnd())
-        if r is None: continue
-        cur, tau, pick = r, new, other
-        if r[0] < best[0]: best = r; kept = (base, tau, pick)
-    state = (kept[0][rs[NH]], {s: (kept[1][j], kept[2][j]) for j, s in enumerate(names)})
-    return [prep[7][best[3][k]][k] for k in range(n)], best, state
-
-
-def slots(ops, V):
-    seen = {}; out = []
-    for o in ops:
-        ph = min(o["t"], 1) if o["t"] < V - 1 else o["t"] - V + 3
-        kd = (o["t"], kind(o)); seen[kd] = seen.get(kd, 0) + 1; out.append((ph, kind(o), seen[kd]))
-    return out
-
-
-def cycle(par, costs, given, moves, heat0):
-    ops = build_ops(par); prep = prepare(ops, costs); name = slots(ops, par["visits"])
-    mid = [k for k, o in enumerate(ops) if o["t"] == 3]; n = len(mid); num = {name[k]: j for j, k in enumerate(mid)}
-    pre = [[(num[name[d]], 3 - ops[d]["t"]) for d in prep[6][k] if ops[d]["t"]] for k in mid]
-    near = ([[d for d, l in p if not l] for p in pre], [[] for _ in mid]); tiles = {}
-    for j, k in enumerate(mid):
-        for d in near[0][j]: near[1][d].append(j)
-        if prep[5][k]: tiles.setdefault(prep[5][k], []).append(j)
-    tiles = list(tiles.values()); late = [(j, d, l) for j in range(n) for d, l in pre[j] if l]
-    engs = [[prep[3][f][k] for k in mid] for f in (0, 1)]
-    runs = [[[s[0][f][k] for k in mid] for f in (0, 1)] for s in prep[4]]
-    lats = [[s[1][k] + (0.0 if ops[k]["nm"][:4] == "send" else c["hop"]) for k in mid] for s, c in zip(prep[4], costs)]
-    rs = [j for j, k in enumerate(mid) if ops[k]["nm"] == "sendr"]; free = [j for j, k in enumerate(mid) if "alt" in ops[k] and ops[k]["nm"] not in par["stay"]]
-    data = [{d for d, l in p} for p in pre]
-    T0 = given[0]; tau = [given[1][name[k]][0] for k in mid]; pick = [given[1][name[k]][1] for k in mid]
-    x = [par["seed"] + moves]; M = par["rounds2"]
-
-    def rnd():
-        x[0] = (x[0] * 1103515245 + 12345) % 2 ** 31
-        return (x[0] >> 8) / 2.0 ** 23
-
-    def program(tau, pick):
-        key = list(tau)
-        for again in range(4):
-            for j in range(n):
-                y = key[j]
-                for d in near[0][j]:
-                    if key[d] >= y: y = key[d] + 1e-3
-                key[j] = y
-            bad = False
-            for j, d, l in late:
-                if key[d] - l * T0 >= key[j]: key[j] = key[d] - l * T0 + 1e-3; bad = True
-            if not bad: break
-        if bad: return None
-        w = [int(y // T0) for y in key]; pos = [y - a * T0 for y, a in zip(key, w)]; eng = [engs[f][j] for j, f in enumerate(pick)]
-        order = sorted(range(n), key=lambda j: pos[j]); extra = {}; ev = []; live = 0
-        for us in tiles:
-            us = sorted(us, key=lambda j: key[j]); a = us[0]
-            for b in us[1:]:
-                if eng[a] != eng[b]: extra[b] = a - (w[b] - w[a]) * n
-                a = b
-            live += w[a] - w[us[0]]; ev.append((pos[us[0]], 1, us[0])); ev.append((pos[a], -1, a))
-        ev.sort(); top = y = live
-        for p, s, j in ev:
-            y += s
-            if y > top: top = y
-        idle = max(8, top) - live; rel = [j for p, s, j in ev if s < 0]; i = -idle
-        for p, s, j in ev:
-            if s > 0:
-                extra[j] = rel[i] - n if i < 0 else rel[i]; i += 1
-        prog = []
-        for j in order:
-            e = eng[j]; a = w[j]
-            dl = [d - (a + l - w[d]) * n for d, l in pre[j] if e != 2 or eng[d] != 2]
-            if j in extra and (e != 2 or eng[extra[j] % n] != 2): dl.append(extra[j])
-            prog.append((j, e, 6 if e == 5 else e, dl))
-        return key, w, prog, max(0, top - 8), pick
-
-    def run(pg, c, state, rounds, trace=False):
-        key, w, prog, over, pick = pg; f0, T = state; lat = lats[c]; rn = runs[c]
-        av = [f - (3 + a) * T for f, a in zip(f0, w)]; av += [y + T for y in av]; av += [y + T for y in av[n:]]; av += [0.0] * (n * rounds)
-        fr = [-1e18] * 7; who = [-1] * len(av); last = [-1] * 7; full = []
-        for j, e, e2, dl in prog:
-            fr[e2] = av[2 * n + j] - lat[j]; full.append((j, e, e2, dl, rn[pick[j]][j], lat[j]))
-        for b in range(3 * n, (3 + rounds) * n, n):
-            if trace:
-                for j, e, e2, dl, r, l in full:
-                    s = fr[e]; p = last[e]
-                    for d in dl:
-                        if av[b + d] > s: s = av[b + d]; p = b + d
-                    s += r; fr[e2] = s; last[e2] = b + j; av[b + j] = s + l; who[b + j] = p
-            else:
-                for j, e, e2, dl, r, l in full:
-                    s = fr[e]
-                    for d in dl:
-                        y = av[b + d]
-                        if y > s: s = y
-                    s += r; fr[e2] = s; av[b + j] = s + l
-        b = (2 + rounds) * n
-        if not trace: return sum(av[b + j] - av[2 * n + j] for j in rs) / (len(rs) * rounds) + 2000.0 * over
-        T = sum(av[b + j] - av[b - 2 * n + j] for j in rs) / (2 * len(rs)); z = av[b + rs[0]]; pairs = []
-        k = b + rs[-1]
-        while who[k] >= b - 2 * n:
-            p = who[k]
-            if p % n not in data[k % n]: pairs.append((p % n, k % n, (k // n - w[k % n]) - (p // n - w[p % n])))
-            k = p
-        return ([av[b + j] - z + w[j] * T for j in range(n)], T), pairs
-
-    def settle(pg, states): return [run(pg, c, s, par["settle"], True) for c, s in enumerate(states)]
-
-    def worth(pg, got): return sum(g[0][1] * c["weight"] for g, c in zip(got, costs)) + 2000.0 * pg[3]
-
-    def shift(new, k, to, side, sign, depth):
-        new[k] = to
-        for d in side[k] if depth else ():
-            if (new[d] - to) * sign > 0: shift(new, d, to - sign, side, sign, depth - 1)
-    def sweep(pg, c, state, part):
-        key, w, prog, over, pick = pg; f0, T = state; lat = lats[c]; rn = [runs[c][f][j] for j, f in enumerate(pick)]
-        s = [f0[j] - lat[j] - rn[j] for j in range(n)]; up = [[] for _ in s]; down = [[] for _ in s]; on = [[] for _ in range(7)]; eng = [0] * n
-        for j, e, e2, dl in prog:
-            on[e].append(j); eng[j] = e
-            for d, gap in [(x % n, rn[x % n] + lat[x % n] - (-(x // n) - w[j] + w[x % n]) * T) for x in dl] + [(d, rn[d] - l * T) for d, l in pre[j]]:
-                up[j].append((d, gap)); down[d].append((j, gap))
-        for sign, links in ((-1.0, down), (1.0, up)):
-            for j in sorted(range(n), key=lambda j: sign * s[j]):
-                if not links[j] or (eng[j] != 5 and rnd() > part): continue
-                to = sign * max(sign * s[d] + gap for d, gap in links[j]); r = rn[j]
-                if eng[j] != 5:
-                    a = to if sign > 0 else -to - r
-                    for b, y in sorted(((((s[x] if sign > 0 else -s[x] - rn[x]) + rn[x] - a) % T - rn[x], rn[x]) for x in on[eng[j]] if x != j)):
-                        at = to if sign > 0 else -to - r
-                        if a + b >= at + r - 1e-6: break
-                        if a + b + y > at: to = a + b + y if sign > 0 else -(a + b + y) - r
-                if sign * (s[j] - to) > 0: s[j] = to
-        return [y + 2 * T + j * 1e-4 for j, y in enumerate(s)], T
-    pg = program(tau, pick); got = settle(pg, [(pg[0], T0)] * len(costs)); got = settle(pg, [g[0] for g in got])
-    best = (worth(pg, got), T0, pg[0], pick, [g[0][1] for g in got])
-    for it in range(moves):
-        heat = heat0 * (1.0 - it / moves) ** par["cool"]
-        if par.get("log") and it % (moves // 10) == 0: par["log"](it, round(worth(pg, got)), round(best[0]))
-        if it % par["again"] == 0:
-            f0, T = got[0][0]; keep = T0; T0 = T
-            p2 = program([f0[j] - lats[0][j] - runs[0][pick[j]][j] + 2 * T + j * 1e-4 for j in range(n)], pick)
-            g2 = p2 and settle(p2, [g[0] for g in got])
-            if p2 and worth(p2, g2) <= worth(pg, got) + heat: pg, got = p2, g2
-            else: T0 = keep
-        if rnd() < par["sweep"]:
-            c = int(rnd() * len(costs)); keep = T0; new, T0 = sweep(pg, c, got[c][0], rnd()); p2 = program(new, pick)
-            g2 = p2 and settle(p2, [g[0] for g in got])
-            if p2 and worth(p2, g2) <= worth(pg, got) + heat * rnd():
-                pg, got = p2, g2
-                if worth(pg, got) < best[0]: best = (worth(pg, got), T0, pg[0], pick, [g[0][1] for g in got])
-            else: T0 = keep
-            continue
-        tau = pg[0]; new = list(tau); other = pick; z = rnd()
-        if z < par["aimed"]:
-            pairs = got[int(rnd() * len(costs))][1]
-            if not pairs: continue
-            j = int(rnd() * len(pairs)); p, k, l = pairs[j]
-            while j + 1 < len(pairs) and pairs[j + 1][1] == p and rnd() < par["far"]:
-                j += 1; p = pairs[j][0]; l += pairs[j][2]
-            z = rnd()
-            if z < .2 and (p in free or k in free):
-                other = list(pick); other[p if p in free else k] ^= 1
-            elif z < .6: shift(new, k, tau[p] - l * T0 - 1.0 - 50.0 * rnd(), near[0], 1.0, 3)
-            else: shift(new, p, tau[k] + l * T0 + 1.0 + 50.0 * rnd(), near[1], -1.0, 3)
-        elif z < par["aimed"] + .05:
-            other = list(pick); other[free[int(rnd() * len(free))]] ^= 1
-        else:
-            k = int(rnd() * n); z = (rnd() - .5) * par["reach"]
-            shift(new, k, tau[k] + z, near[z > 0], 1.0 if z < 0 else -1.0, 3)
-        p2 = program(new, other)
-        if p2 is None or p2[2] == pg[2]: continue
-        worse = -2000.0 * pg[3]; slack = heat * rnd()
-        for c, g in enumerate(got):
-            worse += (run(p2, c, g[0], M) - g[0][1]) * costs[c]["weight"]
-            if worse > slack + par["hope"] * (len(costs) - 1 - c): break
-        if worse > slack: continue
-        if abs(worse) >= 1e-3:
-            g2 = settle(p2, [g[0] for g in got])
-            if worth(p2, g2) > worth(pg, got) + slack: continue
-            got = g2
-        pg, pick = p2, other
-        if worth(pg, got) < best[0]: best = (worth(pg, got), T0, pg[0], pick, [g[0][1] for g in got])
-    out = dict(given[1]); low = min(best[2])
-    for s in out:
-        j = num.get((1,) + s[1:])
-        if j is not None and s[0] < 3: out[s] = (best[2][j] - low, best[3][j])
-    return (best[1], out), best
-
-
-def words(ops, V):
-    return [(s, [e + s[1][1:] + "abcdefghijklmnopqrstuvwxyz"[s[2] - 1] for e in [o["eng"]] + ([o["alt"]["eng"]] if "alt" in o else [])])
-            for o, s in zip(ops, slots(ops, V)) if o["t"] == 3]
-
-
-def read(par, text):
-    ops = build_ops(par); its = text.split(); at = {x.rstrip("'"): 80.0 * (j + len(its) * x.count("'")) for j, x in enumerate(its)}
-    mid = {s[1:]: ([(at[x], f) for f, x in enumerate(ws) if x in at] + [(at[x], 0) for x in at if x[1:] == ws[0][1:]] + [(0.0, 0)])[0] for s, ws in words(ops, par["visits"])}
-    out = {}
-    for o, s in zip(ops, slots(ops, par["visits"])):
-        out[s] = mid[s[1:]] if s[0] < 3 and s[1:] in mid and (s[0] or s[1][1:-1] not in ("yb", "xd")) else (
-            160.0 * len(its) if s[0] > 1 else max([ops[d]["lat"] for d in o["deps"]] + [0.0]), 0)
-    return 80.0 * len(its), out
-
-
-def plan(par, costs):
-    state = read(par, ROUND)
-    for moves, heat in par["cycle"]:
-        state = cycle(par, costs, state, moves, heat)[0]
-    for visits, moves, heat, ends in par["stages"]:
-        ops, best, state = improve(dict(par, visits=visits), costs, state, moves, heat, ends)
-    return ops, best
-
-
-def places_of(ops, succ, lists):
-    name = slots(ops, V); its = lists[1].split(); n = len(its); key = [0.0] * len(ops); form = [0] * len(ops)
-    at = {x.rstrip("'")[1:]: (j + n * x.count("'"), x[0]) for j, x in enumerate(its)}
-    for ph, text in ((0, lists[0]), (2, lists[2])):
-        base = -1e5
-        for j, x in enumerate(text.split()):
-            if ":" in x: base = at[x[1:-2]][0] + n * int(x[-1])
-            else: at[ph, x[1:]] = (base + j * 1e-3, x[0])
-    for k, o in enumerate(ops):
-        w = name[k][1][1:] + "abcdefghijklmnopqrstuvwxyz"[name[k][2] - 1]
-        key[k], e = at[w] if name[k][0] == 1 else at[min(name[k][0], 2), w + "!" * (name[k][0] == 3)]
-        key[k] += n * o["t"] * (name[k][0] == 1); form[k] = int(e != o["eng"])
-    for k, o in enumerate(ops):
-        if o["sem"] and o["sem"][0] == "l": key[k] = k - 1e9
-    return key, form
-
-
-def plan2(par, costs, lists):
-    ops = build_ops(par); prep = prepare(ops, costs); key, form = places_of(ops, prep[0], lists)
-    eng = [prep[3][f][k] for k, f in enumerate(form)]; a = arrange(prep, key, eng, 0)
-    return [prep[7][f][k] for k, f in enumerate(form)], (0, a, [timing(prep, c, a[0], a[2], eng, form) for c in range(len(costs))])
+    return order, bank, extras
 
 
 PLAN = []
@@ -1248,42 +544,38 @@ def rank_program(g, core, T, topo):
     if rank is None:
         return
     if not PLAN:
-        PLAN.append(plan2(PAR, COSTS, (FIRST, ROUND, LAST)) if FIRST else plan(PAR, COSTS))
-    ops = PLAN[0][0]; order, bank, extras = PLAN[0][1][1]
+        ops = build_ops(); key, form = places_of(ops, (FIRST, ROUND, LAST))
+        ops = [dict(o, eng=o["alt"]["eng"], fn=o["alt"]["fn"]) if f else o for o, f in zip(ops, form)]
+        PLAN.append((ops,) + arrange(ops, key))
+    ops, order, bank, extras = PLAN[0]
     nxt = T.cores[(rank + 1) % len(T.cores)]; prv = T.cores[(rank - 1) % len(T.cores)]
     rid, pid, _ = topo.addr(nxt)
     env = {"rid": rid, "pid": pid, "mask": topo.mask(core, nxt)}
     n_out, n_in = len(topo.engines(core, nxt)), len(topo.engines(prv, core))
-
-    todo = {}
+    todo = {}; opened = set()
     for o in ops:
-        if o["eng"] == "P": todo[o["grp"]] = todo.get(o["grp"], 0) + 1
-    opened = set()
+        if o["eng"] == "P": todo[o["ps"]] = todo.get(o["ps"], 0) + 1
 
     def Q(name):
         return env[name] if name in env else T["pb%d" % bank[name]]
     queue = {"V": g.vector, "S": g.scalar, "P": g.tensor, "G": g, "Y": g.sync}
-    count = {e: 0 for e in "VSPG"}; known = {e: {} for e in queue}; mark = {}; top = {}; sent = 0; drain = []
+    count = {e: 0 for e in "VSPG"}; known = {e: {} for e in queue}; mark = {}; top = {}; sent = 0
     for k in order:
         o = ops[k]; e = o["eng"]
         if e == "N":
-            mark[k] = (o["sem"], n_in, {}); top[o["sem"]] = n_in
+            mark[k] = (o["sem"], n_in, {})
             continue
         kn = known[e]
-        pre = set(o["deps"]) | {extras[k]}
-        if e == "V":
-            pre.update(drain); drain[:] = [k] if o.get("drain") else []
-        need = sorted((mark[d] for d in pre if d in mark and not (e == "P" and ops[d]["eng"] == "P")), key=lambda m: -m[1])
+        need = sorted((mark[d] for d in o["deps"] | {extras[k]} if d in mark and not (e == "P" and ops[d]["eng"] == "P")), key=lambda m: -m[1])
         for sem, val, clock in need:
-            if kn.get(sem, 0) >= val: continue
-            if any(c2.get(sem, 0) >= val for s2, v2, c2 in need): continue
+            if kn.get(sem, 0) >= val or any(c2.get(sem, 0) >= val for s2, v2, c2 in need): continue
             queue[e].wait_ge(T.sem[sem], val)
             kn[sem] = val
         for sem, val, clock in need:
             for s2, v2 in list(clock.items()) + [(sem, val)]:
                 if kn.get(s2, 0) < v2: kn[s2] = v2
         if e == "P":
-            tl = o["ps"][0]; todo[o["grp"]] -= 1; env["ends"] = (tl not in opened, todo[o["grp"]] == 0); opened.add(tl)
+            tl = o["ps"]; todo[tl] -= 1; env["ends"] = (tl not in opened, todo[tl] == 0); opened.add(tl)
         ins = o["fn"](g, T, Q)
         if o["sem"] == "remote":
             sent += n_out

import math
from concourse.mybir import AluOpType, ActivationFunctionType

ALU = AluOpType
ACT = ActivationFunctionType
V, W, P = 6, 4096, 128
NH = 2
PW = P // NH
KK = 8
M4 = float((2 ** 23 + 1) * 4)
M1, M32, M4096 = (float(3 * 2 ** 22 * n) for n in (1, 32, 4096))
AN = 192.0
PEN = float(2 ** 24)
BIG = float(2 ** 22)
DMS = 16 + 16 * PW + 16

B, F, I32, U16, H16 = "bfloat16", "float32", "int32", "uint16", "float16"
SCRATCH = {
    "xw": [W, B], "li": [W, I32], "l16": [W, H16], "ji": [P, I32], "wi": [8, I32], "ci": [8, I32], "cf": [32, F], "yzf": [256, F],
    "rin": [(V + 1) * P, U16], "yin": [(V + 1) * P, B], "rout": [V * P, U16], "yout": [V * P, B], "rfin": [P, F], "rlast": [P, F],
    "ioj": [PW, B], "iox": [256, B], "idx": [256, B], "tmp": [800, B], "nc": [16 * 144, B], "hj": [144, H16], "kb": [PW, H16],
    "o8": [16, B], "b16": [16, B], "f0": [4 * PW, B], "rsk": [PW, F], "rs16": [128, F], "td": [256, F], "ca": [8, B], "da": [8, F],
    "wp": [128, H16], "wn": [128, H16], "wou": [32, U16], "ws": [2 * P, F], "ni": [NH * 272, B], "dm": [2 * NH * DMS, B], "lg": [2 * 2048, H16],
    "s4": [2 * NH * (4 * PW + 4) + 4, F], "s4o": [2 * 4 * P, F], "pi": [2 * 2 * P, I32], "ka": [32, I32], "kt": [32, F], "ko": [32, U16], "lf": [32, B],
}
for _n in ("ioc", "iok", "one", "hh", "hz", "hp", "hs"):
    SCRATCH[_n] = [144, B]
for _n in ("iob", "iom", "idn", "nid", "q25", "ida", "i32", "bo", "nbo", "boa", "nba", "by", "tri", "mA", "mB", "wb", "c1", "c32", "c4096", "cc", "c155",
           "c2048", "cm", "cn", "th", "cp", "c4", "non"):
    SCRATCH[_n] = [128, B]
for _n in ("xd", "yb", "zg", "dz"):
    SCRATCH[_n] = [2 * 2048, B]
for _n, _d in (("nu", U16), ("good", B), ("mk", B), ("nbv", H16), ("sa2", B), ("pj", I32), ("km", I32), ("kv", F)):
    SCRATCH[_n] = [2 * P, _d]
SCRATCH = {_n: ("sbuf", [128, _v[0]], _v[1]) for _n, _v in SCRATCH.items()}
for _n in ("ad", "nx"):
    SCRATCH[_n] = ("sbuf", [128, 2 * P // 16, 16, 16], B)
for _n, _r in (("nl", 32), ("zr", 18)):
    SCRATCH[_n] = ("sbuf", [128, _r * NH, KK], H16)
for _n in range(8):
    SCRATCH["pb%d" % _n] = ("psum", [128, 512], F)
SEMAPHORES = (["cV", "cS", "cP", "cG", "sent", "ljur", "lown", "lwgt", "lx", "ll0", "oyz"] + ["o%s%d" % (k, h) for k in "jo" for h in range(NH)]
              + ["a%s%d_%d" % (k, t, h) for k in "ry" for t in range(1, V + 1) for h in range(NH)])

FIRST = """
Yljur0a Slown0a Ylx0a Yll00a Ylwgt0a Vone0a Gci0a Gioc0a Sc10a Vnon0a Sda0b Vci0b Scc0a Vcf0a Sca0c Vc20480a Sf00a Giom0a Vzr0a Sda0c Sca0a Vcf0b Sc320a Vnl0b Vidn0a Std0a
Vtmp0f Vc1550a Giob0a Std0b Vcf0g Vcf0c Scp0a Vnc0j Snc0b Vnc0f Vnc0k Std0c Vcf0i Snid0a Giok0a Vcf0k Vnc0n Snc0p Vcf0h Vnc0m Sda0a Vnl0a Syb0a Vrs160a PfillDx1a Gdm0c Vf00d
Vnc0g Vcf0e PfillDx1b Gni0a Vcf0j Vtmp0d Vnc0l Sru0b Vcf0l Syb0b Pwo00a Vnc0c Vnc0i Vtmp0e Vbo0a Vnc0d Vru0a Vnc0e Vida0a Sc40960a Vca0b Sf00b Vcf0d Scm0a Vnc0h Sb160b Vth0a
Vxd0a Syb1b PDm01a Gdm0d Grf0a Gioj0a Vnc0o Syb1a Vxd0b Giox0a PDx1b PDx1d Pwb0a Sad0a Vnc0a Vnx0a PDx1a Vnx0b Gnc0q PDx1c So80a Vrsk0a Sad1a Vwb0b Vhh0a Gtmp0c Vidx0a Vcf0f
Vtmp0a Pnb0b Vcf0o Sad1b Vcc0b Vhz0a Vhp0a Pnb0a Vkb0a Vb160a Vf00c Vhs0a Gtri0a Vnx1a PKn0a Sad0b Vtmp0b Vcn0a PKn0b Vnba0a Grf1a Vnx1b PKr0a Snbv0a Sgood0a PDm00a Vtri0b
Slg0b Vby0a Vlg0a Giox0b PKa0b PKa0a Gdm0a PDm0a Pnb1b GmB0a Slg1a Vcf0m Vkm0a Pnb1a Vkv0a Vdm0h GmA0a PNt0a Vka0a Vdm0e PKn1a Vgood1a Vdm0g Snl0c PKn1b Slg1b Vkt0a PDm1a Vdm0f
Pn0a PKr1a Vboa0a PKa1b Vko0a Vmk1a Vnu0a Vnr0a Vq250a Vdm1b Snbv1a Szg0a PKd0b PKa1a Vyout0a PNt1a Vcf0n Vnbo0a PKd0a Vkm1a PKd0c Vdm1d PKd0d Gsendy0a Pddz0a Pddz0b Pu00a
Vkv1a Pc00a Szg0b Vwn0a Vnl1a Pcy0a Vka1a Vni0b Pfino0a Vwp0a Vdm1c Pn1a PfillDz0a Nay0a:1 Vkt1a Pc0a Vi320a Vdm1a Pu0a Snu1a Skp0a Pwo0a Sko1a Ssa20a Vdz0c PZz0a Szg1b Vdz0a
Pc01a PKd1c PKd1a Vdz0b Pfiny0a Pfin0d Gdm0b Pfinc0a Vpi0a PKd1d Vdz0d Szr0b Szg1a Pfin0c Vfar0a Pfin0b Vyout1a Pfin0a Vnm0a Pfin0e Vfa0a Vnr1a Pfinr0a Vws0a PKd1b Gsendy1a
Pu01a Pddz1b PfillDz1a Vs4o0a Pddz1a Pfino1a Vdz1d PZz1a Sni1a Nay1a:1 Srout0a Vdz1b Pu1a Skp1a Swou0a Pwo01a Slf0a Pc1a Vdz1a Szr1a Gsendr0a Pfiny1a Pcy1a Pwo1a Vidx0b Pfin1c
Vpi1a Ssa21a Vdz1c Pfin1e Syb0a:1 Pfin1b Nar0a:1 Vfar1a Pfinc1a Vnm1a Vws1a Pfin1a Pfin1d Vfa1a Vxw0a Syb0b:1 Pfinr1a Vs4o1a Pfino0a:1 Vc40a Vwou1a Slf1a Vrout1a Vlw0a PA0a
Gsendr1a Vxw1a Syb1b:1 Vlw1a Nar1a:1 Vhj0a Syb1a:1 Vtd0d
"""
ROUND = """
Nay0a PfillDz0a' Vnu1a' Pu00a' Vdm1b' Pu0a' Sni0a' Pwo0a' Vka1a' Szg1b' Pfiny0a' Vdz0a' Pc00a' Pcy0a' PKd1a' Vdz0b' PKd1d' Pc0a' PZz0a' Vkt1a' Vdz0d' Pfin0b' Vpi0a' Ssa20a'
PKd1c' Sko1a' Vdz0c' Pfin0c' Szr0a' Szg1a' Pfin0e' Vfar0a' Pfinc0a' Vyout1a' Pfin0a' Slf1a' Pfin0d' Vnm0a' Vfa0a' Pfinr0a' Vws0a' Pwo01a' Vnr1a' Gsendy1a' PKd1b' Vlf0a' Pddz1b'
PfillDz1a' Pddz1a' Vs4o0a' Pc01a' Pu01a' Pcy1a' Vdz1a' Sni1a' Nay1a Srout0a' Vdz1d' Pu1a' Skp1a' PZz1a' Pwo1a' Gsendr0a' Vdz1c' Szr1a' Pc1a' Pfino1a' Vpi1a' Pfin1b' Vws1a'
Vdz1b' Ssa21a' Pfin1e' Syb0a Pfiny1a' Pfin1d' Swou0a' Nar0a Vwou1a' Vfar1a' Pfin1a' Vnm1a' Pfinc1a' Pfin1c' Syb0b Vfa1a' Pfinr1a' PA0a' Vs4o1a' PDm01a Pwo00a PDm00a Pfino0a
Vxw1a' Srout1a' Vxw0a' Gsendr1a' Vlw1a' Syb1b Vlw0a' Nar1a Vtd0a' Syb1a Vxd0a Grf0a Slg0a Vxd0b Slg0b Vkp0a Sad0a Vnx0a PNt0a Vnx0b Grf1a Sad0b Vxd1b PKn0b Snl0a Pnb0a Slg1a
Pnb0b Vxd1a PKn0a PKr0a PKa0b Sgood0a Slg1b PKa0a Vnx1b PDm0a Vnx1a Pn0a Vnbv0a Vkm0a Vkv0a Vdm0d Sad1b Pnb1a Vka0a Vnu0a Pnb1b Vdm0b Sad1a PNt1a Vdm0a PKn1b PKn1a Vkt0a
Vgood1a Vdm0c Szg0b Vko0a Vnbv1a PDm1a Vnr0a Vnl1a PKr1a PKa1a Vyout0a Vdm1d PKd0a Szg0a Vdm1a Gsendy0a PKd0d PKa1b Pn1a Vdm1c PKd0b PKd0c Pddz0a Vkm1a Pddz0b Vkv1a
"""
LAST = """
Vkv1a:4 Nay0a Pu1a:4 Nay1a Pfin1e:4 Syb0a Swou0a:4 Nar0a Pfin1c:4 Syb0b Vs4o1a:4 Pfino0a Pwo00a PDm00a PDm01a Vlw1a:4 Syb1b Vlw0a:4 Nar1a Vtd0a:4 Syb1a Vxd0a Grf0a Slg0a Vxd0b
Slg0b Vnx0a Sad0a Vnx0b PNt0a Vxd1b Grf1a Sad0b PKn0b PKn0a Snl0a Slg1a Pnb0a Vxd1a Pnb0b PKr0a PKa0b Sgood0a Slg1b PKa0a Vnx1b Pn0a Vnx1a PDm0a Vkv0a Vkm0a Vdm0a Pnb1a Sad1a
Vnu0a Vka0a Pnb1b Vnbv0a Vdm0d Sad1b PNt1a Vkp0a Vkt0a Vgood1a PKn1b Vdm0c Sko0a Szg0a Vnl1a PDm1a PKn1a Vdm0b PKr1a Vnbv1a Vdm1d PKa1a Vyout0a PKa1b Szg0b Vdm1b PKd0b Pn1a
Vdm1c Gsendy0a PKd0c PKd0d Pwo0a Vkm1a Vnr0a PKd0a Vnu1a Pddz0a Vkv1a Pu00a Vnr1a Pfiny0a Vka1a Pddz0b Nay0a! Vdm1a PfillDz0a Szg1a Pu0a PKd1d Vkt1a PKd1c Vdz0b PKd1b PZz0a
Vni0a PKd1a Vko1a Pc00a Vdz0d Pcy0a Pfin0c Szg1b Vzr0a Pc0a Vws0a Vyout1a Pc01a Vpi0a Pfin0e Vdz0c Pfin0a Pu01a Gsendy1a PfillDz1a Pddz1b Vfar0a Pcy1a Vdz0a Pu1a Ssa20a Pddz1a
Pfin0d Sfa0a Vdz1a PZz1a Swou0a Nay1a! Sni1a Vdz1d Pfin0b Pfinc0a Vdz1c Szr1a Pfinr0a Skp1a Pc1a Snm0a Vdz1b Pfino1a Yoo00a! Pfin1b Vpi1a Ssa21a Pfin1a Vs4o0a Pfin1d Pfin1c
Vfar1a Snm1a Pfinc1a Pfiny1a Pfin1e Vlw0a Sfa1a Pfinr1a Srout0a Pwo01a Pwo1a Vs4o1a Gsendr0a Sl160b! Vws1a Vl160f! Srout1a Vwou1a Sl160e! Nar0a! Vl160d! Pyz0b! Pyz0f! Sl160h!
Gsendr1a Vlw1a Yoo11a! Sl160a! Pyz0d! Vl160g! Sl160c! Pyz0h! Nar1a! Vl161f! Pyz0e! Sl161e! Pyz0a! Vl161h! Pyz0g! Sl161g! Pyz0c! Vl161c! Pyz1f! Sl161b! Pyz1e! Vl161a! Pyz1h!
Pyz1g! Vl161d! Pyz1c! Pyz1a! Pyz1b! Pyz1d! Syzf1a! Yoj00a! Yoyz1a! Yoj11a!
"""


def S(name, a, b, s=1): return ("s", name, 0, 128, a, b, s)


def PS(tile, a, b, s=1, p0=0, p1=128): return ("p", tile, p0, p1, a, b, s)


def IND(win, a, b, offs): return ("i", win, 0, 128, a, b, offs)


def ND(name, *ix): return ("n", name, 0, 128, ix, None, None)


def HBM(name, a=None, b=None): return ("d", name, 0, 128, a, b, 1)


def width(x):
    if x[0] == "i": return 16 * width(x[6])
    if x[0] == "n": return math.prod(len(range(*i)) for i in x[4] if isinstance(i, tuple))
    return len(range(x[4], x[5], x[6]))


def ap(T, Q, x):
    if not isinstance(x, tuple): return x
    k, name, p0, p1, a, b, s = x
    if k == "i": return T[name][:, a:b].indirect(ap(T, Q, s))
    if k == "n": return T[name][(slice(p0, p1),) + tuple(slice(*i) if isinstance(i, tuple) else i for i in a)]
    if k == "d": return T[name][:, a:b]
    t = Q(name) if k == "p" else T[name]
    return t[p0:p1, a:b:s] if s > 1 else t[p0:p1, a:b]


MASKS = {}


def places(x):
    if not isinstance(x, tuple) or x[0] == "d": return []
    k, name, p0, p1, a, b, s = x
    if k == "p": return [("ps " + name, 1)]
    if k == "i": return [(name, ((1 << (b - a)) - 1) << a)] + places(s)
    if x[1:] not in MASKS:
        cols = [0] if k == "n" else range(a, b, s)
        for n, i in zip(SCRATCH[name][1][1:], a) if k == "n" else ():
            cols = [n * o + j for o in cols for j in (range(*i) if isinstance(i, tuple) else (i,))]
        MASKS[x[1:]] = sum(1 << j for j in cols)
    return [(name, MASKS[x[1:]])]


def build_ops():
    ops, live = [], {}
    cur = [0, 0]; dry = [0]

    def op(eng, size, fn, r, w, nm, sem=None, more=()):
        k = len(ops); deps = set(more)
        rd = [y for x in r for y in places(x)]
        wr = [places(x)[0] for x in w if places(x)]
        rd += [y for x in w for y in places(x)[1:]]
        for name, m in rd:
            deps.update(j for j, m2, isw in live.get(name, []) if isw and m & m2)
        for name, m in wr:
            deps.update(j for j, m2, isw in live.get(name, []) if m & m2)
        if dry[0]: return {"eng": eng, "size": size, "fn": fn, "deps": deps, "r": r, "w": w}
        for name, m in wr:
            live[name] = [(j, m2 & ~m, isw) for j, m2, isw in live.get(name, []) if m2 & ~m] + [(k, m, True)]
        for name, m in rd:
            live.setdefault(name, []).append((k, m, False))
        ps = [x[1] for x in list(r) + list(w) if isinstance(x, tuple) and x[0] == "p"]
        ops.append({"eng": eng, "size": size, "fn": fn, "deps": deps - {k}, "ps": ps[0] if ps else None, "sem": sem, "h": cur[0], "t": cur[1], "nm": nm})
        return k

    def rate(out, in0, other):
        if in0[0] == "i": return ("gam", width(in0))
        if out[0] == "i": return ("sca", width(in0))
        return (other or (.5 if all(x[0] in "sn" and SCRATCH[x[1]][2] in (B, H16, U16) for x in (out, in0)) else 1.0), width(in0))

    def ts(out, in0, s1, s2, o0, o1=None, nm=None):
        def fn(g, T, Q):
            if o1 is None: return g.vector.tensor_scalar(ap(T, Q, out), ap(T, Q, in0), ap(T, Q, s1), None, o0)
            return g.vector.tensor_scalar(ap(T, Q, out), ap(T, Q, in0), ap(T, Q, s1), ap(T, Q, s2), o0, o1)
        return op("V", rate(out, in0, 0), fn, [in0, s1, s2], [out], nm or out[1])

    def tt(out, in0, in1, o, nm=None):
        return op("V", rate(out, in0, 1.0 if "p" in (in0[0], in1[0]) else 2.0), lambda g, T, Q: g.vector.tensor_tensor(ap(T, Q, out), ap(T, Q, in0), ap(T, Q, in1), o), [in0, in1], [out], nm or out[1])

    def cp(out, in_, nm=None):
        return op("V", rate(out, in_, 0), lambda g, T, Q: g.vector.tensor_copy(ap(T, Q, out), ap(T, Q, in_)), [in_], [out], nm or out[1])

    def scan(out, d0, d1, o0, o1, first=0.0):
        return op("V", (1.0, width(d0)), lambda g, T, Q: g.vector.tensor_tensor_scan(ap(T, Q, out), ap(T, Q, d0), ap(T, Q, d1), first, o0, o1), [d0, d1], [out], out[1])

    def many(e, calls, nm):
        dry[0] += 1; its = [c() for c in calls]; dry[0] -= 1
        return op(e, (1.0, 64 * len(its)), lambda g, T, Q: [x["fn"](g, T, Q) for x in its], [y for x in its for y in x["r"]], [y for x in its for y in x["w"]], nm)

    def ms(out, val):
        return op("V", rate(out, out, 0), lambda g, T, Q: g.vector.memset(ap(T, Q, out), val), [], [out], out[1])

    def act(out, in_, func, bias=0.0, scale=1.0, nm=None):
        return op("S", rate(out, in_, 1.0), lambda g, T, Q: g.scalar.activation(ap(T, Q, out), ap(T, Q, in_), func, bias=ap(T, Q, bias), scale=ap(T, Q, scale)), [in_, bias, scale], [out], nm or out[1])

    def mm(items, nm=None, closes=False, behind=()):
        def fn(g, T, Q):
            ins = None; first, last = Q("ends")
            for j, it in enumerate(items):
                ins = g.tensor.matmul(ap(T, Q, it[0]), ap(T, Q, it[1]), ap(T, Q, it[2]), first and j == 0, last and all(x[0][2] != it[0][2] for x in items[j + 1:]))
            return ins
        tl = items[0][0][1]; mine = live.setdefault("ps " + tl, [])
        k = op("P", ("pe", sum(max(min(64, width(l)), width(r)) for o, l, r in items)), fn, [x for it in items for x in it[1:]], [],
               nm or "".join(x for x in tl if x.isalpha()), more=[j for j, m, w in mine] if closes else behind)
        ops[k]["ps"] = tl; mine.append((k, 1, True))
        return k

    def steps(items):
        return mm(items[1:], behind=[mm(items[:1], "".join(x for x in items[0][0][1] if x.isalpha()) + "0")])

    def either(one, other, nm=None):
        dry[0] += 1; alt = other(); dry[0] -= 1
        k = one(); ops[k]["deps"] |= alt["deps"]; ops[k]["alt"] = alt; ops[k]["nm"] = nm or ops[k]["nm"]
        return k

    def move(out, in_, add=0.0, nm=None):
        return either(lambda: act(out, in_, ACT.Identity, add), lambda: ts(out, in_, add, None, ALU.add) if add else cp(out, in_), nm)

    def lin(out, in_, scale, bias=0.0, nm=None):
        return either(lambda: act(out, in_, ACT.Identity, bias, scale), lambda: ts(out, in_, scale, bias, ALU.mult, ALU.add), nm)

    def const(out, v):
        if SCRATCH[out[1]][2] == H16: return lin(out, S("one", 0, width(out)), 0.0, v)
        return either(lambda: act(out, S("one", 0, width(out)), ACT.Identity, v, 0.0), lambda: ms(out, v))

    def dma(q, out, in_, sem):
        return op(q, (0.0, 0), lambda g, T, Q: (g.sync if q == "Y" else g.scalar).dma_start(ap(T, Q, out), ap(T, Q, in_)), [in_], [out], sem, sem)

    def iota(name, n, pat, cm, a=0):
        def fn(g, T, Q):
            if SCRATCH[name][2] == I32: return g.iota(T[name][:, a:a + n], pat, 0, cm)
            return g.iota(T[name][:, a:a + n], pat, 0, cm, allow_small_or_imprecise_dtypes=True)
        op("G", ("g", 160 + 2 * n), fn, [], [S(name, a, a + n)], name)

    def hand(out, in_, pat=None, cm=0, how=ALU.is_ge, fill=0.0):
        n = width(in_)
        return op("G", ("g", 205 + 2 * n), lambda g, T, Q: g.affine_select(ap(T, Q, out), ap(T, Q, in_), pat or [[0, n]], how, fill, 0, cm), [in_], [out], out[1])

    def col(j): return S("cf", j, j + 1)

    def full(name): return S(name, 0, 128)

    def cst(name, n=PW): return S(name, 0, n)

    def tmp(j): return S("tmp", 128 * j, 128 * j + 128)

    def hk(name, k): return S(name, 15 - k, 143 - k)

    dma("Y", S("ji", 0, P), HBM("jur"), "ljur")
    dma("S", S("yin", 0, P), HBM("own"), "lown")
    for h in range(NH):
        move(S("rin", h * PW, h * PW + PW), S("ji", h * PW, h * PW + PW), nm="ru")
    dma("Y", S("xw", 0, W), HBM("xc"), "lx")
    dma("Y", S("li", 0, W), HBM("lsr"), "ll0")
    dma("Y", S("wi", 0, 1), HBM("wgt"), "lwgt")

    first = len(ops)
    ms(S("one", 0, 144), 1.0)
    iota("ci", 1, [[0, 1]], 1)
    iota("ioc", 144, [[1, 144]], 0)
    iota("iob", 128, [[16, 8], [0, 16]], 0)
    iota("iom", 128, [[0, 8], [1, 16]], 0)
    iota("ioj", PW, [[16, PW // 16], [PW, 16]], 0)
    iota("iok", 144, [[0, 16], [16, 9]], 0)
    iota("ni", NH * 272, [[0, NH * 272]], 0)
    for j in range(2 * NH):
        iota("dm", 16, [[0, 16]], 0, DMS * j)
    cp(col(0), S("ci", 0, 1))
    ts(S("ci", 4, 5), S("ci", 0, 1), 15, None, ALU.bitwise_and)
    cp(col(1), S("ci", 4, 5))
    tt(col(2), col(0), col(1), ALU.subtract)
    ts(col(3), col(2), 15.0, None, ALU.add)
    ts(col(5), col(1), 37.0 * 32, -2.0 ** 23, ALU.mult, ALU.add)
    ts(col(6), col(1), 1.0, None, ALU.add)
    ts(col(7), col(1), 0.0, None, ALU.is_equal)
    ts(col(8), col(7), -17.0 / 128, 1.0 / 128, ALU.mult, ALU.add)
    tt(col(9), col(7), col(1), ALU.subtract)
    ts(col(14), col(9), 1.0 / 64, 65.0 / 128, ALU.mult, ALU.add)
    ts(full("idn"), full("ioc"), col(0), None, ALU.is_equal)
    for nme, sc in (("nid", -1.0), ("q25", -.25), ("ida", AN), ("i32", -2.0)):
        lin(full(nme), full("idn"), sc)
    for c in range(2):
        iota("iox", 128, [[1, 8], [8 - 16 * c, 2], [16, 8]], -1, 128 * c)
        ts(S("idx", 128 * c, 128 * c + 128), S("iox", 128 * c, 128 * c + 128), -8.0 * c, None, ALU.is_equal)
        const(ND("nl", (32 * c + 1, 32 * c + 32, 2), (0, KK)), 0.0)
    const(ND("zr", (0, 18 * NH, 2), (0, KK)), 0.0)
    ts(S("hh", 0, 144), S("ioc", 0, 144), col(3), None, ALU.is_equal)
    for nme, sc in (("hz", 1.0 / 32), ("hp", PEN * 89 / 2048), ("hs", 32.0 * PW)):
        lin(S(nme, 0, 144), S("hh", 0, 144), sc)
    ts(full("bo"), full("iob"), col(2), None, ALU.is_equal)
    lin(cst("o8", 8), S("bo", 0, 128, 16), 1.0 / 64)
    for c in range(2):
        lin(S("b16", 8 * c, 8 * c + 8), S("bo", 0, 128, 16), 1.0)
    for nme, sc in (("nbo", -1.0), ("boa", AN), ("nba", -AN), ("by", AN / 32)):
        lin(full(nme), full("bo"), sc)
    for j, (nme, off, dg) in enumerate((("mA", 1.0 / 64, -39.0 / 64), ("mB", -1.0 / 64, 89.0 / 128))):
        lin(tmp(j), full("bo"), off)
        hand(full(nme), tmp(j), [[1, 128]], -1, ALU.not_equal, off + dg)
    lin(full("th"), full("bo"), 1.0 / 128)
    hand(tmp(2), full("th"), [[1, 128]], -1, ALU.is_gt)
    hand(full("tri"), tmp(2), [[1, 128]], -1, ALU.not_equal, -1.0 / 128)
    lin(S("tri", 0, 128, 16), S("bo", 0, 128, 16), col(8))
    for k in range(16):
        lin(S("nc", 143 * k, 143 * k + 128), full("idn"), 32.0)
    ts(S("tmp", 640, 784), S("iok", 0, 144), col(2), None, ALU.is_equal)
    hand(S("nc", 0, 16 * 144, 16), S("tmp", 640, 784), [[1, 16], [16, 9]], -1, ALU.not_equal, 33.0)
    ts(S("kb", 0, PW), S("ioj", 0, PW), 16.0, col(1), ALU.add, ALU.add)
    lin(cst("cm"), cst("one"), 0.0, col(14))
    for nme, v, n in (("c1", M1, PW), ("c32", M32, P), ("c4096", M4096, PW), ("c155", 15.5, P), ("c2048", 2048.0, PW), ("cp", M1 * PEN, PW), ("c4", 4 * M1, 4), ("non", -1.0, 128)):
        const(cst(nme, n), v)
    for j, v in enumerate((0.0, -1.0, -39.0 / 64, 39.0 / 128)):
        const(S("f0", j, 4 * PW, 4), v)
    ts(col(17), col(1), 1.0, -0.5, ALU.is_equal, ALU.mult)
    ts(col(22), col(7), 2048.0, col(17), ALU.mult, ALU.add)
    const(S("cc", 0, 128, 2), 0.0)
    lin(S("cc", 1, 128, 2), cst("iom"), 0.0, col(22))
    for a in (0, 128):
        const(S("td", a, a + 128), -64 * PEN)
    const(S("td", PW, 2 * PW, 16), 5 * PEN)
    for a, b, v, w in ((0, 4, -1.0, 0.0), (4, 5, -PEN / 2, 5.5 * PEN), (5, 8, 1.0, 0.0)):
        const(S("ca", a, b), v)
        const(S("da", a, b), w)
    ts(cst("rsk"), cst("iom"), 0.0, 4 * PEN, ALU.is_equal, ALU.mult)
    ts(full("rs16"), full("iom"), 0.0, -BIG, ALU.is_equal, ALU.mult)
    ts(tmp(3), full("iom"), col(1), -16384.0, ALU.not_equal, ALU.mult)
    lin(tmp(4), full("ioc"), 32.0)
    mm([(PS("wb", 0, P), full("idn"), tmp(j)) for j in (3, 4)])
    move(full("wb"), PS("wb", 0, P))
    lin(S("hj", 0, 144), S("hh", 0, 144), col(6))
    ts(col(11), S("wi", 0, 1), 2048.0, -4096.0, ALU.is_ge, ALU.mult)
    tt(col(12), col(11), S("wi", 0, 1), ALU.add)
    ts(col(15), col(1), 1.0 / 128, col(14), ALU.mult, ALU.add)
    lin(cst("cn"), cst("one"), -1.0 / 128, col(15))
    lin(full("wp"), full("bo"), col(12))
    lin(full("wn"), full("nbo"), col(12))
    for o in ops[first:]: o["const"] = True
    IDN, NID = full("idn"), full("nid")

    def modulo(out, Y, big):
        return [(out, full("wn"), Y), (out, NID, big), (out, IDN, big), (out, full("wp"), Y)]

    sends = {}
    for t in range(V):
        a = t & 1; cur[1] = t
        for h in range(NH):
            cur[0] = h
            v = "%d_%d" % (t, h)
            o = a * P + h * PW; ob = a * 2048 + h * 16 * PW; oi = t * P + h * PW; o3 = a * NH + h; n16 = 16 * PW; on = 2 * o

            def sm(name): return S(name, o, o + PW)

            def four(name): return S(name, 8 * o3, 8 * o3 + PW // 16)

            def cube(name, r=(0, 16), k=(0, 16), i0=0, i1=PW): return ND(name, ((o + i0) // 16, (o + i1) // 16), r, k)

            def s4(j, s=4): return S("s4", (4 * PW + 4) * o3 + j, (4 * PW + 4) * o3 + j + 4 * PW, s)

            def half(name, j): return S(name, ob + 512 * j, ob + 512 * j + 512)

            def picks(win, offs, at, j): return IND(win, 0, W, S(offs, at + PW // 2 * j, at + PW // 2 * (j + 1)))

            def juror(name, k, s=16): return S(name, ob + k, ob + n16, s)

            def km(k0, k1): return S("dm", DMS * o3 + 16 + PW * k0, DMS * o3 + 16 + PW * k1)

            RU, YIN, YN = S("rin", oi, oi + PW), S("yin", oi, oi + PW), S("yout", oi, oi + PW)
            if t:
                op("N", (0.0, 0), None, [], [RU], "ar", "ar" + v, [sends["r%d_%d" % (t - 1, h)]])
                op("N", (0.0, 0), None, [], [YIN], "ay", "ay" + v, [sends["y%d_%d" % (t - 1, h)]])
            via = not t and h
            if via:
                for j in range(2):
                    move(half("yb", j), picks("xw", "rin", oi, j))
                for c in range(2):
                    tl = "Dx%s_%d" % (v, c)
                    k = mm([(PS(tl, j, 512, KK), NID, YIN) for j in range(KK)], "fillDx")
                    for j in range(2):
                        mm([(PS(tl, 256 * j, 256 * j + 256), IDN, S("yb", ob + 512 * j + c, ob + 512 * j + 512, 2))], behind=[k])
                    act(cube("ad", k=(c, 16, 2)), PS(tl, 0, 512), ACT.Abs)
            else:
                for j in range(2):
                    many("S", [lambda k=k: act(juror("yb", k), YIN, ACT.Identity) for c in range(4 * j, 4 * j + 4) for k in (c, c + 8)], "yb")
                for j in range(2):
                    tt(half("xd", j), picks("xw", "rin", oi, j), half("yb", j), ALU.subtract)
            either(lambda: cp(s4(3), RU), lambda: hand(s4(3), RU), "rf")
            lin(s4(5), s4(3), 32.0, col(5), "kp")
            for c in range(2):
                if via: ts(cube("nx", k=(c, 16, 2)), cube("ad", k=(c, 16, 2)), 1.0, None, ALU.is_le)
                else: act(cube("ad", i0=32 * c, i1=32 * c + 32), half("xd", c), ACT.Abs)
            for c in range(2) if not via else ():
                ts(cube("nx", i0=32 * c, i1=32 * c + 32), half("xd", c), M4, M4, ALU.add, ALU.is_equal)
            for j in range(2):
                move(half("lg", j), picks("li", "rin", oi, j), -2048.0)
            mm([(PS("Nt" + v, j, 2 * PW, KK), juror("lg", j, KK), S("idx", 16 * ((j + t) % 16), 16 * ((j + t) % 16) + 16)) for j in range(KK)])
            move(ND("nl", (32 * h, 32 * h + 32, 2), (0, KK)), PS("Nt" + v, 0, 2 * PW))
            out = PS("n" + v, 0, PW)
            mm([(out, IDN, cst("c2048"))] + [(out, ND("nl", (32 * h + 15 * c, 32 * h + 15 * c + 16), (0, KK)), S("idn", c, 128, 2)) for c in range(2)])
            move(sm("nu"), out)
            tt(s4(2), out, s4(3), ALU.subtract, "nr")
            for j in range(2):
                either(lambda: act(half("zg", j), picks("xw", "nu", o, j), ACT.Identity, 0.0, AN), lambda: ts(half("zg", j), picks("xw", "nu", o, j), AN, None, ALU.mult))
            out = PS("nb" + v, 0, PW)
            for c in range(2):
                mm([(out, S("nc", 143 * k, 143 * k + 128), cube("nx", k=k)) for k in (range(c, 16, 2) if via else range(KK * c, KK * c + KK))])
            if h: ts(sm("good"), out, 248.0, 2.0, ALU.is_ge, ALU.mult)
            else: act(sm("good"), out, ACT.Sign, -247.5)
            move(sm("nbv"), out, -8.0)
            out = PS("Dm" + v, 0, PW)
            steps([(out, lhs, rhs) for lhs, rhs in ((IDN, cst("cm" if h else "cn")), (full("tri"), sm("good")), (IDN, cst("c1")), (NID, cst("c1")))])
            if via: move(sm("mk"), out)
            for q in range(4):
                if via: many("V", [lambda j=j: tt(km(2 * j + q // 2, 2 * j + q // 2 + 1), PS("Dx%s_%d" % (v, q // 2), j, 512, KK), sm("mk"), ALU.mult) for j in range(q % 2 * 4, q % 2 * 4 + 4)], "dm")
                else: many("V", [lambda k=k: tt(km(k, k + 1), juror("xd", k), out, ALU.mult) for k in range(4 * q, 4 * q + 4)], "dm")
            out = PS("K" + v, 0, PW)
            ks = [mm([(out, hk("hp", r), cube("nx", r=r)) for r in range(r0, r0 + KK)], "Kn") for r0 in (0, KK)]
            k = mm([(out, IDN, cst("cp")), (out, NID, cst("cp")), (out, IDN, cst("kb"))], "Kr", behind=ks)
            for r0 in (0, KK):
                mm([(out, hk("hs", r), cube("ad", r=r)) for r in range(r0, r0 + KK)], "Ka", behind=[k])
            KV = S("kv", o + 15, o + PW, 16)
            scan(sm("km"), cst("rsk"), out, ALU.add, ALU.min)
            scan(sm("kv"), S("td", 128 * a + PW, 128 * a + 2 * PW), out, ALU.max, ALU.subtract)
            ts(four("ka"), S("km", o + 15, o + PW, 16), 32 * PW - 1, None, ALU.bitwise_and)
            tt(four("kt"), four("ka"), KV, ALU.min)
            move(four("ko"), four("kt"))
            tt(YN, IND("dm", DMS * o3, DMS * o3 + 16 + n16, four("ko")), YIN, ALU.add)
            if t < V - 1: either(lambda: act(four("lf"), KV, ACT.Sign), lambda: ts(four("lf"), KV, 0.0, 2.0, ALU.is_gt, ALU.mult))
            tl = "Kd" + v; at = 272 * h + 8
            ks = [mm([(PS(tl, j, 2 * PW, 8), km(2 * j, 2 * j + 2), cst("b16", 16)) for j in (j0, j0 + 1)]) for j0 in range(0, KK, 2)]
            for Y, b in ((YIN, "bo"), (YN, "nbo")):
                mm([(PS(tl, PW, 2 * PW, 1, PW * c, PW * c + PW), Y, S(b, 0, 128, 2)) for c in range(2)], "ddz", behind=ks)
            lin(S("ni", at, at + 256, 2), PS(tl, 0, 2 * PW), AN, 1.0)

            def send(kind, src, dst):
                def fn(g, T, Q, t=t, h=h):
                    return g.remote_dma(ap(T, Q, dst), ap(T, Q, src), T.sem["a%s%d_%d" % (kind, t + 1, h)], T.sem.sent, Q("pid"), Q("rid"), Q("mask"))
                sends["%s%d_%d" % (kind, t, h)] = op("G", ("rem", 1), fn, [src], [], "send" + kind, "remote")
            send("y", YN, S("yin", oi + P, oi + P + PW))
            out = PS("c2" + v, 0, PW)
            k = mm([(out, NID, sm("nbv")), (out, IDN, cst("c32")), (out, NID, cst("c32")), (out, IDN, sm("nbv"))], "c0")
            mm([(out, full("nba"), YIN), (out, full("boa"), YN)], "cy", behind=[k])
            mm([(out, S("ni", at + 128 * s - c, at + 128 * s + 128 - c), S(b, PW * c, PW * c + PW)) for s, b in enumerate(("nid", "idn")) for c in range(2)], behind=[k])
            act(sm("sa2"), out, ACT.Sign, -3.5)
            tl = "u" + v
            steps([(PS(tl, 0, 2 * PW), full("bo"), full("cc"))] + modulo(PS(tl, 1, 2 * PW, 2), YN, cst("c4096")))
            scan(S("pi", on, on + 2 * PW), PS(tl, 0, 2 * PW), s4(3, 2), ALU.mult, ALU.add)
            ts(sm("pj"), S("pi", on + 1, on + 2 * PW, 2), 5, W - 1, ALU.arith_shift_right, ALU.bitwise_and, "far")
            move(s4(0), sm("pj"), nm="fa")
            move(s4(1), sm("nu"), nm="nm")
            out = PS("Dz" + v, 0, PW)
            mm([(out, IDN, cst("non")), (out, full("ida"), YN)], "fillDz")

            def pair(j, c): return S("dz", ob + P * j + c, ob + P * j + P, 2)
            for j0 in range(0, KK, 2):
                many("V", [lambda j=j, c=c: tt(pair(j, c), juror("zg", j + KK * c), out, ALU.subtract) for j in (j0, j0 + 1) for c in range(2)], "dz")
            mm([(PS("Zt" + v, j, PW, KK), juror("zg", j, KK), cst("o8", 8)) for j in range(KK)], "Zz")
            move(ND("zr", (18 * h + 1, 18 * h + 17, 2), (0, KK)), PS("Zt" + v, 0, PW))
            tl = "fin" + v
            TF, CH = PS(tl, 2, 4 * PW, 4), PS(tl, 3, 4 * PW, 4)
            k = mm([(PS(tl, 0, 4 * PW), IDN, S("f0", 0, 4 * PW))], "fino")
            mm([(CH, full("mB"), sm("sa2")), (CH, IDN, cst("c1")), (CH, full("mA"), sm("sa2")), (CH, NID, cst("c1")), (TF, full("q25"), sm("sa2"))], "finc", behind=[k])
            mm([(TF, ND("zr", (18 * h + 1 - c, 18 * h + 17 - c), (0, KK)), S("i32", c, 128, 2)) for c in range(2)], behind=[k])
            mm([(TF, full("by"), YN)], "finy", behind=[k])
            for j0 in range(0, KK, 2):
                mm([(TF, hk("hz", j + KK * c), pair(j, c)) for j in (j0, j0 + 1) for c in range(2)], behind=[k])
            mm([(TF, IDN, cst("c1")), (TF, NID, cst("c1"))], "finr", True)
            scan(S("s4o", 4 * o, 4 * o + 4 * PW), PS(tl, 0, 4 * PW), s4(0, 1), ALU.mult, ALU.add)
            RN = S("rout", oi, oi + PW) if t < V - 1 else S("rlast", h * PW, h * PW + PW)
            move(RN, S("s4o", 4 * o + 3, 4 * o + 4 * PW, 4), nm="rout")
            send("r", RN, S("rin", oi + P, oi + P + PW) if t < V - 1 else S("rfin", h * PW, h * PW + PW))
        cur[0] = 0
        if t < V - 1:
            tl = "A%d" % t; out = PS(tl, 0, 4); lfs = [S("lf", 8 * (a * NH + h), 8 * (a * NH + h) + 4) for h in range(NH)]
            mm([(PS(tl, 0, 8), IDN, cst("ca", 8))] + [(out, full("one"), x) for x in lfs] + [(out, IDN, cst("c4", 4)), (out, NID, cst("c4", 4))]
               + [(out, full("non"), x) for x in lfs] + [(out, IDN, cst("one", 4))])
            scan(S("td", 128 * (1 - a), 128 * (1 - a) + 128, 16), PS(tl, 0, 8), cst("da", 8), ALU.mult, ALU.add, 1.0)
        for h in range(NH):
            cur[0] = h; o = a * P + h * PW
            Y = S("yout", t * P + h * PW, t * P + h * PW + PW); out = PS("wo%d_%d" % (t, h), 0, PW)
            steps([(out, IDN, cst("c155"))] + modulo(out, Y, cst("c32")) + [(out, IDN, cst("wb"))])
            scan(S("ws", o, o + PW), cst("rs16"), out, ALU.add, ALU.max)
            offs = S("wou", 16 * a + 4 * h, 16 * a + 4 * h + 4)
            move(offs, S("ws", o + 15, o + PW, 16))
            if t < V - 1: cp(IND("xw", 32 * PW * h, 32 * PW * (h + 1), offs), Y, "xw")
            cp(IND("li", 32 * PW * h, 32 * PW * (h + 1), offs), S("s4o", 4 * o + 3, 4 * o + 4 * PW, 4), "lw")
    cur[1] = V
    for h in range(NH):
        cur[0] = h
        v = "%d_%d" % (V, h); oi = V * P + h * PW
        op("N", (0.0, 0), None, [], [S("rfin", h * PW, h * PW + PW)], "ar", "ar" + v, [sends["r%d_%d" % (V - 1, h)]])
        op("N", (0.0, 0), None, [], [S("yin", oi, oi + PW)], "ay", "ay" + v, [sends["y%d_%d" % (V - 1, h)]])
        dma("Y", HBM("yo", h * PW, h * PW + PW), S("yin", oi, oi + PW), "oo%d" % h)
        dma("Y", HBM("yj", h * PW, h * PW + PW), S("rfin", h * PW, h * PW + PW), "oj%d" % h)
    for c in range(16):
        cur[0] = c // KK
        move(S("l16", 256 * c, 256 * c + 256), S("li", 256 * c, 256 * c + 256), -2048.0)
        mm([(PS("yz", 0, 256), hk("hj", c), S("l16", 256 * c, 256 * c + 256))])
    act(S("yzf", 0, 256), PS("yz", 0, 256), ACT.Identity, 2048.0 * 136)
    dma("Y", HBM("yz"), S("yzf", 0, 256), "oyz")
    return ops


def slots(ops):
    seen = {}; out = []
    for o in ops:
        kd = (o["t"], "-" + o["nm"] + str(o["h"])); seen[kd] = seen.get(kd, 0) + 1
        out.append((min(o["t"], 1) if o["t"] < V - 1 else o["t"] - V + 3, kd[1], seen[kd]))
    return out


def places_of(ops, lists):
    name = slots(ops); its = lists[1].split(); n = len(its); key = []; form = []
    at = {x.rstrip("'")[1:]: (j + n * x.count("'"), x[0]) for j, x in enumerate(its)}
    for ph in (0, 2):
        base = -1e5
        for j, x in enumerate(lists[ph].split()):
            if ":" in x: base = at[x[1:-2]][0] + n * int(x[-1])
            else: at[ph, x[1:]] = (base + j * 1e-3, x[0])
    for (ph, nm, piece), o in zip(name, ops):
        w = nm[1:] + "abcdefghijklmnopqrstuvwxyz"[piece - 1]
        x, e = at[w] if ph == 1 else at[min(ph, 2), w + "!" * (ph == 3)]
        key.append(x + n * o["t"] * (ph == 1)); form.append(int(e != o["eng"]))
    return key, form


def arrange(ops, key):
    rem = {}
    for k, o in enumerate(ops):
        key[k] = max([key[k]] + [key[d] for d in o["deps"]])
        rem[o["ps"]] = rem.get(o["ps"], 0) + 1
    bank = {}; last = [-1] * 8; free = list(range(8)); order = []; extras = [-1] * len(ops); held = []; done = set()

    def take(k):
        tl = ops[k]["ps"]
        if not ops[k]["deps"] <= done or (tl and tl not in bank and not free): return False
        if tl:
            if tl not in bank:
                bank[tl] = free.pop(0); extras[k] = last[bank[tl]]
            elif ops[last[bank[tl]]]["eng"] != ops[k]["eng"]: extras[k] = last[bank[tl]]
            last[bank[tl]] = k; rem[tl] -= 1
            if rem[tl] == 0: free.append(bank[tl])
        order.append(k); done.add(k)
        return True
    for k in sorted(range(len(ops)), key=lambda k: key[k]):
        if not take(k):
            held.append(k)
            continue
        j = 0
        while j < len(held):
            if take(held[j]):
                del held[j]; j = 0
            else: j += 1
    return order, bank, extras


PLAN = []


def rank_program(g, core, T, topo):
    rank = T.rank_of(core)
    if rank is None:
        return
    if not PLAN:
        ops = build_ops(); key, form = places_of(ops, (FIRST, ROUND, LAST))
        ops = [dict(o, eng=o["alt"]["eng"], fn=o["alt"]["fn"]) if f else o for o, f in zip(ops, form)]
        PLAN.append((ops,) + arrange(ops, key))
    ops, order, bank, extras = PLAN[0]
    nxt = T.cores[(rank + 1) % len(T.cores)]; prv = T.cores[(rank - 1) % len(T.cores)]
    rid, pid, _ = topo.addr(nxt)
    env = {"rid": rid, "pid": pid, "mask": topo.mask(core, nxt)}
    n_out, n_in = len(topo.engines(core, nxt)), len(topo.engines(prv, core))
    todo = {}; opened = set()
    for o in ops:
        if o["eng"] == "P": todo[o["ps"]] = todo.get(o["ps"], 0) + 1

    def Q(name):
        return env[name] if name in env else T["pb%d" % bank[name]]
    queue = {"V": g.vector, "S": g.scalar, "P": g.tensor, "G": g, "Y": g.sync}
    count = {e: 0 for e in "VSPG"}; known = {e: {} for e in queue}; mark = {}; top = {}; sent = 0
    for k in order:
        o = ops[k]; e = o["eng"]
        if e == "N":
            mark[k] = (o["sem"], n_in, {})
            continue
        kn = known[e]
        need = sorted((mark[d] for d in o["deps"] | {extras[k]} if d in mark and not (e == "P" and ops[d]["eng"] == "P")), key=lambda m: -m[1])
        for sem, val, clock in need:
            if kn.get(sem, 0) >= val or any(c2.get(sem, 0) >= val for s2, v2, c2 in need): continue
            queue[e].wait_ge(T.sem[sem], val)
            kn[sem] = val
        for sem, val, clock in need:
            for s2, v2 in list(clock.items()) + [(sem, val)]:
                if kn.get(s2, 0) < v2: kn[s2] = v2
        if e == "P":
            tl = o["ps"]; todo[tl] -= 1; env["ends"] = (tl not in opened, todo[tl] == 0); opened.add(tl)
        ins = o["fn"](g, T, Q)
        if o["sem"] == "remote":
            sent += n_out
        elif o["sem"]:
            ins.then_inc(T.sem[o["sem"]], 16); mark[k] = (o["sem"], 16, dict(kn)); top[o["sem"]] = 16
        else:
            for x in ins if isinstance(ins, list) else [ins]:
                count[e] += 1; x.then_inc(T.sem["c" + e], 1)
            mark[k] = ("c" + e, count[e], dict(kn)); top["c" + e] = count[e]
    g.wait_ge(T.sem.sent, sent)
    for sem, val in top.items():
        if sem[0] in "co": g.wait_ge(T.sem[sem], val)
